import numpy as np, ml_dtypes
CORES = [6,15,38,47]
N = 4
BF = ml_dtypes.bfloat16
S, L, CAP, RO, KM = 4096, 256, 64, 6, 3967
W = S + RO * CAP
def joined(c, T):
    e = np.add.accumulate(4 + (c & 3), axis=1)
    j = np.minimum(np.sum(e[:, :, None] <= (5 * np.arange(L) + 2)[None, None, :], axis=1), L - 2)
    p = np.take_along_axis(c, j, 1); q = np.take_along_axis(c, j + 1, 1)
    left = np.take_along_axis(T, p[:, None, :], 2)[:, 8:]; right = np.take_along_axis(T, q[:, None, :], 2)[:, :8]
    return p, np.concatenate([left, right], axis=1).astype(np.int64)
def places(z, w, k):
    u = np.sum(z * w[:, :, 0:1], axis=1) & (S - 1); v = np.sum(z * w[:, :, 1:2], axis=1) & (S - 1)
    return (((u * v) >> 5)[:, None, :] + k[:, :, None] * u[:, None, :]) & (S - 1)
def probe(z, w, k, b, U):
    h = places(z, w, k)
    d = np.stack([np.sum(np.abs(np.take_along_axis(U, h[:, m:m + 1], 2) - z), axis=1) for m in range(16)], axis=1)
    m = np.argmin(d, axis=1)[:, None, :]
    return np.take_along_axis(h, m, 1)[:, 0], np.take_along_axis(d, m, 1)[:, 0] < b[:, None]
def lowest(h, fit):
    win = np.zeros(fit.shape, bool)
    for g in range(8):
        i = np.flatnonzero(fit[g]); win[g, i[np.unique(h[g, i], return_index=True)[1]]] = True
    return win
def parts(rng):
    return (rng.integers(0, 256, (N, 8, 16, S), dtype=np.int16), rng.integers(0, 256, (N, 8, 16, S), dtype=np.int16), rng.integers(0, S, (N, 8, L)),
            rng.integers(0, 4096, (N, 8, 16, 2)), rng.integers(0, KM + 1, (N, 8, 16)), rng.integers(840, 1040, (N, 8)))
def pack(us, tp, c, w, k, th):
    return {"us": us.reshape(N, 128, S).astype(np.float32).astype(BF), "tp": tp.reshape(N, 128, S).astype(np.float32).astype(BF), "c0": np.ascontiguousarray(c).astype(np.int32),
            "hw": np.ascontiguousarray(w.reshape(N, 128, 2)).astype(np.int32), "km": np.ascontiguousarray(k.reshape(N, 128, 1)).astype(np.int32), "th": np.ascontiguousarray(th.reshape(N, 8, 1)).astype(np.int32)}
def setup_inputs(rng):
    return pack(*parts(rng))
def near(z, d):
    a = d[None, :] // 16 + (np.arange(16)[:, None] < d[None, :] % 16)
    return np.where(z < 128, z + a, z - a)
def setup_inputs_corners(rng):
    us, tp, c, w, k, th = parts(rng); w[:, :, 0, 0] |= 1; cnt = (0, 1, CAP - 1, CAP, CAP + 1, L); used = {}; sent = {}; zs = []
    def plant(q, g, h, z, todo):
        st, sl, ds = [], [], []
        for i, d in todo:
            r = int(rng.integers(0, 16)); cand = h[:, i].tolist()
            for m in range(16):
                s = cand[(m + r) % 16]
                if s not in used[q, g]:
                    used[q, g].add(s); st.append(s); sl.append(i); ds.append(d); break
        if st: us[q, g][:, np.array(st)] = near(z[:, np.array(sl)], np.array(ds))
    for q in range(N):
        for g in range(8):
            v = (g + q) % 8; used[q, g] = set()
            if v == 6: c[q, g] = 4 * rng.integers(0, S // 4, L) + 3; c[q, g, :3] = S - 1
            elif v == 7: c[q, g] = 4 * rng.integers(0, S // 4, L); c[q, g, L - 3:] = 0
            else: c[q, g] = 4 * rng.permutation(S // 4)[:L] + 1; k[q, g] = rng.permutation(min(S, KM + 1))[:16]; th[q, g] = rng.choice(np.array([1, 2, 64, 100]))
            if v in (1, 2, 3): us[q, g, :, 0] = 0; used[q, g].add(0)
        p, z = joined(c[q], tp[q]); even = (np.sum(z * w[q, :, :, 0:1], axis=1) & 1) == 0
        for g in range(8):
            if (g + q) % 8 < 6: tp[q, g, 8, np.unique(p[g, even[g]])] ^= 1
        p, z = joined(c[q], tp[q]); zs.append(z); h = places(z, w[q], k[q])
        for g in range(8):
            v = (g + q) % 8
            if v > 5: continue
            n = cnt[v]; pair = 2 if n >= 2 else 0; front = rng.permutation(L - 2).tolist(); t = int(th[q, g])
            poor = front[:n - pair] + ([L - 2, L - 1] if pair else []); fits = front[n - pair:] + ([] if pair else [L - 2])
            plant(q, g, h[g], z[g], [(i, (t - 1) * int(rng.integers(0, 2))) for i in fits] + [(i, t) for i in poor if i < L - 1 and rng.random() < 0.5])
            sent[q, g] = sorted(poor)[:CAP]
    for q in range(N):
        a = (q + 1) % N; h = places(zs[q], w[a], k[a])
        for g in range(8):
            if (q, g) in sent:
                t = int(th[a, g]); full = (g + q) % 8 == 4
                plant(a, g, h[g], zs[q][g], [(i, (0, t - 1, t)[int(rng.integers(0, 2 if full else 3))]) for i in sent[q, g] if i < L - 1 and (full or rng.random() < 0.6)])
    return pack(us, tp, c, w, k, th)
def setup_inputs_ends(rng):
    us = 255 * rng.integers(0, 2, (N, 8, 16, S), dtype=np.int16); tp = 255 * rng.integers(0, 2, (N, 8, 16, S), dtype=np.int16)
    inner = np.argsort(rng.random((N, 8, L)), axis=-1) < 5 * L // 16; anyc = rng.integers(0, S, (N, 8, L)); roll = rng.random((N, 8, L))
    w = 4095 * rng.integers(0, 2, (N, 8, 16, 2)); w[:, :, 0, 0] = 0; w[:, :, 1, 0] = 4095
    k = np.where(np.argsort(rng.random((N, 8, 16)), axis=-1) < 4, rng.integers(0, KM + 1, (N, 8, 16)), KM * rng.integers(0, 2, (N, 8, 16)))
    th = np.stack([4080 * (rng.permutation(8) % 2) for q in range(N)]); big = np.stack([rng.permutation(8) < 4 for q in range(N)]); big[:, 7] = True; big[0, 0] = True
    if th[N - 1, 7] == 0: th[N - 1, int(np.argmax(th[N - 1]))] = 0; th[N - 1, 7] = 4080
    c = np.where(inner, anyc, (S - 1) * (roll < 0.5)); base = ((S - 1) ** 2 >> 5) & (S - 1); one = np.zeros(16, np.int16); one[0] = 1
    for q in range(N):
        for g in range(8):
            if not big[q, g]: continue
            w[q, g] = 4095; us[q, g, :, 0] = 255; tp[q, g, :, 0] = 255; tp[q, g, :, S - 1] = 0; tp[q, g, :, S - 2] = 0; tp[q, g, 8, S - 2] = 1
            far = (S - 1, 1, 2) if g == 7 or rng.random() < 0.5 else (2, S - 1, 1)
            for lane, s in zip((1, 14, 15), far): k[q, g, lane] = (base - s) & (S - 1); us[q, g, :, s] = one
            k[q, g, 0] = 0; k[q, g, 2] = KM
            c[q, g] = np.where(inner[q, g], anyc[q, g] // 4 * 4, (S - 1) * (roll[q, g] < 0.2))
            if rng.random() < 0.5: c[q, g, 0] = S - 2; c[q, g, 1] = S - 1
            c[q, g, 4:6] = S - 1; c[q, g, 6:9] = 0; c[q, g, L - 2] = S - 2; c[q, g, L - 1] = S - 1
    return pack(us, tp, c, w, k, th)
def setup_inputs_refuse(rng):
    d = setup_inputs_ends(rng); d["th"][1] = 0
    return d
def setup_inputs_spread(rng):
    us, tp, c, w, k, th = parts(rng)
    def stones():
        v = np.floor(np.exp2(8 * rng.random((N, 8, 1, S), dtype=np.float32)) * rng.random((N, 8, 16, S), dtype=np.float32)).astype(np.int16)
        v = np.minimum(v, 255); return np.where(rng.random((N, 8, 1, S)) < 0.25, 255 - v, v)
    c = np.minimum((S * rng.random((N, 8, L)) ** 3).astype(np.int64), S - 1); c[:, ::2] = S - 1 - c[:, ::2]
    w = np.minimum(np.exp2(12.01 * rng.random((N, 8, 16, 2))).astype(np.int64) - (rng.random((N, 8, 16, 2)) < 0.05), 4095)
    k = np.maximum(np.minimum(np.exp2(12 * rng.random((N, 8, 16))).astype(np.int64) - 1, KM), 0)
    th = np.where(rng.random((N, 8)) < 0.25, rng.integers(0, 4081, (N, 8)), np.exp2(6 + 4 * rng.random((N, 8))).astype(np.int64))
    us = stones(); tp = stones()
    for q in range(N):
        g = int(rng.integers(0, 8))
        us[q, g] = rng.integers(0, 8, (16, S)); us[q, g, 0] += 248
        tp[q, g] = rng.integers(248, 256, (16, S)); tp[q, g, 8] = rng.integers(0, 2, S)
        w[q, g, :, 0] = 3072; w[q, g, 0, 0] = 4095; w[q, g, :, 1] = rng.integers(0, 4096, 16)
        k[q, g] = rng.permutation(KM + 1)[:16]; th[q, g] = 4080
    return pack(us, tp, c, w, k, th)
def setup_inputs_ties(rng):
    us, tp, c, w, k, th = parts(rng); flat = int(rng.integers(0, 8)); z = np.full((1, 16, 1), 255); z[0, 0] = 0
    for q in range(N):
        for g in range(8):
            pr = rng.integers(0, 256, (16, 12)); tp[q, g] = pr[:, rng.integers(0, 12, S)]
            us[q, g, :8] = pr[8:, rng.integers(0, 12, S)]; us[q, g, 8:] = pr[:8, rng.integers(0, 12, S)]
            th[q, g] = int(rng.choice(np.array([1, 400, 600, 700, 900])))
        us[q, flat] = 0; us[q, flat, 0] = 255; tp[q, flat] = 255; tp[q, flat, 8] = 0; th[q, flat] = 4080
        w[q, flat, 1, 0] ^= 1 - int(np.sum(w[q, flat, 1:, 0])) % 2
        if places(z, w[q, flat][None], k[q, flat][None])[0, 0, 0] == 0: k[q, flat, 0] ^= 1
    return pack(us, tp, c, w, k, th)
def check_inputs(d):
    bad = []
    for a, lo, hi in (("us", 0, 255), ("tp", 0, 255), ("c0", 0, S - 1), ("hw", 0, 4095), ("km", 0, KM), ("th", 0, 4080)):
        v = np.asarray(d[a]).astype(np.float64)
        if not (np.min(v) >= lo and np.max(v) <= hi): bad.append("range of " + a)
        elif np.any(v != np.floor(v)): bad.append("whole numbers in " + a)
    return bad
def reference(us, tp, c0, hw, km, th):
    U = np.zeros((N, 8, 16, W), np.int64); U[..., :S] = us.astype(np.float32).astype(np.int64).reshape(N, 8, 16, S)
    T = np.zeros((N, 8, 16, W), np.int64); T[..., :S] = tp.astype(np.float32).astype(np.int64).reshape(N, 8, 16, S)
    C = c0.astype(np.int64); w = hw.astype(np.int64).reshape(N, 8, 16, 2); k = km.astype(np.int64).reshape(N, 8, 16); t0 = th.astype(np.int64).reshape(N, 8)
    P = np.zeros(N, np.int64); out = []
    for t in range(RO):
        b = t0 + (P & 63)[:, None]; new, poor, zs = [], [], []
        for a in range(N):
            p, z = joined(C[a], T[a]); h, fit = probe(z, w[a], k[a], b[a], U[a]); win = lowest(h, fit)
            for g in range(8): U[a, g][:, h[g, win[g]]] = 255
            new.append(np.where(win, h, p)); poor.append(~fit); zs.append(z)
        for q in range(N):
            a = (q + 1 + t % (N - 1)) % N; sl = [np.flatnonzero(poor[q][g])[:CAP] for g in range(8)]
            z = np.zeros((8, 16, CAP), np.int64); use = np.zeros((8, CAP), bool)
            for g in range(8): z[g][:, :len(sl[g])] = zs[q][g][:, sl[g]]; use[g, :len(sl[g])] = True
            h, fit = probe(z, w[a], k[a], b[a], U[a]); win = lowest(h, fit & use)
            for g in range(8):
                s = np.flatnonzero(win[g]); n = h[g, s]; own = S + CAP * t + s
                U[q, g][:, own] = U[a, g][:, n]; T[q, g][:, own] = T[a, g][:, n]; U[a, g][:, n] = 255; new[q][g, sl[g][s]] = own
        P = np.array([int(np.sum(m)) for m in poor]); C = np.stack(new); out.append(C)
    return {"yc": np.concatenate(out, axis=2).astype(np.float32), "yu": U.reshape(N, 128, W).astype(np.float32).astype(BF)}

@@ -1,0 +1,671 @@
+import math
+from concourse.mybir import dt, AluOpType, AxisListType, ActivationFunctionType
+import comms_topo
+
+RO, L, S, CAP = 6, 256, 4096, 64
+UNF = -2048.0
+
+_B = {}
+
+
+def _b(name, cols, dtype, rows=128):
+    _B[name] = ("sbuf", [rows, cols], dtype)
+
+
+F, BF, H, I, U16 = "float32", "bfloat16", "float16", "int32", "uint16"
+_b("US", 4352, BF); _b("TP", 4096, BF)
+_b("c8", 256, I, 8); _b("hwi", 2, I); _b("kmi", 1, I); _b("th8", 1, I, 8)
+_b("c8h", 256, H, 8); _b("th8h", 1, H, 8); _b("hwf", 2, F); _b("hwg", 2, F); _b("hwh", 2, H); _b("wl", 2, F); _b("wr", 2, F); _b("ws", 2, F)
+_b("kh", 16, H); _b("KR", 16, F); _b("th16", 1, F); _b("b16a", 1, F); _b("b16b", 1, F); _b("ksc", 1, F)
+_b("IC", 256, I); _b("pI", 1, I); _b("sI", 1, I); _b("gI", 1, I); _b("s8I", 1, I); _b("s2I", 1, I)
+_b("pF", 1, F); _b("sF", 1, F); _b("gF", 1, F); _b("s8F", 1, F); _b("s2F", 1, F); _b("sge8", 1, F); _b("slt8", 1, F)
+_b("CS", 256, I); _b("CG", 256, I); _b("C3", 128, I); _b("CSB", 128, BF); _b("CQB", 128, BF); _b("tmpA", 128, F); _b("tmpB", 128, F)
+_b("MWR", 256, F); _b("RST", 256, F); _b("BLKH", 128, H); _b("BLKB", 128, BF); _b("ONEB", 128, BF); _b("IDH", 128, H); _b("IDB", 128, BF); _b("IDN", 128, BF); _b("EQM", 256, F)
+_b("TRIMB", 128, BF); _b("PL", 128, BF); _b("PR", 128, BF); _b("PH", 128, H); _b("SEL", 2048, BF); _b("REP8", 128, H, 8)
+_b("WT", 24 * 128, H); _b("MQ", 128, F); _b("MC", 256, F); _b("MCL", 64, F); _b("t256", 256, I); _b("TRP", 256, F)
+_b("C255", 256, BF); _b("T5", 256, F); _b("KONST", 256, BF); _b("one16", 16, F); _b("oneR", 256, H); _b("CC", 16, F); _b("JW0", 16, F); _b("jI", 16, I)
+_b("J256", 16, F); _b("D4096", 16, F); _b("FIX", 32, F); _b("CLf", 16, F); _b("CL", 16, U16); _b("IC64", 64, F); _b("PF64", 64, F); _b("CCL", 4, F)
+for _k in "01":
+    _b("CX" + _k, 640, F); _b("TX" + _k, 640, BF); _b("WX" + _k, 640, BF)
+_b("WTAB", 4096, BF); _b("W64", 64, BF); _b("B256", 128, BF); _b("rsc", 1, F); _b("rs1", 1, F); _b("rs2", 1, F); _b("rs3", 1, F)
+_b("CM", 256, F); _b("CM2", 256, F); _b("CL0", 16, U16)
+_b("ZB", 512, BF); _b("UVM", 128, F); _b("UT", 64, F); _b("UVI", 32, I); _b("UVA", 32, I); _b("UVW", 16, I); _b("UQ", 32, F)
+_b("HV", 256, I); _b("HF", 64, F); _b("HI", 256, I); _b("HO", 256, U16); _b("HT", 1056, F)
+_b("X", 4096, BF); _b("A", 4096, BF); _b("K", 256, F); _b("K2", 64, F); _b("K3", 64, F); _b("K5", 32, F); _b("RM", 576, F); _b("KQ", 32, F); _b("MP", 512, BF); _b("k3I", 64, I); _b("PZ", 64, BF); _b("PZQ", 64, BF); _b("SLQ", 512, BF); _b("B512", 128, BF); _b("lRM", 320, F); _b("ML", 256, BF); _b("SLP", 1024, BF); _b("s3F", 1, F); _b("k2I", 128, I); _b("pz", 128, F); _b("kz1", 256, I); _b("kz2", 256, F); _b("C7B", 128, BF); _b("TRH", 256, H); _b("BLK8", 128, BF); _b("ID8", 128, BF); _b("NM", 256, BF); _b("RSTB", 256, F); _b("WD", 256, BF); _b("UR", 256, BF); _b("KEY", 16, I)
+_b("PO", 16, F); _b("PN", 16, BF); _b("SC", 16, BF); _b("UA", 16, F); _b("PEN", 16, H); _b("OF", 16, U16); _b("ZA", 768, BF)
+_b("PPI", 1, I); _b("PPJ", 1, I); _b("PPF", 1, F)
+_b("KI", 16, I); _b("MI", 16, I); _b("LA", 16, F); _b("LB", 16, F); _b("LC", 16, F); _b("LD", 16, F); _b("LL", 16, U16)
+_b("HM", 256, H); _b("HS", 256, F); _b("HRH", 256, H); _b("HRT", 256, F); _b("HW", 16, F); _b("HD", 16, F); _b("HL", 16, U16)
+_b("ET", 17 * 256, BF); _b("WN", 256, BF); _b("WM", 256, F); _b("WS", 256, F); _b("LO1", 16, F); _b("LO2", 16, F); _b("LO", 16, U16)
+_b("CI", 256, I); _b("CI3", 256, I); _b("W16", 256, H); _b("EE", 512, H); _b("FI", 32, I); _b("FB", 32, F); _b("FC", 32, F); _b("NW", 16, F); _b("UN0", 16, F); _b("UNC", 16, F)
+_b("EB", 16, F); _b("SG", 4096, BF); _b("RJ", 272, BF); _b("FIRST", 256, BF); _b("JW", 16, F); _b("JL", 16, U16); _b("FW", 256, BF); _b("JX", 16, F); _b("JL2", 16, U16)
+_b("EA", 768, F); _b("EM", 64, F); _b("EQ", 64, F); _b("FAI", 4, I); _b("FA", 4, F); _b("OB", 4, F); _b("OBU", 4, U16)
+for _k in range(RO):
+    _b("ZL%d" % _k, 64, BF); _b("RB%d" % _k, 72, BF); _b("RV%d" % _k, 64, BF)
+_b("ZT", 256, BF); _b("lUVM", 32, F); _b("lUT", 16, F); _b("lUVI", 8, I); _b("lUVA", 8, I); _b("lUVW", 4, I); _b("lUQ", 8, F)
+_b("lHV", 64, I); _b("lHI", 64, I); _b("lHO", 64, U16); _b("lHT", 144, F); _b("lX", 1024, BF); _b("lA", 1024, BF)
+_b("lK", 128, F); _b("lK0", 64, F); _b("lK1", 32, F); _b("lK2", 16, F); _b("lK3", 8, F); _b("lKEY", 4, I); _b("lKI", 4, I); _b("lMI", 4, I); _b("lPO", 4, F); _b("lLA", 4, F); _b("lLB", 4, F)
+_b("lLC", 4, F); _b("lLD", 4, F); _b("lLL", 4, U16); _b("lHM", 64, H); _b("lHS", 64, F); _b("lHRH", 64, H); _b("lHRT", 64, F); _b("lHW", 4, F); _b("lHD", 4, F); _b("lHL", 4, U16)
+_b("lET", 320, BF); _b("GR", 64, BF); _b("GM", 64, F); _b("GS", 64, F); _b("RS", 72, BF); _b("RSU", 64, BF); _b("lO1", 4, F); _b("lO2", 4, F); _b("lLO", 4, U16)
+_PS = ["UVP", "ZP", "DA", "DB", "HR", "CT", "MS", "JP"]
+_SIZE = {F: 4, BF: 2, H: 2, I: 4, U16: 2}
+_OWN = ("US", "TP", "X", "A", "ZA")
+NET = 0
+XCH = False
+HB = (0, 1, 2, 3, 4, 6, 5, 7)
+BYS = {3: "ZP", 7: "CT", 13: "ZP"}
+SCRATCH = {}
+_AT = {}
+_fill = {}
+for _n, (_w, _sh, _d) in _B.items():
+    if _n in _OWN or _n[:2] in ("ZL", "RB", "RV") or _n in ("RS", "RSU") or _sh[0] != 128:
+        SCRATCH[_n] = (_w, _sh, _d); _AT[_n] = (_n, 0)
+    else:
+        _q = 32 // _SIZE[_d]
+        _AT[_n] = ("ar_" + _d, _fill.get(_d, 0))
+        _fill[_d] = _fill.get(_d, 0) + (_sh[1] + _q - 1) // _q * _q
+for _d, _c in _fill.items():
+    SCRATCH["ar_" + _d] = ("sbuf", [128, _c], _d)
+for _n in _PS:
+    SCRATCH[_n] = ("psum", [128, 512], F); _AT[_n] = (_n, 0); _B[_n] = SCRATCH[_n]
+ND = 24
+SEMAPHORES = ["sV", "sS", "sP", "sG", "la", "lr", "lu"] + ["reu%d" % k for k in range(RO)] + ["ask%d" % k for k in range(RO)] + ["rep%d" % k for k in range(RO)] + ["d%d" % k for k in range(ND)]
+
+CY = 0.001
+GA, SCT = 1.56, 3.8
+HOP, OWN = 0.10, 0.05
+FLIGHT = 2.8
+AHEAD = 0.0
+
+
+def build(rank, core, T, topo):
+    ops = []
+    start = [-1000]
+
+    def ap(name, lo=0, hi=None, st=1, rows=None):
+        hi = _B[name][1][1] if hi is None else hi
+        return ("a", name, lo, hi, st, rows)
+
+    def ind(win, off):
+        return ("i", win, off)
+
+    def ext(name, lo, hi):
+        return ("x", name, lo, hi)
+
+    def res(d):
+        if d[0] == "i":
+            return res(d[1]).indirect(res(d[2]))
+        if d[0] == "x":
+            return T[d[1]][:, d[2]:d[3]]
+        _, name, lo, hi, st, rows = d
+        t, off = _AT[name]
+        n = _B[name][1][0]
+        rs = slice(0, n) if rows is None else rows
+        return T[t][rs, off + lo:off + hi] if st == 1 else T[t][rs, off + lo:off + hi:st]
+
+    def acc(d):
+        if d[0] == "x":
+            return []
+        if d[0] == "i":
+            return acc(d[1]) + acc(d[2])
+        return [(d[1], d[2], d[3], d[4])]
+
+    def n_of(d):
+        return 16 * n_of(d[2]) if d[0] == "i" else (d[3] - d[2] + d[4] - 1) // d[4]
+
+    def size(d):
+        return _SIZE[_B[d[1]][2]]
+
+    def isps(d):
+        return d[0] == "a" and d[1] in _PS
+
+    def put(q, fn, reads, writes, cost, sem=None, inc=1):
+        R, W = [], []
+        for d in reads:
+            R += acc(d)
+        for d in writes:
+            if d[0] == "i":
+                W += acc(d[1]); R += acc(d[2])
+            else:
+                W += acc(d)
+        ops.append({"q": q, "fn": fn, "R": R, "W": W, "c": cost, "sem": sem, "inc": inc, "k": len(ops) - start[0]})
+
+    class V:
+        pass
+
+    from_ops = AluOpType
+
+    def vcost(n, full, inds, outs_ind):
+        if outs_ind:
+            return 0.06 + n * SCT * CY
+        if inds:
+            return 0.06 + n * GA * CY
+        return max(64, n * full) * CY
+
+    def sc(x):
+        return res(x) if isinstance(x, tuple) else x
+
+    def tt(o, a, b, op):
+        full = 1 if isps(a) or isps(b) else 2
+        put("V", lambda g: g.vector.tensor_tensor(res(o), res(a), res(b), op), [a, b], [o], vcost(n_of(o), full, a[0] == "i", o[0] == "i"))
+
+    def ts(o, a, s1, op0, s2=None, op1=None):
+        two = 0.5 if not isps(a) and not isps(o) and o[0] == "a" and size(a) == 2 and size(o) == 2 else 1
+        rd = [a] + [x for x in (s1, s2) if isinstance(x, tuple)]
+        if op1 is None:
+            put("V", lambda g: g.vector.tensor_scalar(res(o), res(a), sc(s1), None, op0), rd, [o], vcost(n_of(o), two, a[0] == "i", o[0] == "i"))
+        else:
+            put("V", lambda g: g.vector.tensor_scalar(res(o), res(a), sc(s1), sc(s2), op0, op1), rd, [o], vcost(n_of(o), two, a[0] == "i", o[0] == "i"))
+
+    def cp(o, a):
+        two = 0.5 if a[0] == "a" and o[0] == "a" and not isps(a) and size(a) == 2 and size(o) == 2 else 1
+        put("V", lambda g: g.vector.tensor_copy(res(o), res(a)), [a], [o], vcost(n_of(o), two, a[0] == "i", o[0] == "i"))
+
+    def scan(o, a, b, op0=AluOpType.mult, op1=AluOpType.add):
+        put("V", lambda g: g.vector.tensor_tensor_scan(res(o), res(a), res(b), 0.0, op0, op1), [a, b], [o], vcost(n_of(o), 1, False, False))
+
+    def fill(o, v):
+        put("V", lambda g: g.vector.memset(res(o), v), [], [o], vcost(n_of(o), 0.5, False, False))
+
+    def act(o, a, func, bias=0.0, scale=1.0):
+        rd = [a] + [x for x in (bias, scale) if isinstance(x, tuple)]
+        put("S", lambda g: g.scalar.activation(res(o), res(a), func, bias=sc(bias), scale=sc(scale)), rd, [o],
+            0.08 + n_of(o) * (GA if a[0] == "i" else 1) * CY)
+
+    def mm(lst):
+        def fn(g):
+            r = None
+            for o, l, rh, st, sp in lst:
+                r = g.tensor.matmul(res(o), res(l), res(rh), st, sp)
+            return r
+        put("P", fn, [x[1] for x in lst] + [x[2] for x in lst], [x[0] for x in lst], sum(max(64, n_of(x[2])) for x in lst) * CY)
+
+    def later(k):
+        ops[-1].setdefault("after", []).append(k)
+
+    nd = [0]
+
+    def dma(o, a, cost):
+        k = "d%d" % nd[0]; nd[0] += 1
+        put("Y", lambda g: g.sync.dma_start(res(o) if isinstance(o, tuple) else o, res(a) if isinstance(a, tuple) else a),
+            [a] if isinstance(a, tuple) else [], [o] if isinstance(o, tuple) else [], cost, sem=k, inc=16)
+
+    ADD, SUB, MUL, MIN, MAX = from_ops.add, from_ops.subtract, from_ops.mult, from_ops.min, from_ops.max
+    EQ, NE, GE, GT, LT, LE = from_ops.is_equal, from_ops.not_equal, from_ops.is_ge, from_ops.is_gt, from_ops.is_lt, from_ops.is_le
+    SHR, AND = from_ops.arith_shift_right, from_ops.bitwise_and
+    AF = ActivationFunctionType
+
+    dma(ap("c8"), T.c0[:, :], 2.0); dma(ap("hwi"), T.hw[:, :], 2.0); dma(ap("kmi"), T.km[:, :], 2.0); dma(ap("th8"), T.th[:, :], 2.0)
+    dma(ap("TP"), ext("tp", 0, 4096), 6.0)
+    for k in range(4):
+        later(k)
+    dma(ap("US", 0, 4096), ext("us", 0, 4096), 8.0); later(4)
+
+    put("G", lambda g: g.iota(res(ap("pI")), [[0, 1]], 0, 1), [], [ap("pI")], 0.2)
+    put("G", lambda g: g.iota(res(ap("IC")), [[1, 256]], 0, 0), [], [ap("IC")], 0.6)
+    ts(ap("sI"), ap("pI"), 15, AND); ts(ap("gI"), ap("pI"), 4, SHR); ts(ap("s2I"), ap("sI"), 2, SHR)
+    ts(ap("s8I"), ap("pI"), 8, ADD); ts(ap("s8I"), ap("s8I"), 15, AND)
+    for a, b in (("pF", "pI"), ("sF", "sI"), ("gF", "gI"), ("s8F", "s8I"), ("s2F", "s2I")):
+        cp(ap(a), ap(b))
+    ts(ap("sge8"), ap("sF"), 7.5, GT); ts(ap("slt8"), ap("sF"), 7.5, LT)
+    ts(ap("CS"), ap("IC"), 15, AND); ts(ap("CG"), ap("IC"), 4, SHR); ts(ap("C3"), ap("IC", 0, 128), 3, AND)
+    ts(ap("BLKB"), ap("CG", 0, 128), ap("gF"), EQ); cp(ap("BLKH"), ap("BLKB"))
+    r8 = slice(0, 8)
+    ts(ap("REP8"), ap("CG", 0, 128, 1, r8), ap("pF", 0, 1, 1, r8), EQ)
+    ts(ap("tmpA"), ap("C3"), 1.0, ADD); tt(ap("tmpB"), ap("tmpA"), ap("BLKB"), MUL); ts(ap("CQB"), ap("tmpB"), -1.0, ADD)
+    ts(ap("tmpA"), ap("CS", 0, 128), 1.0, ADD); tt(ap("tmpB"), ap("tmpA"), ap("BLKB"), MUL); ts(ap("CSB"), ap("tmpB"), -1.0, ADD)
+    ts(ap("PH"), ap("CSB"), ap("s8F"), EQ)
+    ts(ap("PL"), ap("CSB"), ap("s8F"), EQ, ap("sge8"), MUL); ts(ap("PR"), ap("CSB"), ap("s8F"), EQ, ap("slt8"), MUL)
+    cp(ap("hwf"), ap("hwi")); ts(ap("hwg"), ap("hwf"), 2047.5, GT, -4096.0, MUL); tt(ap("hwg"), ap("hwf"), ap("hwg"), ADD); cp(ap("hwh"), ap("hwg"))
+    mm([(ap("MS", 0, 2), ap("PH"), ap("hwh"), True, True)])
+    cp(ap("ws"), ap("MS", 0, 2)); ts(ap("wl"), ap("ws"), ap("sge8"), MUL); ts(ap("wr"), ap("ws"), ap("slt8"), MUL)
+
+    def wt(k, qv, r):
+        i = (k * 2 + qv) * 4 + r
+        return ap("WT", i * 128, i * 128 + 128)
+    ts(ap("rsc"), ap("slt8"), -1.0, MUL)
+    for r in (1, 2, 3):
+        ts(ap("rs%d" % r), ap("rsc"), float(r), ADD)
+    for qv in (0, 1):
+        ts(wt(0, qv, 0), ap("CQB"), 0.0, EQ, ap("wl", qv, qv + 1), MUL)
+        for r in (1, 2, 3):
+            ts(wt(0, qv, r), ap("CQB"), ap("rs%d" % r), EQ, ap("ws", qv, qv + 1), MUL)
+        ts(wt(1, qv, 3), ap("CQB"), 3.0, EQ, ap("wr", qv, qv + 1), MUL)
+    for qv in (0, 1):
+        for r in range(4):
+            ts(wt(2, qv, r), ap("CQB"), float(r), EQ, ap("hwg", qv, qv + 1), MUL)
+    ts(ap("MQ"), ap("C3"), ap("s2F"), EQ)
+    ts(ap("MWR"), ap("CS"), ap("sF"), EQ); ts(ap("RST"), ap("CS"), 0.5, GT)
+    ts(ap("ksc"), ap("kmi"), -2048.0, ADD); ts(ap("kh"), ap("CS", 0, 16), ap("sF"), EQ, ap("ksc"), MUL)
+    mm([(ap("MS", 16, 32), ap("BLKH"), ap("kh"), True, True)])
+    ts(ap("KR"), ap("MS", 16, 32), 2048.0, ADD)
+    ts(ap("th8h"), ap("th8"), -2048.0, ADD)
+    mm([(ap("MS", 8, 9), ap("REP8"), ap("th8h"), True, True)])
+    ts(ap("th16"), ap("MS", 8, 9), 2048.0 - 1.0 / 512, ADD, 512.0, MUL)
+    ts(ap("c8h"), ap("c8"), -2048.0, ADD)
+    mm([(ap("HR", 0, 256), ap("REP8"), ap("c8h"), True, True)])
+    act(ap("CX0", 0, 256), ap("HR", 0, 256), AF.Copy, bias=2048.0)
+    tt(ap("CM"), ap("CX0", 0, 256), ap("MWR"), MUL); scan(ap("CM2"), ap("RST"), ap("CM")); cp(ap("CL0"), ap("CM2", 15, 256, 16))
+    for k in "01":
+        fill(ap("TX" + k, 256, 640), 0.0)
+    act(ap("TX0", 0, 256), ind(ap("TP"), ap("CL0")), AF.Copy)
+    act(ap("BLK8"), ap("BLKB"), AF.Copy, scale=8192.0);
+    ts(ap("NM"), ap("CS"), ap("sF"), NE, 4194304.0, MUL); ts(ap("RSTB"), ap("CS"), 0.5, LT, 8388608.0, MUL)
+    act(ap("B512"), ap("BLKB"), AF.Copy, scale=512.0); act(ap("B256"), ap("BLKB"), AF.Copy, scale=16.0)
+
+
+    def keep(o, src, pattern, base):
+        put("G", lambda g: g.affine_select(res(o), res(ap(src)), pattern, EQ, 0.0, base, 0), [ap(src)], [o], 0.4)
+    for r in range(8):
+        keep(ap("SLP", 128 * r, 128 * r + 128), "B512", [[0, 16], [1, 8]], -r)
+    slp = len(ops) - 1
+    for s in range(16):
+        keep(ap("SEL", 128 * s, 128 * s + 128), "B256", [[0, 8], [1, 16]], -s); later(slp)
+    slp = len(ops) - 1
+    for r in range(4):
+        keep(ap("SLQ", 128 * r, 128 * r + 128), "B512", [[0, 32], [1, 4]], -r); later(slp)
+    slp = len(ops) - 1
+    put("G", lambda g: g.iota(res(ap("WTAB")), [[0, 1024], [1, 4]], 4, 0, allow_small_or_imprecise_dtypes=True), [], [ap("WTAB")], 7.0); later(slp)
+    cp(ap("CI"), ap("CX0", 0, 256)); ts(ap("CI3"), ap("CI"), 3, AND); ts(ap("WX0", 0, 256), ap("CI3"), 4.0, ADD)
+    ts(ap("W64"), ap("C3", 0, 64), 4.0, ADD)
+    ts(ap("s3F"), ap("sF"), 7.5, GT)
+    put("G", lambda g: g.iota(res(ap("MP")), [[16, 16], [0, 32]], 0, 0, allow_small_or_imprecise_dtypes=True), [], [ap("MP")], 1.0)
+    put("G", lambda g: g.iota(res(ap("ML")), [[16, 16], [4, 4], [0, 4]], 0, 0, allow_small_or_imprecise_dtypes=True), [], [ap("ML")], 0.6)
+    ts(ap("k3I"), ap("IC", 0, 64), 1, AND); ts(ap("PZ"), ap("k3I"), ap("s3F"), NE, 4194304.0, MUL)
+    ts(ap("PZQ"), ap("C3", 0, 64), ap("s2F"), NE, 4194304.0, MUL)
+    ts(ap("CC"), ap("IC", 0, 16), 1.0, MUL); ts(ap("CCL"), ap("IC", 0, 4), 1.0, MUL)
+    ts(ap("JW0"), ap("IC", 0, 16), 16.0, MUL, ap("sF"), ADD)
+    ts(ap("J256"), ap("JW0"), 256.0, ADD); ts(ap("D4096"), ap("JW0"), 4096.0, ADD)
+    ts(ap("FIX", 0, 16), ap("JW0"), 254.5, GT, 256.0, MUL); ts(ap("FIX", 16, 32), ap("JW0"), 253.5, GT, 256.0, MUL)
+    ts(ap("CL"), ap("CC"), 16.0, MUL, 15.0, ADD)
+    ts(ap("oneR"), ap("CS"), -1.0, GT); ts(ap("EE", 0, 1), ap("pF"), 0.0, MUL)
+    ts(ap("tmpA"), ap("CS", 0, 128), ap("sF"), LE, -1.0, MUL); tt(ap("TRIMB"), ap("tmpA"), ap("BLKB"), MUL)
+    ts(ap("IDH"), ap("IC", 0, 128), ap("pF"), EQ); cp(ap("IDB"), ap("IDH")); act(ap("ID8"), ap("IDB"), AF.Copy, scale=8192.0); ts(ap("IDN"), ap("IDH"), -1.0, MUL); ts(ap("EQM"), ap("MWR"), -1.0, ADD); fill(ap("ONEB"), 1.0); fill(ap("one16"), 1.0); fill(ap("C255"), 255.0)
+    ts(ap("TRP"), ap("CS"), ap("sF"), LE, 16384.0, MUL); ts(ap("TRH"), ap("CS"), ap("sF"), LE, 16384.0, MUL)
+    ts(ap("T5"), ap("IC"), 5.0, MUL, 2.0, ADD)
+    rng = []
+    for c in range(16):
+        lo = -((-(64 * c + 2)) // 5); hi = min(256, -((-(112 * c + 110)) // 5))
+        rng.append((lo, hi))
+    ts(ap("kz1"), ap("IC"), 5.0, MUL, 62.0, ADD); ts(ap("kz1"), ap("kz1"), 6, SHR); ts(ap("kz2"), ap("kz1"), 16.0, MIN)
+    ts(ap("kz1"), ap("T5"), -55.5, ADD, 1.0 / 112, MUL); tt(ap("KONST"), ap("kz2"), ap("kz1"), ADD)
+    fill(ap("RJ", 0, 16), 300.0)
+    ts(ap("IC64"), ap("IC", 0, 64), 1.0, MUL); ts(ap("PF64"), ap("IC64"), 5.0, MUL, 1280.0, ADD)
+    fill(ap("HT", 256, 1056), UNF); fill(ap("lHT", 64, 144), UNF); fill(ap("RS", 64, 72), 0.0)
+
+    def sel(bank, o, name, lo, n):
+        return [(ap(bank, o, o + n), ap("SEL", 128 * s, 128 * s + 128), ap(name, lo + s, lo + s + 16 * (n - 1) + 1, 16), s == 0, s == 15) for s in range(16)]
+
+    def pair(m):
+        return m < 14 and m not in BYS and (m ^ 1) not in BYS
+
+    for t in range(RO):
+        start[0] = len(ops)
+        cur, nxt = str(t % 2), str(1 - t % 2)
+        cx, tx, cy, ty, wx, wy = "CX" + cur, "TX" + cur, "CX" + nxt, "TX" + nxt, "WX" + cur, "WX" + nxt
+        last = t == RO - 1
+        b16 = ap("th16") if t == 0 else ap("b16a" if t % 2 else "b16b")
+        lst = []
+        for qv in (0, 1):
+            for r in range(4):
+                lst.append((ap("UVP", 64 * qv, 64 * qv + 64), wt(0, qv, r), ap(tx, r, r + 253, 4), r == 0, False))
+            lst.append((ap("UVP", 64 * qv, 64 * qv + 64), wt(1, qv, 3), ap(tx, 4, 257, 4), False, True))
+        mm(lst)
+        mm([(ap("ZP", 0, 256), ap("PL"), ap(tx, 0, 256), True, False), (ap("ZP", 0, 256), ap("PR"), ap(tx, 1, 257), False, True)])
+        act(ap("ZB", 0, 256), ap("ZP", 0, 256), AF.Copy); act(ap("ZB", 256, 512), ap("ZP", 0, 256), AF.Copy)
+        tt(ap("UVM"), ap("UVP", 0, 128), ap("MQ"), MUL)
+        tt(ap("UT"), ap("UVM", 0, 128, 2), ap("UVM", 1, 128, 2), ADD)
+        tt(ap("UVI"), ap("UT", 0, 64, 2), ap("UT", 1, 64, 2), ADD)
+        ts(ap("UVA"), ap("UVI"), 4095, AND)
+        tt(ap("UVW"), ap("UVA", 0, 16), ap("UVA", 16, 32), MUL)
+        ts(ap("UVA", 16, 32), ap("UVW"), 5, SHR)
+        cp(ap("UQ"), ap("UVA"))
+        for c in range(16):
+            if c % 4 == 3:
+                act(ap("HF", c // 4, 64, 4), ap("KR"), AF.Identity, bias=ap("UQ", 16 + c, 17 + c), scale=ap("UQ", c, c + 1))
+            else:
+                ts(ap("HV", c, 256, 16), ap("KR"), ap("UQ", c, c + 1), MUL, ap("UQ", 16 + c, 17 + c), ADD)
+        cp(ap("HV", 3, 256, 4), ap("HF"))
+        for h in (0, 1):
+            ts(ap("HI", 128 * h, 128 * h + 128), ap("HV", 128 * h, 128 * h + 128), 4095, AND)
+            cp(ap("HO", 128 * h, 128 * h + 128), ap("HI", 128 * h, 128 * h + 128))
+        for mb in range(4):
+            if mb == 0:
+                scan(ap("EE", 256, 512), ap("oneR"), ap(wx, 0, 256)); cp(ap("EE", 1, 256), ap("EE", 256, 511))
+                mm(sel("MS", 32, "EE", 0, 32))
+            for m in range(4 * mb, 4 * mb + 4):
+                x, u = ap("X", 256 * m, 256 * m + 256), ind(ap("US", 0, 4096), ap("HO", 16 * m, 16 * m + 16))
+                if m in BYS:
+                    act(x, u, AF.Copy)
+                elif not pair(m):
+                    tt(x, u, ap("ZB", 0, 256), SUB)
+                    if XCH and m > 2:
+                        later(x15)
+                    x15 = len(ops) - 1
+                elif m % 2 == 0:
+                    tt(ap("X", 256 * m, 256 * m + 512), ind(ap("US", 0, 4096), ap("HO", 16 * m, 16 * m + 32)), ap("ZB"), SUB)
+                    if XCH and m > 2:
+                        later(x15)
+                    x15 = len(ops) - 1
+            for m in range(4):
+                lo = 1024 * mb + 256 * m
+                k = 2 if pair(4 * mb + m) else 1
+                if k == 2 and m % 2:
+                    continue
+                if 4 * mb + m in BYS:
+                    bank = BYS[4 * mb + m]
+                    mm([(ap(bank, 256, 512), ap("IDB"), ap("X", lo, lo + 256), True, False), (ap(bank, 256, 512), ap("IDN"), ap("ZB", 0, 256), False, True)])
+                    act(ap("A", lo, lo + 256), ap(bank, 256, 512), AF.Abs)
+                else:
+                    act(ap("A", lo, lo + 256 * k), ap("X", lo, lo + 256 * k), AF.Abs)
+        ts(ap("RM", 0, 64), ap("IC64"), 0.0, MUL, b16, ADD)
+        for n, h in enumerate(HB):
+            d, lo = ("DA", "DB")[n % 2], 512 * h
+            mm([(ap(d, 0, 64), ap("IDB"), ap("MP", 64 * h, 64 * h + 64), True, False), (ap(d, 0, 64), ap("IDB"), ap("PZ"), False, False)] +
+               [(ap(d, 0, 64), ap("SLP", 128 * r, 128 * r + 128), ap("A", lo + r, lo + 512, 8), False, r == 7) for r in range(8)])
+            tt(ap("RM", 64 * n + 64, 64 * n + 128), ap(d, 0, 64), ap("RM", 64 * n, 64 * n + 64), MIN)
+        ts(ap("HT", 0, 256), ap("HI"), -2047.0, ADD); later(x15)
+        tt(ap("KQ"), ap("RM", 512, 575, 2), ap("RM", 513, 576, 2), MIN)
+        tt(ap("KEY"), ap("KQ", 0, 16), ap("KQ", 16, 32), MIN)
+        ts(ap("FI"), ap("MS", 32, 64), 0.2 / 256, MUL); later(x15); ts(ap("EB"), ap("MS", 48, 64), -1.0 / 256, MUL, 0.5, ADD); later(x15)
+        ts(ap("FB"), ap("FI"), 256.0, MIN); tt(ap("FC"), ap("FB"), ap("FIX"), MAX)
+        tt(ap("NW"), ap("FC", 16, 32), ap("FC", 0, 16), SUB)
+        ts(ap("UN0"), ap("NW"), 0.0, EQ, 512.0, MUL); tt(ap("UNC"), ap("UN0"), ap("CC"), ADD)
+        if t:
+            ts(ind(ap(cx), ap("OBU")), ap("IC64"), 1.0, MUL, float(S + CAP * (t - 1)), ADD); later(x15)
+            dma(ext("yc", L * (t - 1), L * t), ap(cx, 0, 256, 1, slice(0, 128, 16)), 2.0)
+        fill(ap("ZA", 0, 64), 1024.0)
+        ts(ap("PO"), ap("KEY"), b16, GE); tt(ap("PN"), ap("PO"), ap("NW"), MUL); scan(ap("SC"), ap("one16"), ap("PN"))
+        scn = len(ops) - 1
+        ts(ap("UA"), ap("PN"), 0.5, LT); tt(ap("PEN"), ap("UA"), ap("J256"), MUL)
+        pen = len(ops) - 1
+        mm([(ap("MS", 64, 80), ap("TRIMB"), ap("PN"), True, False), (ap("MS", 64, 80), ap("BLKB"), ap("SC"), False, False), (ap("MS", 64, 80), ap("IDH"), ap("PEN"), False, True)])
+        cp(ap("OF"), ap("MS", 64, 80))
+        lender = T.cores[(rank + 1 + t % 3) % 4]
+        borrower = T.cores[(rank - 1 - t % 3) % 4]
+
+        def send(o, a, sem, loc, dst):
+            rid, pid, se = topo.addr(dst)
+            m = 0
+            for e in topo.engines(core, dst)[:8]:
+                m |= 1 << e
+            put("G", lambda g: g.remote_dma(T[o][:, :], res(a), T.sem[sem], T.sem[loc], pid, rid, m), [a], [], 1.0, sem=loc, inc=0)
+            ops[-1]["n"] = len(topo.engines(core, dst)[:8])
+            put("N", None, [], [ap(o)], FLIGHT, sem=sem, inc=8)
+            ops[-1]["after"] = [len(ops) - 2]
+        if not last:
+            bn = "b16a" if t % 2 == 0 else "b16b"
+            mm([(ap("MS", 96, 97), ap("ONEB"), ap("SC", 15, 16), True, True)])
+            cp(ap("PPI"), ap("MS", 96, 97)); ts(ap("PPJ"), ap("PPI"), 63, AND); ts(ap(bn), ap("PPJ"), 512.0, MUL, ap("th16"), ADD)
+        ts(ap("MI"), ap("KEY"), 511, AND); tt(ap("LD"), ap("MI"), ap("UNC"), ADD); cp(ap("LL"), ap("LD"))
+        tt(ap("HM"), ind(ap("HT"), ap("LL")), ap("MWR"), MUL); later(pen); later(scn)
+        scan(ap("HS"), ap("RST"), ap("HM"))
+        mm([(ap("HR", 0, 256), ap("BLKH"), ap("HM"), True, True)])
+        cp(ap("HRH"), ap("HR", 0, 256))
+        act(ap(cx, 256, 512), ap("HR", 0, 256), AF.Copy, bias=2047.0)
+        ts(ap("HW"), ap("HS", 15, 256, 16), 2047.0, ADD); cp(ap("HL"), ap("HW"))
+        mm([(ap("DA", 256, 512), ap("BLKH"), ap("HM"), True, False), (ap("DA", 256, 512), ap("IDH"), ap("TRH"), False, True)])
+        act(ap("HRT"), ap("DA", 256, 512), AF.Copy)
+        ts(ap("UR"), ap("HRH"), UNF, EQ)
+        mm([(ap("CT", 0, 256), ap("ID8"), ap("UR"), True, False), (ap("CT", 0, 256), ap("IDB"), ap("NM"), False, False)])
+        for c in range(15):
+            ts(ap("ET", 256 * c, 256 * c + 240 - 16 * c), ap("HRH", 16 * c + 16, 256), ap("HS", 16 * c + 15, 16 * c + 16), EQ)
+            if c <= NET:
+                later(len(ops) - 3)
+            mm([(ap("CT", 16 * c + 16, 256), ap("BLK8"), ap("ET", 256 * c, 256 * c + 240 - 16 * c), False, False)])
+            if c == max(NET, 0):
+                net = len(ops) - 2
+                cp(ind(ap("ZA"), ap("OF")), ap("ZB", 0, 256))
+                if NET >= 0:
+                    later(net)
+                send("ZL%d" % t, ap("ZA", 0, 64), "ask%d" % t, "la", lender)
+        tt(ap("ET", 3840, 4096), ind(ap("HS"), ap("CL")), ap("HRT"), EQ)
+        mm([(ap("CT", 0, 256), ap("BLK8"), ap("ET", 3840, 4096), False, True)])
+        ctl = len(ops) - 1
+        scan(ap("WS"), ap("RSTB"), ap("CT", 0, 256), ADD, MIN)
+        act(ap("WD"), ap("CT", 0, 256), AF.Relu, bias=1.0, scale=-1.0)
+        mm([(ap("MS", 256, 512), ap("BLKB"), ap("WD"), True, True)])
+        act(ap("WN"), ap("MS", 256, 512), AF.Copy)
+        tt(ap("LO1"), ap("WS", 15, 256, 16), ap("HW"), ADD); tt(ap("LO2"), ap("LO1"), ap("D4096"), MIN); cp(ap("LO"), ap("LO2"))
+        cp(ind(ap("US"), ap("LO")), ap("C255"))
+        zl = "ZL%d" % t
+        lst = []
+        for qv in (0, 1):
+            for r in range(4):
+                lst.append((ap("UVP", 128 + 16 * qv, 144 + 16 * qv), wt(2, qv, r), ap(zl, r, r + 61, 4), r == 0, r == 3))
+        mm(lst)
+        luv = len(ops) - 1
+        for k in range(4):
+            act(ap("ZT", 64 * k, 64 * k + 64), ap(zl), AF.Copy)
+        tt(ap("lUVM"), ap("UVP", 128, 160), ap("MQ", 0, 32), MUL)
+        tt(ap("lUT"), ap("lUVM", 0, 32, 2), ap("lUVM", 1, 32, 2), ADD)
+        tt(ap("lUVI"), ap("lUT", 0, 16, 2), ap("lUT", 1, 16, 2), ADD)
+        ts(ap("lUVA"), ap("lUVI"), 4095, AND)
+        tt(ap("lUVW"), ap("lUVA", 0, 4), ap("lUVA", 4, 8), MUL)
+        ts(ap("lUVA", 4, 8), ap("lUVW"), 5, SHR)
+        cp(ap("lUQ"), ap("lUVA"))
+        for c in range(4):
+            ts(ap("lHV", c, 64, 4), ap("KR"), ap("lUQ", c, c + 1), MUL, ap("lUQ", 4 + c, 5 + c), ADD)
+        ts(ap("lHI"), ap("lHV"), 4095, AND); cp(ap("lHO"), ap("lHI"));
+        for mb in range(4):
+            w = 256 if mb < 3 else 128
+            tt(ap("lX", 256 * mb, 256 * mb + w), ind(ap("US", 0, 4096), ap("lHO", 16 * mb, 16 * mb + w // 16)), ap("ZT", 0, w), SUB)
+            lx = len(ops) - 1
+        act(ap("lX", 896, 1024), ind(ap("US", 0, 4096), ap("lHO", 56, 64)), AF.Copy)
+        mm([(ap("ZP", 256, 384), ap("IDB"), ap("lX", 896, 1024), True, False), (ap("ZP", 256, 384), ap("IDN"), ap("ZT", 0, 128), False, True)])
+        ts(ap("lHT", 0, 64), ap("lHI"), -2047.0, ADD); later(lx)
+        for mb in range(3):
+            act(ap("lA", 256 * mb, 256 * mb + 256), ap("lX", 256 * mb, 256 * mb + 256), AF.Abs)
+        act(ap("lA", 896, 1024), ap("ZP", 256, 384), AF.Abs)
+        act(ap("lA", 768, 896), ap("lX", 768, 896), AF.Abs)
+        ts(ap("lRM", 0, 64), ap("IC64"), 0.0, MUL, b16, ADD)
+        for n, h in enumerate((0, 1, 2, 3)):
+            d = ("DA", "DB")[n % 2]
+            mm([(ap(d, 64, 128), ap("IDB"), ap("ML", 64 * h, 64 * h + 64), True, False), (ap(d, 64, 128), ap("IDB"), ap("PZQ"), False, False)] +
+               [(ap(d, 64, 128), ap("SLQ", 128 * r, 128 * r + 128), ap("lA", 256 * h + r, 256 * h + 256, 4), False, r == 3) for r in range(4)])
+            tt(ap("lRM", 64 * n + 64, 64 * n + 128), ap(d, 64, 128), ap("lRM", 64 * n, 64 * n + 64), MIN)
+        tt(ap("lK1"), ap("lRM", 256, 288), ap("lRM", 288, 320), MIN); tt(ap("lK2"), ap("lK1", 0, 16), ap("lK1", 16, 32), MIN)
+        tt(ap("lK3"), ap("lK2", 0, 16, 2), ap("lK2", 1, 16, 2), MIN); tt(ap("lKEY"), ap("lK3", 0, 8, 2), ap("lK3", 1, 8, 2), MIN)
+        ts(ap("lMI"), ap("lKEY"), 2, SHR, 127, AND); cp(ap("lLL"), ap("lMI"))
+        tt(ap("lHM"), ind(ap("lHT"), ap("lLL")), ap("MWR", 0, 64), MUL)
+        scan(ap("lHS"), ap("RST", 0, 64), ap("lHM"))
+        mm([(ap("HR", 256, 320), ap("BLKH"), ap("lHM"), True, True)])
+        tt(ap("lHRT"), ap("HR", 256, 320), ap("TRP", 0, 64), ADD)
+        ts(ap("lHW"), ap("lHS", 15, 64, 16), 2047.0, ADD); tt(ap("lHD"), ap("lHW"), ap("D4096", 0, 4), SUB); cp(ap("lHL"), ap("lHW"))
+        ts(ap("lET", 256, 320), ap("HR", 256, 320), UNF, EQ)
+        mm([(ap("CT", 256, 320), ap("BLKB"), ap("lET", 256, 320), True, False)])
+        for c in range(3):
+            ts(ap("lET", 64 * c, 64 * c + 48 - 16 * c), ap("HR", 272 + 16 * c, 320), ap("lHS", 16 * c + 15, 16 * c + 16), EQ)
+            mm([(ap("CT", 272 + 16 * c, 320), ap("BLKB"), ap("lET", 64 * c, 64 * c + 48 - 16 * c), False, False)])
+        tt(ap("lET", 192, 256), ind(ap("lHS"), ap("CL", 0, 4)), ap("lHRT"), EQ)
+        mm([(ap("CT", 256, 320), ap("BLKB"), ap("lET", 192, 256), False, True)])
+        lct = len(ops) - 1
+        ts(ap("GR"), ap("CT", 256, 320), 0.0, EQ)
+        tt(ap("RS", 0, 64), ind(ap("TP"), ap("lHL")), ap("GR"), MUL)
+        tt(ap("GM"), ap("CT", 256, 320), ap("EQM", 0, 64), EQ); scan(ap("GS"), ap("RST", 0, 64), ap("GM"))
+        ts(ap("RS", 64, 68), ap("GS", 15, 64, 16), -256.0, MUL, 256.0, ADD)
+        send("RB%d" % t, ap("RS"), "rep%d" % t, "lr", borrower)
+        tt(ap("RSU"), ind(ap("US", 0, 4096), ap("lHL")), ap("GR"), MUL)
+        send("RV%d" % t, ap("RSU"), "reu%d" % t, "lu", borrower)
+        tt(ap("lO1"), ap("GS", 15, 64, 16), ap("lHD"), MUL); tt(ap("lO2"), ap("lO1"), ap("D4096", 0, 4), ADD); cp(ap("lLO"), ap("lO2"))
+        cp(ind(ap("US"), ap("lLO")), ap("C255", 0, 64))
+        lend = len(ops) - 1
+        mm([(ap("JP", 0, 256), ap("BLKB"), ap("KONST"), True, False)])
+        off = 0
+        for c in range(16):
+            lo, hi = rng[c]
+            act(ap("SG", off, off + hi - lo), ap("T5", lo, hi), AF.Sign, bias=ap("EB", c, c + 1))
+            mm([(ap("JP", lo, hi), ap("BLKB"), ap("SG", off, off + hi - lo), False, c == 15)])
+            off += (hi - lo + 15) // 16 * 16
+        act(ap("RJ", 1, 257), ap("JP", 0, 256), AF.Relu, bias=254.0, scale=-0.5)
+        mm(sel("JP", 256, "RJ", 1, 16)); later(ctl); later(luv)
+        ts(ap("JW"), ap("JP", 256, 272), -1.0 / 256, MUL, 254.0, ADD); later(lx); cp(ap("JL"), ap("JW"))
+        mm([(ap("MS", 256, 512), ap("IDB"), ap("RJ", 0, 256), True, False), (ap("MS", 256, 512), ap("IDN"), ap("RJ", 1, 257), False, True)]); later(luv)
+        act(ap("FIRST"), ap("MS", 256, 512), AF.Sign)
+        tt(ap("FW"), ind(ap("WN"), ap("JL")), ap("FIRST"), MUL); later(lx)
+        mm(sel("JP", 272, "FW", 0, 16)); later(lct)
+        tt(ap("JX"), ap("JP", 272, 288), ap("JW"), ADD); cp(ap("JL2"), ap("JX"))
+        jl2 = len(ops) - 1
+        if not last:
+            act(ap(tx, 256, 512), ind(ap("TP"), ap("HL")), AF.Copy)
+            act(ap(wx, 256, 512), ind(ap("WTAB"), ap("HL")), AF.Copy)
+            act(ap(ty, 0, 256), ind(ap(tx, 0, 512), ap("JL2")), AF.Copy)
+            act(ap(wy, 0, 256), ind(ap(wx, 0, 512), ap("JL2")), AF.Copy)
+        act(ap(cy, 0, 256), ind(ap(cx, 0, 512), ap("JL2")), AF.Copy)
+        act(ap("EA", 0, 64), ap("PF64"), AF.Copy)
+        cp(ind(ap("EA"), ap("OF")), ap("EE", 0, 256)); later(lend); later(jl2)
+        tt(ap("EM"), ap("EA", 0, 64), ap("MWR", 0, 64), MUL); scan(ap("EQ"), ap("RST", 0, 64), ap("EM"))
+        ts(ap("FAI"), ap("EQ", 15, 64, 16), 0.2, MUL); cp(ap("FA"), ap("FAI"))
+        rb = "RB%d" % t
+        tt(ap("OB"), ap(rb, 64, 68), ap("FA"), ADD); cp(ap("OBU"), ap("OB"))
+        if not last:
+            cp(ind(ap(ty), ap("OBU")), ap(rb, 0, 64)); cp(ind(ap(wy), ap("OBU")), ap("W64"))
+        dma(ext("yu", S + CAP * t, S + CAP * t + CAP), ap("RV%d" % t), 2.0)
+        if last:
+            ts(ind(ap(cy), ap("OBU")), ap("IC64"), 1.0, MUL, float(S + CAP * t), ADD)
+            dma(ext("yc", L * t, L * t + L), ap(cy, 0, 256, 1, slice(0, 128, 16)), 2.0)
+    dma(ext("yu", 0, S), ap("US", 0, 4096), 6.0)
+    return ops
+
+
+def order(ops, noise=None):
+    last = {}
+    for i, o in enumerate(ops):
+        pre = {}
+
+        def add(j, wait):
+            if j != i:
+                pre[j] = pre.get(j, False) or wait
+        for j in o.get("after", ()):
+            pre[j] = False
+        for kind in ("R", "W"):
+            for nm, lo, hi, st in o[kind]:
+                ps = nm in _PS
+                for j, k2, lo2, hi2, st2 in last.get(nm, []):
+                    same = ops[j]["q"] == o["q"]
+                    if ps:
+                        if same and o["q"] == "P":
+                            add(j, False)
+                        elif not same:
+                            add(j, True)
+                        continue
+                    if kind == "R" and k2 == "R":
+                        continue
+                    if hi <= lo2 or hi2 <= lo or (st == st2 and st > 1 and (lo - lo2) % st):
+                        continue
+                    add(j, True)
+        for kind in ("R", "W"):
+            for nm, lo, hi, st in o[kind]:
+                ps = nm in _PS
+                lst = last.setdefault(nm, [])
+                if ps:
+                    if lst and ops[lst[-1][0]]["q"] != o["q"]:
+                        keep = []
+                        other = [e for e in lst if ops[e[0]]["q"] != o["q"]]
+                        lst[:] = other[-40:]
+                elif kind == "W" and st == 1:
+                    lst[:] = [e for e in lst if not (lo <= e[2] and e[3] <= hi) or e[0] == i]
+                lst.append((i, kind, lo, hi, st))
+        o["pre"] = pre
+    n = len(ops)
+    succ = [[] for _ in range(n)]
+    for i, o in enumerate(ops):
+        for j in o["pre"]:
+            succ[j].append(i)
+    pri = [0.0] * n
+    for i in range(n - 1, -1, -1):
+        pri[i] = ops[i]["c"] + max([pri[k] + HOP for k in succ[i]], default=0.0)
+    if noise is not None:
+        pri = [pri[i] + noise[ops[i]["k"]] for i in range(n)]
+    left = [len(o["pre"]) for o in ops]
+    ready = {}
+    est = [0.0] * n
+    fin = [0.0] * n
+    free = {}
+    for i in range(n):
+        if left[i] == 0:
+            ready.setdefault(ops[i]["q"], []).append(i)
+    seq = []
+    while len(seq) < n:
+        best = None
+        for q, lst in ready.items():
+            if not lst:
+                continue
+            f = 0.0 if q == "N" else free.get(q, 0.0)
+            m = min(max(f, est[i]) for i in lst)
+            c = [i for i in lst if max(f, est[i]) <= m + 0.03]
+            b = max(c, key=lambda i: pri[i])
+            tm = max(f, est[b])
+            h = max((i for i in lst if est[i] <= tm + AHEAD), key=lambda i: pri[i]) if AHEAD else b
+            if pri[h] > pri[b] + 0.5 and est[h] > tm and tm + ops[b]["c"] > est[h] + 0.02 and q != "N":
+                c = [i for i in lst if max(f, est[i]) + ops[i]["c"] <= est[h] + 0.02]
+                b = max(c, key=lambda i: pri[i]) if c else h
+                tm = max(f, est[b])
+            if best is None or tm < best[0]:
+                best = (tm, q, b)
+        tm, q, b = best
+        ready[q].remove(b)
+        o = ops[b]
+        o["t"] = tm
+        if q == "Y":
+            free[q] = tm + 0.1
+            fin[b] = tm + o["c"]
+        elif q == "N":
+            fin[b] = tm + o["c"]
+        else:
+            free[q] = tm + o["c"]
+            fin[b] = tm + o["c"]
+        seq.append(b)
+        for k in succ[b]:
+            left[k] -= 1
+            hop = (OWN if ops[k]["q"] == q else HOP) if ops[k]["pre"][b] else 0.0
+            est[k] = max(est[k], tm if ops[k]["q"] == q and not ops[k]["pre"][b] else fin[b] + hop)
+            if left[k] == 0:
+                ready.setdefault(ops[k]["q"], []).append(k)
+    return seq, max(fin)
+
+
+def rank_program(g, core, T, topo):
+    rank = T.rank_of(core)
+    if rank is None:
+        return
+    ops = build(rank, core, T, topo)
+    seq, _ = order(ops)
+    eng = {"V": g.vector, "S": g.scalar, "P": g.tensor, "G": g, "Y": g.sync}
+    total = {}
+    known = {q: {} for q in eng}
+    for i in seq:
+        o = ops[i]
+        q = o["q"]
+        if q == "N":
+            o["at"] = (o["sem"], o["inc"]); o["clock"] = {}
+            total[o["sem"]] = o["inc"]
+            continue
+        kn = known[q]
+        need = [ops[j] for j, w in o["pre"].items() if w]
+        need.sort(key=lambda p: -p.get("t", 0.0))
+        for p in need:
+            sem, val = p["at"]
+            if kn.get(sem, 0) >= val:
+                continue
+            eng[q].wait_ge(T.sem[sem], val)
+            kn[sem] = val
+            for a, b in p["clock"].items():
+                if kn.get(a, 0) < b:
+                    kn[a] = b
+        r = o["fn"](g)
+        if o["sem"] is None:
+            sem = "s" + q
+            total[sem] = total.get(sem, 0) + 1
+            r.then_inc(T.sem[sem], 1)
+        elif "n" in o:
+            sem = o["sem"]
+            total[sem] = total.get(sem, 0) + o["n"]
+        else:
+            sem = o["sem"]
+            total[sem] = o["inc"]
+            r.then_inc(T.sem[sem], o["inc"])
+        o["at"] = (sem, total[sem])
+        o["clock"] = dict(kn)
+    for sem, val in total.items():
+        g.wait_ge(T.sem[sem], val)

@@ -1,64 +1,68 @@
-import math
+import numpy as np
 from concourse.mybir import dt, AluOpType, AxisListType, ActivationFunctionType
 import comms_topo
 
 RO, L, S, CAP = 6, 256, 4096, 64
-UNF = -2048.0
+UNF = 4000.0
+BIG = 4194304.0
+NEW = 400
+ZD = 4352
 
 _B = {}
 
 
-def _b(name, cols, dtype, rows=128):
-    _B[name] = ("sbuf", [rows, cols], dtype)
+def _b(name, cols, dtype, rows=128, inner=0):
+    _B[name] = ("sbuf", [rows, cols], dtype, inner)
 
 
 F, BF, H, I, U16 = "float32", "bfloat16", "float16", "int32", "uint16"
-_b("US", 4352, BF); _b("TP", 4096, BF)
+_b("US", 4480, BF); _b("TP", 4096, BF); _b("WTAB", 4096, BF)
 _b("c8", 256, I, 8); _b("hwi", 2, I); _b("kmi", 1, I); _b("th8", 1, I, 8)
-_b("c8h", 256, H, 8); _b("th8h", 1, H, 8); _b("hwf", 2, F); _b("hwg", 2, F); _b("hwh", 2, H); _b("wl", 2, F); _b("wr", 2, F); _b("ws", 2, F)
+_b("c8h", 256, H, 8); _b("c8i", 256, I, 8); _b("c8w", 256, H, 8); _b("th8h", 1, H, 8); _b("hwf", 2, F); _b("hwg", 2, F); _b("hwh", 2, H); _b("wl", 2, F); _b("wr", 2, F); _b("ws", 2, F)
 _b("kh", 16, H); _b("KR", 16, F); _b("th16", 1, F); _b("b16a", 1, F); _b("b16b", 1, F); _b("ksc", 1, F)
-_b("IC", 256, I); _b("pI", 1, I); _b("sI", 1, I); _b("gI", 1, I); _b("s8I", 1, I); _b("s2I", 1, I)
-_b("pF", 1, F); _b("sF", 1, F); _b("gF", 1, F); _b("s8F", 1, F); _b("s2F", 1, F); _b("sge8", 1, F); _b("slt8", 1, F)
-_b("CS", 256, I); _b("CG", 256, I); _b("C3", 128, I); _b("CSB", 128, BF); _b("CQB", 128, BF); _b("tmpA", 128, F); _b("tmpB", 128, F)
-_b("MWR", 256, F); _b("RST", 256, F); _b("BLKH", 128, H); _b("BLKB", 128, BF); _b("ONEB", 128, BF); _b("IDH", 128, H); _b("IDB", 128, BF); _b("IDN", 128, BF); _b("EQM", 256, F)
+_b("IC", 256, BF); _b("CS", 256, BF); _b("CG", 128, BF); _b("CG8", 128, BF); _b("C3", 128, BF); _b("pI", 1, I); _b("sI", 1, I); _b("s2I", 1, I)
+for _n in ("pF", "sF", "gF", "s2F", "sge8", "slt8", "pm8", "gx8", "g8p", "nsB", "ns2", "s1T", "gx4", "pm1", "rF", "s1F"):
+    _b(_n, 1, F)
+_b("g16", 16, F); _b("g8", 4, F); _b("g8m", 4, F); _b("pen2", 2, F); _b("pen4", 4, F)
+_b("MWR", 256, F); _b("RST", 256, F); _b("BLKH", 128, H); _b("BLKB", 128, BF); _b("BLKN", 128, BF); _b("ONEB", 128, BF)
+_b("IDH", 128, H); _b("IDB", 128, BF); _b("IDN", 128, BF); _b("IDHN", 128, H)
 _b("TRIMB", 128, BF); _b("PL", 128, BF); _b("PR", 128, BF); _b("PH", 128, H); _b("SEL", 2048, BF); _b("REP8", 128, H, 8)
-_b("WT", 24 * 128, H); _b("MQ", 128, F); _b("MC", 256, F); _b("MCL", 64, F); _b("t256", 256, I); _b("TRP", 256, F)
-_b("C255", 256, BF); _b("T5", 256, F); _b("KONST", 256, BF); _b("one16", 16, F); _b("oneR", 256, H); _b("CC", 16, F); _b("JW0", 16, F); _b("jI", 16, I)
-_b("J256", 16, F); _b("D4096", 16, F); _b("FIX", 32, F); _b("CLf", 16, F); _b("CL", 16, U16); _b("IC64", 64, F); _b("PF64", 64, F); _b("CCL", 4, F)
+_b("WT", 24 * 128, H); _b("PZ4", 128, BF); _b("RS4", 128, F); _b("RS16", 64, F)
+_b("C255", 128, BF); _b("T5", 256, F); _b("KONST", 256, BF); _b("one16", 16, F); _b("oneR", 256, BF); _b("JW0", 16, F)
+_b("J256", 16, H); _b("FIX", 32, F); _b("CL", 16, U16); _b("CJ", 32, U16); _b("IC64", 64, F); _b("PF64", 64, F)
+_b("DRS", 256, F); _b("DR1", 64, F); _b("lNM", 64, BF); _b("lTR", 160, BF)
+_b("SLQ", 512, BF); _b("SLP", 1024, BF); _b("B512", 128, BF); _b("B256", 128, BF); _b("BLK8", 128, BF); _b("NM", 256, BF); _b("TRH", 64, BF)
+_b("MP", 512, BF); _b("MS1", 256, BF); _b("ML", 256, BF); _b("kz1", 256, BF); _b("kz2", 256, BF); _b("CM2", 256, F); _b("CL0", 16, U16)
 for _k in "01":
-    _b("CX" + _k, 640, F); _b("TX" + _k, 640, BF); _b("WX" + _k, 640, BF)
-_b("WTAB", 4096, BF); _b("W64", 64, BF); _b("B256", 128, BF); _b("rsc", 1, F); _b("rs1", 1, F); _b("rs2", 1, F); _b("rs3", 1, F)
-_b("CM", 256, F); _b("CM2", 256, F); _b("CL0", 16, U16)
-_b("ZB", 512, BF); _b("UVM", 128, F); _b("UT", 64, F); _b("UVI", 32, I); _b("UVA", 32, I); _b("UVW", 16, I); _b("UQ", 32, F)
-_b("HV", 256, I); _b("HF", 64, F); _b("HI", 256, I); _b("HO", 256, U16); _b("HT", 1056, F)
-_b("X", 4096, BF); _b("A", 4096, BF); _b("K", 256, F); _b("K2", 64, F); _b("K3", 64, F); _b("K5", 32, F); _b("RM", 576, F); _b("KQ", 32, F); _b("MP", 512, BF); _b("k3I", 64, I); _b("PZ", 64, BF); _b("PZQ", 64, BF); _b("SLQ", 512, BF); _b("B512", 128, BF); _b("lRM", 320, F); _b("ML", 256, BF); _b("SLP", 1024, BF); _b("s3F", 1, F); _b("k2I", 128, I); _b("pz", 128, F); _b("kz1", 256, I); _b("kz2", 256, F); _b("C7B", 128, BF); _b("TRH", 256, H); _b("BLK8", 128, BF); _b("ID8", 128, BF); _b("NM", 256, BF); _b("RSTB", 256, F); _b("WD", 256, BF); _b("UR", 256, BF); _b("KEY", 16, I)
-_b("PO", 16, F); _b("PN", 16, BF); _b("SC", 16, BF); _b("UA", 16, F); _b("PEN", 16, H); _b("OF", 16, U16); _b("ZA", 768, BF)
-_b("PPI", 1, I); _b("PPJ", 1, I); _b("PPF", 1, F)
-_b("KI", 16, I); _b("MI", 16, I); _b("LA", 16, F); _b("LB", 16, F); _b("LC", 16, F); _b("LD", 16, F); _b("LL", 16, U16)
-_b("HM", 256, H); _b("HS", 256, F); _b("HRH", 256, H); _b("HRT", 256, F); _b("HW", 16, F); _b("HD", 16, F); _b("HL", 16, U16)
-_b("ET", 17 * 256, BF); _b("WN", 256, BF); _b("WM", 256, F); _b("WS", 256, F); _b("LO1", 16, F); _b("LO2", 16, F); _b("LO", 16, U16)
-_b("CI", 256, I); _b("CI3", 256, I); _b("W16", 256, H); _b("EE", 512, H); _b("FI", 32, I); _b("FB", 32, F); _b("FC", 32, F); _b("NW", 16, F); _b("UN0", 16, F); _b("UNC", 16, F)
+    _b("CX" + _k, NEW + L, F); _b("TX" + _k, NEW + L, BF); _b("WX" + _k, NEW + L, BF)
+_b("ZB", 512, BF); _b("UVS", 128, I); _b("UVA", 32, I); _b("UVW", 16, I); _b("UQ", 32, F)
+_b("HV", 256, I, inner=16); _b("HF", 256, F, inner=16); _b("HI", 256, I); _b("HO", 256, U16); _b("HT", 528, F)
+_b("X", 4096, BF); _b("A", 4096, BF); _b("RM", 512, F); _b("RI", 320, F); _b("KS", 64, I)
+_b("PO", 16, F); _b("PN", 16, BF); _b("SC", 16, BF); _b("POJ", 16, H); _b("OF", 16, U16); _b("ZA", 768, BF)
+_b("PPI", 1, I); _b("PPJ", 1, I); _b("MI", 16, I); _b("LL", 16, U16)
+_b("HM", 256, H); _b("HS", 256, F); _b("HD", 16, F); _b("LA", 16, F); _b("UR", 256, BF); _b("W2", 128, BF); _b("B30", 128, BF); _b("NM2", 128, BF); _b("P2", 48, F); _b("HRH", 256, H); _b("HL", 16, U16)
+_b("ET", 24 * 128, BF, inner=128); _b("WD", 256, BF); _b("WN", 256, BF); _b("WS", 256, F); _b("LO", 16, U16)
+_b("EE", 512, H); _b("FI", 32, I); _b("FB", 32, F); _b("FC", 32, F); _b("NW", 16, F); _b("UN0", 16, F)
 _b("EB", 16, F); _b("SG", 4096, BF); _b("RJ", 272, BF); _b("FIRST", 256, BF); _b("JW", 16, F); _b("JL", 16, U16); _b("FW", 256, BF); _b("JX", 16, F); _b("JL2", 16, U16)
 _b("EA", 768, F); _b("EM", 64, F); _b("EQ", 64, F); _b("FAI", 4, I); _b("FA", 4, F); _b("OB", 4, F); _b("OBU", 4, U16)
 for _k in range(RO):
-    _b("ZL%d" % _k, 64, BF); _b("RB%d" % _k, 72, BF); _b("RV%d" % _k, 64, BF)
-_b("ZT", 256, BF); _b("lUVM", 32, F); _b("lUT", 16, F); _b("lUVI", 8, I); _b("lUVA", 8, I); _b("lUVW", 4, I); _b("lUQ", 8, F)
-_b("lHV", 64, I); _b("lHI", 64, I); _b("lHO", 64, U16); _b("lHT", 144, F); _b("lX", 1024, BF); _b("lA", 1024, BF)
-_b("lK", 128, F); _b("lK0", 64, F); _b("lK1", 32, F); _b("lK2", 16, F); _b("lK3", 8, F); _b("lKEY", 4, I); _b("lKI", 4, I); _b("lMI", 4, I); _b("lPO", 4, F); _b("lLA", 4, F); _b("lLB", 4, F)
-_b("lLC", 4, F); _b("lLD", 4, F); _b("lLL", 4, U16); _b("lHM", 64, H); _b("lHS", 64, F); _b("lHRH", 64, H); _b("lHRT", 64, F); _b("lHW", 4, F); _b("lHD", 4, F); _b("lHL", 4, U16)
-_b("lET", 320, BF); _b("GR", 64, BF); _b("GM", 64, F); _b("GS", 64, F); _b("RS", 72, BF); _b("RSU", 64, BF); _b("lO1", 4, F); _b("lO2", 4, F); _b("lLO", 4, U16)
+    _b("ZL%d" % _k, 64, BF); _b("RB%d" % _k, 128, BF); _b("RV%d" % _k, 64, BF)
+_b("ZT", 512, BF); _b("lUVS", 64, I); _b("lUVA", 64, I); _b("lUVW", 32, I); _b("lUQ", 32, I); _b("lKU", 64, F)
+_b("lHV", 64, I); _b("lHI", 64, I); _b("lHO", 64, U16); _b("lHT", 528, F); _b("lX", 1024, BF); _b("lA", 1024, BF, inner=32)
+_b("CG2", 128, BF); _b("CZ", 64, BF); _b("PZL", 64, BF); _b("RS32", 64, F); _b("RL", 1024, BF); _b("lHH", 64, H); _b("PK", 256, BF)
+_b("kc", 2, F); _b("k1", 1, H); _b("s1I", 1, I)
+_b("lRM", 256, F); _b("lKS", 128, I); _b("lMI", 4, I); _b("lLL", 4, U16); _b("lHM", 64, H); _b("lHS", 64, F); _b("lHL", 4, U16)
+_b("lET", 160, BF); _b("RS", 128, BF); _b("RSU", 64, BF); _b("lWS", 64, F); _b("lLO", 4, U16)
 _PS = ["UVP", "ZP", "DA", "DB", "HR", "CT", "MS", "JP"]
 _SIZE = {F: 4, BF: 2, H: 2, I: 4, U16: 2}
-_OWN = ("US", "TP", "X", "A", "ZA")
-NET = 0
-XCH = False
-HB = (0, 1, 2, 3, 4, 6, 5, 7)
-BYS = {3: "ZP", 7: "CT", 13: "ZP"}
+_OWN = ("US", "TP", "WTAB", "X", "A", "ZA", "RS", "RSU")
 SCRATCH = {}
 _AT = {}
 _fill = {}
-for _n, (_w, _sh, _d) in _B.items():
-    if _n in _OWN or _n[:2] in ("ZL", "RB", "RV") or _n in ("RS", "RSU") or _sh[0] != 128:
+for _n, (_w, _sh, _d, _in) in _B.items():
+    if _in:
+        SCRATCH[_n] = (_w, [128, _sh[1] // _in, _in], _d); _AT[_n] = (_n, 0)
+    elif _n in _OWN or _n[:2] in ("ZL", "RB", "RV") or _sh[0] != 128:
         SCRATCH[_n] = (_w, _sh, _d); _AT[_n] = (_n, 0)
     else:
         _q = 32 // _SIZE[_d]
@@ -67,15 +71,31 @@ for _n, (_w, _sh, _d) in _B.items():
 for _d, _c in _fill.items():
     SCRATCH["ar_" + _d] = ("sbuf", [128, _c], _d)
 for _n in _PS:
-    SCRATCH[_n] = ("psum", [128, 512], F); _AT[_n] = (_n, 0); _B[_n] = SCRATCH[_n]
-ND = 24
+    SCRATCH[_n] = ("psum", [128, 512], F); _AT[_n] = (_n, 0); _B[_n] = ("psum", [128, 512], F, 0)
+ND = 32
 SEMAPHORES = ["sV", "sS", "sP", "sG", "la", "lr", "lu"] + ["reu%d" % k for k in range(RO)] + ["ask%d" % k for k in range(RO)] + ["rep%d" % k for k in range(RO)] + ["d%d" % k for k in range(ND)]
 
-CY = 0.001
+NS = 4
+BYS = {2: "CT", 3: "CT", 7: "ZP"}
+PROBE = [("gather", 0, 2), ("gather", 2, 2), ("abs", 0, 2), ("gather", 4, 2), ("gather", 7, 1), ("abs", 2, 2), ("gather", 6, 1), ("abs", 4, 2),
+         ("gather", 8, 2), ("abs", 7, 1), ("abs", 6, 1), ("least", 0, 0), ("gather", 10, 2), ("abs", 8, 2), ("least", 1, 0), ("gather", 12, 2),
+         ("abs", 10, 2), ("least", 2, 0), ("gather", 14, 1), ("abs", 12, 2), ("least", 3, 0), ("gather", 15, 1), ("abs", 14, 1), ("abs", 15, 1),
+         ("least", 4, 0), ("slots", 0, 0), ("least", 5, 0), ("slots", 2, 0), ("slots", 1, 0), ("least", 6, 0), ("slots", 3, 0)]
+PAIRS, LAST = 7, 1
+PARTS = 2
+ZBF = 1
+INORDER = 0
+BEHIND, INIAT = 4, 16
+PASSES = 6
+GSEL = 10
+JA = 8
+
+CY = 0.00114
 GA, SCT = 1.56, 3.8
-HOP, OWN = 0.10, 0.05
-FLIGHT = 2.8
-AHEAD = 0.0
+HOP, OWN, ISSUE = 0.11, 0.055, 0.1
+FLIGHT, SEND, SFIX = 3.1, 1.0, 0.09
+GUESSES = ((CY, GA, SCT, HOP, OWN, FLIGHT, SFIX), (0.00105, 1.3, 3.0, 0.15, 0.07, 3.6, 0.12), (0.00125, 1.9, 5.5, 0.13, 0.06, 3.0, 0.09))
+TRIES, SEED = 5500, 1
 
 
 def build(rank, core, T, topo):
@@ -85,6 +105,9 @@ def build(rank, core, T, topo):
     def ap(name, lo=0, hi=None, st=1, rows=None):
         hi = _B[name][1][1] if hi is None else hi
         return ("a", name, lo, hi, st, rows)
+
+    def ap3(name, a0, a1, b0, b1=None):
+        return ("m", name, a0, a1, b0, b1)
 
     def ind(win, off):
         return ("i", win, off)
@@ -97,6 +120,8 @@ def build(rank, core, T, topo):
             return res(d[1]).indirect(res(d[2]))
         if d[0] == "x":
             return T[d[1]][:, d[2]:d[3]]
+        if d[0] == "m":
+            return T[d[1]][:, d[2]:d[3], d[4]] if d[5] is None else T[d[1]][:, d[2]:d[3], d[4]:d[5]]
         _, name, lo, hi, st, rows = d
         t, off = _AT[name]
         n = _B[name][1][0]
@@ -108,9 +133,16 @@ def build(rank, core, T, topo):
             return []
         if d[0] == "i":
             return acc(d[1]) + acc(d[2])
+        if d[0] == "m":
+            w = _B[d[1]][3]
+            if d[5] is None:
+                return [(d[1], w * d[2] + d[4], w * d[3], w)]
+            return [(d[1], w * a + d[4], w * a + d[5], 1) for a in range(d[2], d[3])]
         return [(d[1], d[2], d[3], d[4])]
 
     def n_of(d):
+        if d[0] == "m":
+            return (d[3] - d[2]) * (1 if d[5] is None else d[5] - d[4])
         return 16 * n_of(d[2]) if d[0] == "i" else (d[3] - d[2] + d[4] - 1) // d[4]
 
     def size(d):
@@ -128,49 +160,47 @@ def build(rank, core, T, topo):
                 W += acc(d[1]); R += acc(d[2])
             else:
                 W += acc(d)
-        ops.append({"q": q, "fn": fn, "R": R, "W": W, "c": cost, "sem": sem, "inc": inc, "k": len(ops) - start[0]})
-
-    class V:
-        pass
-
-    from_ops = AluOpType
+        a, b, ga, sct = cost if isinstance(cost, tuple) else (cost, 0, 0, 0)
+        ops.append({"q": q, "fn": fn, "R": R, "W": W, "v": (a, b, ga, sct), "sem": sem, "inc": inc, "k": len(ops) - start[0],
+                    "c": a + CY * (b + GA * ga + SCT * sct) + SFIX * (q == "S") + FLIGHT * (q == "N")})
+        return len(ops) - 1
 
     def vcost(n, full, inds, outs_ind):
         if outs_ind:
-            return 0.06 + n * SCT * CY
+            return (0.06, 0, 0, n)
         if inds:
-            return 0.06 + n * GA * CY
-        return max(64, n * full) * CY
+            return (0.06, 0, n, 0)
+        return (0.0, max(64, n * full), 0, 0)
 
     def sc(x):
         return res(x) if isinstance(x, tuple) else x
 
     def tt(o, a, b, op):
         full = 1 if isps(a) or isps(b) else 2
-        put("V", lambda g: g.vector.tensor_tensor(res(o), res(a), res(b), op), [a, b], [o], vcost(n_of(o), full, a[0] == "i", o[0] == "i"))
+        return put("V", lambda g: g.vector.tensor_tensor(res(o), res(a), res(b), op), [a, b], [o], vcost(n_of(o), full, a[0] == "i", o[0] == "i"))
 
     def ts(o, a, s1, op0, s2=None, op1=None):
-        two = 0.5 if not isps(a) and not isps(o) and o[0] == "a" and size(a) == 2 and size(o) == 2 else 1
+        two = 0.5 if o[0] != "i" and a[0] != "i" and size(a) == 2 and size(o) == 2 else 1
         rd = [a] + [x for x in (s1, s2) if isinstance(x, tuple)]
         if op1 is None:
-            put("V", lambda g: g.vector.tensor_scalar(res(o), res(a), sc(s1), None, op0), rd, [o], vcost(n_of(o), two, a[0] == "i", o[0] == "i"))
-        else:
-            put("V", lambda g: g.vector.tensor_scalar(res(o), res(a), sc(s1), sc(s2), op0, op1), rd, [o], vcost(n_of(o), two, a[0] == "i", o[0] == "i"))
+            return put("V", lambda g: g.vector.tensor_scalar(res(o), res(a), sc(s1), None, op0), rd, [o], vcost(n_of(o), two, a[0] == "i", o[0] == "i"))
+        return put("V", lambda g: g.vector.tensor_scalar(res(o), res(a), sc(s1), sc(s2), op0, op1), rd, [o], vcost(n_of(o), two, a[0] == "i", o[0] == "i"))
 
     def cp(o, a):
-        two = 0.5 if a[0] == "a" and o[0] == "a" and not isps(a) and size(a) == 2 and size(o) == 2 else 1
-        put("V", lambda g: g.vector.tensor_copy(res(o), res(a)), [a], [o], vcost(n_of(o), two, a[0] == "i", o[0] == "i"))
+        two = 0.5 if o[0] != "i" and a[0] != "i" and size(a) == 2 and size(o) == 2 else 1
+        return put("V", lambda g: g.vector.tensor_copy(res(o), res(a)), [a], [o], vcost(n_of(o), two, a[0] == "i", o[0] == "i"))
 
-    def scan(o, a, b, op0=AluOpType.mult, op1=AluOpType.add):
-        put("V", lambda g: g.vector.tensor_tensor_scan(res(o), res(a), res(b), 0.0, op0, op1), [a, b], [o], vcost(n_of(o), 1, False, False))
+    def scan(o, a, b, op0=AluOpType.mult, op1=AluOpType.add, first=0.0):
+        return put("V", lambda g: g.vector.tensor_tensor_scan(res(o), res(a), res(b), first, op0, op1), [a, b], [o],
+                   vcost(n_of(o), 0.5 if size(o) == size(a) == size(b) == 2 else 1, False, False))
 
     def fill(o, v):
-        put("V", lambda g: g.vector.memset(res(o), v), [], [o], vcost(n_of(o), 0.5, False, False))
+        return put("V", lambda g: g.vector.memset(res(o), v), [], [o], vcost(n_of(o), size(o) / 4, False, False))
 
     def act(o, a, func, bias=0.0, scale=1.0):
         rd = [a] + [x for x in (bias, scale) if isinstance(x, tuple)]
-        put("S", lambda g: g.scalar.activation(res(o), res(a), func, bias=sc(bias), scale=sc(scale)), rd, [o],
-            0.08 + n_of(o) * (GA if a[0] == "i" else 1) * CY)
+        return put("S", lambda g: g.scalar.activation(res(o), res(a), func, bias=sc(bias), scale=sc(scale)), rd, [o],
+                   (0.0, 0, n_of(o), 0) if a[0] == "i" else (0.0, n_of(o), 0, 0))
 
     def mm(lst):
         def fn(g):
@@ -178,126 +208,166 @@ def build(rank, core, T, topo):
             for o, l, rh, st, sp in lst:
                 r = g.tensor.matmul(res(o), res(l), res(rh), st, sp)
             return r
-        put("P", fn, [x[1] for x in lst] + [x[2] for x in lst], [x[0] for x in lst], sum(max(64, n_of(x[2])) for x in lst) * CY)
+        return put("P", fn, [x[1] for x in lst] + [x[2] for x in lst], [x[0] for x in lst], (0.0, sum(max(64, n_of(x[2])) for x in lst), 0, 0))
 
-    def later(k):
-        ops[-1].setdefault("after", []).append(k)
+    def iota(o, pattern, base, step=0):
+        if _B[o[1]][2] == I:
+            return put("G", lambda g: g.iota(res(o), pattern, base, step), [], [o], (0.15, 2 * n_of(o), 0, 0))
+        return put("G", lambda g: g.iota(res(o), pattern, base, step, allow_small_or_imprecise_dtypes=True), [], [o], (0.15, 2 * n_of(o), 0, 0))
+
+    def later(*ks):
+        ops[-1].setdefault("after", []).extend(ks)
 
     nd = [0]
 
     def dma(o, a, cost):
         k = "d%d" % nd[0]; nd[0] += 1
-        put("Y", lambda g: g.sync.dma_start(res(o) if isinstance(o, tuple) else o, res(a) if isinstance(a, tuple) else a),
-            [a] if isinstance(a, tuple) else [], [o] if isinstance(o, tuple) else [], cost, sem=k, inc=16)
+        return put("Y", lambda g: g.sync.dma_start(res(o) if isinstance(o, tuple) else o, res(a) if isinstance(a, tuple) else a),
+                   [a] if isinstance(a, tuple) else [], [o] if isinstance(o, tuple) else [], cost, sem=k, inc=16)
 
-    ADD, SUB, MUL, MIN, MAX = from_ops.add, from_ops.subtract, from_ops.mult, from_ops.min, from_ops.max
-    EQ, NE, GE, GT, LT, LE = from_ops.is_equal, from_ops.not_equal, from_ops.is_ge, from_ops.is_gt, from_ops.is_lt, from_ops.is_le
-    SHR, AND = from_ops.arith_shift_right, from_ops.bitwise_and
+    def send(o, a, sem, loc, dst):
+        rid, pid, se = topo.addr(dst)
+        m = 0
+        for e in topo.engines(core, dst)[:8]:
+            m |= 1 << e
+        k = put("G", lambda g: g.remote_dma(T[o][:, :], res(a), T.sem[sem], T.sem[loc], pid, rid, m), [a], [], SEND, sem=loc, inc=0)
+        ops[-1]["n"] = len(topo.engines(core, dst)[:8])
+        put("N", None, [], [ap(o)], 0.0, sem=sem, inc=8)
+        ops[-1]["after"] = [k]
+
+    ADD, SUB, MUL, MIN, MAX = AluOpType.add, AluOpType.subtract, AluOpType.mult, AluOpType.min, AluOpType.max
+    EQ, NE, GE, GT, LT, LE = AluOpType.is_equal, AluOpType.not_equal, AluOpType.is_ge, AluOpType.is_gt, AluOpType.is_lt, AluOpType.is_le
+    SHR, AND = AluOpType.arith_shift_right, AluOpType.bitwise_and
     AF = ActivationFunctionType
 
-    dma(ap("c8"), T.c0[:, :], 2.0); dma(ap("hwi"), T.hw[:, :], 2.0); dma(ap("kmi"), T.km[:, :], 2.0); dma(ap("th8"), T.th[:, :], 2.0)
-    dma(ap("TP"), ext("tp", 0, 4096), 6.0)
-    for k in range(4):
-        later(k)
-    dma(ap("US", 0, 4096), ext("us", 0, 4096), 8.0); later(4)
+    def keep(o, src, pattern, base, op=EQ, step=0):
+        return put("G", lambda g: g.affine_select(res(o), res(ap(src)), pattern, op, 0.0, base, step), [ap(src)], [o], (0.18, 256, 0, 0))
 
-    put("G", lambda g: g.iota(res(ap("pI")), [[0, 1]], 0, 1), [], [ap("pI")], 0.2)
-    put("G", lambda g: g.iota(res(ap("IC")), [[1, 256]], 0, 0), [], [ap("IC")], 0.6)
-    ts(ap("sI"), ap("pI"), 15, AND); ts(ap("gI"), ap("pI"), 4, SHR); ts(ap("s2I"), ap("sI"), 2, SHR)
-    ts(ap("s8I"), ap("pI"), 8, ADD); ts(ap("s8I"), ap("s8I"), 15, AND)
-    for a, b in (("pF", "pI"), ("sF", "sI"), ("gF", "gI"), ("s8F", "s8I"), ("s2F", "s2I")):
+    dma(ap("c8"), T.c0[:, :], 2.0); dma(ap("hwi"), T.hw[:, :], 2.0); later(0)
+    dma(ap("TP"), ext("tp", 0, S), 6.0); later(1)
+    dma(ap("kmi"), T.km[:, :], 6.0); later(2); dma(ap("th8"), T.th[:, :], 6.0); later(3)
+    ldu = dma(ap("US", 0, S), ext("us", 0, S), 8.0); later(4)
+
+    iota(ap("pI"), [[0, 1]], 0, 1); iota(ap("CG"), [[1, 8], [0, 16]], 0); iota(ap("IC"), [[1, 256]], 0); iota(ap("CS"), [[0, 16], [1, 16]], 0)
+    iota(ap("CG8"), [[8, 8], [0, 4], [1, 4]], 0); iota(ap("C3"), [[0, 32], [1, 4]], 0)
+    ts(ap("sI"), ap("pI"), 15, AND); ts(ap("s2I"), ap("sI"), 2, SHR)
+    for a, b in (("pF", "pI"), ("sF", "sI"), ("s2F", "s2I")):
         cp(ap(a), ap(b))
+    ts(ap("gF"), ap("pF"), ap("sF"), SUB, 1.0 / 16, MUL); ts(ap("gx8"), ap("pF"), ap("sF"), SUB, 0.5, MUL)
     ts(ap("sge8"), ap("sF"), 7.5, GT); ts(ap("slt8"), ap("sF"), 7.5, LT)
-    ts(ap("CS"), ap("IC"), 15, AND); ts(ap("CG"), ap("IC"), 4, SHR); ts(ap("C3"), ap("IC", 0, 128), 3, AND)
-    ts(ap("BLKB"), ap("CG", 0, 128), ap("gF"), EQ); cp(ap("BLKH"), ap("BLKB"))
+    ts(ap("pm8"), ap("sge8"), -16.0, MUL, 8.0, ADD); ts(ap("pm8"), ap("pm8"), ap("pF"), ADD)
+    ts(ap("nsB"), ap("sF"), -BIG, MUL); ts(ap("ns2"), ap("s2F"), -8 * BIG, MUL); ts(ap("s1T"), ap("sF"), 1.0, ADD, 16384.0, MUL)
+    ts(ap("BLKB"), ap("CG"), ap("gF"), EQ); ts(ap("BLKH"), ap("CG"), ap("gF"), EQ)
     r8 = slice(0, 8)
     ts(ap("REP8"), ap("CG", 0, 128, 1, r8), ap("pF", 0, 1, 1, r8), EQ)
-    ts(ap("tmpA"), ap("C3"), 1.0, ADD); tt(ap("tmpB"), ap("tmpA"), ap("BLKB"), MUL); ts(ap("CQB"), ap("tmpB"), -1.0, ADD)
-    ts(ap("tmpA"), ap("CS", 0, 128), 1.0, ADD); tt(ap("tmpB"), ap("tmpA"), ap("BLKB"), MUL); ts(ap("CSB"), ap("tmpB"), -1.0, ADD)
-    ts(ap("PH"), ap("CSB"), ap("s8F"), EQ)
-    ts(ap("PL"), ap("CSB"), ap("s8F"), EQ, ap("sge8"), MUL); ts(ap("PR"), ap("CSB"), ap("s8F"), EQ, ap("slt8"), MUL)
-    cp(ap("hwf"), ap("hwi")); ts(ap("hwg"), ap("hwf"), 2047.5, GT, -4096.0, MUL); tt(ap("hwg"), ap("hwf"), ap("hwg"), ADD); cp(ap("hwh"), ap("hwg"))
+    ts(ap("PH"), ap("IC", 0, 128), ap("pm8"), EQ)
+    ts(ap("PL"), ap("IC", 0, 128), ap("pm8"), EQ, ap("sge8"), MUL); ts(ap("PR"), ap("IC", 0, 128), ap("pm8"), EQ, ap("slt8"), MUL)
+    ts(ap("hwf"), ap("hwi"), 2047.5, GT, -4096.0, MUL); tt(ap("hwg"), ap("hwi"), ap("hwf"), ADD); tt(ap("hwh"), ap("hwi"), ap("hwf"), ADD)
     mm([(ap("MS", 0, 2), ap("PH"), ap("hwh"), True, True)])
-    cp(ap("ws"), ap("MS", 0, 2)); ts(ap("wl"), ap("ws"), ap("sge8"), MUL); ts(ap("wr"), ap("ws"), ap("slt8"), MUL)
+    cp(ap("ws"), ap("MS", 0, 2))
 
     def wt(k, qv, r):
         i = (k * 2 + qv) * 4 + r
         return ap("WT", i * 128, i * 128 + 128)
-    ts(ap("rsc"), ap("slt8"), -1.0, MUL)
-    for r in (1, 2, 3):
-        ts(ap("rs%d" % r), ap("rsc"), float(r), ADD)
-    for qv in (0, 1):
-        ts(wt(0, qv, 0), ap("CQB"), 0.0, EQ, ap("wl", qv, qv + 1), MUL)
-        for r in (1, 2, 3):
-            ts(wt(0, qv, r), ap("CQB"), ap("rs%d" % r), EQ, ap("ws", qv, qv + 1), MUL)
-        ts(wt(1, qv, 3), ap("CQB"), 3.0, EQ, ap("wr", qv, qv + 1), MUL)
+    ts(ap("g8"), ap("IC", 0, 4), ap("gx8"), ADD); ts(ap("g8m"), ap("g8"), ap("slt8"), SUB); ts(ap("g8p"), ap("g8", 3, 4), ap("slt8"), MUL, ap("sge8"), SUB)
     for qv in (0, 1):
         for r in range(4):
-            ts(wt(2, qv, r), ap("CQB"), float(r), EQ, ap("hwg", qv, qv + 1), MUL)
-    ts(ap("MQ"), ap("C3"), ap("s2F"), EQ)
-    ts(ap("MWR"), ap("CS"), ap("sF"), EQ); ts(ap("RST"), ap("CS"), 0.5, GT)
+            ts(wt(0, qv, r), ap("CG8"), ap("g8m", r, r + 1), EQ, ap("ws", qv, qv + 1), MUL)
+        ts(wt(1, qv, 3), ap("CG8"), ap("g8p"), EQ, ap("ws", qv, qv + 1), MUL)
+    iota(ap("CG2"), [[8, 8], [1, 2], [0, 8]], 0); iota(ap("CZ"), [[0, 2], [1, 4], [0, 8]], 0); iota(ap("ML"), [[8, 8], [0, 4], [64, 8]], 0)
+    fill(ap("ONEB"), 1.0)
+    for qv in (0, 1):
+        for i in (0, 1):
+            ts(wt(2, qv, i), ap("CG2"), ap("g8", i, i + 1), EQ, ap("hwg", qv, qv + 1), MUL)
+    ts(ap("k1"), ap("kmi"), -2048.0, ADD)
+    for k in range(2):
+        keep(ap("PK", 128 * k, 128 * k + 128), "ONEB", [[16, 8], [0, 2], [2, 8]], k, EQ, -1)
+    mm([(ap("MS", 4 + k, 5 + k), ap("PK", 128 * k, 128 * k + 128), ap("k1"), True, True) for k in range(2)])
+    ts(ap("kc"), ap("MS", 4, 6), 2048.0, ADD)
+    for r in range(8):
+        keep(ap("RL", 128 * r, 128 * r + 128), "ONEB", [[16, 8], [0, 8], [8, 2]], r, EQ, -1)
+    ts(ap("s1I"), ap("sI"), 1, SHR); cp(ap("s1F"), ap("s1I"))
+    act(ap("PZL"), ap("CZ"), AF.Abs, bias=ap("ns2"), scale=8 * BIG); act(ap("PZL"), ap("PZL"), AF.Identity, bias=ap("s1F"))
+    fill(ap("RS32"), 0.0); ts(ap("RS32", 0, 64, 32), ap("IC", 0, 2), 0.0, MUL, 8 * BIG, ADD)
+    ts(ap("CJ"), ap("IC", 0, 64, 2), ap("sge8"), ADD)
+    for o, v in (("IDB", 1.0), ("IDH", 1.0), ("IDN", -1.0), ("IDHN", -1.0)):
+        ts(ap(o), ap("IC", 0, 128), ap("pF"), EQ, v, MUL)
+    act(ap("NM"), ap("CS"), AF.Abs, bias=ap("nsB"), scale=BIG)
+    act(ap("PZ4"), ap("C3"), AF.Abs, bias=ap("ns2"), scale=8 * BIG); act(ap("RS4"), ap("C3"), AF.Relu, bias=8 * BIG, scale=-8 * BIG)
+    act(ap("MWR"), ap("NM"), AF.Relu, bias=1.0, scale=-1.0); act(ap("RST"), ap("CS"), AF.Sign)
+    act(ap("TRH"), ap("CS", 0, 64), AF.Relu, bias=ap("s1T"), scale=-16384.0)
+    for o, v in (("B512", 1024.0), ("B256", 16.0), ("BLK8", 8192.0), ("BLKN", -1.0)):
+        act(ap(o), ap("BLKB"), AF.Copy, scale=v)
     ts(ap("ksc"), ap("kmi"), -2048.0, ADD); ts(ap("kh"), ap("CS", 0, 16), ap("sF"), EQ, ap("ksc"), MUL)
     mm([(ap("MS", 16, 32), ap("BLKH"), ap("kh"), True, True)])
     ts(ap("KR"), ap("MS", 16, 32), 2048.0, ADD)
     ts(ap("th8h"), ap("th8"), -2048.0, ADD)
     mm([(ap("MS", 8, 9), ap("REP8"), ap("th8h"), True, True)])
-    ts(ap("th16"), ap("MS", 8, 9), 2048.0 - 1.0 / 512, ADD, 512.0, MUL)
+    ts(ap("th16"), ap("MS", 8, 9), 2047.5, ADD, 1024.0, MUL)
+    ts(ap("JW0"), ap("IC", 0, 256, 16), ap("sF"), ADD)
+    act(ap("DRS"), ap("CS"), AF.Copy, bias=-BIG, scale=0.0); ts(ap("DRS", 0, 256, 16), ap("JW0"), S - 2047.0, ADD)
+    fill(ap("DR1"), -BIG); ts(ap("DR1", 0, 64, 16), ap("JW0", 0, 4), 2.0, MUL, 258.0, ADD)
     ts(ap("c8h"), ap("c8"), -2048.0, ADD)
+    mm([(ap("CT", 0, 256), ap("IDB"), ap("NM"), True, False), (ap("CT", 0, 256), ap("REP8"), ap("c8h"), False, True)])
+    scan(ap("CM2"), ap("DRS"), ap("CT", 0, 256), MAX, MIN); ts(ap("CL0"), ap("CM2", 15, 256, 16), 2048.0, ADD)
     mm([(ap("HR", 0, 256), ap("REP8"), ap("c8h"), True, True)])
     act(ap("CX0", 0, 256), ap("HR", 0, 256), AF.Copy, bias=2048.0)
-    tt(ap("CM"), ap("CX0", 0, 256), ap("MWR"), MUL); scan(ap("CM2"), ap("RST"), ap("CM")); cp(ap("CL0"), ap("CM2", 15, 256, 16))
     for k in "01":
-        fill(ap("TX" + k, 256, 640), 0.0)
+        fill(ap("TX" + k, L, NEW), 0.0); fill(ap("WX" + k, L, NEW), 0.0); act(ap("CX" + k, L, NEW), ap("IC", 0, NEW - L), AF.Copy)
     act(ap("TX0", 0, 256), ind(ap("TP"), ap("CL0")), AF.Copy)
-    act(ap("BLK8"), ap("BLKB"), AF.Copy, scale=8192.0);
-    ts(ap("NM"), ap("CS"), ap("sF"), NE, 4194304.0, MUL); ts(ap("RSTB"), ap("CS"), 0.5, LT, 8388608.0, MUL)
-    act(ap("B512"), ap("BLKB"), AF.Copy, scale=512.0); act(ap("B256"), ap("BLKB"), AF.Copy, scale=16.0)
 
-
-    def keep(o, src, pattern, base):
-        put("G", lambda g: g.affine_select(res(o), res(ap(src)), pattern, EQ, 0.0, base, 0), [ap(src)], [o], 0.4)
     for r in range(8):
         keep(ap("SLP", 128 * r, 128 * r + 128), "B512", [[0, 16], [1, 8]], -r)
-    slp = len(ops) - 1
+    ts(ap("g16"), ap("IC", 0, 16), ap("gx8"), ADD, ap("gx8"), ADD)
     for s in range(16):
-        keep(ap("SEL", 128 * s, 128 * s + 128), "B256", [[0, 8], [1, 16]], -s); later(slp)
-    slp = len(ops) - 1
+        if s < GSEL:
+            keep(ap("SEL", 128 * s, 128 * s + 128), "B256", [[0, 8], [1, 16]], -s)
+        else:
+            ts(ap("SEL", 128 * s, 128 * s + 128), ap("IC", 0, 128), ap("g16", s, s + 1), EQ, 16.0, MUL)
     for r in range(4):
-        keep(ap("SLQ", 128 * r, 128 * r + 128), "B512", [[0, 32], [1, 4]], -r); later(slp)
-    slp = len(ops) - 1
-    put("G", lambda g: g.iota(res(ap("WTAB")), [[0, 1024], [1, 4]], 4, 0, allow_small_or_imprecise_dtypes=True), [], [ap("WTAB")], 7.0); later(slp)
-    cp(ap("CI"), ap("CX0", 0, 256)); ts(ap("CI3"), ap("CI"), 3, AND); ts(ap("WX0", 0, 256), ap("CI3"), 4.0, ADD)
-    ts(ap("W64"), ap("C3", 0, 64), 4.0, ADD)
-    ts(ap("s3F"), ap("sF"), 7.5, GT)
-    put("G", lambda g: g.iota(res(ap("MP")), [[16, 16], [0, 32]], 0, 0, allow_small_or_imprecise_dtypes=True), [], [ap("MP")], 1.0)
-    put("G", lambda g: g.iota(res(ap("ML")), [[16, 16], [4, 4], [0, 4]], 0, 0, allow_small_or_imprecise_dtypes=True), [], [ap("ML")], 0.6)
-    ts(ap("k3I"), ap("IC", 0, 64), 1, AND); ts(ap("PZ"), ap("k3I"), ap("s3F"), NE, 4194304.0, MUL)
-    ts(ap("PZQ"), ap("C3", 0, 64), ap("s2F"), NE, 4194304.0, MUL)
-    ts(ap("CC"), ap("IC", 0, 16), 1.0, MUL); ts(ap("CCL"), ap("IC", 0, 4), 1.0, MUL)
-    ts(ap("JW0"), ap("IC", 0, 16), 16.0, MUL, ap("sF"), ADD)
-    ts(ap("J256"), ap("JW0"), 256.0, ADD); ts(ap("D4096"), ap("JW0"), 4096.0, ADD)
-    ts(ap("FIX", 0, 16), ap("JW0"), 254.5, GT, 256.0, MUL); ts(ap("FIX", 16, 32), ap("JW0"), 253.5, GT, 256.0, MUL)
-    ts(ap("CL"), ap("CC"), 16.0, MUL, 15.0, ADD)
-    ts(ap("oneR"), ap("CS"), -1.0, GT); ts(ap("EE", 0, 1), ap("pF"), 0.0, MUL)
-    ts(ap("tmpA"), ap("CS", 0, 128), ap("sF"), LE, -1.0, MUL); tt(ap("TRIMB"), ap("tmpA"), ap("BLKB"), MUL)
-    ts(ap("IDH"), ap("IC", 0, 128), ap("pF"), EQ); cp(ap("IDB"), ap("IDH")); act(ap("ID8"), ap("IDB"), AF.Copy, scale=8192.0); ts(ap("IDN"), ap("IDH"), -1.0, MUL); ts(ap("EQM"), ap("MWR"), -1.0, ADD); fill(ap("ONEB"), 1.0); fill(ap("one16"), 1.0); fill(ap("C255"), 255.0)
-    ts(ap("TRP"), ap("CS"), ap("sF"), LE, 16384.0, MUL); ts(ap("TRH"), ap("CS"), ap("sF"), LE, 16384.0, MUL)
-    ts(ap("T5"), ap("IC"), 5.0, MUL, 2.0, ADD)
+        keep(ap("SLQ", 128 * r, 128 * r + 128), "B512", [[0, 32], [1, 4]], -r)
+    keep(ap("TRIMB"), "BLKN", [[-1, 128]], 0, GE, 1)
+    iota(ap("WTAB", 0, 512), [[0, 128], [1, 4]], 4)
+    for k in range(1, 8):
+        dma(ap("WTAB", 512 * k, 512 * k + 512), ap("WTAB", 0, 512), 7.0); later(ldu)
+    ts(ap("c8i"), ap("c8"), 3, AND); ts(ap("c8w"), ap("c8i"), 4.0, ADD)
+    mm([(ap("DB", 0, 256), ap("REP8"), ap("c8w"), True, True)])
+    act(ap("WX0", 0, 256), ap("DB", 0, 256), AF.Copy)
+    ts(ap("pen2"), ap("IC", 0, 2), ap("sge8"), NE, 2 * BIG, MUL); ts(ap("pen4"), ap("IC", 0, 4), ap("s2F"), NE, 2 * BIG, MUL)
+    for h in range(2):
+        ts(ap("MP", h, 512, 2), ap("IC"), ap("pen2", h, h + 1), ADD)
+    for h in range(4):
+        ts(ap("MS1", h, 256, 4), ap("IC", 192, 256), ap("pen4", h, h + 1), ADD)
+    ts(ap("J256"), ap("JW0"), 256.0, ADD)
+    ts(ap("EE", 510, 512), ap("IC", 0, 2), 0.0, MUL, 1282.0, ADD)
+    fill(ap("one16"), 1.0); fill(ap("P2", 0, 16), 0.5); scan(ap("P2", 16, 32), ap("P2", 0, 16), ap("one16"), MUL, MAX, 2.0 ** 29)
+    tt(ap("P2", 32, 48), ap("P2", 16, 32), ap("MWR", 0, 16), MUL); scan(ap("P2", 0, 16), ap("one16"), ap("P2", 32, 48)); ts(ap("rF"), ap("P2", 15, 16), -2.0, MUL)
+    act(ap("W2"), ap("BLKB"), AF.Identity, scale=ap("P2", 15, 16)); act(ap("B30"), ap("BLKB"), AF.Copy, scale=2.0 ** 30)
+    act(ap("NM2"), ap("NM", 0, 128), AF.Identity, bias=ap("rF"), scale=2.0 ** 23)
+    ts(ap("EE", 0, 1), ap("pF"), 0.0, MUL)
+    fill(ap("oneR"), 1.0); fill(ap("C255"), 255.0)
+    act(ap("T5"), ap("IC"), AF.Copy, bias=2.0, scale=5.0)
+    ts(ap("lNM"), ap("NM", 0, 64), -2048.0, ADD)
+    LR = (0, 64, 112, 144)
+    fill(ap("lTR"), 0.0)
+    for c in range(4):
+        cp(ap("lTR", LR[c], LR[c] + 16), ap("TRH", 0, 16))
     rng = []
     for c in range(16):
         lo = -((-(64 * c + 2)) // 5); hi = min(256, -((-(112 * c + 110)) // 5))
         rng.append((lo, hi))
-    ts(ap("kz1"), ap("IC"), 5.0, MUL, 62.0, ADD); ts(ap("kz1"), ap("kz1"), 6, SHR); ts(ap("kz2"), ap("kz1"), 16.0, MIN)
-    ts(ap("kz1"), ap("T5"), -55.5, ADD, 1.0 / 112, MUL); tt(ap("KONST"), ap("kz2"), ap("kz1"), ADD)
+    act(ap("kz1", 0, rng[15][0]), ap("IC", 0, rng[15][0]), AF.Copy, bias=128.0 + 30.5 / 64, scale=5.0 / 64); fill(ap("kz1", rng[15][0], 256), 144.0)
+    act(ap("kz2"), ap("IC"), AF.Copy, bias=160.0 - 53.5 / 112, scale=5.0 / 112)
+    mm([(ap("JP", 0, 256), ap("IDB"), ap("kz1"), True, False), (ap("JP", 0, 256), ap("IDB"), ap("kz2"), False, True)])
+    act(ap("KONST"), ap("JP", 0, 256), AF.Copy, bias=-288.0)
     fill(ap("RJ", 0, 16), 300.0)
-    ts(ap("IC64"), ap("IC", 0, 64), 1.0, MUL); ts(ap("PF64"), ap("IC64"), 5.0, MUL, 1280.0, ADD)
-    fill(ap("HT", 256, 1056), UNF); fill(ap("lHT", 64, 144), UNF); fill(ap("RS", 64, 72), 0.0)
+    cp(ap("IC64"), ap("IC", 0, 64)); ts(ap("PF64"), ap("IC", 0, 64), 5.0, MUL, 1280.0, ADD)
+    act(ap("HT", 256, 512), ap("IC"), AF.Copy); fill(ap("HT", 512, 528), UNF); fill(ap("lHT", 512, 528), UNF)
+    fill(ap("RI", 0, 64), 8 * BIG); fill(ap("US", S, 4480), 0.0)
 
     def sel(bank, o, name, lo, n):
-        return [(ap(bank, o, o + n), ap("SEL", 128 * s, 128 * s + 128), ap(name, lo + s, lo + s + 16 * (n - 1) + 1, 16), s == 0, s == 15) for s in range(16)]
-
-    def pair(m):
-        return m < 14 and m not in BYS and (m ^ 1) not in BYS
+        for k in range(0, 16, 4):
+            mm([(ap(bank, o, o + n), ap("SEL", 128 * s, 128 * s + 128), ap(name, lo + s, lo + s + 16 * (n - 1) + 1, 16), s == 0, s == 15) for s in range(k, k + 4)])
 
     for t in range(RO):
         start[0] = len(ops)
@@ -305,230 +375,218 @@ def build(rank, core, T, topo):
         cx, tx, cy, ty, wx, wy = "CX" + cur, "TX" + cur, "CX" + nxt, "TX" + nxt, "WX" + cur, "WX" + nxt
         last = t == RO - 1
         b16 = ap("th16") if t == 0 else ap("b16a" if t % 2 else "b16b")
+        lender = T.cores[(rank + 1 + t % 3) % 4]
+        borrower = T.cores[(rank - 1 - t % 3) % 4]
+        mm([(ap("UVP", 0, 128), ap("IDB"), ap("PZ4"), True, False)])
         lst = []
         for qv in (0, 1):
             for r in range(4):
-                lst.append((ap("UVP", 64 * qv, 64 * qv + 64), wt(0, qv, r), ap(tx, r, r + 253, 4), r == 0, False))
-            lst.append((ap("UVP", 64 * qv, 64 * qv + 64), wt(1, qv, 3), ap(tx, 4, 257, 4), False, True))
+                lst.append((ap("UVP", 64 * qv, 64 * qv + 64), wt(0, qv, r), ap(tx, r, r + 253, 4), False, False))
+            lst.append((ap("UVP", 64 * qv, 64 * qv + 64), wt(1, qv, 3), ap(tx, 4, 257, 4), False, qv == 1))
         mm(lst)
         mm([(ap("ZP", 0, 256), ap("PL"), ap(tx, 0, 256), True, False), (ap("ZP", 0, 256), ap("PR"), ap(tx, 1, 257), False, True)])
-        act(ap("ZB", 0, 256), ap("ZP", 0, 256), AF.Copy); act(ap("ZB", 256, 512), ap("ZP", 0, 256), AF.Copy)
-        tt(ap("UVM"), ap("UVP", 0, 128), ap("MQ"), MUL)
-        tt(ap("UT"), ap("UVM", 0, 128, 2), ap("UVM", 1, 128, 2), ADD)
-        tt(ap("UVI"), ap("UT", 0, 64, 2), ap("UT", 1, 64, 2), ADD)
-        ts(ap("UVA"), ap("UVI"), 4095, AND)
+        zb = [act(ap("ZB", 256 * k, 256 * k + 256), ap("ZP", 0, 256), AF.Copy) for k in range(2)]
+        scan(ap("UVS"), ap("RS4"), ap("UVP", 0, 128), ADD, MIN)
+        ts(ap("UVA"), ap("UVS", 3, 128, 4), 4095, AND)
         tt(ap("UVW"), ap("UVA", 0, 16), ap("UVA", 16, 32), MUL)
         ts(ap("UVA", 16, 32), ap("UVW"), 5, SHR)
         cp(ap("UQ"), ap("UVA"))
         for c in range(16):
-            if c % 4 == 3:
-                act(ap("HF", c // 4, 64, 4), ap("KR"), AF.Identity, bias=ap("UQ", 16 + c, 17 + c), scale=ap("UQ", c, c + 1))
+            if c >= 16 - NS:
+                act(ap3("HF", 0, 16, c), ap("KR"), AF.Identity, bias=ap("UQ", 16 + c, 17 + c), scale=ap("UQ", c, c + 1)); later(*zb[:ZBF])
             else:
-                ts(ap("HV", c, 256, 16), ap("KR"), ap("UQ", c, c + 1), MUL, ap("UQ", 16 + c, 17 + c), ADD)
-        cp(ap("HV", 3, 256, 4), ap("HF"))
-        for h in (0, 1):
-            ts(ap("HI", 128 * h, 128 * h + 128), ap("HV", 128 * h, 128 * h + 128), 4095, AND)
-            cp(ap("HO", 128 * h, 128 * h + 128), ap("HI", 128 * h, 128 * h + 128))
-        for mb in range(4):
-            if mb == 0:
-                scan(ap("EE", 256, 512), ap("oneR"), ap(wx, 0, 256)); cp(ap("EE", 1, 256), ap("EE", 256, 511))
-                mm(sel("MS", 32, "EE", 0, 32))
-            for m in range(4 * mb, 4 * mb + 4):
-                x, u = ap("X", 256 * m, 256 * m + 256), ind(ap("US", 0, 4096), ap("HO", 16 * m, 16 * m + 16))
-                if m in BYS:
-                    act(x, u, AF.Copy)
-                elif not pair(m):
-                    tt(x, u, ap("ZB", 0, 256), SUB)
-                    if XCH and m > 2:
-                        later(x15)
-                    x15 = len(ops) - 1
-                elif m % 2 == 0:
-                    tt(ap("X", 256 * m, 256 * m + 512), ind(ap("US", 0, 4096), ap("HO", 16 * m, 16 * m + 32)), ap("ZB"), SUB)
-                    if XCH and m > 2:
-                        later(x15)
-                    x15 = len(ops) - 1
-            for m in range(4):
-                lo = 1024 * mb + 256 * m
-                k = 2 if pair(4 * mb + m) else 1
-                if k == 2 and m % 2:
-                    continue
-                if 4 * mb + m in BYS:
-                    bank = BYS[4 * mb + m]
-                    mm([(ap(bank, 256, 512), ap("IDB"), ap("X", lo, lo + 256), True, False), (ap(bank, 256, 512), ap("IDN"), ap("ZB", 0, 256), False, True)])
-                    act(ap("A", lo, lo + 256), ap(bank, 256, 512), AF.Abs)
+                ts(ap3("HV", 0, 16, c), ap("KR"), ap("UQ", c, c + 1), MUL, ap("UQ", 16 + c, 17 + c), ADD)
+        cp(ap3("HV", 0, 16, 16 - NS, 16), ap3("HF", 0, 16, 16 - NS, 16))
+        for a, b in ((0, 4), (4, 16)):
+            ts(ap("HI", 16 * a, 16 * b), ap3("HV", a, b, 0, 16), 4095, AND)
+            cp(ap("HO", 16 * a, 16 * b), ap("HI", 16 * a, 16 * b))
+        scan(ap("EE", 256, 510), ap("oneR", 0, 254), ap(wx, 0, 254)); cp(ap("EE", 1, 256), ap("EE", 256, 511))
+        sel("MS", 32, "EE", 0, 32)
+        slots = [lambda: ts(ap("FI"), ap("MS", 32, 64), 0.2 / 256, MUL, 256.0, MIN), lambda: ts(ap("EB"), ap("MS", 48, 64), -1.0 / 256, MUL, 0.5, ADD),
+                 lambda: tt(ap("NW"), ap("FI", 16, 32), ap("FI", 0, 16), SUB),
+                 lambda: ts(ap("RI", 1, 64, 4), ap("NW"), 4 * BIG, MUL, 512.0 - 2 * BIG, ADD)]
+        banks = ("DA", "DB", "JP", "HR", "UVP")
+        prev = {}
+        for step, m, k in PROBE:
+            x, d = ap("X", 256 * m, 256 * (m + k)), ap(BYS.get(m, "ZP"), 512 - 256 * k, 512)
+            if step == "gather" and m in BYS:
+                j = act(x, ind(ap("US", 0, S), ap("HO", 16 * m, 16 * (m + k))), AF.Copy)
+                mm([(d, ap("IDN"), ap("ZB", 0, 256 * k), True, False)]); mm([(d, ap("IDB"), x, False, True)])
+            elif step == "gather":
+                j = tt(x, ind(ap("US", 0, S), ap("HO", 16 * m, 16 * (m + k))), ap("ZB", 0, 256 * k), SUB)
+            elif step == "abs":
+                j = absl = act(ap("A", 256 * m, 256 * (m + k)), d if m in BYS else x, AF.Abs)
+            elif step == "slots":
+                j = slots[m]()
+            else:
+                d = ap(banks[m % 5], 0, 64)
+                mm([(d, ap("IDB"), ap("MP", 64 * m, 64 * m + 64), True, False)])
+                mm([(d, ap("SLP", 128 * r, 128 * r + 128), ap("A", 512 * m + r, 512 * m + 512, 8), False, r == 7) for r in range(8)])
+                if m == 0:
+                    j = ts(ap("RM", 0, 64), d, b16, MIN)
                 else:
-                    act(ap("A", lo, lo + 256 * k), ap("X", lo, lo + 256 * k), AF.Abs)
-        ts(ap("RM", 0, 64), ap("IC64"), 0.0, MUL, b16, ADD)
-        for n, h in enumerate(HB):
-            d, lo = ("DA", "DB")[n % 2], 512 * h
-            mm([(ap(d, 0, 64), ap("IDB"), ap("MP", 64 * h, 64 * h + 64), True, False), (ap(d, 0, 64), ap("IDB"), ap("PZ"), False, False)] +
-               [(ap(d, 0, 64), ap("SLP", 128 * r, 128 * r + 128), ap("A", lo + r, lo + 512, 8), False, r == 7) for r in range(8)])
-            tt(ap("RM", 64 * n + 64, 64 * n + 128), ap(d, 0, 64), ap("RM", 64 * n, 64 * n + 64), MIN)
-        ts(ap("HT", 0, 256), ap("HI"), -2047.0, ADD); later(x15)
-        tt(ap("KQ"), ap("RM", 512, 575, 2), ap("RM", 513, 576, 2), MIN)
-        tt(ap("KEY"), ap("KQ", 0, 16), ap("KQ", 16, 32), MIN)
-        ts(ap("FI"), ap("MS", 32, 64), 0.2 / 256, MUL); later(x15); ts(ap("EB"), ap("MS", 48, 64), -1.0 / 256, MUL, 0.5, ADD); later(x15)
-        ts(ap("FB"), ap("FI"), 256.0, MIN); tt(ap("FC"), ap("FB"), ap("FIX"), MAX)
-        tt(ap("NW"), ap("FC", 16, 32), ap("FC", 0, 16), SUB)
-        ts(ap("UN0"), ap("NW"), 0.0, EQ, 512.0, MUL); tt(ap("UNC"), ap("UN0"), ap("CC"), ADD)
-        if t:
-            ts(ind(ap(cx), ap("OBU")), ap("IC64"), 1.0, MUL, float(S + CAP * (t - 1)), ADD); later(x15)
-            dma(ext("yc", L * (t - 1), L * t), ap(cx, 0, 256, 1, slice(0, 128, 16)), 2.0)
-        fill(ap("ZA", 0, 64), 1024.0)
-        ts(ap("PO"), ap("KEY"), b16, GE); tt(ap("PN"), ap("PO"), ap("NW"), MUL); scan(ap("SC"), ap("one16"), ap("PN"))
-        scn = len(ops) - 1
-        ts(ap("UA"), ap("PN"), 0.5, LT); tt(ap("PEN"), ap("UA"), ap("J256"), MUL)
-        pen = len(ops) - 1
-        mm([(ap("MS", 64, 80), ap("TRIMB"), ap("PN"), True, False), (ap("MS", 64, 80), ap("BLKB"), ap("SC"), False, False), (ap("MS", 64, 80), ap("IDH"), ap("PEN"), False, True)])
+                    j = tt(ap("RM", 64 * m, 64 * m + 64), d, ap("RM", 64 * m - 64, 64 * m), MIN)
+            if ops[j]["q"] in prev:
+                ops[j].setdefault("after", []).append(prev[ops[j]["q"]])
+            prev[ops[j]["q"]] = j
+        for k in range(2):
+            lo = 64 * PAIRS - 64 + 32 * k
+            tt(ap("RI", 2 + k, 64, 4), ap("RM", lo, lo + 31, 2), ap("RM", lo + 1, lo + 32, 2), MIN)
+        for n in range(16 - 2 * PAIRS):
+            m = 2 * PAIRS + n
+            d = banks[(PAIRS + n) % 5]
+            mm([(ap(d, 0, 64), ap("IDB"), ap("MS1", 64 * (m - 12), 64 * (m - 11)), True, False)])
+            mm([(ap(d, 0, 64), ap("SLQ", 128 * r, 128 * r + 128), ap("A", 256 * m + r, 256 * m + 256, 4), False, r == 3) for r in range(4)])
+            tt(ap("RI", 64 * n + 64, 64 * n + 128), ap(d, 0, 64), ap("RI", 64 * n, 64 * n + 64), MIN)
+        scan(ap("KS"), ap("RS4", 0, 64), ap("RI", 64 * n + 64, 64 * n + 128), ADD, MIN)
+        key = ap("KS", 3, 64, 4)
+        ts(ap("HT", 0, 256), ap("HI"), -2047.0, ADD)
+        iota(ap("ZA", 0, 64), [[0, 64]], 1024)
+        mm([(ap("MS", 64, 80), ap("IDH"), ap("J256"), True, False)])
+        ts(ap("PO"), key, b16, GE); tt(ap("PN"), ap("PO"), ap("NW"), MUL); tt(ap("POJ"), ap("PO"), ap("J256"), MUL); scan(ap("SC"), ap("one16"), ap("PN"))
+        mm([(ap("MS", 64, 80), ap("TRIMB"), ap("PN"), False, False), (ap("MS", 64, 80), ap("IDHN"), ap("POJ"), False, False)])
+        ofm = mm([(ap("MS", 64, 80), ap("BLKB"), ap("SC"), False, True)])
         cp(ap("OF"), ap("MS", 64, 80))
-        lender = T.cores[(rank + 1 + t % 3) % 4]
-        borrower = T.cores[(rank - 1 - t % 3) % 4]
-
-        def send(o, a, sem, loc, dst):
-            rid, pid, se = topo.addr(dst)
-            m = 0
-            for e in topo.engines(core, dst)[:8]:
-                m |= 1 << e
-            put("G", lambda g: g.remote_dma(T[o][:, :], res(a), T.sem[sem], T.sem[loc], pid, rid, m), [a], [], 1.0, sem=loc, inc=0)
-            ops[-1]["n"] = len(topo.engines(core, dst)[:8])
-            put("N", None, [], [ap(o)], FLIGHT, sem=sem, inc=8)
-            ops[-1]["after"] = [len(ops) - 2]
-        if not last:
-            bn = "b16a" if t % 2 == 0 else "b16b"
-            mm([(ap("MS", 96, 97), ap("ONEB"), ap("SC", 15, 16), True, True)])
-            cp(ap("PPI"), ap("MS", 96, 97)); ts(ap("PPJ"), ap("PPI"), 63, AND); ts(ap(bn), ap("PPJ"), 512.0, MUL, ap("th16"), ADD)
-        ts(ap("MI"), ap("KEY"), 511, AND); tt(ap("LD"), ap("MI"), ap("UNC"), ADD); cp(ap("LL"), ap("LD"))
-        tt(ap("HM"), ind(ap("HT"), ap("LL")), ap("MWR"), MUL); later(pen); later(scn)
+        cp(ind(ap("ZA"), ap("OF")), ap("ZB", 0, 256))
+        send("ZL%d" % t, ap("ZA", 0, 64), "ask%d" % t, "la", lender)
+        ts(ap("MI"), key, 1023, AND); cp(ap("LL"), ap("MI"))
+        tt(ap("HM"), ind(ap("HT"), ap("LL")), ap("MWR"), MUL)
         scan(ap("HS"), ap("RST"), ap("HM"))
         mm([(ap("HR", 0, 256), ap("BLKH"), ap("HM"), True, True)])
         cp(ap("HRH"), ap("HR", 0, 256))
-        act(ap(cx, 256, 512), ap("HR", 0, 256), AF.Copy, bias=2047.0)
-        ts(ap("HW"), ap("HS", 15, 256, 16), 2047.0, ADD); cp(ap("HL"), ap("HW"))
-        mm([(ap("DA", 256, 512), ap("BLKH"), ap("HM"), True, False), (ap("DA", 256, 512), ap("IDH"), ap("TRH"), False, True)])
-        act(ap("HRT"), ap("DA", 256, 512), AF.Copy)
-        ts(ap("UR"), ap("HRH"), UNF, EQ)
-        mm([(ap("CT", 0, 256), ap("ID8"), ap("UR"), True, False), (ap("CT", 0, 256), ap("IDB"), ap("NM"), False, False)])
-        for c in range(15):
-            ts(ap("ET", 256 * c, 256 * c + 240 - 16 * c), ap("HRH", 16 * c + 16, 256), ap("HS", 16 * c + 15, 16 * c + 16), EQ)
-            if c <= NET:
-                later(len(ops) - 3)
-            mm([(ap("CT", 16 * c + 16, 256), ap("BLK8"), ap("ET", 256 * c, 256 * c + 240 - 16 * c), False, False)])
-            if c == max(NET, 0):
-                net = len(ops) - 2
-                cp(ind(ap("ZA"), ap("OF")), ap("ZB", 0, 256))
-                if NET >= 0:
-                    later(net)
-                send("ZL%d" % t, ap("ZA", 0, 64), "ask%d" % t, "la", lender)
-        tt(ap("ET", 3840, 4096), ind(ap("HS"), ap("CL")), ap("HRT"), EQ)
-        mm([(ap("CT", 0, 256), ap("BLK8"), ap("ET", 3840, 4096), False, True)])
-        ctl = len(ops) - 1
-        scan(ap("WS"), ap("RSTB"), ap("CT", 0, 256), ADD, MIN)
-        act(ap("WD"), ap("CT", 0, 256), AF.Relu, bias=1.0, scale=-1.0)
-        mm([(ap("MS", 256, 512), ap("BLKB"), ap("WD"), True, True)])
-        act(ap("WN"), ap("MS", 256, 512), AF.Copy)
-        tt(ap("LO1"), ap("WS", 15, 256, 16), ap("HW"), ADD); tt(ap("LO2"), ap("LO1"), ap("D4096"), MIN); cp(ap("LO"), ap("LO2"))
-        cp(ind(ap("US"), ap("LO")), ap("C255"))
+        hsx = act(ap(cx, NEW, NEW + L), ap("HR", 0, 256), AF.Copy, bias=2047.0)
+        act(ap("UR"), ap("HR", 0, 256), AF.Relu, bias=-3000.0)
+        tt(ap("HD"), ap("HS", 15, 256, 16), ap("DRS", 0, 256, 16), MIN)
+        for h, d in enumerate(("CT", "DB")):
+            mm([(ap(d, 256, 384), ap("IDB"), ap("NM2", 0, 128), True, False)])
+            for c in range(8):
+                ts(ap3("ET", 8 * h + c, 8 * h + c + 1, 0, 128 - 16 * c), ap("HRH", 128 * h + 16 * c, 128 * h + 128), ap("HS", 128 * h + 16 * c + 15, 128 * h + 16 * c + 16), EQ)
+                if c < 7:
+                    mm([(ap(d, 272 + 16 * c, 384), ap("B30"), ap3("ET", 8 * h + c, 8 * h + c + 1, 16, 128 - 16 * c), False, False)])
+            ctl = mm([(ap(d, 256, 384), ap("W2"), ap3("ET", 8 * h, 8 * h + 8, 0, 16), False, True)])
+            scan(ap("WS", 128 * h, 128 * h + 128), ap("DRS", 128 * h, 128 * h + 128), ap(d, 256, 384), MAX, MIN)
+            tt(ap("LA", 8 * h, 8 * h + 8), ap("WS", 128 * h + 15, 128 * h + 128, 16), ap("HD", 8 * h, 8 * h + 8), MAX)
+            ts(ap("LO", 8 * h, 8 * h + 8), ap("LA", 8 * h, 8 * h + 8), 2047.0, ADD)
+            lay = cp(ind(ap("US", 0, ZD), ap("LO", 8 * h, 8 * h + 8)), ap("C255", 0, 128))
+            act(ap("WD", 128 * h, 128 * h + 128), ap(d, 256, 384), AF.Sign)
+        ts(ap("HL"), ap("HS", 15, 256, 16), 2047.0, ADD, 4095.0, MIN)
+        mm([(ap("MS", 256, 512), ap("IDB"), ap("UR"), True, False)]); mm([(ap("MS", 256, 512), ap("BLKB"), ap("WD"), False, False)])
+        for c in range(8):
+            ts(ap3("ET", 16 + c, 17 + c, 0, 128), ap("HRH", 128, 256), ap("HS", 16 * c + 15, 16 * c + 16), EQ); later(lay)
+            mm([(ap("MS", 384, 512), ap("BLK8"), ap3("ET", 16 + c, 17 + c, 0, 128), False, c == 7)])
+        act(ap("WN"), ap("MS", 256, 512), AF.Relu, bias=NEW / 32, scale=-NEW / 512)
         zl = "ZL%d" % t
-        lst = []
-        for qv in (0, 1):
-            for r in range(4):
-                lst.append((ap("UVP", 128 + 16 * qv, 144 + 16 * qv), wt(2, qv, r), ap(zl, r, r + 61, 4), r == 0, r == 3))
-        mm(lst)
-        luv = len(ops) - 1
-        for k in range(4):
-            act(ap("ZT", 64 * k, 64 * k + 64), ap(zl), AF.Copy)
-        tt(ap("lUVM"), ap("UVP", 128, 160), ap("MQ", 0, 32), MUL)
-        tt(ap("lUT"), ap("lUVM", 0, 32, 2), ap("lUVM", 1, 32, 2), ADD)
-        tt(ap("lUVI"), ap("lUT", 0, 16, 2), ap("lUT", 1, 16, 2), ADD)
-        ts(ap("lUVA"), ap("lUVI"), 4095, AND)
-        tt(ap("lUVW"), ap("lUVA", 0, 4), ap("lUVA", 4, 8), MUL)
-        ts(ap("lUVA", 4, 8), ap("lUVW"), 5, SHR)
-        cp(ap("lUQ"), ap("lUVA"))
-        for c in range(4):
-            ts(ap("lHV", c, 64, 4), ap("KR"), ap("lUQ", c, c + 1), MUL, ap("lUQ", 4 + c, 5 + c), ADD)
-        ts(ap("lHI"), ap("lHV"), 4095, AND); cp(ap("lHO"), ap("lHI"));
-        for mb in range(4):
-            w = 256 if mb < 3 else 128
-            tt(ap("lX", 256 * mb, 256 * mb + w), ind(ap("US", 0, 4096), ap("lHO", 16 * mb, 16 * mb + w // 16)), ap("ZT", 0, w), SUB)
-            lx = len(ops) - 1
-        act(ap("lX", 896, 1024), ind(ap("US", 0, 4096), ap("lHO", 56, 64)), AF.Copy)
-        mm([(ap("ZP", 256, 384), ap("IDB"), ap("lX", 896, 1024), True, False), (ap("ZP", 256, 384), ap("IDN"), ap("ZT", 0, 128), False, True)])
-        ts(ap("lHT", 0, 64), ap("lHI"), -2047.0, ADD); later(lx)
-        for mb in range(3):
-            act(ap("lA", 256 * mb, 256 * mb + 256), ap("lX", 256 * mb, 256 * mb + 256), AF.Abs)
-        act(ap("lA", 896, 1024), ap("ZP", 256, 384), AF.Abs)
-        act(ap("lA", 768, 896), ap("lX", 768, 896), AF.Abs)
-        ts(ap("lRM", 0, 64), ap("IC64"), 0.0, MUL, b16, ADD)
-        for n, h in enumerate((0, 1, 2, 3)):
-            d = ("DA", "DB")[n % 2]
-            mm([(ap(d, 64, 128), ap("IDB"), ap("ML", 64 * h, 64 * h + 64), True, False), (ap(d, 64, 128), ap("IDB"), ap("PZQ"), False, False)] +
-               [(ap(d, 64, 128), ap("SLQ", 128 * r, 128 * r + 128), ap("lA", 256 * h + r, 256 * h + 256, 4), False, r == 3) for r in range(4)])
-            tt(ap("lRM", 64 * n + 64, 64 * n + 128), ap(d, 64, 128), ap("lRM", 64 * n, 64 * n + 64), MIN)
-        tt(ap("lK1"), ap("lRM", 256, 288), ap("lRM", 288, 320), MIN); tt(ap("lK2"), ap("lK1", 0, 16), ap("lK1", 16, 32), MIN)
-        tt(ap("lK3"), ap("lK2", 0, 16, 2), ap("lK2", 1, 16, 2), MIN); tt(ap("lKEY"), ap("lK3", 0, 8, 2), ap("lK3", 1, 8, 2), MIN)
-        ts(ap("lMI"), ap("lKEY"), 2, SHR, 127, AND); cp(ap("lLL"), ap("lMI"))
+        mm([(ap("UVP", 128 + 32 * qv, 160 + 32 * qv), wt(2, qv, i), ap(zl, i, i + 63, 2), i == 0, i == 1) for qv in (0, 1) for i in (0, 1)])
+        for k in range(2):
+            act(ap("ZT", 256 * k, 256 * k + 256), ind(ap(zl), ap("CJ", 16 * k, 16 * k + 16)), AF.Copy)
+        cp(ap("lUVS"), ap("UVP", 128, 192))
+        ts(ap("lUVA"), ap("lUVS"), 4095, AND)
+        tt(ap("lUVW"), ap("lUVA", 0, 32), ap("lUVA", 32, 64), MUL)
+        for k in range(2):
+            ts(ap("lKU", 32 * k, 32 * k + 32), ap("lUVA", 0, 32), ap("kc", k, k + 1), MUL)
+        ts(ap("lUQ"), ap("lUVW"), 5, SHR)
+        for k in range(2):
+            tt(ap("lHV", 32 * k, 32 * k + 32), ap("lKU", 32 * k, 32 * k + 32), ap("lUQ"), ADD)
+        ts(ap("lHI"), ap("lHV"), 4095, AND); cp(ap("lHO"), ap("lHI"))
+        act(ap("lX", 768, 896), ind(ap("US", 0, S), ap("lHO", 48, 56)), AF.Copy)
+        mm([(ap("ZP", 256, 384), ap("IDN"), ap("ZT", 256, 384), True, False)]); mm([(ap("ZP", 256, 384), ap("IDB"), ap("lX", 768, 896), False, True)])
+        for n in range(4):
+            lo = 256 * n if n < 3 else 896
+            lx = tt(ap("lX", lo, 256 * n + 256), ind(ap("US", 0, S), ap("lHO", lo // 16, 16 * n + 16)), ap("ZT", lo % 512, 256 * (n % 2) + 256), SUB)
+            act(ap3("lA", lo // 32, 8 * n + 8, 0, 32), ap("lX", lo, 256 * n + 256), AF.Abs)
+            if n == 0:
+                half = act(ap3("lA", 24, 28, 0, 32), ap("ZP", 256, 384), AF.Abs)
+            if n == 1:
+                later(half)
+        ts(ap("lHH"), ap("lHI"), -2047.0, ADD)
+        mm([(ap("ZP", 64 * r, 64 * r + 64), ap("RL", 128 * r, 128 * r + 128), ap("lHH"), True, True) for r in range(8)])
+        act(ap("lHT", 0, 512), ap("ZP"), AF.Copy)
+        for n in range(4):
+            d = ("DA", "DB", "UVP", "HR")[n]
+            mm([(ap(d, 64, 128), ap("IDB"), ap("ML", 64 * n, 64 * n + 64), True, False), (ap(d, 64, 128), ap("IDB"), ap("PZL"), False, False)])
+            mm([(ap(d, 64, 128), ap("SLQ", 128 * r, 128 * r + 128), ap3("lA", 8 * n, 8 * n + 8, 8 * r, 8 * r + 8), False, r == 3) for r in range(4)])
+            if n < 2:
+                ts(ap("lRM", 64 * n, 64 * n + 64), ap(d, 64, 128), b16, MIN)
+            else:
+                tt(ap("lRM", 64 * n, 64 * n + 64), ap(d, 64, 128), ap("lRM", 64 * n - 128, 64 * n - 64), MIN)
+                scan(ap("lKS", 64 * n - 128, 64 * n - 64), ap("RS32"), ap("lRM", 64 * n, 64 * n + 64), ADD, MIN)
+        ts(ap("lMI"), ap("lKS", 31, 128, 32), 1023, AND); cp(ap("lLL"), ap("lMI"))
         tt(ap("lHM"), ind(ap("lHT"), ap("lLL")), ap("MWR", 0, 64), MUL)
         scan(ap("lHS"), ap("RST", 0, 64), ap("lHM"))
-        mm([(ap("HR", 256, 320), ap("BLKH"), ap("lHM"), True, True)])
-        tt(ap("lHRT"), ap("HR", 256, 320), ap("TRP", 0, 64), ADD)
-        ts(ap("lHW"), ap("lHS", 15, 64, 16), 2047.0, ADD); tt(ap("lHD"), ap("lHW"), ap("D4096", 0, 4), SUB); cp(ap("lHL"), ap("lHW"))
-        ts(ap("lET", 256, 320), ap("HR", 256, 320), UNF, EQ)
-        mm([(ap("CT", 256, 320), ap("BLKB"), ap("lET", 256, 320), True, False)])
-        for c in range(3):
-            ts(ap("lET", 64 * c, 64 * c + 48 - 16 * c), ap("HR", 272 + 16 * c, 320), ap("lHS", 16 * c + 15, 16 * c + 16), EQ)
-            mm([(ap("CT", 272 + 16 * c, 320), ap("BLKB"), ap("lET", 64 * c, 64 * c + 48 - 16 * c), False, False)])
-        tt(ap("lET", 192, 256), ind(ap("lHS"), ap("CL", 0, 4)), ap("lHRT"), EQ)
-        mm([(ap("CT", 256, 320), ap("BLKB"), ap("lET", 192, 256), False, True)])
-        lct = len(ops) - 1
-        ts(ap("GR"), ap("CT", 256, 320), 0.0, EQ)
-        tt(ap("RS", 0, 64), ind(ap("TP"), ap("lHL")), ap("GR"), MUL)
-        tt(ap("GM"), ap("CT", 256, 320), ap("EQM", 0, 64), EQ); scan(ap("GS"), ap("RST", 0, 64), ap("GM"))
-        ts(ap("RS", 64, 68), ap("GS", 15, 64, 16), -256.0, MUL, 256.0, ADD)
+        reg = [ap(("HR", "ZP")[c // 2], 256 + LR[c], 320 + LR[c] - 16 * c) for c in range(4)]
+        for d, lo, hi in (("HR", 0, 112), ("ZP", 112, 160)):
+            mm([(ap(d, 256 + lo, 256 + hi), ap("IDB"), ap("lTR", lo, hi), True, False)])
+        for c in (0, 2):
+            mm([(reg[k], ap("BLKH"), ap("lHM", 16 * k, 64), False, k % 2 == 1) for k in (c, c + 1)])
+        lhl = ts(ap("lHL"), ap("lHS", 15, 64, 16), 2047.0, ADD, 4095.0, MIN)
+        act(ap("RS", 0, 64), ind(ap("TP"), ap("lHL")), AF.Copy)
+        mm([(ap("CT", 256, 320), ap("IDB"), ap("lNM"), True, False)])
+        mm([(ap("CT", 256, 320), ap("IDH"), ap("lHM"), False, False)])
+        for c in range(4):
+            e = ap("lET", LR[c], LR[c] + 64 - 16 * c)
+            ts(e, reg[c], ap("lHS", 16 * c + 15, 16 * c + 16), EQ)
+            if c == 1:
+                later(lhl)
+            lct = mm([(ap("CT", 256 + 16 * c, 320), ap("BLK8"), e, False, c == 3)])
+        scan(ap("RS", 64, 128), ap("DR1"), ap("CT", 256, 320), MAX, MIN)
         send("RB%d" % t, ap("RS"), "rep%d" % t, "lr", borrower)
-        tt(ap("RSU"), ind(ap("US", 0, 4096), ap("lHL")), ap("GR"), MUL)
+        scan(ap("lWS"), ap("DR1"), ap("CT", 256, 320), MAX, MIN)
+        ts(ap("lLO"), ap("lWS", 15, 64, 16), 4095.0, ADD)
+        if last:
+            cp(ap("RSU"), ind(ap("US"), ap("lLO")))
+        else:
+            act(ap("RSU"), ind(ap("US"), ap("lLO")), AF.Copy)
         send("RV%d" % t, ap("RSU"), "reu%d" % t, "lu", borrower)
-        tt(ap("lO1"), ap("GS", 15, 64, 16), ap("lHD"), MUL); tt(ap("lO2"), ap("lO1"), ap("D4096", 0, 4), ADD); cp(ap("lLO"), ap("lO2"))
-        cp(ind(ap("US"), ap("lLO")), ap("C255", 0, 64))
-        lend = len(ops) - 1
+        lend = cp(ind(ap("US"), ap("lLO")), ap("C255", 0, 64))
+        if not last:
+            iota(ap("US", ZD, 4480), [[0, 4480 - ZD]], 0)
+            mm([(ap("MS", 96, 97), ap("ONEB"), ap("SC", 15, 16), True, True)])
+            cp(ap("PPI"), ap("MS", 96, 97)); ts(ap("PPJ"), ap("PPI"), 63, AND); ts(ap("b16b" if t % 2 else "b16a"), ap("PPJ"), 1024.0, MUL, ap("th16"), ADD)
+        if t:
+            ts(ind(ap(cx, 0, NEW), ap("OBU")), ap("IC64"), 1.0, MUL, float(S + CAP * (t - 1)), ADD); later(lay)
+            dma(ext("yc", L * (t - 1), L * t), ap(cx, 0, 256, 1, slice(0, 128, 16)), 2.0)
         mm([(ap("JP", 0, 256), ap("BLKB"), ap("KONST"), True, False)])
         off = 0
         for c in range(16):
             lo, hi = rng[c]
-            act(ap("SG", off, off + hi - lo), ap("T5", lo, hi), AF.Sign, bias=ap("EB", c, c + 1))
-            mm([(ap("JP", lo, hi), ap("BLKB"), ap("SG", off, off + hi - lo), False, c == 15)])
+            act(ap("SG", off, off + hi - lo), ap("T5", lo, hi), AF.Sign, bias=ap("EB", c, c + 1)); later(absl)
+            mm([(ap("JP", lo, hi), ap("BLKB"), ap("SG", off, off + hi - lo), False, c == 15)]); later(ofm)
             off += (hi - lo + 15) // 16 * 16
         act(ap("RJ", 1, 257), ap("JP", 0, 256), AF.Relu, bias=254.0, scale=-0.5)
-        mm(sel("JP", 256, "RJ", 1, 16)); later(ctl); later(luv)
-        ts(ap("JW"), ap("JP", 256, 272), -1.0 / 256, MUL, 254.0, ADD); later(lx); cp(ap("JL"), ap("JW"))
-        mm([(ap("MS", 256, 512), ap("IDB"), ap("RJ", 0, 256), True, False), (ap("MS", 256, 512), ap("IDN"), ap("RJ", 1, 257), False, True)]); later(luv)
-        act(ap("FIRST"), ap("MS", 256, 512), AF.Sign)
-        tt(ap("FW"), ind(ap("WN"), ap("JL")), ap("FIRST"), MUL); later(lx)
-        mm(sel("JP", 272, "FW", 0, 16)); later(lct)
-        tt(ap("JX"), ap("JP", 272, 288), ap("JW"), ADD); cp(ap("JL2"), ap("JX"))
-        jl2 = len(ops) - 1
+        sel("JP", 256, "RJ", 1, 16)
+        ts(ap("JL"), ap("JP", 256, 272), -1.0 / 256, MUL, 254.0, ADD); act(ap("JW"), ap("JP", 256, 272), AF.Copy, bias=254.0, scale=-1.0 / 256)
+        mm([(ap("JP", 0, 256), ap("IDB"), ap("RJ", 0, 256), True, False), (ap("JP", 0, 256), ap("IDN"), ap("RJ", 1, 257), False, True)])
+        act(ap("FIRST"), ap("JP", 0, 256), AF.Sign)
+        tt(ap("FW"), ind(ap("WN"), ap("JL")), ap("FIRST"), MUL)
+        sel("JP", 272, "FW", 0, 16)
+        tt(ap("JX"), ap("JP", 272, 288), ap("JW"), ADD); jl2 = cp(ap("JL2"), ap("JX"))
         if not last:
-            act(ap(tx, 256, 512), ind(ap("TP"), ap("HL")), AF.Copy)
-            act(ap(wx, 256, 512), ind(ap("WTAB"), ap("HL")), AF.Copy)
-            act(ap(ty, 0, 256), ind(ap(tx, 0, 512), ap("JL2")), AF.Copy)
-            act(ap(wy, 0, 256), ind(ap(wx, 0, 512), ap("JL2")), AF.Copy)
-        act(ap(cy, 0, 256), ind(ap(cx, 0, 512), ap("JL2")), AF.Copy)
+            act(ap(tx, NEW, NEW + L), ind(ap("TP"), ap("HL")), AF.Copy)
+            act(ap(wx, NEW, NEW + L), ind(ap("WTAB"), ap("HL")), AF.Copy)
+            act(ap(ty, 0, 256), ind(ap(tx), ap("JL2")), AF.Copy)
+            act(ap(wy, 0, 256), ind(ap(wx), ap("JL2")), AF.Copy)
+        act(ap(cy, 0, 256), ind(ap(cx), ap("JL2")), AF.Copy)
         act(ap("EA", 0, 64), ap("PF64"), AF.Copy)
-        cp(ind(ap("EA"), ap("OF")), ap("EE", 0, 256)); later(lend); later(jl2)
-        tt(ap("EM"), ap("EA", 0, 64), ap("MWR", 0, 64), MUL); scan(ap("EQ"), ap("RST", 0, 64), ap("EM"))
-        ts(ap("FAI"), ap("EQ", 15, 64, 16), 0.2, MUL); cp(ap("FA"), ap("FAI"))
+        cp(ind(ap("EA"), ap("OF")), ap("EE", 0, 256)); later(lend)
+        scan(ap("EQ"), ap("TRH", 0, 64), ap("EA", 0, 64), MAX, MIN)
+        ts(ap("FAI"), ap("EQ", 15, 64, 16), 0.2, MUL)
         rb = "RB%d" % t
-        tt(ap("OB"), ap(rb, 64, 68), ap("FA"), ADD); cp(ap("OBU"), ap("OB"))
+        tt(ap("OB"), ap(rb, 79, 128, 16), ap("FAI"), MAX); cp(ap("OBU"), ap("OB"))
         if not last:
-            cp(ind(ap(ty), ap("OBU")), ap(rb, 0, 64)); cp(ind(ap(wy), ap("OBU")), ap("W64"))
+            cp(ind(ap(ty, 0, NEW), ap("OBU")), ap(rb, 0, 64)); cp(ind(ap(wy, 0, NEW), ap("OBU")), ap("WTAB", 0, 64))
         dma(ext("yu", S + CAP * t, S + CAP * t + CAP), ap("RV%d" % t), 2.0)
         if last:
-            ts(ind(ap(cy), ap("OBU")), ap("IC64"), 1.0, MUL, float(S + CAP * t), ADD)
+            ts(ind(ap(cy, 0, NEW), ap("OBU")), ap("IC64"), 1.0, MUL, float(S + CAP * t), ADD)
             dma(ext("yc", L * t, L * t + L), ap(cy, 0, 256, 1, slice(0, 128, 16)), 2.0)
-    dma(ext("yu", 0, S), ap("US", 0, 4096), 6.0)
+    dma(ext("yu", 0, S), ap("US", 0, S), 6.0)
     return ops
 
 
-def order(ops, noise=None):
+_MEMO = {}
+
+
+def order(ops, memo=None):
+    memo = {} if memo is None else memo
     last = {}
     for i, o in enumerate(ops):
         pre = {}
@@ -553,16 +611,14 @@ def order(ops, noise=None):
                         continue
                     if hi <= lo2 or hi2 <= lo or (st == st2 and st > 1 and (lo - lo2) % st):
                         continue
-                    add(j, True)
+                    add(j, not (INORDER and same and o["q"] in "VS" and kind == "W"))
         for kind in ("R", "W"):
             for nm, lo, hi, st in o[kind]:
                 ps = nm in _PS
                 lst = last.setdefault(nm, [])
                 if ps:
                     if lst and ops[lst[-1][0]]["q"] != o["q"]:
-                        keep = []
-                        other = [e for e in lst if ops[e[0]]["q"] != o["q"]]
-                        lst[:] = other[-40:]
+                        lst[:] = [e for e in lst if ops[e[0]]["q"] != o["q"]][-40:]
                 elif kind == "W" and st == 1:
                     lst[:] = [e for e in lst if not (lo <= e[2] and e[3] <= hi) or e[0] == i]
                 lst.append((i, kind, lo, hi, st))
@@ -572,57 +628,118 @@ def order(ops, noise=None):
     for i, o in enumerate(ops):
         for j in o["pre"]:
             succ[j].append(i)
+
+    def lag(j, k):
+        if ops[k]["pre"][j]:
+            return OWN if ops[k]["q"] == ops[j]["q"] else HOP
+        return ISSUE - ops[j]["c"] if ops[j]["q"] == "Y" else 0.0
+    pres = [[(j, lag(j, i)) for j in ops[i]["pre"]] for i in range(n)]
+    posts = [[(k, lag(i, k)) for k in succ[i]] for i in range(n)]
+
+    def place(key, back, n=n):
+        before, after = (posts, pres) if back else (pres, posts)
+        left = [len(x) for x in before]
+        ready = sorted((key[i], i) for i in range(n) if not left[i])
+        beg, end, busy = [0.0] * n, [0.0] * n, {}
+        while ready:
+            i = ready.pop(0)[1]
+            q, c, t = ops[i]["q"], ops[i]["c"], 0.0
+            for j, d in before[i]:
+                if end[j] + d > t:
+                    t = end[j] + d
+            if q != "N":
+                hold = ISSUE if q == "Y" else c
+                skip = c - hold if back else 0.0
+                lst = busy.setdefault(q, [])
+                p = len(lst)
+                while p and lst[p - 1][1] > t + skip:
+                    p -= 1
+                while p < len(lst) and lst[p][0] < t + skip + hold - 1e-9:
+                    t = max(t, lst[p][1] - skip); p += 1
+                lst.insert(p, (t + skip, t + skip + hold))
+            beg[i], end[i] = t, t + c
+            for k, d in after[i]:
+                left[k] -= 1
+                if not left[k] and k < n:
+                    ready.append((key[k], k)); ready.sort()
+        return beg, end
     pri = [0.0] * n
     for i in range(n - 1, -1, -1):
-        pri[i] = ops[i]["c"] + max([pri[k] + HOP for k in succ[i]], default=0.0)
-    if noise is not None:
-        pri = [pri[i] + noise[ops[i]["k"]] for i in range(n)]
-    left = [len(o["pre"]) for o in ops]
-    ready = {}
-    est = [0.0] * n
-    fin = [0.0] * n
-    free = {}
+        pri[i] = ops[i]["c"] + max([pri[k] + d for k, d in posts[i]], default=0.0)
+    beg, end = place([-x for x in pri], False)
+    best = (max(end), [max(pri) - x for x in pri])
+    for _ in range(PASSES):
+        beg, end = place([-x for x in end], True)
+        late = [max(end) - x for x in end]
+        beg, end = place(late, False)
+        best = min(best, (max(end), late))
+    base = best[1]
+    part = [i for i in range(n) if ops[i]["k"] == 0][3]
+    name, seen = [], {}
+    for o in ops:
+        if o["k"] == 0:
+            seen = {}
+        w = (o["k"] < 0, o["q"], o["W"][0][0].rstrip("0123456789ab") if o["W"] else "")
+        seen[w] = seen.get(w, 0) + 1
+        name.append(w + (seen[w],))
+    names = sorted(set(w for w in name if not w[0]))
+    first = [i for i in range(n) if ops[i]["k"] == 0] + [n]
+    mid = {name[i]: base[i] - base[first[2] + 1] for i in range(first[2], first[3])}
+    for r in range(RO):
+        zero = base[first[r] + 1]
+        for i in range(first[r], first[r + 1]):
+            base[i] = zero + mid[name[i]] if name[i] in mid else base[i - 1]
+    guess = []
+    for cy, ga, sct, hop, own, flight, sfix in GUESSES:
+        c = [a + cy * (b + ga * g + sct * s) + sfix * (o["q"] == "S") + flight * (o["q"] == "N") for o in ops for a, b, g, s in [o["v"]]]
+        guess.append((c, [[(j, 0.0 if not w else own if ops[j]["q"] == o["q"] else hop) for j, w in o["pre"].items() if w or o["q"] == "N"] for o in ops]))
+
+    def keys(shift, n):
+        key = [base[i] + shift.get(name[i], 0.0) for i in range(n)]
+        for i in range(first[0] - 1, -1, -1):
+            key[i] = min([key[k] - d for k, d in posts[i] if k < n], default=first[0]) - ops[i]["c"] + shift.get(name[i], 0.0)
+        return key
+
+    def length(shift):
+        beg, end = place(keys(shift, part), False, part)
+        seq, total, held = sorted(range(part), key=lambda i: (beg[i], i)), 0.0, set()
+        for c, pre in guess:
+            free, why = {}, [-1] * part
+            for i in seq:
+                q = ops[i]["q"]
+                t, why[i] = free.get(q, (0.0, -1))
+                for j, d in pre[i]:
+                    if end[j] + d > t:
+                        t, why[i] = end[j] + d, j
+                end[i] = t + c[i]
+                if q != "N":
+                    free[q] = (t + (ISSUE if q == "Y" else c[i]), i)
+            total += max(end)
+            i = end.index(max(end))
+            while why[i] >= 0:
+                if why[i] not in ops[i]["pre"]:
+                    held.add((i, why[i]))
+                i = why[i]
+        return total, sorted(held)
+    rnd = np.random.RandomState(SEED)
+    shift = memo.get("shift", {})
+    cur, held = length(shift)
+    for _ in range(0 if memo else TRIES):
+        new = dict(shift)
+        for _ in range(1 + int(rnd.randint(2))):
+            w, d = names[int(rnd.randint(len(names)))], float(rnd.normal()) * (0.3, 1.0, 3.0)[int(rnd.randint(3))]
+            if held and rnd.randint(3):
+                i, j = held[int(rnd.randint(len(held)))]
+                w, d = (name[i], -abs(d)) if rnd.randint(2) else (name[j], abs(d))
+            new[w] = new.get(w, 0.0) + d
+        x, h = length(new)
+        if x <= cur:
+            cur, held, shift = x, h, new
+    memo["shift"] = shift
+    beg, end = place(keys(shift, n), False)
     for i in range(n):
-        if left[i] == 0:
-            ready.setdefault(ops[i]["q"], []).append(i)
-    seq = []
-    while len(seq) < n:
-        best = None
-        for q, lst in ready.items():
-            if not lst:
-                continue
-            f = 0.0 if q == "N" else free.get(q, 0.0)
-            m = min(max(f, est[i]) for i in lst)
-            c = [i for i in lst if max(f, est[i]) <= m + 0.03]
-            b = max(c, key=lambda i: pri[i])
-            tm = max(f, est[b])
-            h = max((i for i in lst if est[i] <= tm + AHEAD), key=lambda i: pri[i]) if AHEAD else b
-            if pri[h] > pri[b] + 0.5 and est[h] > tm and tm + ops[b]["c"] > est[h] + 0.02 and q != "N":
-                c = [i for i in lst if max(f, est[i]) + ops[i]["c"] <= est[h] + 0.02]
-                b = max(c, key=lambda i: pri[i]) if c else h
-                tm = max(f, est[b])
-            if best is None or tm < best[0]:
-                best = (tm, q, b)
-        tm, q, b = best
-        ready[q].remove(b)
-        o = ops[b]
-        o["t"] = tm
-        if q == "Y":
-            free[q] = tm + 0.1
-            fin[b] = tm + o["c"]
-        elif q == "N":
-            fin[b] = tm + o["c"]
-        else:
-            free[q] = tm + o["c"]
-            fin[b] = tm + o["c"]
-        seq.append(b)
-        for k in succ[b]:
-            left[k] -= 1
-            hop = (OWN if ops[k]["q"] == q else HOP) if ops[k]["pre"][b] else 0.0
-            est[k] = max(est[k], tm if ops[k]["q"] == q and not ops[k]["pre"][b] else fin[b] + hop)
-            if left[k] == 0:
-                ready.setdefault(ops[k]["q"], []).append(k)
-    return seq, max(fin)
+        ops[i]["t"] = beg[i]
+    return sorted(range(n), key=lambda i: (beg[i], i)), max(end)
 
 
 def rank_program(g, core, T, topo):
@@ -630,7 +747,7 @@ def rank_program(g, core, T, topo):
     if rank is None:
         return
     ops = build(rank, core, T, topo)
-    seq, _ = order(ops)
+    seq, _ = order(ops, _MEMO)
     eng = {"V": g.vector, "S": g.scalar, "P": g.tensor, "G": g, "Y": g.sync}
     total = {}
     known = {q: {} for q in eng}

@@ -25,7 +25,7 @@ for _n in ("pF", "sF", "gF", "s2F", "sge8", "slt8", "pm8", "gx8", "g8p", "nsB", 
     _b(_n, 1, F)
 _b("g16", 16, F); _b("g8", 4, F); _b("g8m", 4, F); _b("pen2", 2, F); _b("pen4", 4, F)
 _b("MWR", 256, F); _b("RST", 256, F); _b("BLKH", 128, H); _b("BLKB", 128, BF); _b("BLKN", 128, BF); _b("ONEB", 128, BF)
-_b("IDH", 128, H); _b("IDB", 128, BF); _b("IDN", 128, BF); _b("IDHN", 128, H)
+_b("IDH", 128, H); _b("IDB", 128, BF); _b("IDN", 128, BF); _b("I256", 128, BF); _b("IDHN", 128, H)
 _b("TRIMB", 128, BF); _b("PL", 128, BF); _b("PR", 128, BF); _b("PH", 128, H); _b("SEL", 2048, BF); _b("REP8", 128, H, 8)
 _b("WT", 24 * 128, H); _b("PZ4", 128, BF); _b("RS4", 128, F); _b("RS16", 64, F)
 _b("C255", 128, BF); _b("T5", 256, F); _b("KONST", 256, BF); _b("one16", 16, F); _b("oneR", 256, BF); _b("JW0", 16, F)
@@ -40,11 +40,11 @@ _b("HV", 256, I, inner=16); _b("HF", 256, F, inner=16); _b("HI", 256, I); _b("HO
 _b("X", 4096, BF); _b("A", 4096, BF); _b("RM", 512, F); _b("RI", 320, F); _b("KS", 64, I)
 _b("PO", 16, F); _b("PN", 16, BF); _b("SC", 16, BF); _b("POJ", 16, H); _b("OF", 16, U16); _b("ZA", 768, BF)
 _b("PPI", 1, I); _b("PPJ", 1, I); _b("MI", 16, I); _b("LL", 16, U16)
-_b("HM", 256, H); _b("HS", 256, F); _b("HD", 16, F); _b("LA", 16, F); _b("UR", 256, BF); _b("W2", 128, BF); _b("B30", 128, BF); _b("NM2", 128, BF); _b("P2", 48, F); _b("HRH", 256, H); _b("HL", 16, U16)
+_b("HM", 256, H); _b("HS", 256, F); _b("HD", 16, F); _b("LA", 16, F); _b("UR", 256, BF); _b("EX", 1024, BF); _b("W2", 128, BF); _b("B30", 128, BF); _b("NM2", 128, BF); _b("P2", 48, F); _b("HRH", 256, H); _b("HL", 16, U16)
 _b("ET", 24 * 128, BF, inner=128); _b("WD", 256, BF); _b("WN", 256, BF); _b("WS", 256, F); _b("LO", 16, U16)
 _b("EE", 512, H); _b("FI", 32, I); _b("FB", 32, F); _b("FC", 32, F); _b("NW", 16, F); _b("UN0", 16, F)
 _b("EB", 16, F); _b("SG", 4096, BF); _b("RJ", 272, BF); _b("FIRST", 256, BF); _b("JW", 16, F); _b("JL", 16, U16); _b("FW", 256, BF); _b("JX", 16, F); _b("JL2", 16, U16)
-_b("EA", 768, F); _b("EM", 64, F); _b("EQ", 64, F); _b("FAI", 4, I); _b("FA", 4, F); _b("OB", 4, F); _b("OBU", 4, U16)
+_b("EA", 768, F); _b("E32", 256, F); _b("EM", 64, F); _b("EQ", 64, F); _b("FAI", 4, I); _b("FA", 4, F); _b("OB", 4, F); _b("OBU", 4, U16)
 for _k in range(RO):
     _b("ZL%d" % _k, 64, BF); _b("RB%d" % _k, 128, BF); _b("RV%d" % _k, 64, BF)
 _b("ZT", 512, BF); _b("lUVS", 64, I); _b("lUVA", 64, I); _b("lUVW", 32, I); _b("lUQ", 32, I); _b("lKU", 64, F)
@@ -75,16 +75,24 @@ for _n in _PS:
 ND = 32
 SEMAPHORES = ["sV", "sS", "sP", "sG", "la", "lr", "lu"] + ["reu%d" % k for k in range(RO)] + ["ask%d" % k for k in range(RO)] + ["rep%d" % k for k in range(RO)] + ["d%d" % k for k in range(ND)]
 
-NS = 4
-BYS = {2: "CT", 3: "CT", 7: "ZP"}
-PROBE = [("gather", 0, 2), ("gather", 2, 2), ("abs", 0, 2), ("gather", 4, 2), ("gather", 7, 1), ("abs", 2, 2), ("gather", 6, 1), ("abs", 4, 2),
-         ("gather", 8, 2), ("abs", 7, 1), ("abs", 6, 1), ("least", 0, 0), ("gather", 10, 2), ("abs", 8, 2), ("least", 1, 0), ("gather", 12, 2),
-         ("abs", 10, 2), ("least", 2, 0), ("gather", 14, 1), ("abs", 12, 2), ("least", 3, 0), ("gather", 15, 1), ("abs", 14, 1), ("abs", 15, 1),
-         ("least", 4, 0), ("slots", 0, 0), ("least", 5, 0), ("slots", 2, 0), ("slots", 1, 0), ("least", 6, 0), ("slots", 3, 0)]
+NS = 5
+BYS = {2: "CT", 3: "CT", 4: "ZP", 5: "ZP"}
+PROBE = [("gather", 0, 2), ("gather", 2, 2), ("gather", 4, 2), ("gather", 6, 2), ("abs", 0, 2), ("abs", 2, 2), ("gather", 8, 2), ("abs", 4, 2),
+         ("gather", 10, 2), ("abs", 6, 2), ("abs", 8, 2), ("least", 0, 2), ("gather", 12, 2), ("abs", 10, 2), ("gather", 14, 1), ("abs", 12, 2),
+         ("least", 1, 2), ("gather", 15, 1), ("abs", 14, 1), ("abs", 15, 1), ("slots", 0, 0), ("slots", 2, 0), ("least", 2, 2), ("slots", 3, 0),
+         ("slots", 1, 0), ("least", 3, 1)]
 PAIRS, LAST = 7, 1
 PARTS = 2
 ZBF = 1
 INORDER = 0
+EAS = 1
+ABSW = 512
+EARLY = 6
+CLATE = 2
+LB = 256
+LORD = ((0, 256), (256, 512), (768, 1024), (512, 768))
+SE = 2
+SX = 3
 BEHIND, INIAT = 4, 16
 PASSES = 6
 GSEL = 10
@@ -93,9 +101,10 @@ JA = 8
 CY = 0.00114
 GA, SCT = 1.56, 3.8
 HOP, OWN, ISSUE = 0.11, 0.055, 0.1
-FLIGHT, SEND, SFIX = 3.1, 1.0, 0.09
-GUESSES = ((CY, GA, SCT, HOP, OWN, FLIGHT, SFIX), (0.00105, 1.3, 3.0, 0.15, 0.07, 3.6, 0.12), (0.00125, 1.9, 5.5, 0.13, 0.06, 3.0, 0.09))
-TRIES, SEED = 5500, 1
+FLIGHT, SEND, SFIX = 2.6, 1.0, 0.03
+GUESSES = ((CY, GA, SCT, HOP, OWN, FLIGHT, SFIX), (0.001, 1.15, 2.0, 0.13, 0.07, 3.0, 0.03), (0.00125, 1.9, 5.5, 0.13, 0.06, 3.3, 0.03),
+           (0.0011, 1.4, 3.0, 0.12, 0.06, 1.5, 0.05))
+TRIES, SEED = 5000, 1
 
 
 def build(rank, core, T, topo):
@@ -199,8 +208,10 @@ def build(rank, core, T, topo):
 
     def act(o, a, func, bias=0.0, scale=1.0):
         rd = [a] + [x for x in (bias, scale) if isinstance(x, tuple)]
+        if o[0] == "i":
+            return put("S", lambda g: g.scalar.activation(res(o), res(a), func), rd, [o], (0.0, 0, 0, n_of(o)))
         return put("S", lambda g: g.scalar.activation(res(o), res(a), func, bias=sc(bias), scale=sc(scale)), rd, [o],
-                   (0.0, 0, n_of(o), 0) if a[0] == "i" else (0.0, n_of(o), 0, 0))
+                   (0.05, 0, n_of(o), 0) if a[0] == "i" else (0.0, max(64, n_of(o)), 0, 0))
 
     def mm(lst):
         def fn(g):
@@ -220,9 +231,9 @@ def build(rank, core, T, topo):
 
     nd = [0]
 
-    def dma(o, a, cost):
+    def dma(o, a, cost, q="Y"):
         k = "d%d" % nd[0]; nd[0] += 1
-        return put("Y", lambda g: g.sync.dma_start(res(o) if isinstance(o, tuple) else o, res(a) if isinstance(a, tuple) else a),
+        return put(q, lambda g: (g.sync if q == "Y" else g.scalar).dma_start(res(o) if isinstance(o, tuple) else o, res(a) if isinstance(a, tuple) else a),
                    [a] if isinstance(a, tuple) else [], [o] if isinstance(o, tuple) else [], cost, sem=k, inc=16)
 
     def send(o, a, sem, loc, dst):
@@ -230,7 +241,7 @@ def build(rank, core, T, topo):
         m = 0
         for e in topo.engines(core, dst)[:8]:
             m |= 1 << e
-        k = put("G", lambda g: g.remote_dma(T[o][:, :], res(a), T.sem[sem], T.sem[loc], pid, rid, m), [a], [], SEND, sem=loc, inc=0)
+        k = put("G", lambda g: g.remote_dma(T[o][:, a[2]:a[3]], res(a), T.sem[sem], T.sem[loc], pid, rid, m), [a], [], SEND, sem=loc, inc=0)
         ops[-1]["n"] = len(topo.engines(core, dst)[:8])
         put("N", None, [], [ap(o)], 0.0, sem=sem, inc=8)
         ops[-1]["after"] = [k]
@@ -288,10 +299,10 @@ def build(rank, core, T, topo):
         keep(ap("RL", 128 * r, 128 * r + 128), "ONEB", [[16, 8], [0, 8], [8, 2]], r, EQ, -1)
     ts(ap("s1I"), ap("sI"), 1, SHR); cp(ap("s1F"), ap("s1I"))
     act(ap("PZL"), ap("CZ"), AF.Abs, bias=ap("ns2"), scale=8 * BIG); act(ap("PZL"), ap("PZL"), AF.Identity, bias=ap("s1F"))
-    fill(ap("RS32"), 0.0); ts(ap("RS32", 0, 64, 32), ap("IC", 0, 2), 0.0, MUL, 8 * BIG, ADD)
     ts(ap("CJ"), ap("IC", 0, 64, 2), ap("sge8"), ADD)
     for o, v in (("IDB", 1.0), ("IDH", 1.0), ("IDN", -1.0), ("IDHN", -1.0)):
         ts(ap(o), ap("IC", 0, 128), ap("pF"), EQ, v, MUL)
+    act(ap("I256"), ap("IDB"), AF.Copy, scale=-256.0)
     act(ap("NM"), ap("CS"), AF.Abs, bias=ap("nsB"), scale=BIG)
     act(ap("PZ4"), ap("C3"), AF.Abs, bias=ap("ns2"), scale=8 * BIG); act(ap("RS4"), ap("C3"), AF.Relu, bias=8 * BIG, scale=-8 * BIG)
     act(ap("MWR"), ap("NM"), AF.Relu, bias=1.0, scale=-1.0); act(ap("RST"), ap("CS"), AF.Sign)
@@ -314,7 +325,7 @@ def build(rank, core, T, topo):
     act(ap("CX0", 0, 256), ap("HR", 0, 256), AF.Copy, bias=2048.0)
     for k in "01":
         fill(ap("TX" + k, L, NEW), 0.0); fill(ap("WX" + k, L, NEW), 0.0); act(ap("CX" + k, L, NEW), ap("IC", 0, NEW - L), AF.Copy)
-    act(ap("TX0", 0, 256), ind(ap("TP"), ap("CL0")), AF.Copy)
+    act(ap("TX0", 0, 128), ind(ap("TP"), ap("CL0", 0, 8)), AF.Copy); cp(ap("TX0", 128, 256), ind(ap("TP"), ap("CL0", 8, 16)))
 
     for r in range(8):
         keep(ap("SLP", 128 * r, 128 * r + 128), "B512", [[0, 16], [1, 8]], -r)
@@ -327,9 +338,10 @@ def build(rank, core, T, topo):
     for r in range(4):
         keep(ap("SLQ", 128 * r, 128 * r + 128), "B512", [[0, 32], [1, 4]], -r)
     keep(ap("TRIMB"), "BLKN", [[-1, 128]], 0, GE, 1)
-    iota(ap("WTAB", 0, 512), [[0, 128], [1, 4]], 4)
+    for k in range(4):
+        act(ap("WTAB", 128 * k, 128 * k + 128), ap("C3"), AF.Copy, bias=4.0)
     for k in range(1, 8):
-        dma(ap("WTAB", 512 * k, 512 * k + 512), ap("WTAB", 0, 512), 7.0); later(ldu)
+        wtab = dma(ap("WTAB", 512 * k, 512 * k + 512), ap("WTAB", 0, 512), 7.0); later(ldu, len(ops) - 2)
     ts(ap("c8i"), ap("c8"), 3, AND); ts(ap("c8w"), ap("c8i"), 4.0, ADD)
     mm([(ap("DB", 0, 256), ap("REP8"), ap("c8w"), True, True)])
     act(ap("WX0", 0, 256), ap("DB", 0, 256), AF.Copy)
@@ -361,13 +373,13 @@ def build(rank, core, T, topo):
     mm([(ap("JP", 0, 256), ap("IDB"), ap("kz1"), True, False), (ap("JP", 0, 256), ap("IDB"), ap("kz2"), False, True)])
     act(ap("KONST"), ap("JP", 0, 256), AF.Copy, bias=-288.0)
     fill(ap("RJ", 0, 16), 300.0)
-    cp(ap("IC64"), ap("IC", 0, 64)); ts(ap("PF64"), ap("IC", 0, 64), 5.0, MUL, 1280.0, ADD)
+    cp(ap("IC64"), ap("IC", 0, 64)); ts(ap("PF64"), ap("IC", 0, 64), 5.0, MUL, 1344.0, ADD)
     act(ap("HT", 256, 512), ap("IC"), AF.Copy); fill(ap("HT", 512, 528), UNF); fill(ap("lHT", 512, 528), UNF)
     fill(ap("RI", 0, 64), 8 * BIG); fill(ap("US", S, 4480), 0.0)
 
     def sel(bank, o, name, lo, n):
-        for k in range(0, 16, 4):
-            mm([(ap(bank, o, o + n), ap("SEL", 128 * s, 128 * s + 128), ap(name, lo + s, lo + s + 16 * (n - 1) + 1, 16), s == 0, s == 15) for s in range(k, k + 4)])
+        for k in range(0, 16, 2):
+            mm([(ap(bank, o, o + n), ap("SEL", 128 * s, 128 * s + 128), ap(name, lo + s, lo + s + 16 * (n - 1) + 1, 16), s == 0, s == 15) for s in range(k, k + 2)])
 
     for t in range(RO):
         start[0] = len(ops)
@@ -386,7 +398,7 @@ def build(rank, core, T, topo):
         mm(lst)
         mm([(ap("ZP", 0, 256), ap("PL"), ap(tx, 0, 256), True, False), (ap("ZP", 0, 256), ap("PR"), ap(tx, 1, 257), False, True)])
         zb = [act(ap("ZB", 256 * k, 256 * k + 256), ap("ZP", 0, 256), AF.Copy) for k in range(2)]
-        scan(ap("UVS"), ap("RS4"), ap("UVP", 0, 128), ADD, MIN)
+        scan(ap("UVS"), ap("RS4"), ap("UVP", 0, 128), ADD, MIN); later(wtab)
         ts(ap("UVA"), ap("UVS", 3, 128, 4), 4095, AND)
         tt(ap("UVW"), ap("UVA", 0, 16), ap("UVA", 16, 32), MUL)
         ts(ap("UVA", 16, 32), ap("UVW"), 5, SHR)
@@ -397,15 +409,15 @@ def build(rank, core, T, topo):
             else:
                 ts(ap3("HV", 0, 16, c), ap("KR"), ap("UQ", c, c + 1), MUL, ap("UQ", 16 + c, 17 + c), ADD)
         cp(ap3("HV", 0, 16, 16 - NS, 16), ap3("HF", 0, 16, 16 - NS, 16))
-        for a, b in ((0, 4), (4, 16)):
+        for a, b in ((0, EARLY), (EARLY, 16)):
             ts(ap("HI", 16 * a, 16 * b), ap3("HV", a, b, 0, 16), 4095, AND)
             cp(ap("HO", 16 * a, 16 * b), ap("HI", 16 * a, 16 * b))
         scan(ap("EE", 256, 510), ap("oneR", 0, 254), ap(wx, 0, 254)); cp(ap("EE", 1, 256), ap("EE", 256, 511))
         sel("MS", 32, "EE", 0, 32)
-        slots = [lambda: ts(ap("FI"), ap("MS", 32, 64), 0.2 / 256, MUL, 256.0, MIN), lambda: ts(ap("EB"), ap("MS", 48, 64), -1.0 / 256, MUL, 0.5, ADD),
+        slots = [lambda: ts(ap("FI"), ap("MS", 32, 64), 0.2 / 256, MUL, 256.0, MIN), lambda: act(ap("EB"), ap("MS", 48, 64), AF.Copy, bias=0.5, scale=-1.0 / 256),
                  lambda: tt(ap("NW"), ap("FI", 16, 32), ap("FI", 0, 16), SUB),
-                 lambda: ts(ap("RI", 1, 64, 4), ap("NW"), 4 * BIG, MUL, 512.0 - 2 * BIG, ADD)]
-        banks = ("DA", "DB", "JP", "HR", "UVP")
+                 lambda: act(ap("RI", 1, 64, 4), ap("NW"), AF.Copy, bias=512.0 - 2 * BIG, scale=4 * BIG)]
+        banks = ("DA", "DB", "JP", "HR", "UVP", "CT", "ZP")
         prev = {}
         for step, m, k in PROBE:
             x, d = ap("X", 256 * m, 256 * (m + k)), ap(BYS.get(m, "ZP"), 512 - 256 * k, 512)
@@ -415,41 +427,54 @@ def build(rank, core, T, topo):
             elif step == "gather":
                 j = tt(x, ind(ap("US", 0, S), ap("HO", 16 * m, 16 * (m + k))), ap("ZB", 0, 256 * k), SUB)
             elif step == "abs":
-                j = absl = act(ap("A", 256 * m, 256 * (m + k)), d if m in BYS else x, AF.Abs)
+                w = min(ABSW, 256 * k)
+                for lo in range(0, 256 * k, w):
+                    y = d if m in BYS else x
+                    j = absl = act(ap("A", 256 * m + lo, 256 * m + lo + w), ap(y[1], y[2] + lo, y[2] + lo + w), AF.Abs)
+                    if lo + w < 256 * k:
+                        later(prev["S"]); prev["S"] = j
             elif step == "slots":
                 j = slots[m]()
             else:
-                d = ap(banks[m % 5], 0, 64)
-                mm([(d, ap("IDB"), ap("MP", 64 * m, 64 * m + 64), True, False)])
-                mm([(d, ap("SLP", 128 * r, 128 * r + 128), ap("A", 512 * m + r, 512 * m + 512, 8), False, r == 7) for r in range(8)])
+                mm([(ap(banks[m], 0, 64 * k), ap("IDB"), ap("MP", 128 * m, 128 * m + 64 * k), True, False)])
+                for h in range(k):
+                    lo = 1024 * m + 512 * h
+                    mm([(ap(banks[m], 64 * h, 64 * h + 64), ap("SLP", 128 * r, 128 * r + 128), ap("A", lo + r, lo + 512, 8), False, h == k - 1 and r == 7) for r in range(8)])
                 if m == 0:
-                    j = ts(ap("RM", 0, 64), d, b16, MIN)
+                    j = ts(ap("RM", 0, 128), ap(banks[m], 0, 128), b16, MIN)
+                elif k == 2:
+                    j = tt(ap("RM", 128 * m, 128 * m + 128), ap(banks[m], 0, 128), ap("RM", 128 * m - 128, 128 * m), MIN)
                 else:
-                    j = tt(ap("RM", 64 * m, 64 * m + 64), d, ap("RM", 64 * m - 64, 64 * m), MIN)
+                    later_v = tt(ap("RM", 448, 512), ap("RM", 256, 320), ap("RM", 320, 384), MIN); later(prev["V"]); prev["V"] = later_v
+                    j = tt(ap("RM", 384, 448), ap(banks[m], 0, 64), ap("RM", 448, 512), MIN)
             if ops[j]["q"] in prev:
                 ops[j].setdefault("after", []).append(prev[ops[j]["q"]])
             prev[ops[j]["q"]] = j
+        if PAIRS == 6:
+            tt(ap("RM", 384, 448), ap("RM", 256, 320), ap("RM", 320, 384), MIN)
         for k in range(2):
-            lo = 64 * PAIRS - 64 + 32 * k
+            lo = 384 + 32 * k
             tt(ap("RI", 2 + k, 64, 4), ap("RM", lo, lo + 31, 2), ap("RM", lo + 1, lo + 32, 2), MIN)
         for n in range(16 - 2 * PAIRS):
             m = 2 * PAIRS + n
-            d = banks[(PAIRS + n) % 5]
+            d = banks[PAIRS - 3 + n]
             mm([(ap(d, 0, 64), ap("IDB"), ap("MS1", 64 * (m - 12), 64 * (m - 11)), True, False)])
             mm([(ap(d, 0, 64), ap("SLQ", 128 * r, 128 * r + 128), ap("A", 256 * m + r, 256 * m + 256, 4), False, r == 3) for r in range(4)])
             tt(ap("RI", 64 * n + 64, 64 * n + 128), ap(d, 0, 64), ap("RI", 64 * n, 64 * n + 64), MIN)
         scan(ap("KS"), ap("RS4", 0, 64), ap("RI", 64 * n + 64, 64 * n + 128), ADD, MIN)
         key = ap("KS", 3, 64, 4)
-        ts(ap("HT", 0, 256), ap("HI"), -2047.0, ADD)
         iota(ap("ZA", 0, 64), [[0, 64]], 1024)
         mm([(ap("MS", 64, 80), ap("IDH"), ap("J256"), True, False)])
-        ts(ap("PO"), key, b16, GE); tt(ap("PN"), ap("PO"), ap("NW"), MUL); tt(ap("POJ"), ap("PO"), ap("J256"), MUL); scan(ap("SC"), ap("one16"), ap("PN"))
+        ts(ap("PO"), key, b16, GE); tt(ap("PN"), ap("PO"), ap("NW"), MUL); tt(ap("POJ"), ap("PO"), ap("J256"), MUL)
+        scn = scan(ap("SC"), ap("one16"), ap("PN"))
+        ts(ap("HT", 0, 256), ap("HI"), -2047.0, ADD); later(scn)
         mm([(ap("MS", 64, 80), ap("TRIMB"), ap("PN"), False, False), (ap("MS", 64, 80), ap("IDHN"), ap("POJ"), False, False)])
         ofm = mm([(ap("MS", 64, 80), ap("BLKB"), ap("SC"), False, True)])
+        ts(ap("MI"), key, 1023, AND)
         cp(ap("OF"), ap("MS", 64, 80))
-        cp(ind(ap("ZA"), ap("OF")), ap("ZB", 0, 256))
+        cp(ap("LL"), ap("MI")); later(len(ops) - 2)
+        cp(ind(ap("ZA"), ap("OF")), ap("ZB", 0, 256)); later(len(ops) - 2)
         send("ZL%d" % t, ap("ZA", 0, 64), "ask%d" % t, "la", lender)
-        ts(ap("MI"), key, 1023, AND); cp(ap("LL"), ap("MI"))
         tt(ap("HM"), ind(ap("HT"), ap("LL")), ap("MWR"), MUL)
         scan(ap("HS"), ap("RST"), ap("HM"))
         mm([(ap("HR", 0, 256), ap("BLKH"), ap("HM"), True, True)])
@@ -457,10 +482,23 @@ def build(rank, core, T, topo):
         hsx = act(ap(cx, NEW, NEW + L), ap("HR", 0, 256), AF.Copy, bias=2047.0)
         act(ap("UR"), ap("HR", 0, 256), AF.Relu, bias=-3000.0)
         tt(ap("HD"), ap("HS", 15, 256, 16), ap("DRS", 0, 256, 16), MIN)
+
+        made = []
+
+        def equal(k, lo, hi, c, scalar):
+            e, own = ap3("ET", k, k + 1, 0, hi - lo), ap("HS", 16 * c + 15, 16 * c + 16)
+            if scalar:
+                x = ap("EX", 128 * (k % 8), 128 * (k % 8) + hi - lo)
+                act(x, ap("HR", lo, hi), AF.Abs, bias=own, scale=-1.0)
+                if k >= 16:
+                    later(*made)
+                made.append(act(e, x, AF.Relu, bias=1.0, scale=-1.0))
+            else:
+                ts(e, ap("HRH", lo, hi), own, EQ)
         for h, d in enumerate(("CT", "DB")):
             mm([(ap(d, 256, 384), ap("IDB"), ap("NM2", 0, 128), True, False)])
             for c in range(8):
-                ts(ap3("ET", 8 * h + c, 8 * h + c + 1, 0, 128 - 16 * c), ap("HRH", 128 * h + 16 * c, 128 * h + 128), ap("HS", 128 * h + 16 * c + 15, 128 * h + 16 * c + 16), EQ)
+                equal(8 * h + c, 128 * h + 16 * c, 128 * h + 128, 8 * h + c, 16 - 2 * c - h <= SE)
                 if c < 7:
                     mm([(ap(d, 272 + 16 * c, 384), ap("B30"), ap3("ET", 8 * h + c, 8 * h + c + 1, 16, 128 - 16 * c), False, False)])
             ctl = mm([(ap(d, 256, 384), ap("W2"), ap3("ET", 8 * h, 8 * h + 8, 0, 16), False, True)])
@@ -469,82 +507,10 @@ def build(rank, core, T, topo):
             ts(ap("LO", 8 * h, 8 * h + 8), ap("LA", 8 * h, 8 * h + 8), 2047.0, ADD)
             lay = cp(ind(ap("US", 0, ZD), ap("LO", 8 * h, 8 * h + 8)), ap("C255", 0, 128))
             act(ap("WD", 128 * h, 128 * h + 128), ap(d, 256, 384), AF.Sign)
-        ts(ap("HL"), ap("HS", 15, 256, 16), 2047.0, ADD, 4095.0, MIN)
-        mm([(ap("MS", 256, 512), ap("IDB"), ap("UR"), True, False)]); mm([(ap("MS", 256, 512), ap("BLKB"), ap("WD"), False, False)])
-        for c in range(8):
-            ts(ap3("ET", 16 + c, 17 + c, 0, 128), ap("HRH", 128, 256), ap("HS", 16 * c + 15, 16 * c + 16), EQ); later(lay)
-            mm([(ap("MS", 384, 512), ap("BLK8"), ap3("ET", 16 + c, 17 + c, 0, 128), False, c == 7)])
-        act(ap("WN"), ap("MS", 256, 512), AF.Relu, bias=NEW / 32, scale=-NEW / 512)
-        zl = "ZL%d" % t
-        mm([(ap("UVP", 128 + 32 * qv, 160 + 32 * qv), wt(2, qv, i), ap(zl, i, i + 63, 2), i == 0, i == 1) for qv in (0, 1) for i in (0, 1)])
-        for k in range(2):
-            act(ap("ZT", 256 * k, 256 * k + 256), ind(ap(zl), ap("CJ", 16 * k, 16 * k + 16)), AF.Copy)
-        cp(ap("lUVS"), ap("UVP", 128, 192))
-        ts(ap("lUVA"), ap("lUVS"), 4095, AND)
-        tt(ap("lUVW"), ap("lUVA", 0, 32), ap("lUVA", 32, 64), MUL)
-        for k in range(2):
-            ts(ap("lKU", 32 * k, 32 * k + 32), ap("lUVA", 0, 32), ap("kc", k, k + 1), MUL)
-        ts(ap("lUQ"), ap("lUVW"), 5, SHR)
-        for k in range(2):
-            tt(ap("lHV", 32 * k, 32 * k + 32), ap("lKU", 32 * k, 32 * k + 32), ap("lUQ"), ADD)
-        ts(ap("lHI"), ap("lHV"), 4095, AND); cp(ap("lHO"), ap("lHI"))
-        act(ap("lX", 768, 896), ind(ap("US", 0, S), ap("lHO", 48, 56)), AF.Copy)
-        mm([(ap("ZP", 256, 384), ap("IDN"), ap("ZT", 256, 384), True, False)]); mm([(ap("ZP", 256, 384), ap("IDB"), ap("lX", 768, 896), False, True)])
-        for n in range(4):
-            lo = 256 * n if n < 3 else 896
-            lx = tt(ap("lX", lo, 256 * n + 256), ind(ap("US", 0, S), ap("lHO", lo // 16, 16 * n + 16)), ap("ZT", lo % 512, 256 * (n % 2) + 256), SUB)
-            act(ap3("lA", lo // 32, 8 * n + 8, 0, 32), ap("lX", lo, 256 * n + 256), AF.Abs)
-            if n == 0:
-                half = act(ap3("lA", 24, 28, 0, 32), ap("ZP", 256, 384), AF.Abs)
-            if n == 1:
-                later(half)
-        ts(ap("lHH"), ap("lHI"), -2047.0, ADD)
-        mm([(ap("ZP", 64 * r, 64 * r + 64), ap("RL", 128 * r, 128 * r + 128), ap("lHH"), True, True) for r in range(8)])
-        act(ap("lHT", 0, 512), ap("ZP"), AF.Copy)
-        for n in range(4):
-            d = ("DA", "DB", "UVP", "HR")[n]
-            mm([(ap(d, 64, 128), ap("IDB"), ap("ML", 64 * n, 64 * n + 64), True, False), (ap(d, 64, 128), ap("IDB"), ap("PZL"), False, False)])
-            mm([(ap(d, 64, 128), ap("SLQ", 128 * r, 128 * r + 128), ap3("lA", 8 * n, 8 * n + 8, 8 * r, 8 * r + 8), False, r == 3) for r in range(4)])
-            if n < 2:
-                ts(ap("lRM", 64 * n, 64 * n + 64), ap(d, 64, 128), b16, MIN)
-            else:
-                tt(ap("lRM", 64 * n, 64 * n + 64), ap(d, 64, 128), ap("lRM", 64 * n - 128, 64 * n - 64), MIN)
-                scan(ap("lKS", 64 * n - 128, 64 * n - 64), ap("RS32"), ap("lRM", 64 * n, 64 * n + 64), ADD, MIN)
-        ts(ap("lMI"), ap("lKS", 31, 128, 32), 1023, AND); cp(ap("lLL"), ap("lMI"))
-        tt(ap("lHM"), ind(ap("lHT"), ap("lLL")), ap("MWR", 0, 64), MUL)
-        scan(ap("lHS"), ap("RST", 0, 64), ap("lHM"))
-        reg = [ap(("HR", "ZP")[c // 2], 256 + LR[c], 320 + LR[c] - 16 * c) for c in range(4)]
-        for d, lo, hi in (("HR", 0, 112), ("ZP", 112, 160)):
-            mm([(ap(d, 256 + lo, 256 + hi), ap("IDB"), ap("lTR", lo, hi), True, False)])
-        for c in (0, 2):
-            mm([(reg[k], ap("BLKH"), ap("lHM", 16 * k, 64), False, k % 2 == 1) for k in (c, c + 1)])
-        lhl = ts(ap("lHL"), ap("lHS", 15, 64, 16), 2047.0, ADD, 4095.0, MIN)
-        act(ap("RS", 0, 64), ind(ap("TP"), ap("lHL")), AF.Copy)
-        mm([(ap("CT", 256, 320), ap("IDB"), ap("lNM"), True, False)])
-        mm([(ap("CT", 256, 320), ap("IDH"), ap("lHM"), False, False)])
-        for c in range(4):
-            e = ap("lET", LR[c], LR[c] + 64 - 16 * c)
-            ts(e, reg[c], ap("lHS", 16 * c + 15, 16 * c + 16), EQ)
-            if c == 1:
-                later(lhl)
-            lct = mm([(ap("CT", 256 + 16 * c, 320), ap("BLK8"), e, False, c == 3)])
-        scan(ap("RS", 64, 128), ap("DR1"), ap("CT", 256, 320), MAX, MIN)
-        send("RB%d" % t, ap("RS"), "rep%d" % t, "lr", borrower)
-        scan(ap("lWS"), ap("DR1"), ap("CT", 256, 320), MAX, MIN)
-        ts(ap("lLO"), ap("lWS", 15, 64, 16), 4095.0, ADD)
-        if last:
-            cp(ap("RSU"), ind(ap("US"), ap("lLO")))
-        else:
-            act(ap("RSU"), ind(ap("US"), ap("lLO")), AF.Copy)
-        send("RV%d" % t, ap("RSU"), "reu%d" % t, "lu", borrower)
-        lend = cp(ind(ap("US"), ap("lLO")), ap("C255", 0, 64))
         if not last:
-            iota(ap("US", ZD, 4480), [[0, 4480 - ZD]], 0)
-            mm([(ap("MS", 96, 97), ap("ONEB"), ap("SC", 15, 16), True, True)])
-            cp(ap("PPI"), ap("MS", 96, 97)); ts(ap("PPJ"), ap("PPI"), 63, AND); ts(ap("b16b" if t % 2 else "b16a"), ap("PPJ"), 1024.0, MUL, ap("th16"), ADD)
-        if t:
-            ts(ind(ap(cx, 0, NEW), ap("OBU")), ap("IC64"), 1.0, MUL, float(S + CAP * (t - 1)), ADD); later(lay)
-            dma(ext("yc", L * (t - 1), L * t), ap(cx, 0, 256, 1, slice(0, 128, 16)), 2.0)
+            ts(ap("HL"), ap("HS", 15, 256, 16), 2047.0, ADD, 4095.0, MIN)
+        mm([(ap("DA", 256, 512), ap("IDH"), ap("EE", 0, 256), True, True)])
+        act(ap("E32"), ap("DA", 256, 512), AF.Copy, bias=64.0)
         mm([(ap("JP", 0, 256), ap("BLKB"), ap("KONST"), True, False)])
         off = 0
         for c in range(16):
@@ -553,13 +519,90 @@ def build(rank, core, T, topo):
             mm([(ap("JP", lo, hi), ap("BLKB"), ap("SG", off, off + hi - lo), False, c == 15)]); later(ofm)
             off += (hi - lo + 15) // 16 * 16
         act(ap("RJ", 1, 257), ap("JP", 0, 256), AF.Relu, bias=254.0, scale=-0.5)
+        mm([(ap("DA", 256, 512), ap("IDB"), ap("RJ", 0, 256), True, False)]); mm([(ap("DA", 256, 512), ap("IDN"), ap("RJ", 1, 257), False, True)])
+        fst = act(ap("FIRST"), ap("DA", 256, 512), AF.Sign)
         sel("JP", 256, "RJ", 1, 16)
-        ts(ap("JL"), ap("JP", 256, 272), -1.0 / 256, MUL, 254.0, ADD); act(ap("JW"), ap("JP", 256, 272), AF.Copy, bias=254.0, scale=-1.0 / 256)
-        mm([(ap("JP", 0, 256), ap("IDB"), ap("RJ", 0, 256), True, False), (ap("JP", 0, 256), ap("IDN"), ap("RJ", 1, 257), False, True)])
-        act(ap("FIRST"), ap("JP", 0, 256), AF.Sign)
+        jl = ts(ap("JL"), ap("JP", 256, 272), -1.0 / 256, MUL, 254.0, ADD); jw = act(ap("JW"), ap("JP", 256, 272), AF.Copy, bias=254.0, scale=-1.0 / 256)
+        mm([(ap("MS", 256, 512), ap("IDB"), ap("UR"), True, False)])
+        for c in range(8):
+            if c == SX:
+                wdm = mm([(ap("MS", 256, 512), ap("BLKB"), ap("WD"), False, False)])
+            equal(16 + c, 128, 256, c, c < SX)
+            if c >= SX:
+                later(lay)
+            crs = mm([(ap("MS", 384, 512), ap("BLK8"), ap3("ET", 16 + c, 17 + c, 0, 128), False, c == 7)])
+        wn = act(ap("WN"), ap("MS", 256, 512), AF.Relu, bias=NEW / 32, scale=-NEW / 512)
+        mm([(ap("UVP", 128 + 32 * qv, 160 + 32 * qv), wt(2, qv, i), ap("ZL%d" % t, i, i + 63, 2), i == 0, i == 1) for qv in (0, 1) for i in (0, 1)])
+        for k in range(2):
+            act(ap("ZT", 256 * k, 256 * k + 256), ind(ap("ZL%d" % t), ap("CJ", 16 * k, 16 * k + 16)), AF.Copy)
+        cp(ap("lUVS"), ap("UVP", 128, 192))
+        ts(ap("lUVA"), ap("lUVS"), 4095, AND)
+        tt(ap("lUVW"), ap("lUVA", 0, 32), ap("lUVA", 32, 64), MUL)
+        for k in range(2):
+            ts(ap("lKU", 32 * k, 32 * k + 32), ap("lUVA", 0, 32), ap("kc", k, k + 1), MUL)
+        ts(ap("lUQ"), ap("lUVW"), 5, SHR)
+        for k in range(2):
+            tt(ap("lHV", 32 * k, 32 * k + 32), ap("lKU", 32 * k, 32 * k + 32), ap("lUQ"), ADD)
+        ts(ap("lHI"), ap("lHV"), 4095, AND); lhh = ts(ap("lHH"), ap("lHI"), -2047.0, ADD); cp(ap("lHO"), ap("lHI")); later(lhh, jl)
+        k = act(ap("lX", 768, 768 + LB), ind(ap("US", 0, S), ap("lHO", 48, 48 + LB // 16)), AF.Copy); later(fst, jw)
+        mm([(ap("ZP", 256, 256 + LB), ap("IDN"), ap("ZT", 256, 256 + LB), True, False)]); mm([(ap("ZP", 256, 256 + LB), ap("IDB"), ap("lX", 768, 768 + LB), False, True)])
+        for lo, hi in LORD:
+            if lo != 768:
+                tt(ap("lX", lo, hi), ind(ap("US", 0, S), ap("lHO", lo // 16, hi // 16)), ap("ZT", lo % 512, (hi - 1) % 512 + 1), SUB)
+            act(ap3("lA", lo // 32, hi // 32, 0, 32), ap("lX", lo, hi) if lo != 768 else ap("ZP", 256, 256 + LB), AF.Abs); later(k)
+            k = len(ops) - 1
+        mm([(ap("CT", 64 * r, 64 * r + 64), ap("RL", 128 * r, 128 * r + 128), ap("lHH"), True, True) for r in range(8)]); later(wdm)
+        act(ap("lHT", 0, 512), ap("CT"), AF.Copy); later(k)
+        for n in range(4):
+            d = ("DA", "DB", "UVP", "HR")[n]
+            mm([(ap(d, 64, 128), ap("IDB"), ap("ML", 64 * n, 64 * n + 64), True, False), (ap(d, 64, 128), ap("IDB"), ap("PZL"), False, False)])
+            mm([(ap(d, 64, 128), ap("SLQ", 128 * r, 128 * r + 128), ap3("lA", 8 * n, 8 * n + 8, 8 * r, 8 * r + 8), False, r == 3) for r in range(4)])
+            if n < 2:
+                ts(ap("lRM", 64 * n, 64 * n + 64), ap(d, 64, 128), b16, MIN)
+            else:
+                for k in range(2):
+                    lo = 64 * n - 128 + 32 * k
+                    scan(ap("lKS", lo, lo + 32), ap("lRM", lo, lo + 32), ap(d, 64 + 32 * k, 96 + 32 * k), MIN, MIN, 8 * BIG)
+        ts(ap("lMI"), ap("lKS", 31, 128, 32), 1023, AND); cp(ap("lLL"), ap("lMI"))
+        tt(ap("lHM"), ind(ap("lHT"), ap("lLL")), ap("MWR", 0, 64), MUL)
+        scan(ap("lHS"), ap("RST", 0, 64), ap("lHM"))
+        reg = [ap(("HR", "ZP")[c // 2], 256 + LR[c], 320 + LR[c] - 16 * c) for c in range(4)]
+        for d, lo, hi in (("HR", 0, 112), ("ZP", 112, 160)):
+            mm([(ap(d, 256 + lo, 256 + hi), ap("IDB"), ap("lTR", lo, hi), True, False)])
+        for c in (0, 2):
+            mm([(reg[k], ap("BLKH"), ap("lHM", 16 * k, 64), False, k % 2 == 1) for k in (c, c + 1)]); later(crs - 2 * CLATE)
+        if not last:
+            lhl = ts(ap("lHL"), ap("lHS", 15, 64, 16), 2047.0, ADD, 4095.0, MIN)
+            act(ap("RS", 0, 64), ind(ap("TP"), ap("lHL")), AF.Copy)
+        mm([(ap("CT", 256, 320), ap("IDB"), ap("lNM"), True, False)])
+        mm([(ap("CT", 256, 320), ap("IDH"), ap("lHM"), False, False)])
+        for c in range(4):
+            e = ap("lET", LR[c], LR[c] + 64 - 16 * c)
+            ts(e, reg[c], ap("lHS", 16 * c + 15, 16 * c + 16), EQ)
+            if c == 1 and not last:
+                later(lhl)
+            lct = mm([(ap("CT", 256 + 16 * c, 320), ap("BLK8"), e, False, c == 3)])
+        scan(ap("RS", 64, 128), ap("DR1"), ap("CT", 256, 320), MAX, MIN)
+        send("RB%d" % t, ap("RS", 64 * last, 128), "rep%d" % t, "lr", borrower)
+        scan(ap("lWS"), ap("DR1"), ap("CT", 256, 320), MAX, MIN)
+        ts(ap("lLO"), ap("lWS", 15, 64, 16), 4095.0, ADD)
+        if last:
+            cp(ap("RSU"), ind(ap("US"), ap("lLO")))
+        else:
+            act(ap("RSU"), ind(ap("US"), ap("lLO")), AF.Copy); later(wn)
+        send("RV%d" % t, ap("RSU"), "reu%d" % t, "lu", borrower)
+        lend = cp(ind(ap("US"), ap("lLO")), ap("C255", 0, 64))
+        if not last:
+            iota(ap("US", ZD, 4480), [[0, 4480 - ZD]], 0)
+            mm([(ap("MS", 96, 97), ap("ONEB"), ap("SC", 15, 16), True, True)])
+            cp(ap("PPI"), ap("MS", 96, 97)); ts(ap("PPJ"), ap("PPI"), 63, AND); ts(ap("b16b" if t % 2 else "b16a"), ap("PPJ"), 1024.0, MUL, ap("th16"), ADD)
+        if t:
+            ts(ind(ap(cx, 0, NEW), ap("OBU")), ap("IC64"), 1.0, MUL, float(S + CAP * (t - 1)), ADD); later(lend)
+            dma(ext("yc", L * (t - 1), L * t), ap(cx, 0, 256, 1, slice(0, 128, 16)), 2.0)
         tt(ap("FW"), ind(ap("WN"), ap("JL")), ap("FIRST"), MUL)
-        sel("JP", 272, "FW", 0, 16)
-        tt(ap("JX"), ap("JP", 272, 288), ap("JW"), ADD); jl2 = cp(ap("JL2"), ap("JX"))
+        mm([(ap("JP", 0, 256), ap("IDB"), ap("NM"), True, False)]); mm([(ap("JP", 0, 256), ap("I256"), ap("FW"), False, True)])
+        scan(ap("CM2"), ap("DRS"), ap("JP", 0, 256), MAX, MIN)
+        tt(ap("JX"), ap("JW"), ap("CM2", 15, 256, 16), SUB); cp(ap("JL2"), ap("JX"))
         if not last:
             act(ap(tx, NEW, NEW + L), ind(ap("TP"), ap("HL")), AF.Copy)
             act(ap(wx, NEW, NEW + L), ind(ap("WTAB"), ap("HL")), AF.Copy)
@@ -567,9 +610,12 @@ def build(rank, core, T, topo):
             act(ap(wy, 0, 256), ind(ap(wx), ap("JL2")), AF.Copy)
         act(ap(cy, 0, 256), ind(ap(cx), ap("JL2")), AF.Copy)
         act(ap("EA", 0, 64), ap("PF64"), AF.Copy)
-        cp(ind(ap("EA"), ap("OF")), ap("EE", 0, 256)); later(lend)
+        if EAS:
+            act(ind(ap("EA"), ap("OF")), ap("E32"), AF.Silu)
+        else:
+            cp(ind(ap("EA"), ap("OF")), ap("EE", 0, 256)); later(lend)
         scan(ap("EQ"), ap("TRH", 0, 64), ap("EA", 0, 64), MAX, MIN)
-        ts(ap("FAI"), ap("EQ", 15, 64, 16), 0.2, MUL)
+        ts(ap("FAI"), ap("EQ", 15, 64, 16), -64.0 * EAS, ADD, 0.2, MUL)
         rb = "RB%d" % t
         tt(ap("OB"), ap(rb, 79, 128, 16), ap("FAI"), MAX); cp(ap("OBU"), ap("OB"))
         if not last:
@@ -632,7 +678,7 @@ def order(ops, memo=None):
     def lag(j, k):
         if ops[k]["pre"][j]:
             return OWN if ops[k]["q"] == ops[j]["q"] else HOP
-        return ISSUE - ops[j]["c"] if ops[j]["q"] == "Y" else 0.0
+        return ISSUE - ops[j]["c"] if ops[j]["q"] in "YZ" else 0.0
     pres = [[(j, lag(j, i)) for j in ops[i]["pre"]] for i in range(n)]
     posts = [[(k, lag(i, k)) for k in succ[i]] for i in range(n)]
 
@@ -648,7 +694,7 @@ def order(ops, memo=None):
                 if end[j] + d > t:
                     t = end[j] + d
             if q != "N":
-                hold = ISSUE if q == "Y" else c
+                hold = ISSUE if q in "YZ" else c
                 skip = c - hold if back else 0.0
                 lst = busy.setdefault(q, [])
                 p = len(lst)
@@ -713,7 +759,7 @@ def order(ops, memo=None):
                         t, why[i] = end[j] + d, j
                 end[i] = t + c[i]
                 if q != "N":
-                    free[q] = (t + (ISSUE if q == "Y" else c[i]), i)
+                    free[q] = (t + (ISSUE if q in "YZ" else c[i]), i)
             total += max(end)
             i = end.index(max(end))
             while why[i] >= 0:
@@ -748,7 +794,7 @@ def rank_program(g, core, T, topo):
         return
     ops = build(rank, core, T, topo)
     seq, _ = order(ops, _MEMO)
-    eng = {"V": g.vector, "S": g.scalar, "P": g.tensor, "G": g, "Y": g.sync}
+    eng = {"V": g.vector, "S": g.scalar, "P": g.tensor, "G": g, "Y": g.sync, "Z": g.scalar}
     total = {}
     known = {q: {} for q in eng}
     for i in seq:

@@ -5,7 +5,8 @@ import comms_topo
 RO, L, S, CAP = 6, 256, 4096, 64
 UNF = 4000.0
 BIG = 4194304.0
-NEW = 400
+OLD, END = 256, 656
+TINY = 1e-7
 ZD = 4352
 
 _B = {}
@@ -16,7 +17,7 @@ def _b(name, cols, dtype, rows=128, inner=0):
 
 
 F, BF, H, I, U16 = "float32", "bfloat16", "float16", "int32", "uint16"
-_b("US", 4480, BF); _b("TP", 4096, BF); _b("WTAB", 4096, BF)
+_b("US", 4480, BF); _b("TP", 4096, BF); _b("WTAB", 4096, BF); _b("UF", 4480, F); _b("ZERO", 128, F)
 _b("c8", 256, I, 8); _b("hwi", 2, I); _b("kmi", 1, I); _b("th8", 1, I, 8)
 _b("c8h", 256, H, 8); _b("c8i", 256, I, 8); _b("c8w", 256, H, 8); _b("th8h", 1, H, 8); _b("hwf", 2, F); _b("hwg", 2, F); _b("hwh", 2, H); _b("wl", 2, F); _b("wr", 2, F); _b("ws", 2, F)
 _b("kh", 16, H); _b("KR", 16, F); _b("th16", 1, F); _b("b16a", 1, F); _b("b16b", 1, F); _b("ksc", 1, F)
@@ -25,44 +26,45 @@ for _n in ("pF", "sF", "gF", "s2F", "sge8", "slt8", "pm8", "gx8", "g8p", "nsB", 
     _b(_n, 1, F)
 _b("g16", 16, F); _b("g8", 4, F); _b("g8m", 4, F); _b("pen2", 2, F); _b("pen4", 4, F)
 _b("MWR", 256, F); _b("RST", 256, F); _b("BLKH", 128, H); _b("BLKB", 128, BF); _b("BLKN", 128, BF); _b("ONEB", 128, BF)
-_b("IDH", 128, H); _b("IDB", 128, BF); _b("IDN", 128, BF); _b("I256", 128, BF); _b("IDHN", 128, H)
-_b("TRIMB", 128, BF); _b("PL", 128, BF); _b("PR", 128, BF); _b("PH", 128, H); _b("SEL", 2048, BF); _b("REP8", 128, H, 8)
+_b("IDH", 128, H); _b("IDB", 128, BF); _b("IDN", 128, BF); _b("IDHN", 128, H); _b("I255", 128, BF); _b("SH1", 128, BF); _b("SH2", 128, BF)
+_b("TRIMB", 128, BF); _b("PL", 128, BF); _b("PR", 128, BF); _b("PH", 128, H); _b("SEL", 144, BF); _b("REP8", 128, H, 8)
 _b("WT", 24 * 128, H); _b("PZ4", 128, BF); _b("RS4", 128, F); _b("RS16", 64, F)
-_b("C255", 128, BF); _b("T5", 256, F); _b("KONST", 256, BF); _b("one16", 16, F); _b("oneR", 256, BF); _b("JW0", 16, F)
+_b("C255", 128, BF); _b("THR", 16, F); _b("KJ", 48, F); _b("K256", 16, BF); _b("ZZ", 128, BF); _b("one16", 16, F); _b("oneR", 256, BF); _b("JW0", 16, F)
 _b("J256", 16, H); _b("FIX", 32, F); _b("CL", 16, U16); _b("CJ", 32, U16); _b("IC64", 64, F); _b("PF64", 64, F)
 _b("DRS", 256, F); _b("DR1", 64, F); _b("lNM", 64, BF); _b("lTR", 160, BF)
-_b("SLQ", 512, BF); _b("SLP", 1024, BF); _b("B512", 128, BF); _b("B256", 128, BF); _b("BLK8", 128, BF); _b("NM", 256, BF); _b("TRH", 64, BF)
-_b("MP", 512, BF); _b("MS1", 256, BF); _b("ML", 256, BF); _b("kz1", 256, BF); _b("kz2", 256, BF); _b("CM2", 256, F); _b("CL0", 16, U16)
+_b("SLQ", 144, BF); _b("B512", 128, BF); _b("B256", 128, BF); _b("BLK8", 128, BF); _b("NM", 256, BF); _b("TRH", 64, BF)
+_b("MP", 512, BF); _b("MS1", 256, BF); _b("ML", 256, BF); _b("CM2", 256, F); _b("CMH", 256, H); _b("DJ", 256, H); _b("CL0", 16, U16)
 for _k in "01":
-    _b("CX" + _k, NEW + L, F); _b("TX" + _k, NEW + L, BF); _b("WX" + _k, NEW + L, BF)
-_b("ZB", 512, BF); _b("UVS", 128, I); _b("UVA", 32, I); _b("UVW", 16, I); _b("UQ", 32, F)
-_b("HV", 256, I, inner=16); _b("HF", 256, F, inner=16); _b("HI", 256, I); _b("HO", 256, U16); _b("HT", 528, F)
-_b("X", 4096, BF); _b("A", 4096, BF); _b("RM", 512, F); _b("RI", 320, F); _b("KS", 64, I)
+    _b("CX" + _k, END, F); _b("TX" + _k, END, BF); _b("WX" + _k, END, BF)
+_b("ZB", 512, BF); _b("UVS", 128, I); _b("UVA", 32, I); _b("UVW", 16, I); _b("UVQ", 16, I)
+_b("HV", 256, I); _b("KU", 256, F); _b("KRX", 256, F); _b("LS", 16, U16); _b("LC", 16, U16); _b("RS5", 128, F); _b("R5", 128, F); _b("K5", 128, I); _b("HI", 256, I); _b("HO", 256, U16); _b("HT", 528, F)
+_b("X", ZD, BF); _b("STB", 128, BF); _b("A", 4096, BF); _b("RM", 512, F); _b("RI", 320, F); _b("KS", 64, I)
 _b("PO", 16, F); _b("PN", 16, BF); _b("SC", 16, BF); _b("POJ", 16, H); _b("OF", 16, U16); _b("ZA", 768, BF)
 _b("PPI", 1, I); _b("PPJ", 1, I); _b("MI", 16, I); _b("LL", 16, U16)
 _b("HM", 256, H); _b("HS", 256, F); _b("HD", 16, F); _b("LA", 16, F); _b("UR", 256, BF); _b("EX", 1024, BF); _b("W2", 128, BF); _b("B30", 128, BF); _b("NM2", 128, BF); _b("P2", 48, F); _b("HRH", 256, H); _b("HL", 16, U16)
-_b("ET", 24 * 128, BF, inner=128); _b("WD", 256, BF); _b("WN", 256, BF); _b("WS", 256, F); _b("LO", 16, U16)
+_b("ET", 16 * 128, BF, inner=128); _b("WD", 256, BF); _b("WN", 512, BF); _b("STP", 128, F); _b("MF", 128, BF); _b("WS", 256, F); _b("LO", 16, U16)
 _b("EE", 512, H); _b("FI", 32, I); _b("FB", 32, F); _b("FC", 32, F); _b("NW", 16, F); _b("UN0", 16, F)
-_b("EB", 16, F); _b("SG", 4096, BF); _b("RJ", 272, BF); _b("FIRST", 256, BF); _b("JW", 16, F); _b("JL", 16, U16); _b("FW", 256, BF); _b("JX", 16, F); _b("JL2", 16, U16)
+_b("SG", 2048, BF); _b("SJ", 16, F); _b("J2", 16, F); _b("JB", 32, BF); _b("JL", 16, U16); _b("FW", 256, BF); _b("JX", 16, F); _b("JL2", 16, U16)
 _b("EA", 768, F); _b("E32", 256, F); _b("EM", 64, F); _b("EQ", 64, F); _b("FAI", 4, I); _b("FA", 4, F); _b("OB", 4, F); _b("OBU", 4, U16)
 for _k in range(RO):
-    _b("ZL%d" % _k, 64, BF); _b("RB%d" % _k, 128, BF); _b("RV%d" % _k, 64, BF)
+    _b("ZL%d" % _k, 64, BF); _b("RB%d" % _k, 128, BF); _b("RV%d" % _k, 64, BF); _b("FL%d" % _k, 8, BF)
+_b("FS", 8, BF); _b("lUF", 64, BF)
 _b("ZT", 512, BF); _b("lUVS", 64, I); _b("lUVA", 64, I); _b("lUVW", 32, I); _b("lUQ", 32, I); _b("lKU", 64, F)
-_b("lHV", 64, I); _b("lHI", 64, I); _b("lHO", 64, U16); _b("lHT", 528, F); _b("lX", 1024, BF); _b("lA", 1024, BF, inner=32)
+_b("lHV", 64, I); _b("lHI", 64, I); _b("lHO", 64, U16); _b("lHT", 528, F); _b("lX", 1024, BF); _b("lA", 1024, BF, inner=32); _b("lY", 256, BF, inner=32)
 _b("CG2", 128, BF); _b("CZ", 64, BF); _b("PZL", 64, BF); _b("RS32", 64, F); _b("RL", 1024, BF); _b("lHH", 64, H); _b("PK", 256, BF)
 _b("kc", 2, F); _b("k1", 1, H); _b("s1I", 1, I)
 _b("lRM", 256, F); _b("lKS", 128, I); _b("lMI", 4, I); _b("lLL", 4, U16); _b("lHM", 64, H); _b("lHS", 64, F); _b("lHL", 4, U16)
 _b("lET", 160, BF); _b("RS", 128, BF); _b("RSU", 64, BF); _b("lWS", 64, F); _b("lLO", 4, U16)
 _PS = ["UVP", "ZP", "DA", "DB", "HR", "CT", "MS", "JP"]
 _SIZE = {F: 4, BF: 2, H: 2, I: 4, U16: 2}
-_OWN = ("US", "TP", "WTAB", "X", "A", "ZA", "RS", "RSU")
+_OWN = ("US", "TP", "WTAB", "UF", "X", "A", "ZA", "RS", "RSU", "FS")
 SCRATCH = {}
 _AT = {}
 _fill = {}
 for _n, (_w, _sh, _d, _in) in _B.items():
     if _in:
         SCRATCH[_n] = (_w, [128, _sh[1] // _in, _in], _d); _AT[_n] = (_n, 0)
-    elif _n in _OWN or _n[:2] in ("ZL", "RB", "RV") or _sh[0] != 128:
+    elif _n in _OWN or _n[:2] in ("ZL", "RB", "RV", "FL") or _sh[0] != 128:
         SCRATCH[_n] = (_w, _sh, _d); _AT[_n] = (_n, 0)
     else:
         _q = 32 // _SIZE[_d]
@@ -72,22 +74,28 @@ for _d, _c in _fill.items():
     SCRATCH["ar_" + _d] = ("sbuf", [128, _c], _d)
 for _n in _PS:
     SCRATCH[_n] = ("psum", [128, 512], F); _AT[_n] = (_n, 0); _B[_n] = ("psum", [128, 512], F, 0)
-ND = 32
-SEMAPHORES = ["sV", "sS", "sP", "sG", "la", "lr", "lu"] + ["reu%d" % k for k in range(RO)] + ["ask%d" % k for k in range(RO)] + ["rep%d" % k for k in range(RO)] + ["d%d" % k for k in range(ND)]
+ND = 40
+SEMAPHORES = ["sV", "sS", "sP", "sG", "la", "lr", "lu", "lf"] + ["fai%d" % k for k in range(RO)] + ["reu%d" % k for k in range(RO)] + ["ask%d" % k for k in range(RO)] + ["rep%d" % k for k in range(RO)] + ["d%d" % k for k in range(ND)]
 
 NS = 5
-BYS = {2: "CT", 3: "CT", 4: "ZP", 5: "ZP"}
-PROBE = [("gather", 0, 2), ("gather", 2, 2), ("gather", 4, 2), ("gather", 6, 2), ("abs", 0, 2), ("abs", 2, 2), ("gather", 8, 2), ("abs", 4, 2),
-         ("gather", 10, 2), ("abs", 6, 2), ("abs", 8, 2), ("least", 0, 2), ("gather", 12, 2), ("abs", 10, 2), ("gather", 14, 1), ("abs", 12, 2),
-         ("least", 1, 2), ("gather", 15, 1), ("abs", 14, 1), ("abs", 15, 1), ("slots", 0, 0), ("slots", 2, 0), ("least", 2, 2), ("slots", 3, 0),
-         ("slots", 1, 0), ("least", 3, 1)]
-PAIRS, LAST = 7, 1
+BYS = {0: "CT", 2: "ZP", 14: "UVP"}
+SUMS = {0: "DA", 4: "DB", 8: "JP", 12: "HR", 13: "CT", 14: "ZP", 15: "DA"}
+PROBE = [("gather", 0, 2), ("gather", 4, 2), ("gather", 2, 2), ("abs", 0, 2), ("gather", 6, 2), ("gather", 14, 1), ("abs", 2, 2), ("gather", 8, 2),
+         ("abs", 4, 2), ("gather", 10, 2), ("abs", 6, 2), ("four", 0, 0), ("slots", 0, 0), ("gather", 12, 1), ("abs", 8, 2), ("slots", 1, 0),
+         ("gather", 13, 1), ("abs", 10, 2), ("four", 4, 0), ("gather", 15, 1), ("abs", 14, 1), ("slots", 3, 0), ("abs", 12, 1), ("abs", 13, 1),
+         ("slots", 2, 0), ("four", 8, 0), ("abs", 15, 1), ("single", 14, 0), ("fold", 0, 0), ("single", 12, 1), ("single", 13, 2), ("single", 15, 3)]
+KEPT = ("gather", "abs", "four", "minus", "slots")
+MERGE = 3
+ZERO = 0
+SLOTS = 1
+CONV = 3
 PARTS = 2
 ZBF = 1
 INORDER = 0
 EAS = 1
 ABSW = 512
-EARLY = 6
+EARLY = ((0, 6), (6, 16))
+LRELU = 0
 CLATE = 2
 LB = 256
 LORD = ((0, 256), (256, 512), (768, 1024), (512, 768))
@@ -98,13 +106,13 @@ PASSES = 6
 GSEL = 10
 JA = 8
 
-CY = 0.00114
+CY = 0.00104
 GA, SCT = 1.56, 3.8
-HOP, OWN, ISSUE = 0.11, 0.055, 0.1
-FLIGHT, SEND, SFIX = 2.6, 1.0, 0.03
-GUESSES = ((CY, GA, SCT, HOP, OWN, FLIGHT, SFIX), (0.001, 1.15, 2.0, 0.13, 0.07, 3.0, 0.03), (0.00125, 1.9, 5.5, 0.13, 0.06, 3.3, 0.03),
-           (0.0011, 1.4, 3.0, 0.12, 0.06, 1.5, 0.05))
-TRIES, SEED = 5000, 1
+HOP, OWN, ISSUE = 0.14, 0.08, 0.1
+FLIGHT, SEND, SFIX, PE = 2.4, 0.6, 0.03, 0.5
+GUESSES = ((CY, GA, SCT, HOP, OWN, FLIGHT, SFIX, 1.0), (0.0009, 1.15, 2.5, 0.2, 0.1, 1.2, 0.05, 1.2), (0.00125, 1.9, 5.5, 0.13, 0.07, 3.6, 0.03, 1.0),
+           (0.00092, 1.5, 3.5, 0.18, 0.1, 3.0, 0.06, 2.0))
+TRIES, SEED, HEAT = 7000, 1, 0.03
 
 
 def build(rank, core, T, topo):
@@ -203,11 +211,18 @@ def build(rank, core, T, topo):
         return put("V", lambda g: g.vector.tensor_tensor_scan(res(o), res(a), res(b), first, op0, op1), [a, b], [o],
                    vcost(n_of(o), 0.5 if size(o) == size(a) == size(b) == 2 else 1, False, False))
 
-    def fill(o, v):
+    def fill(o, v, q="V"):
+        if q == "G":
+            return iota(o, [[0, n_of(o)]], int(v))
+        if q == "S":
+            return act(o, ap("IC", 0, n_of(o)), AF.Copy, bias=v, scale=0.0)
         return put("V", lambda g: g.vector.memset(res(o), v), [], [o], vcost(n_of(o), size(o) / 4, False, False))
 
-    def act(o, a, func, bias=0.0, scale=1.0):
+    def act(o, a, func, bias=0.0, scale=1.0, total=None):
         rd = [a] + [x for x in (bias, scale) if isinstance(x, tuple)]
+        if total:
+            return put("S", lambda g: g.scalar.activation(res(o), res(a), func, bias=sc(bias), scale=sc(scale), accum_out=res(total)), rd, [total, o],
+                       (0.02, max(64, n_of(o)), 0, 0))
         if o[0] == "i":
             return put("S", lambda g: g.scalar.activation(res(o), res(a), func), rd, [o], (0.0, 0, 0, n_of(o)))
         return put("S", lambda g: g.scalar.activation(res(o), res(a), func, bias=sc(bias), scale=sc(scale)), rd, [o],
@@ -219,7 +234,7 @@ def build(rank, core, T, topo):
             for o, l, rh, st, sp in lst:
                 r = g.tensor.matmul(res(o), res(l), res(rh), st, sp)
             return r
-        return put("P", fn, [x[1] for x in lst] + [x[2] for x in lst], [x[0] for x in lst], (0.0, sum(max(64, n_of(x[2])) for x in lst), 0, 0))
+        return put("P", fn, [x[1] for x in lst] + [x[2] for x in lst], [x[0] for x in lst], (0.0, PE * sum(max(64, n_of(x[2])) for x in lst), 0, 0))
 
     def iota(o, pattern, base, step=0):
         if _B[o[1]][2] == I:
@@ -231,10 +246,17 @@ def build(rank, core, T, topo):
 
     nd = [0]
 
-    def dma(o, a, cost, q="Y"):
+    def dma(o, a, cost, behind=()):
         k = "d%d" % nd[0]; nd[0] += 1
-        return put(q, lambda g: (g.sync if q == "Y" else g.scalar).dma_start(res(o) if isinstance(o, tuple) else o, res(a) if isinstance(a, tuple) else a),
-                   [a] if isinstance(a, tuple) else [], [o] if isinstance(o, tuple) else [], cost, sem=k, inc=16)
+        put("Y", lambda g: g.sync.dma_start(res(o) if isinstance(o, tuple) else o, res(a) if isinstance(a, tuple) else a),
+            ([a] if isinstance(a, tuple) else []) + list(behind), [o] if isinstance(o, tuple) else [], cost, sem=k, inc=16)
+        ops[-1]["hold"] = ISSUE
+        return len(ops) - 1
+
+    def dma_add(o, a, cost, behind=()):
+        k = "d%d" % nd[0]; nd[0] += 1
+        put("G", lambda g: g.dma_start(res(o), res(a), accum_op=AluOpType.add, max_dma_last_dim=4096), [a, o] + list(behind), [o], cost, sem=k, inc=16)
+        ops[-1]["hold"] = 1.0
 
     def send(o, a, sem, loc, dst):
         rid, pid, se = topo.addr(dst)
@@ -245,6 +267,8 @@ def build(rank, core, T, topo):
         ops[-1]["n"] = len(topo.engines(core, dst)[:8])
         put("N", None, [], [ap(o)], 0.0, sem=sem, inc=8)
         ops[-1]["after"] = [k]
+        put("N", None, [a], [], 0.0)
+        ops[-1]["after"] = [k]; ops[-1]["left"] = k
 
     ADD, SUB, MUL, MIN, MAX = AluOpType.add, AluOpType.subtract, AluOpType.mult, AluOpType.min, AluOpType.max
     EQ, NE, GE, GT, LT, LE = AluOpType.is_equal, AluOpType.not_equal, AluOpType.is_ge, AluOpType.is_gt, AluOpType.is_lt, AluOpType.is_le
@@ -254,10 +278,10 @@ def build(rank, core, T, topo):
     def keep(o, src, pattern, base, op=EQ, step=0):
         return put("G", lambda g: g.affine_select(res(o), res(ap(src)), pattern, op, 0.0, base, step), [ap(src)], [o], (0.18, 256, 0, 0))
 
-    dma(ap("c8"), T.c0[:, :], 2.0); dma(ap("hwi"), T.hw[:, :], 2.0); later(0)
-    dma(ap("TP"), ext("tp", 0, S), 6.0); later(1)
-    dma(ap("kmi"), T.km[:, :], 6.0); later(2); dma(ap("th8"), T.th[:, :], 6.0); later(3)
-    ldu = dma(ap("US", 0, S), ext("us", 0, S), 8.0); later(4)
+    dma(ap("c8"), T.c0[:, :], 1.7); dma(ap("hwi"), T.hw[:, :], 1.7); later(0)
+    dma(ap("kmi"), T.km[:, :], 1.7); later(1); dma(ap("th8"), T.th[:, :], 1.7); later(2)
+    dma(ap("TP"), ext("tp", 0, S), 3.8); later(3)
+    ldu = dma(ap("US", 0, S), ext("us", 0, S), 6.2); later(4)
 
     iota(ap("pI"), [[0, 1]], 0, 1); iota(ap("CG"), [[1, 8], [0, 16]], 0); iota(ap("IC"), [[1, 256]], 0); iota(ap("CS"), [[0, 16], [1, 16]], 0)
     iota(ap("CG8"), [[8, 8], [0, 4], [1, 4]], 0); iota(ap("C3"), [[0, 32], [1, 4]], 0)
@@ -286,7 +310,7 @@ def build(rank, core, T, topo):
             ts(wt(0, qv, r), ap("CG8"), ap("g8m", r, r + 1), EQ, ap("ws", qv, qv + 1), MUL)
         ts(wt(1, qv, 3), ap("CG8"), ap("g8p"), EQ, ap("ws", qv, qv + 1), MUL)
     iota(ap("CG2"), [[8, 8], [1, 2], [0, 8]], 0); iota(ap("CZ"), [[0, 2], [1, 4], [0, 8]], 0); iota(ap("ML"), [[8, 8], [0, 4], [64, 8]], 0)
-    fill(ap("ONEB"), 1.0)
+    fill(ap("ONEB"), 1.0, "G")
     for qv in (0, 1):
         for i in (0, 1):
             ts(wt(2, qv, i), ap("CG2"), ap("g8", i, i + 1), EQ, ap("hwg", qv, qv + 1), MUL)
@@ -299,44 +323,44 @@ def build(rank, core, T, topo):
         keep(ap("RL", 128 * r, 128 * r + 128), "ONEB", [[16, 8], [0, 8], [8, 2]], r, EQ, -1)
     ts(ap("s1I"), ap("sI"), 1, SHR); cp(ap("s1F"), ap("s1I"))
     act(ap("PZL"), ap("CZ"), AF.Abs, bias=ap("ns2"), scale=8 * BIG); act(ap("PZL"), ap("PZL"), AF.Identity, bias=ap("s1F"))
-    ts(ap("CJ"), ap("IC", 0, 64, 2), ap("sge8"), ADD)
     for o, v in (("IDB", 1.0), ("IDH", 1.0), ("IDN", -1.0), ("IDHN", -1.0)):
         ts(ap(o), ap("IC", 0, 128), ap("pF"), EQ, v, MUL)
-    act(ap("I256"), ap("IDB"), AF.Copy, scale=-256.0)
+    act(ap("I255"), ap("IDB"), AF.Copy, scale=-255.0)
     act(ap("NM"), ap("CS"), AF.Abs, bias=ap("nsB"), scale=BIG)
     act(ap("PZ4"), ap("C3"), AF.Abs, bias=ap("ns2"), scale=8 * BIG); act(ap("RS4"), ap("C3"), AF.Relu, bias=8 * BIG, scale=-8 * BIG)
     act(ap("MWR"), ap("NM"), AF.Relu, bias=1.0, scale=-1.0); act(ap("RST"), ap("CS"), AF.Sign)
-    act(ap("TRH"), ap("CS", 0, 64), AF.Relu, bias=ap("s1T"), scale=-16384.0)
-    for o, v in (("B512", 1024.0), ("B256", 16.0), ("BLK8", 8192.0), ("BLKN", -1.0)):
+    act(ap("TRH"), ap("CS", 0, 64), AF.Relu, bias=ap("s1T"), scale=-16384.0); act(ap("lTR", 0, 64), ap("IC", 0, 64), AF.Relu, bias=ap("s1T"), scale=-16384.0)
+    for o, v in (("B512", 1024.0), ("B256", 256.0), ("BLK8", 8192.0), ("BLKN", -1.0)):
         act(ap(o), ap("BLKB"), AF.Copy, scale=v)
     ts(ap("ksc"), ap("kmi"), -2048.0, ADD); ts(ap("kh"), ap("CS", 0, 16), ap("sF"), EQ, ap("ksc"), MUL)
     mm([(ap("MS", 16, 32), ap("BLKH"), ap("kh"), True, True)])
     ts(ap("KR"), ap("MS", 16, 32), 2048.0, ADD)
+    ts(ap("LS"), ap("IC", 0, 16), 0.0, MUL, ap("sF"), ADD); cp(ap("LC"), ap("IC", 0, 16))
+    act(ap("KRX"), ind(ap("KR"), ap("LC")), AF.Copy)
+    fill(ap("RS5"), 0.0, "G"); fill(ap("RS5", 0, 128, 8), 8 * BIG, "S"); fill(ap("R5", 1, 128, 2), 8 * BIG, "S")
     ts(ap("th8h"), ap("th8"), -2048.0, ADD)
     mm([(ap("MS", 8, 9), ap("REP8"), ap("th8h"), True, True)])
     ts(ap("th16"), ap("MS", 8, 9), 2047.5, ADD, 1024.0, MUL)
     ts(ap("JW0"), ap("IC", 0, 256, 16), ap("sF"), ADD)
     act(ap("DRS"), ap("CS"), AF.Copy, bias=-BIG, scale=0.0); ts(ap("DRS", 0, 256, 16), ap("JW0"), S - 2047.0, ADD)
-    fill(ap("DR1"), -BIG); ts(ap("DR1", 0, 64, 16), ap("JW0", 0, 4), 2.0, MUL, 258.0, ADD)
+    fill(ap("DR1"), -BIG, "G"); ts(ap("DR1", 0, 64, 16), ap("JW0", 0, 4), 2.0, MUL, 258.0, ADD)
     ts(ap("c8h"), ap("c8"), -2048.0, ADD)
     mm([(ap("CT", 0, 256), ap("IDB"), ap("NM"), True, False), (ap("CT", 0, 256), ap("REP8"), ap("c8h"), False, True)])
     scan(ap("CM2"), ap("DRS"), ap("CT", 0, 256), MAX, MIN); ts(ap("CL0"), ap("CM2", 15, 256, 16), 2048.0, ADD)
     mm([(ap("HR", 0, 256), ap("REP8"), ap("c8h"), True, True)])
-    act(ap("CX0", 0, 256), ap("HR", 0, 256), AF.Copy, bias=2048.0)
+    act(ap("CX0", OLD, OLD + L), ap("HR", 0, 256), AF.Copy, bias=2048.0)
     for k in "01":
-        fill(ap("TX" + k, L, NEW), 0.0); fill(ap("WX" + k, L, NEW), 0.0); act(ap("CX" + k, L, NEW), ap("IC", 0, NEW - L), AF.Copy)
-    act(ap("TX0", 0, 128), ind(ap("TP"), ap("CL0", 0, 8)), AF.Copy); cp(ap("TX0", 128, 256), ind(ap("TP"), ap("CL0", 8, 16)))
+        fill(ap("TX" + k, OLD + L, END), 0.0, "G" if k == "1" else "S"); fill(ap("WX" + k, OLD + L, END), 0.0, "G"); act(ap("CX" + k, OLD + L, END), ap("IC", 0, END - OLD - L), AF.Copy)
+    act(ap("TX0", OLD, OLD + 128), ind(ap("TP"), ap("CL0", 0, 8)), AF.Copy); cp(ap("TX0", OLD + 128, OLD + L), ind(ap("TP"), ap("CL0", 8, 16)))
 
-    for r in range(8):
-        keep(ap("SLP", 128 * r, 128 * r + 128), "B512", [[0, 16], [1, 8]], -r)
-    ts(ap("g16"), ap("IC", 0, 16), ap("gx8"), ADD, ap("gx8"), ADD)
-    for s in range(16):
-        if s < GSEL:
-            keep(ap("SEL", 128 * s, 128 * s + 128), "B256", [[0, 8], [1, 16]], -s)
-        else:
-            ts(ap("SEL", 128 * s, 128 * s + 128), ap("IC", 0, 128), ap("g16", s, s + 1), EQ, 16.0, MUL)
-    for r in range(4):
-        keep(ap("SLQ", 128 * r, 128 * r + 128), "B512", [[0, 32], [1, 4]], -r)
+    keep(ap("SEL", 0, 128), "B512", [[0, 8], [1, 16]], -15); fill(ap("SEL", 128, 144), 0.0, "S")
+    keep(ap("SLQ", 0, 128), "B512", [[0, 32], [1, 4]], -3); fill(ap("SLQ", 128, 144), 0.0, "S")
+
+    def sel(s):
+        return ap("SEL", 15 - s, 143 - s)
+
+    def slq(r):
+        return ap("SLQ", 3 - r, 131 - r)
     keep(ap("TRIMB"), "BLKN", [[-1, 128]], 0, GE, 1)
     for k in range(4):
         act(ap("WTAB", 128 * k, 128 * k + 128), ap("C3"), AF.Copy, bias=4.0)
@@ -344,42 +368,32 @@ def build(rank, core, T, topo):
         wtab = dma(ap("WTAB", 512 * k, 512 * k + 512), ap("WTAB", 0, 512), 7.0); later(ldu, len(ops) - 2)
     ts(ap("c8i"), ap("c8"), 3, AND); ts(ap("c8w"), ap("c8i"), 4.0, ADD)
     mm([(ap("DB", 0, 256), ap("REP8"), ap("c8w"), True, True)])
-    act(ap("WX0", 0, 256), ap("DB", 0, 256), AF.Copy)
-    ts(ap("pen2"), ap("IC", 0, 2), ap("sge8"), NE, 2 * BIG, MUL); ts(ap("pen4"), ap("IC", 0, 4), ap("s2F"), NE, 2 * BIG, MUL)
-    for h in range(2):
-        ts(ap("MP", h, 512, 2), ap("IC"), ap("pen2", h, h + 1), ADD)
-    for h in range(4):
-        ts(ap("MS1", h, 256, 4), ap("IC", 192, 256), ap("pen4", h, h + 1), ADD)
+    act(ap("WX0", OLD, OLD + L), ap("DB", 0, 256), AF.Copy)
+    iota(ap("MS1"), [[1, 64], [0, 4]], 192)
     ts(ap("J256"), ap("JW0"), 256.0, ADD)
     ts(ap("EE", 510, 512), ap("IC", 0, 2), 0.0, MUL, 1282.0, ADD)
-    fill(ap("one16"), 1.0); fill(ap("P2", 0, 16), 0.5); scan(ap("P2", 16, 32), ap("P2", 0, 16), ap("one16"), MUL, MAX, 2.0 ** 29)
+    fill(ap("one16"), 1.0, "S"); fill(ap("P2", 0, 16), 0.5, "S"); scan(ap("P2", 16, 32), ap("P2", 0, 16), ap("one16"), MUL, MAX, 2.0 ** 29)
     tt(ap("P2", 32, 48), ap("P2", 16, 32), ap("MWR", 0, 16), MUL); scan(ap("P2", 0, 16), ap("one16"), ap("P2", 32, 48)); ts(ap("rF"), ap("P2", 15, 16), -2.0, MUL)
     act(ap("W2"), ap("BLKB"), AF.Identity, scale=ap("P2", 15, 16)); act(ap("B30"), ap("BLKB"), AF.Copy, scale=2.0 ** 30)
     act(ap("NM2"), ap("NM", 0, 128), AF.Identity, bias=ap("rF"), scale=2.0 ** 23)
     ts(ap("EE", 0, 1), ap("pF"), 0.0, MUL)
-    fill(ap("oneR"), 1.0); fill(ap("C255"), 255.0)
-    act(ap("T5"), ap("IC"), AF.Copy, bias=2.0, scale=5.0)
+    fill(ap("oneR"), 1.0, "G"); fill(ap("C255"), 255.0, "G")
     ts(ap("lNM"), ap("NM", 0, 64), -2048.0, ADD)
     LR = (0, 64, 112, 144)
-    fill(ap("lTR"), 0.0)
-    for c in range(4):
-        cp(ap("lTR", LR[c], LR[c] + 16), ap("TRH", 0, 16))
-    rng = []
-    for c in range(16):
-        lo = -((-(64 * c + 2)) // 5); hi = min(256, -((-(112 * c + 110)) // 5))
-        rng.append((lo, hi))
-    act(ap("kz1", 0, rng[15][0]), ap("IC", 0, rng[15][0]), AF.Copy, bias=128.0 + 30.5 / 64, scale=5.0 / 64); fill(ap("kz1", rng[15][0], 256), 144.0)
-    act(ap("kz2"), ap("IC"), AF.Copy, bias=160.0 - 53.5 / 112, scale=5.0 / 112)
-    mm([(ap("JP", 0, 256), ap("IDB"), ap("kz1"), True, False), (ap("JP", 0, 256), ap("IDB"), ap("kz2"), False, True)])
-    act(ap("KONST"), ap("JP", 0, 256), AF.Copy, bias=-288.0)
-    fill(ap("RJ", 0, 16), 300.0)
+    rng = [(11 * c, min(254, 20 * c + 19)) for c in range(16)]
+    ts(ap("THR"), ap("JW0"), 5.0, MUL, 66.5, ADD)
+    ts(ap("KJ", 16, 32), ap("IC", 0, 16), 31.0, MUL, 19.0, ADD); ts(ap("KJ", 32, 48), ap("IC", 0, 16), 11.0, MUL, 254.0, ADD)
+    tt(ap("KJ", 0, 16), ap("KJ", 16, 32), ap("KJ", 32, 48), MIN)
+    keep(ap("SH1"), "B256", [[-1, 128]], 1, EQ, 1); keep(ap("SH2"), "B256", [[-1, 128]], -15, EQ, 1)
+    if ZERO:
+        fill(ap("ZZ"), 0.0)
+    if SLOTS:
+        fill(ap("FS"), 0.0, "G")
+    fill(ap("K256"), 256.0, "G"); fill(ap("JB", 0, 16), -260.0, "G"); fill(ap("DJ"), 0.0); fill(ap("WN", 256, 512), BIG, "G")
+    iota(ap("X", S, ZD), [[0, ZD - S]], 0); iota(ap("STB"), [[0, 128]], 1024)
     cp(ap("IC64"), ap("IC", 0, 64)); ts(ap("PF64"), ap("IC", 0, 64), 5.0, MUL, 1344.0, ADD)
-    act(ap("HT", 256, 512), ap("IC"), AF.Copy); fill(ap("HT", 512, 528), UNF); fill(ap("lHT", 512, 528), UNF)
-    fill(ap("RI", 0, 64), 8 * BIG); fill(ap("US", S, 4480), 0.0)
-
-    def sel(bank, o, name, lo, n):
-        for k in range(0, 16, 2):
-            mm([(ap(bank, o, o + n), ap("SEL", 128 * s, 128 * s + 128), ap(name, lo + s, lo + s + 16 * (n - 1) + 1, 16), s == 0, s == 15) for s in range(k, k + 2)])
+    act(ap("HT", 256, 512), ap("IC"), AF.Copy); fill(ap("HT", 512, 528), UNF, "G"); fill(ap("lHT", 512, 528), UNF, "G")
+    fill(ap("RI", 0, 64), 8 * BIG, "S"); fill(ap("US", S, 4480), 0.0, "G")
 
     for t in range(RO):
         start[0] = len(ops)
@@ -393,79 +407,92 @@ def build(rank, core, T, topo):
         lst = []
         for qv in (0, 1):
             for r in range(4):
-                lst.append((ap("UVP", 64 * qv, 64 * qv + 64), wt(0, qv, r), ap(tx, r, r + 253, 4), False, False))
-            lst.append((ap("UVP", 64 * qv, 64 * qv + 64), wt(1, qv, 3), ap(tx, 4, 257, 4), False, qv == 1))
+                lst.append((ap("UVP", 64 * qv, 64 * qv + 64), wt(0, qv, r), ap(tx, OLD + r, OLD + r + 253, 4), False, False))
+            lst.append((ap("UVP", 64 * qv, 64 * qv + 64), wt(1, qv, 3), ap(tx, OLD + 4, OLD + 257, 4), False, qv == 1))
+        if ZERO:
+            lst = [(ap("UVP", 0, 128), ap("ZZ"), ap(tx, OLD, OLD + 128), False, False)] * ZERO + lst
         mm(lst)
-        mm([(ap("ZP", 0, 256), ap("PL"), ap(tx, 0, 256), True, False), (ap("ZP", 0, 256), ap("PR"), ap(tx, 1, 257), False, True)])
-        zb = [act(ap("ZB", 256 * k, 256 * k + 256), ap("ZP", 0, 256), AF.Copy) for k in range(2)]
+        mm([(ap("ZP", 0, 256), ap("PL"), ap(tx, OLD, OLD + L), True, False), (ap("ZP", 0, 256), ap("PR"), ap(tx, OLD + 1, OLD + 257), False, True)])
+        zb = [act(ap("ZB", 256 * k, 256 * k + 256), ap("ZP", 0, 256), AF.Copy, bias=-255.0 if t > 1 else 0.0) for k in range(2)]
+        under = ap("UF" if t > 1 else "US", 0, S)
+        lent = "UF" if t else "US"
+        if t == 2:
+            iota(ap("US", 0, 512), [[0, 512]], 255)
+            for k in range(512, S, 512):
+                dma(ap("US", k, k + 512), ap("US", 0, 512), 7.0, [ap("ZB")])
+        if last:
+            for k in range(0, S, 2048):
+                dma_add(ap("US", k, k + 2048), ap("UF", k, k + 2048), 7.0, [ap("ZB")])
         scan(ap("UVS"), ap("RS4"), ap("UVP", 0, 128), ADD, MIN); later(wtab)
         ts(ap("UVA"), ap("UVS", 3, 128, 4), 4095, AND)
         tt(ap("UVW"), ap("UVA", 0, 16), ap("UVA", 16, 32), MUL)
-        ts(ap("UVA", 16, 32), ap("UVW"), 5, SHR)
-        cp(ap("UQ"), ap("UVA"))
-        for c in range(16):
-            if c >= 16 - NS:
-                act(ap3("HF", 0, 16, c), ap("KR"), AF.Identity, bias=ap("UQ", 16 + c, 17 + c), scale=ap("UQ", c, c + 1)); later(*zb[:ZBF])
-            else:
-                ts(ap3("HV", 0, 16, c), ap("KR"), ap("UQ", c, c + 1), MUL, ap("UQ", 16 + c, 17 + c), ADD)
-        cp(ap3("HV", 0, 16, 16 - NS, 16), ap3("HF", 0, 16, 16 - NS, 16))
-        for a, b in ((0, EARLY), (EARLY, 16)):
-            ts(ap("HI", 16 * a, 16 * b), ap3("HV", a, b, 0, 16), 4095, AND)
+        ts(ap("UVQ"), ap("UVW"), 5, SHR)
+        for a, b in EARLY:
+            tt(ap("KU", 16 * a, 16 * b), ind(ap("UVA", 0, 16), ap("LS", a, b)), ap("KRX", 16 * a, 16 * b), MUL)
+            tt(ap("HV", 16 * a, 16 * b), ind(ap("UVQ"), ap("LS", a, b)), ap("KU", 16 * a, 16 * b), ADD)
+            ts(ap("HI", 16 * a, 16 * b), ap("HV", 16 * a, 16 * b), 4095, AND)
             cp(ap("HO", 16 * a, 16 * b), ap("HI", 16 * a, 16 * b))
-        scan(ap("EE", 256, 510), ap("oneR", 0, 254), ap(wx, 0, 254)); cp(ap("EE", 1, 256), ap("EE", 256, 511))
-        sel("MS", 32, "EE", 0, 32)
-        slots = [lambda: ts(ap("FI"), ap("MS", 32, 64), 0.2 / 256, MUL, 256.0, MIN), lambda: act(ap("EB"), ap("MS", 48, 64), AF.Copy, bias=0.5, scale=-1.0 / 256),
+        scan(ap("EE", 256, 510), ap("oneR", 0, 254), ap(wx, OLD, OLD + 254)); cp(ap("EE", 1, 256), ap("EE", 256, 511))
+        for k in range(0, 16, 4):
+            mm([(ap("MS", 32, 64), sel(s), ap("EE", s, s + 497, 16), s == 0, s == 15) for s in range(k, k + 4)])
+        slots = [lambda: ts(ap("FI"), ap("MS", 32, 64), 0.2 / 16384, MUL, 256.0, MIN),
                  lambda: tt(ap("NW"), ap("FI", 16, 32), ap("FI", 0, 16), SUB),
-                 lambda: act(ap("RI", 1, 64, 4), ap("NW"), AF.Copy, bias=512.0 - 2 * BIG, scale=4 * BIG)]
-        banks = ("DA", "DB", "JP", "HR", "UVP", "CT", "ZP")
-        prev = {}
+                 lambda: act(ap("RI", 1, 64, 4), ap("NW"), AF.Copy, bias=512.0 - 2 * BIG, scale=4 * BIG),
+                 lambda: ts(ap("RS5", 7, 128, 8), ap("NW"), b16, SUB)]
+        prev, where, fours = {}, {}, 0
+        minus = [m + i for step, m, k in PROBE if step == "minus" for i in range(k)]
         for step, m, k in PROBE:
-            x, d = ap("X", 256 * m, 256 * (m + k)), ap(BYS.get(m, "ZP"), 512 - 256 * k, 512)
+            x = ap("X", 256 * m, 256 * (m + k))
             if step == "gather" and m in BYS:
-                j = act(x, ind(ap("US", 0, S), ap("HO", 16 * m, 16 * (m + k))), AF.Copy)
+                d = ap(BYS[m], 512 - 256 * k, 512)
+                for i in range(k):
+                    where[m + i] = (d[1], d[2] + 256 * i)
+                j = act(x, ind(under, ap("HO", 16 * m, 16 * (m + k))), AF.Copy)
                 mm([(d, ap("IDN"), ap("ZB", 0, 256 * k), True, False)]); mm([(d, ap("IDB"), x, False, True)])
             elif step == "gather":
-                j = tt(x, ind(ap("US", 0, S), ap("HO", 16 * m, 16 * (m + k))), ap("ZB", 0, 256 * k), SUB)
-            elif step == "abs":
-                w = min(ABSW, 256 * k)
-                for lo in range(0, 256 * k, w):
-                    y = d if m in BYS else x
-                    j = absl = act(ap("A", 256 * m + lo, 256 * m + lo + w), ap(y[1], y[2] + lo, y[2] + lo + w), AF.Abs)
-                    if lo + w < 256 * k:
-                        later(prev["S"]); prev["S"] = j
-            elif step == "slots":
-                j = slots[m]()
-            else:
-                mm([(ap(banks[m], 0, 64 * k), ap("IDB"), ap("MP", 128 * m, 128 * m + 64 * k), True, False)])
-                for h in range(k):
-                    lo = 1024 * m + 512 * h
-                    mm([(ap(banks[m], 64 * h, 64 * h + 64), ap("SLP", 128 * r, 128 * r + 128), ap("A", lo + r, lo + 512, 8), False, h == k - 1 and r == 7) for r in range(8)])
-                if m == 0:
-                    j = ts(ap("RM", 0, 128), ap(banks[m], 0, 128), b16, MIN)
-                elif k == 2:
-                    j = tt(ap("RM", 128 * m, 128 * m + 128), ap(banks[m], 0, 128), ap("RM", 128 * m - 128, 128 * m), MIN)
+                j = tt(x, ind(under, ap("HO", 16 * m, 16 * (m + k))), ap("ZB", 0, 256 * k), SUB)
+            elif step == "minus":
+                j = ts(ap("A", 256 * m, 256 * (m + k)), x, 0.0, MIN, -2.0, MUL)
+            elif step == "fold":
+                for h in range(2):
+                    j = tt(ap("RI", 2 + h, 64, 4), ap("RM", 128 + 32 * h, 144 + 32 * h), ap("RM", 144 + 32 * h, 160 + 32 * h), MIN)
+            elif step == "four":
+                d = SUMS[m]
+                mm([(ap(d, 0, 64), ap("IDB"), ap("IC", 16 * m, 16 * m + 64), True, False)])
+                own = [i for i in range(m, m + 4) if i in minus]
+                if own:
+                    lo, hi = own[0], own[-1] + 1
+                    mm([(ap(d, 16 * (lo - m), 16 * (hi - m)), sel(r), ap("X", 256 * lo + r, 256 * hi, 16), False, False) for r in range(16)])
+                mm([(ap(d, 0, 64), sel(r), ap("A", 256 * m + r, 256 * m + 1024, 16), False, r == 15) for r in range(16)])
+                y = ap("RM", fours, fours + 64)
+                j = tt(y, ap(d, 0, 64), ap("RM", fours - 64, fours), MIN) if fours else ts(y, ap(d, 0, 64), b16, MIN)
+                fours += 64
+            elif step == "single":
+                d = ap(SUMS[m], 0, 64)
+                mm([(d, ap("IDB"), ap("MS1", 64 * (m - 12), 64 * (m - 11)), True, False), (d, ap("IDB"), ap("PZ4", 0, 64), False, False)])
+                if m in minus:
+                    mm([(d, slq(r), ap("X", 256 * m + r, 256 * m + 256, 4), False, False) for r in range(4)])
+                mm([(d, slq(r), ap("A", 256 * m + r, 256 * m + 256, 4), False, r == 3) for r in range(4)])
+                if k == 0 and MERGE:
+                    j = cp(ap("RI", 64, 128), d)
                 else:
-                    later_v = tt(ap("RM", 448, 512), ap("RM", 256, 320), ap("RM", 320, 384), MIN); later(prev["V"]); prev["V"] = later_v
-                    j = tt(ap("RM", 384, 448), ap(banks[m], 0, 64), ap("RM", 448, 512), MIN)
-            if ops[j]["q"] in prev:
-                ops[j].setdefault("after", []).append(prev[ops[j]["q"]])
-            prev[ops[j]["q"]] = j
-        if PAIRS == 6:
-            tt(ap("RM", 384, 448), ap("RM", 256, 320), ap("RM", 320, 384), MIN)
-        for k in range(2):
-            lo = 384 + 32 * k
-            tt(ap("RI", 2 + k, 64, 4), ap("RM", lo, lo + 31, 2), ap("RM", lo + 1, lo + 32, 2), MIN)
-        for n in range(16 - 2 * PAIRS):
-            m = 2 * PAIRS + n
-            d = banks[PAIRS - 3 + n]
-            mm([(ap(d, 0, 64), ap("IDB"), ap("MS1", 64 * (m - 12), 64 * (m - 11)), True, False)])
-            mm([(ap(d, 0, 64), ap("SLQ", 128 * r, 128 * r + 128), ap("A", 256 * m + r, 256 * m + 256, 4), False, r == 3) for r in range(4)])
-            tt(ap("RI", 64 * n + 64, 64 * n + 128), ap(d, 0, 64), ap("RI", 64 * n, 64 * n + 64), MIN)
-        scan(ap("KS"), ap("RS4", 0, 64), ap("RI", 64 * n + 64, 64 * n + 128), ADD, MIN)
-        key = ap("KS", 3, 64, 4)
-        iota(ap("ZA", 0, 64), [[0, 64]], 1024)
+                    y = ap("RI", 64 * k, 64 * k + 64)
+                    if k == MERGE and k:
+                        tt(ap("RI", 256, 320), ap("RI", 0, 64), y, MIN); y = ap("RI", 256, 320)
+                    j = tt(ap("RI", 64 * k + 64, 64 * k + 128) if k < 3 else ap("R5", 0, 128, 2), d, y, MIN)
+            elif step == "abs":
+                j = act(ap("A", 256 * m, 256 * (m + k)), ap(where[m][0], where[m][1], where[m][1] + 256 * k) if m in where else x, AF.Abs)
+            else:
+                j = slots[m]()
+            if step in KEPT:
+                if ops[j]["q"] in prev:
+                    ops[j].setdefault("after", []).append(prev[ops[j]["q"]])
+                prev[ops[j]["q"]] = j
+        scan(ap("K5"), ap("RS5"), ap("R5"), ADD, MIN)
+        key = ap("K5", 6, 128, 8)
+        iota(ap("ZA", 0, 64), [[0, 64]], 768)
         mm([(ap("MS", 64, 80), ap("IDH"), ap("J256"), True, False)])
-        ts(ap("PO"), key, b16, GE); tt(ap("PN"), ap("PO"), ap("NW"), MUL); tt(ap("POJ"), ap("PO"), ap("J256"), MUL)
+        ts(ap("PN"), ap("K5", 7, 128, 8), 0.0, MAX); ts(ap("PO"), key, b16, GE); tt(ap("POJ"), ap("PO"), ap("J256"), MUL)
         scn = scan(ap("SC"), ap("one16"), ap("PN"))
         ts(ap("HT", 0, 256), ap("HI"), -2047.0, ADD); later(scn)
         mm([(ap("MS", 64, 80), ap("TRIMB"), ap("PN"), False, False), (ap("MS", 64, 80), ap("IDHN"), ap("POJ"), False, False)])
@@ -479,7 +506,7 @@ def build(rank, core, T, topo):
         scan(ap("HS"), ap("RST"), ap("HM"))
         mm([(ap("HR", 0, 256), ap("BLKH"), ap("HM"), True, True)])
         cp(ap("HRH"), ap("HR", 0, 256))
-        hsx = act(ap(cx, NEW, NEW + L), ap("HR", 0, 256), AF.Copy, bias=2047.0)
+        hsx = act(ap(cx, 0, L), ap("HR", 0, 256), AF.Copy, bias=2047.0)
         act(ap("UR"), ap("HR", 0, 256), AF.Relu, bias=-3000.0)
         tt(ap("HD"), ap("HS", 15, 256, 16), ap("DRS", 0, 256, 16), MIN)
 
@@ -490,12 +517,12 @@ def build(rank, core, T, topo):
             if scalar:
                 x = ap("EX", 128 * (k % 8), 128 * (k % 8) + hi - lo)
                 act(x, ap("HR", lo, hi), AF.Abs, bias=own, scale=-1.0)
-                if k >= 16:
-                    later(*made)
                 made.append(act(e, x, AF.Relu, bias=1.0, scale=-1.0))
             else:
                 ts(e, ap("HRH", lo, hi), own, EQ)
-        for h, d in enumerate(("CT", "DB")):
+        if t:
+            put("G", lambda g, v=(t + 1) * TINY: g.affine_select(res(ap("STP")), res(ap("ZERO")), [[0, 128]], GT, v, 0, 0), [ap("ZERO")], [ap("STP")], (0.18, 256, 0, 0))
+        for h, d in ((1, "CT"), (0, "DB")):
             mm([(ap(d, 256, 384), ap("IDB"), ap("NM2", 0, 128), True, False)])
             for c in range(8):
                 equal(8 * h + c, 128 * h + 16 * c, 128 * h + 128, 8 * h + c, 16 - 2 * c - h <= SE)
@@ -505,36 +532,44 @@ def build(rank, core, T, topo):
             scan(ap("WS", 128 * h, 128 * h + 128), ap("DRS", 128 * h, 128 * h + 128), ap(d, 256, 384), MAX, MIN)
             tt(ap("LA", 8 * h, 8 * h + 8), ap("WS", 128 * h + 15, 128 * h + 128, 16), ap("HD", 8 * h, 8 * h + 8), MAX)
             ts(ap("LO", 8 * h, 8 * h + 8), ap("LA", 8 * h, 8 * h + 8), 2047.0, ADD)
-            lay = cp(ind(ap("US", 0, ZD), ap("LO", 8 * h, 8 * h + 8)), ap("C255", 0, 128))
+            if t:
+                act(ind(ap("UF", 0, ZD), ap("LO", 8 * h, 8 * h + 8)), ap("ZERO" if h else "STP"), AF.Silu)
+            if last or not t:
+                cp(ind(ap("US", 0, ZD), ap("LO", 8 * h, 8 * h + 8)), ap("C255", 0, 128))
             act(ap("WD", 128 * h, 128 * h + 128), ap(d, 256, 384), AF.Sign)
-        if not last:
-            ts(ap("HL"), ap("HS", 15, 256, 16), 2047.0, ADD, 4095.0, MIN)
+        ts(ap("HL"), ap("HS", 15, 256, 16), 2047.0, ADD, 4095.0, MIN)
         mm([(ap("DA", 256, 512), ap("IDH"), ap("EE", 0, 256), True, True)])
         act(ap("E32"), ap("DA", 256, 512), AF.Copy, bias=64.0)
-        mm([(ap("JP", 0, 256), ap("BLKB"), ap("KONST"), True, False)])
-        off = 0
-        for c in range(16):
-            lo, hi = rng[c]
-            act(ap("SG", off, off + hi - lo), ap("T5", lo, hi), AF.Sign, bias=ap("EB", c, c + 1)); later(absl)
-            mm([(ap("JP", lo, hi), ap("BLKB"), ap("SG", off, off + hi - lo), False, c == 15)]); later(ofm)
-            off += (hi - lo + 15) // 16 * 16
-        act(ap("RJ", 1, 257), ap("JP", 0, 256), AF.Relu, bias=254.0, scale=-0.5)
-        mm([(ap("DA", 256, 512), ap("IDB"), ap("RJ", 0, 256), True, False)]); mm([(ap("DA", 256, 512), ap("IDN"), ap("RJ", 1, 257), False, True)])
-        fst = act(ap("FIRST"), ap("DA", 256, 512), AF.Sign)
-        sel("JP", 256, "RJ", 1, 16)
-        jl = ts(ap("JL"), ap("JP", 256, 272), -1.0 / 256, MUL, 254.0, ADD); jw = act(ap("JW"), ap("JP", 256, 272), AF.Copy, bias=254.0, scale=-1.0 / 256)
-        mm([(ap("MS", 256, 512), ap("IDB"), ap("UR"), True, False)])
-        for c in range(8):
-            if c == SX:
-                wdm = mm([(ap("MS", 256, 512), ap("BLKB"), ap("WD"), False, False)])
-            equal(16 + c, 128, 256, c, c < SX)
-            if c >= SX:
-                later(lay)
-            crs = mm([(ap("MS", 384, 512), ap("BLK8"), ap3("ET", 16 + c, 17 + c, 0, 128), False, c == 7)])
-        wn = act(ap("WN"), ap("MS", 256, 512), AF.Relu, bias=NEW / 32, scale=-NEW / 512)
-        mm([(ap("UVP", 128 + 32 * qv, 160 + 32 * qv), wt(2, qv, i), ap("ZL%d" % t, i, i + 63, 2), i == 0, i == 1) for qv in (0, 1) for i in (0, 1)])
+        act(ap("EA", 0, 64), ap("PF64"), AF.Copy)
+        act(ind(ap("EA"), ap("OF")), ap("E32"), AF.Silu)
+        scan(ap("EQ"), ap("TRH", 0, 64), ap("EA", 0, 64), MAX, MIN)
+        ts(ap("FAI"), ap("EQ", 15, 64, 16), -64.0, ADD, 0.2, MUL)
+        if SLOTS:
+            cp(ap("FS", 0, 4), ap("FAI"))
+            send("FL%d" % t, ap("FS"), "fai%d" % t, "lf", lender)
+        for c, (lo, hi) in enumerate(rng):
+            act(ap("SG", 128 * c, 128 * c + hi - lo), ap("E32", lo + 1, hi + 1), AF.Sign, bias=ap("THR", c, c + 1), scale=-1.0, total=ap("SJ", c, c + 1))
+        tt(ap("J2"), ap("SJ"), ap("KJ", 0, 16), ADD)
+        ts(ap("JB", 16, 32), ap("J2"), 0.5, MUL, -256.0, ADD); ts(ap("DJ", 0, 256, 16), ap("J2"), 0.5, MUL, float(OLD), ADD)
+        mm([(ap("DA", 256, 272), ap("IDB"), ap("K256"), True, False), (ap("DA", 256, 272), ap("I255"), ap("JB", 16, 32), False, False),
+            (ap("DA", 256, 272), ap("SH1"), ap("JB", 16, 32), False, False), (ap("DA", 256, 272), ap("SH2"), ap("JB", 15, 31), False, True)])
+        tt(ap("JX"), ap("DA", 256, 272), ap("JB", 16, 32), MAX); ts(ap("JL"), ap("JX"), 256.0, ADD)
+        if t:
+            act(ap("MF"), ind(ap("UF", 0, S), ap("HL", 8, 16)), AF.Relu, bias=-2000.0 * t - 1000.0, scale=4000.0 / TINY)
+        else:
+            cp(ind(ap("X"), ap("LO", 0, 8)), ap("STB"))
+            act(ap("MF"), ind(ap("X"), ap("HL", 8, 16)), AF.Relu, bias=-256.0)
+        mm([(ap("MS", 256, 512), ap("IDB"), ap("IC"), True, False)]); mm([(ap("MS", 256, 512), ap("IDB"), ap("UR"), False, False)])
+        mm([(ap("MS", 256, 512), ap("B512"), ap("WD"), False, False)])
+        mm([(ap("MS", 384, 512), ap("IDB"), ap("MF"), False, True)])
+        wn = act(ap("WN", 0, 256), ap("MS", 256, 512), AF.Copy, bias=-14336.0)
+        if t > 1:
+            mm([(ap("UVP", 128 + 32 * qv, 160 + 32 * qv), wt(2, qv, i), ap("C255", 0, 32), qv + i == 0, False) for qv in (0, 1) for i in (0, 1)])
+        mm([(ap("UVP", 128 + 32 * qv, 160 + 32 * qv), wt(2, qv, i), ap("ZL%d" % t, i, i + 63, 2), t < 2 and qv + i == 0, qv + i == 2) for qv in (0, 1) for i in (0, 1)])
+        for k in range(0, 8, 4):
+            mm([(ap("JP", r, 512, 8), ap("IDB"), ap("ZL%d" % t), r == 0, r == 7) for r in range(k, k + 4)])
         for k in range(2):
-            act(ap("ZT", 256 * k, 256 * k + 256), ind(ap("ZL%d" % t), ap("CJ", 16 * k, 16 * k + 16)), AF.Copy)
+            act(ap("ZT", 256 * k, 256 * k + 256), ap("JP", 256 * k, 256 * k + 256), AF.Copy, bias=-255.0 if t == 1 else 0.0)
         cp(ap("lUVS"), ap("UVP", 128, 192))
         ts(ap("lUVA"), ap("lUVS"), 4095, AND)
         tt(ap("lUVW"), ap("lUVA", 0, 32), ap("lUVA", 32, 64), MUL)
@@ -543,20 +578,26 @@ def build(rank, core, T, topo):
         ts(ap("lUQ"), ap("lUVW"), 5, SHR)
         for k in range(2):
             tt(ap("lHV", 32 * k, 32 * k + 32), ap("lKU", 32 * k, 32 * k + 32), ap("lUQ"), ADD)
-        ts(ap("lHI"), ap("lHV"), 4095, AND); lhh = ts(ap("lHH"), ap("lHI"), -2047.0, ADD); cp(ap("lHO"), ap("lHI")); later(lhh, jl)
-        k = act(ap("lX", 768, 768 + LB), ind(ap("US", 0, S), ap("lHO", 48, 48 + LB // 16)), AF.Copy); later(fst, jw)
+        ts(ap("lHI"), ap("lHV"), 4095, AND); cp(ap("lHO"), ap("lHI")); ts(ap("lHH"), ap("lHI"), -2047.0, ADD)
+        k = act(ap("lX", 768, 768 + LB), ind(ap(lent, 0, S), ap("lHO", 48, 48 + LB // 16)), AF.Copy)
         mm([(ap("ZP", 256, 256 + LB), ap("IDN"), ap("ZT", 256, 256 + LB), True, False)]); mm([(ap("ZP", 256, 256 + LB), ap("IDB"), ap("lX", 768, 768 + LB), False, True)])
         for lo, hi in LORD:
+            x = ap3("lY", 0, 8, 0, 32) if lo == 512 and LRELU else ap("lX", lo, hi)
             if lo != 768:
-                tt(ap("lX", lo, hi), ind(ap("US", 0, S), ap("lHO", lo // 16, hi // 16)), ap("ZT", lo % 512, (hi - 1) % 512 + 1), SUB)
-            act(ap3("lA", lo // 32, hi // 32, 0, 32), ap("lX", lo, hi) if lo != 768 else ap("ZP", 256, 256 + LB), AF.Abs); later(k)
+                tt(x, ind(ap(lent, 0, S), ap("lHO", lo // 16, hi // 16)), ap("ZT", lo % 512, (hi - 1) % 512 + 1), SUB)
+            if lo == 512 and LRELU:
+                ts(ap3("lA", lo // 32, hi // 32, 0, 32), x, 0.0, MIN, -2.0, MUL)
+                continue
+            act(ap3("lA", lo // 32, hi // 32, 0, 32), x if lo != 768 else ap("ZP", 256, 256 + LB), AF.Abs); later(k)
             k = len(ops) - 1
-        mm([(ap("CT", 64 * r, 64 * r + 64), ap("RL", 128 * r, 128 * r + 128), ap("lHH"), True, True) for r in range(8)]); later(wdm)
+        mm([(ap("CT", 64 * r, 64 * r + 64), ap("RL", 128 * r, 128 * r + 128), ap("lHH"), True, True) for r in range(8)])
         act(ap("lHT", 0, 512), ap("CT"), AF.Copy); later(k)
         for n in range(4):
             d = ("DA", "DB", "UVP", "HR")[n]
             mm([(ap(d, 64, 128), ap("IDB"), ap("ML", 64 * n, 64 * n + 64), True, False), (ap(d, 64, 128), ap("IDB"), ap("PZL"), False, False)])
-            mm([(ap(d, 64, 128), ap("SLQ", 128 * r, 128 * r + 128), ap3("lA", 8 * n, 8 * n + 8, 8 * r, 8 * r + 8), False, r == 3) for r in range(4)])
+            if n == 2 and LRELU:
+                mm([(ap(d, 64, 128), slq(r), ap3("lY", 0, 8, 8 * r, 8 * r + 8), False, False) for r in range(4)])
+            mm([(ap(d, 64, 128), slq(r), ap3("lA", 8 * n, 8 * n + 8, 8 * r, 8 * r + 8), False, r == 3) for r in range(4)])
             if n < 2:
                 ts(ap("lRM", 64 * n, 64 * n + 64), ap(d, 64, 128), b16, MIN)
             else:
@@ -567,63 +608,73 @@ def build(rank, core, T, topo):
         tt(ap("lHM"), ind(ap("lHT"), ap("lLL")), ap("MWR", 0, 64), MUL)
         scan(ap("lHS"), ap("RST", 0, 64), ap("lHM"))
         reg = [ap(("HR", "ZP")[c // 2], 256 + LR[c], 320 + LR[c] - 16 * c) for c in range(4)]
-        for d, lo, hi in (("HR", 0, 112), ("ZP", 112, 160)):
-            mm([(ap(d, 256 + lo, 256 + hi), ap("IDB"), ap("lTR", lo, hi), True, False)])
         for c in (0, 2):
-            mm([(reg[k], ap("BLKH"), ap("lHM", 16 * k, 64), False, k % 2 == 1) for k in (c, c + 1)]); later(crs - 2 * CLATE)
+            mm([(reg[k], ap("IDB"), ap("lTR", 0, 64 - 16 * k), k == c, False) for k in (c, c + 1)])
+        for c in (0, 2):
+            mm([(reg[k], ap("BLKH"), ap("lHM", 16 * k, 64), False, k % 2 == 1) for k in (c, c + 1)])
         if not last:
             lhl = ts(ap("lHL"), ap("lHS", 15, 64, 16), 2047.0, ADD, 4095.0, MIN)
             act(ap("RS", 0, 64), ind(ap("TP"), ap("lHL")), AF.Copy)
         mm([(ap("CT", 256, 320), ap("IDB"), ap("lNM"), True, False)])
         mm([(ap("CT", 256, 320), ap("IDH"), ap("lHM"), False, False)])
+        if SLOTS:
+            mm([(ap("JP", 0, 64), ap("IDB"), ap("NM", 0, 64), True, False)] + [(ap("JP", s, 64, 16), ap("IDB"), ap("FL%d" % t, 0, 4), False, False) for s in range(16)])
+            ts(ap("lUF"), ap("lHM"), 3000.0, GT, 1024.0, MUL)
+            mm([(ap("JP", 0, 64), ap("IDB"), ap("lUF"), False, False)])
         for c in range(4):
             e = ap("lET", LR[c], LR[c] + 64 - 16 * c)
             ts(e, reg[c], ap("lHS", 16 * c + 15, 16 * c + 16), EQ)
             if c == 1 and not last:
                 later(lhl)
-            lct = mm([(ap("CT", 256 + 16 * c, 320), ap("BLK8"), e, False, c == 3)])
-        scan(ap("RS", 64, 128), ap("DR1"), ap("CT", 256, 320), MAX, MIN)
+            if SLOTS:
+                mm([(ap("JP", 16 * c, 64), ap("BLK8"), e, False, c == 3)])
+            mm([(ap("CT", 256 + 16 * c, 320), ap("BLK8"), e, False, c == 3)])
+        scan(ap("RS", 64, 128), ap("DR1"), ap("JP", 0, 64) if SLOTS else ap("CT", 256, 320), MAX, MIN)
         send("RB%d" % t, ap("RS", 64 * last, 128), "rep%d" % t, "lr", borrower)
         scan(ap("lWS"), ap("DR1"), ap("CT", 256, 320), MAX, MIN)
         ts(ap("lLO"), ap("lWS", 15, 64, 16), 4095.0, ADD)
         if last:
             cp(ap("RSU"), ind(ap("US"), ap("lLO")))
         else:
-            act(ap("RSU"), ind(ap("US"), ap("lLO")), AF.Copy); later(wn)
+            act(ap("RSU"), ind(ap(lent), ap("lLO")), AF.Copy, bias=255.0 if t else 0.0)
         send("RV%d" % t, ap("RSU"), "reu%d" % t, "lu", borrower)
-        lend = cp(ind(ap("US"), ap("lLO")), ap("C255", 0, 64))
+        if last or not t:
+            cp(ind(ap("US"), ap("lLO")), ap("C255", 0, 64))
+        else:
+            act(ind(ap("UF"), ap("lLO")), ap("ZERO", 0, 64), AF.Silu)
+            iota(ap("UF", ZD, 4480), [[0, 4480 - ZD]], -255)
+        if not t:
+            for k in range(0, S, 256):
+                if k < 256 * CONV:
+                    ts(ap("UF", k, k + 256), ap("US", k, k + 256), -255.0, ADD)
+                else:
+                    act(ap("UF", k, k + 256), ap("US", k, k + 256), AF.Copy, bias=-255.0)
+            iota(ap("UF", S, 4480), [[0, 4480 - S]], -255); iota(ap("ZERO"), [[0, 128]], 0); iota(ap("US", ZD, 4480), [[0, 4480 - ZD]], 0)
         if not last:
-            iota(ap("US", ZD, 4480), [[0, 4480 - ZD]], 0)
             mm([(ap("MS", 96, 97), ap("ONEB"), ap("SC", 15, 16), True, True)])
             cp(ap("PPI"), ap("MS", 96, 97)); ts(ap("PPJ"), ap("PPI"), 63, AND); ts(ap("b16b" if t % 2 else "b16a"), ap("PPJ"), 1024.0, MUL, ap("th16"), ADD)
         if t:
-            ts(ind(ap(cx, 0, NEW), ap("OBU")), ap("IC64"), 1.0, MUL, float(S + CAP * (t - 1)), ADD); later(lend)
-            dma(ext("yc", L * (t - 1), L * t), ap(cx, 0, 256, 1, slice(0, 128, 16)), 2.0)
-        tt(ap("FW"), ind(ap("WN"), ap("JL")), ap("FIRST"), MUL)
-        mm([(ap("JP", 0, 256), ap("IDB"), ap("NM"), True, False)]); mm([(ap("JP", 0, 256), ap("I256"), ap("FW"), False, True)])
-        scan(ap("CM2"), ap("DRS"), ap("JP", 0, 256), MAX, MIN)
-        tt(ap("JX"), ap("JW"), ap("CM2", 15, 256, 16), SUB); cp(ap("JL2"), ap("JX"))
+            ts(ind(ap(cx, OLD, END), ap("OBU")), ap("IC64"), 1.0, MUL, float(S + CAP * (t - 1)), ADD); later(scn)
+            dma(ext("yc", L * (t - 1), L * t), ap(cx, OLD, OLD + L, 1, slice(0, 128, 16)), 2.0)
+        tt(ap("FW"), ind(ap("WN"), ap("JL")), ap("NM"), ADD)
+        scan(ap("CMH"), ap("DJ"), ap("FW"), MAX, MIN); cp(ap("JL2"), ap("CMH", 15, 256, 16))
         if not last:
-            act(ap(tx, NEW, NEW + L), ind(ap("TP"), ap("HL")), AF.Copy)
-            act(ap(wx, NEW, NEW + L), ind(ap("WTAB"), ap("HL")), AF.Copy)
-            act(ap(ty, 0, 256), ind(ap(tx), ap("JL2")), AF.Copy)
-            act(ap(wy, 0, 256), ind(ap(wx), ap("JL2")), AF.Copy)
-        act(ap(cy, 0, 256), ind(ap(cx), ap("JL2")), AF.Copy)
-        act(ap("EA", 0, 64), ap("PF64"), AF.Copy)
-        if EAS:
-            act(ind(ap("EA"), ap("OF")), ap("E32"), AF.Silu)
-        else:
-            cp(ind(ap("EA"), ap("OF")), ap("EE", 0, 256)); later(lend)
-        scan(ap("EQ"), ap("TRH", 0, 64), ap("EA", 0, 64), MAX, MIN)
-        ts(ap("FAI"), ap("EQ", 15, 64, 16), -64.0 * EAS, ADD, 0.2, MUL)
+            act(ap(tx, 0, L), ind(ap("TP"), ap("HL")), AF.Copy)
+            act(ap(wx, 0, L), ind(ap("WTAB"), ap("HL")), AF.Copy)
+            act(ap(ty, OLD, OLD + L), ind(ap(tx), ap("JL2")), AF.Copy)
+            act(ap(wy, OLD, OLD + L), ind(ap(wx), ap("JL2")), AF.Copy)
+        act(ap(cy, OLD, OLD + L), ind(ap(cx), ap("JL2")), AF.Copy)
         rb = "RB%d" % t
-        tt(ap("OB"), ap(rb, 79, 128, 16), ap("FAI"), MAX); cp(ap("OBU"), ap("OB"))
+        if SLOTS:
+            cp(ap("OBU"), ap(rb, 79, 128, 16))
+        else:
+            tt(ap("OB"), ap(rb, 79, 128, 16), ap("FAI"), MAX); cp(ap("OBU"), ap("OB"))
         if not last:
-            cp(ind(ap(ty, 0, NEW), ap("OBU")), ap(rb, 0, 64)); cp(ind(ap(wy, 0, NEW), ap("OBU")), ap("WTAB", 0, 64))
+            cp(ind(ap(ty, OLD, END), ap("OBU")), ap(rb, 0, 64)); cp(ind(ap(wy, OLD, END), ap("OBU")), ap("WTAB", 0, 64))
         dma(ext("yu", S + CAP * t, S + CAP * t + CAP), ap("RV%d" % t), 2.0)
         if last:
-            ts(ind(ap(cy, 0, NEW), ap("OBU")), ap("IC64"), 1.0, MUL, float(S + CAP * t), ADD)
-            dma(ext("yc", L * t, L * t + L), ap(cy, 0, 256, 1, slice(0, 128, 16)), 2.0)
+            ts(ind(ap(cy, OLD, END), ap("OBU")), ap("IC64"), 1.0, MUL, float(S + CAP * t), ADD)
+            dma(ext("yc", L * t, L * t + L), ap(cy, OLD, OLD + L, 1, slice(0, 128, 16)), 2.0)
     dma(ext("yu", 0, S), ap("US", 0, S), 6.0)
     return ops
 
@@ -678,7 +729,7 @@ def order(ops, memo=None):
     def lag(j, k):
         if ops[k]["pre"][j]:
             return OWN if ops[k]["q"] == ops[j]["q"] else HOP
-        return ISSUE - ops[j]["c"] if ops[j]["q"] in "YZ" else 0.0
+        return ops[j]["hold"] - ops[j]["c"] if "hold" in ops[j] else 0.0
     pres = [[(j, lag(j, i)) for j in ops[i]["pre"]] for i in range(n)]
     posts = [[(k, lag(i, k)) for k in succ[i]] for i in range(n)]
 
@@ -694,7 +745,7 @@ def order(ops, memo=None):
                 if end[j] + d > t:
                     t = end[j] + d
             if q != "N":
-                hold = ISSUE if q in "YZ" else c
+                hold = ops[i].get("hold", c)
                 skip = c - hold if back else 0.0
                 lst = busy.setdefault(q, [])
                 p = len(lst)
@@ -720,72 +771,142 @@ def order(ops, memo=None):
         beg, end = place(late, False)
         best = min(best, (max(end), late))
     base = best[1]
-    part = [i for i in range(n) if ops[i]["k"] == 0][3]
     name, seen = [], {}
     for o in ops:
         if o["k"] == 0:
             seen = {}
-        w = (o["k"] < 0, o["q"], o["W"][0][0].rstrip("0123456789ab") if o["W"] else "")
+        w = (o["k"] < 0, o["q"], o["W"][0][0].rstrip("0123456789ab") if o["W"] else "", o["R"][-1][0].rstrip("0123456789ab") if o["R"] else "")
         seen[w] = seen.get(w, 0) + 1
         name.append(w + (seen[w],))
-    names = sorted(set(w for w in name if not w[0]))
     first = [i for i in range(n) if ops[i]["k"] == 0] + [n]
     mid = {name[i]: base[i] - base[first[2] + 1] for i in range(first[2], first[3])}
     for r in range(RO):
         zero = base[first[r] + 1]
         for i in range(first[r], first[r + 1]):
             base[i] = zero + mid[name[i]] if name[i] in mid else base[i - 1]
+    above, near = [], []
+    for i, o in enumerate(ops):
+        waits = [j for j, w in o["pre"].items() if w or o["q"] == "N"]
+        far = 0
+        for j in waits:
+            far |= above[j]
+        near.append([j for j in waits if not far >> j & 1])
+        for j in waits:
+            far |= 1 << j
+        above.append(far)
     guess = []
-    for cy, ga, sct, hop, own, flight, sfix in GUESSES:
-        c = [a + cy * (b + ga * g + sct * s) + sfix * (o["q"] == "S") + flight * (o["q"] == "N") for o in ops for a, b, g, s in [o["v"]]]
-        guess.append((c, [[(j, 0.0 if not w else own if ops[j]["q"] == o["q"] else hop) for j, w in o["pre"].items() if w or o["q"] == "N"] for o in ops]))
+    for cy, ga, sct, hop, own, flight, sfix, pe in GUESSES:
+        c = [a + cy * (b * (pe if o["q"] == "P" else 1) + ga * g + sct * s) + sfix * (o["q"] == "S") + flight * (o["q"] == "N") for o in ops for a, b, g, s in [o["v"]]]
+        guess.append((c, [o.get("hold", x) for o, x in zip(ops, c)], [[(j, 0.0 if o["q"] == "N" and not o["pre"][j] else own if ops[j]["q"] == o["q"] else hop) for j in near[i]] for i, o in enumerate(ops)]))
 
-    def keys(shift, n):
-        key = [base[i] + shift.get(name[i], 0.0) for i in range(n)]
-        for i in range(first[0] - 1, -1, -1):
-            key[i] = min([key[k] - d for k, d in posts[i] if k < n], default=first[0]) - ops[i]["c"] + shift.get(name[i], 0.0)
-        return key
+    key, _ = place(base, False)
+    span = key[first[3] + 1] - key[first[2] + 1]
+    mid = {name[i]: key[i] - key[first[2] + 1] for i in range(first[2], first[3])}
+    zero = key[first[0] + 1]
+    for r in range(RO):
+        for i in range(first[r], first[r + 1]):
+            key[i] = zero + r * span + mid[name[i]] if name[i] in mid else key[i - 1]
+    qn = ["NVSPGY".index(o["q"]) for o in ops]
+    deps = [list(o["pre"]) for o in ops]
 
-    def length(shift):
-        beg, end = place(keys(shift, part), False, part)
-        seq, total, held = sorted(range(part), key=lambda i: (beg[i], i)), 0.0, set()
-        for c, pre in guess:
-            free, why = {}, [-1] * part
+    def sequence(key, lo, hi):
+        left = [0] * n
+        for i in range(lo, hi):
+            left[i] = sum(j >= lo for j in deps[i])
+        ready = sorted((key[i], i) for i in range(lo, hi) if not left[i])
+        seq = []
+        while ready:
+            i = ready.pop(0)[1]
+            seq.append(i)
+            grown = False
+            for k in succ[i]:
+                left[k] -= 1
+                if not left[k] and k < hi:
+                    ready.append((key[k], k)); grown = True
+            if grown:
+                ready.sort()
+        return seq
+
+    def length(seq, goal):
+        total, held = 0.0, set()
+        if goal is not None:
+            seq = seq[:seq.index(goal) + 1]
+        for c, hold, pre in guess:
+            free, by, end, why = [0.0] * 6, [-1] * 6, [-1.0] * n, [-1] * n
             for i in seq:
-                q = ops[i]["q"]
-                t, why[i] = free.get(q, (0.0, -1))
+                q = qn[i]
+                t, w = free[q], by[q]
                 for j, d in pre[i]:
                     if end[j] + d > t:
-                        t, why[i] = end[j] + d, j
-                end[i] = t + c[i]
-                if q != "N":
-                    free[q] = (t + (ISSUE if q in "YZ" else c[i]), i)
-            total += max(end)
-            i = end.index(max(end))
+                        t, w = end[j] + d, j
+                end[i], why[i] = t + c[i], w
+                if q:
+                    free[q], by[q] = t + hold[i], i
+            i = end.index(max(end)) if goal is None else goal
+            total += end[i]
             while why[i] >= 0:
                 if why[i] not in ops[i]["pre"]:
                     held.add((i, why[i]))
                 i = why[i]
         return total, sorted(held)
-    rnd = np.random.RandomState(SEED)
-    shift = memo.get("shift", {})
-    cur, held = length(shift)
-    for _ in range(0 if memo else TRIES):
-        new = dict(shift)
-        for _ in range(1 + int(rnd.randint(2))):
-            w, d = names[int(rnd.randint(len(names)))], float(rnd.normal()) * (0.3, 1.0, 3.0)[int(rnd.randint(3))]
-            if held and rnd.randint(3):
-                i, j = held[int(rnd.randint(len(held)))]
-                w, d = (name[i], -abs(d)) if rnd.randint(2) else (name[j], abs(d))
-            new[w] = new.get(w, 0.0) + d
-        x, h = length(new)
-        if x <= cur:
-            cur, held, shift = x, h, new
-    memo["shift"] = shift
-    beg, end = place(keys(shift, n), False)
-    for i in range(n):
-        ops[i]["t"] = beg[i]
-    return sorted(range(n), key=lambda i: (beg[i], i)), max(end)
+
+    def filled(key, lo, hi):
+        beg, _ = place(key, False, hi)
+        return sorted(range(hi), key=lambda i: (beg[i], i))
+
+    def improve(key, lo, hi, goal, alike, tries, fill=False):
+        movable = sorted(alike)
+        cur, held = length((filled if fill else sequence)(key, lo, hi), goal)
+        best = (cur, key)
+        for step in range(tries):
+            new = list(key)
+            pick = [p for p in held if p[0] in alike or p[1] in alike]
+            kind = int(rnd.randint(5)) if pick else 4
+            i, j = pick[int(rnd.randint(len(pick)))] if pick else (0, 0)
+            more = abs(float(rnd.normal())) * (0.001, 0.2, 0.8)[int(rnd.randint(3))] + 1e-4
+            if kind < 2 and i in alike:
+                todo = [(i, key[j] - more)]
+            elif kind < 4 and j in alike:
+                far = min([key[k] for k in succ[j]], default=key[i] + 5.0) - 1e-4
+                todo = [(j, key[i] + more if kind == 2 or far < key[i] else far - (far - key[i]) * float(rnd.random_sample()) ** 2)]
+            else:
+                i = movable[int(rnd.randint(len(movable)))]
+                todo = [(i, key[i] + float(rnd.normal()) * (0.2, 0.8, 2.5)[int(rnd.randint(3))])]
+            while todo:
+                i, x = todo.pop()
+                d = x - new[i]
+                for k in alike[i]:
+                    new[k] += d
+                if d < 0:
+                    todo += [(j, x - 1e-4) for j in deps[i] if j in alike and new[j] > x]
+            x, h = length((filled if fill else sequence)(new, lo, hi), goal)
+            if x <= cur + HEAT * (1 - step / tries) * float(rnd.exponential()):
+                cur, held, key = x, h, new
+                best = min(best, (cur, key))
+        return best[1]
+    if not memo:
+        rnd = np.random.RandomState(SEED)
+        goal = [[i for i in range(first[r], first[r + 1]) if name[i][2] == "ZA" and name[i][1] == "V"][0] for r in range(RO)]
+        same = {}
+        for i in range(first[0], n):
+            same.setdefault(name[i], []).append(i)
+        key = improve(key, first[2], first[5], goal[4], {i: same[name[i]] for i in range(first[2], first[5])}, 2 * TRIES)
+        for i in range(first[1] - 1, -1, -1):
+            if name[i] not in mid:
+                key[i] = min([key[k] - d for k, d in posts[i]], default=zero) - ops[i]["c"]
+        key = improve(key, 0, first[2], goal[1], {i: [i] for i in range(first[1])}, TRIES // 8, True)
+        beg, _ = place(key, False, first[3])
+        shift = key[first[2] + 1] - beg[first[2] + 1]
+        key[:first[2]] = [x + shift for x in beg[:first[2]]]
+        key = improve(key, 0, first[1], goal[0], {i: [i] for i in range(goal[0])}, TRIES // 2)
+        key = improve(key, 0, first[2], goal[1], {i: [i] for i in range(first[1])}, TRIES // 2)
+        key = improve(key, first[1] - 80, first[3], goal[2], {i: [i] for i in range(first[1] - 80, first[2])}, TRIES // 4)
+        key = improve(key, first[4], n, None, {i: [i] for i in range(first[5], n)}, TRIES // 4)
+        memo["key"] = key
+    seq = sequence(memo["key"], 0, n)
+    for k, i in enumerate(seq):
+        ops[i]["t"] = k
+    return seq, span
 
 
 def rank_program(g, core, T, topo):
@@ -800,6 +921,9 @@ def rank_program(g, core, T, topo):
     for i in seq:
         o = ops[i]
         q = o["q"]
+        if "left" in o:
+            o["at"], o["clock"] = ops[o["left"]]["at"], ops[o["left"]]["clock"]
+            continue
         if q == "N":
             o["at"] = (o["sem"], o["inc"]); o["clock"] = {}
             total[o["sem"]] = o["inc"]

@@ -27,19 +27,19 @@ for _n in ("pF", "sF", "gF", "s2F", "sge8", "slt8", "pm8", "gx8", "g8p", "nsB", 
 _b("g16", 16, F); _b("g8", 4, F); _b("g8m", 4, F); _b("pen2", 2, F); _b("pen4", 4, F)
 _b("MWR", 256, F); _b("RST", 256, F); _b("BLKH", 128, H); _b("BLKB", 128, BF); _b("BLKN", 128, BF); _b("ONEB", 128, BF)
 _b("IDH", 128, H); _b("IDB", 128, BF); _b("IDN", 128, BF); _b("IDHN", 128, H); _b("I255", 128, BF); _b("SH1", 128, BF); _b("SH2", 128, BF)
-_b("TRIMB", 128, BF); _b("PL", 128, BF); _b("PR", 128, BF); _b("PH", 128, H); _b("SEL", 144, BF); _b("REP8", 128, H, 8)
+_b("TRL", 128, BF); _b("TRG", 128, BF); _b("PL", 128, BF); _b("PR", 128, BF); _b("PH", 128, H); _b("SEL", 144, BF); _b("REP8", 128, H, 8)
 _b("WT", 24 * 128, H); _b("PZ4", 128, BF); _b("RS4", 128, F); _b("RS16", 64, F)
 _b("C255", 128, BF); _b("THR", 16, F); _b("KJ", 48, F); _b("K256", 16, BF); _b("ZZ", 128, BF); _b("one16", 16, F); _b("oneR", 256, BF); _b("JW0", 16, F)
 _b("J256", 16, H); _b("FIX", 32, F); _b("CL", 16, U16); _b("CJ", 32, U16); _b("IC64", 64, F); _b("PF64", 64, F)
-_b("DRS", 256, F); _b("DR1", 64, F); _b("lNM", 64, BF); _b("lTR", 160, BF)
-_b("SLQ", 144, BF); _b("B512", 128, BF); _b("B256", 128, BF); _b("BLK8", 128, BF); _b("NM", 256, BF); _b("TRH", 64, BF)
-_b("MP", 512, BF); _b("MS1", 256, BF); _b("ML", 256, BF); _b("CM2", 256, F); _b("CMH", 256, H); _b("DJ", 256, H); _b("CL0", 16, U16)
+_b("DRS", 256, F); _b("DMP", 16, F); _b("NJ", 16, F); _b("I512", 128, H); _b("lTR", 160, BF)
+_b("SLQ", 144, BF); _b("SLP", 144, BF); _b("B512", 128, BF); _b("B256", 128, BF); _b("BLK8", 128, BF); _b("NM", 256, BF); _b("TRH", 64, BF)
+_b("MP", 512, BF); _b("MS1", 256, BF); _b("kz1", 256, BF); _b("ML", 256, BF); _b("CM2", 256, F); _b("CMH", 256, H); _b("DJ", 256, H); _b("CL0", 16, U16)
 for _k in "01":
     _b("CX" + _k, END, F); _b("TX" + _k, END, BF); _b("WX" + _k, END, BF)
 _b("ZB", 512, BF); _b("UVS", 128, I); _b("UVA", 32, I); _b("UVW", 16, I); _b("UVQ", 16, I)
 _b("HV", 256, I); _b("KU", 256, F); _b("KRX", 256, F); _b("LS", 16, U16); _b("LC", 16, U16); _b("RS5", 128, F); _b("R5", 128, F); _b("K5", 128, I); _b("HI", 256, I); _b("HO", 256, U16); _b("HT", 528, F)
 _b("X", ZD, BF); _b("STB", 128, BF); _b("A", 4096, BF); _b("RM", 512, F); _b("RI", 320, F); _b("KS", 64, I)
-_b("PO", 16, F); _b("PN", 16, BF); _b("SC", 16, BF); _b("POJ", 16, H); _b("OF", 16, U16); _b("ZA", 768, BF)
+_b("PO", 16, F); _b("PN", 16, BF); _b("SC", 32, BF); _b("POJ", 16, H); _b("OF", 16, U16); _b("ZA", 768, BF)
 _b("PPI", 1, I); _b("PPJ", 1, I); _b("MI", 16, I); _b("LL", 16, U16)
 _b("HM", 256, H); _b("HS", 256, F); _b("HD", 16, F); _b("LA", 16, F); _b("UR", 256, BF); _b("EX", 1024, BF); _b("W2", 128, BF); _b("B30", 128, BF); _b("NM2", 128, BF); _b("P2", 48, F); _b("HRH", 256, H); _b("HL", 16, U16)
 _b("ET", 16 * 128, BF, inner=128); _b("WD", 256, BF); _b("WN", 512, BF); _b("STP", 128, F); _b("MF", 128, BF); _b("WS", 256, F); _b("LO", 16, U16)
@@ -47,14 +47,14 @@ _b("EE", 512, H); _b("FI", 32, I); _b("FB", 32, F); _b("FC", 32, F); _b("NW", 16
 _b("SG", 2048, BF); _b("SJ", 16, F); _b("J2", 16, F); _b("JB", 32, BF); _b("JL", 16, U16); _b("FW", 256, BF); _b("JX", 16, F); _b("JL2", 16, U16)
 _b("EA", 768, F); _b("E32", 256, F); _b("EM", 64, F); _b("EQ", 64, F); _b("FAI", 4, I); _b("FA", 4, F); _b("OB", 4, F); _b("OBU", 4, U16)
 for _k in range(RO):
-    _b("ZL%d" % _k, 64, BF); _b("RB%d" % _k, 128, BF); _b("RV%d" % _k, 64, BF); _b("FL%d" % _k, 8, BF)
+    _b("ZL%d" % _k, 64, BF); _b("RB%d" % _k, 72, BF); _b("RV%d" % _k, 64, BF); _b("FL%d" % _k, 8, BF)
 _b("FS", 8, BF); _b("lUF", 64, BF)
 _b("ZT", 512, BF); _b("lUVS", 64, I); _b("lUVA", 64, I); _b("lUVW", 32, I); _b("lUQ", 32, I); _b("lKU", 64, F)
 _b("lHV", 64, I); _b("lHI", 64, I); _b("lHO", 64, U16); _b("lHT", 528, F); _b("lX", 1024, BF); _b("lA", 1024, BF, inner=32); _b("lY", 256, BF, inner=32)
-_b("CG2", 128, BF); _b("CZ", 64, BF); _b("PZL", 64, BF); _b("RS32", 64, F); _b("RL", 1024, BF); _b("lHH", 64, H); _b("PK", 256, BF)
+_b("CG2", 128, BF); _b("CZ", 64, BF); _b("PZL", 64, BF); _b("RS32", 64, F); _b("RL", 1024, BF); _b("lHH", 64, H); _b("PK", 256, BF); _b("RW", 128, BF)
 _b("kc", 2, F); _b("k1", 1, H); _b("s1I", 1, I)
 _b("lRM", 256, F); _b("lKS", 128, I); _b("lMI", 4, I); _b("lLL", 4, U16); _b("lHM", 64, H); _b("lHS", 64, F); _b("lHL", 4, U16)
-_b("lET", 160, BF); _b("RS", 128, BF); _b("RSU", 64, BF); _b("lWS", 64, F); _b("lLO", 4, U16)
+_b("lET", 320, BF); _b("RS", 72, BF); _b("RSU", 64, BF); _b("lWS", 64, F); _b("lLO", 4, U16)
 _PS = ["UVP", "ZP", "DA", "DB", "HR", "CT", "MS", "JP"]
 _SIZE = {F: 4, BF: 2, H: 2, I: 4, U16: 2}
 _OWN = ("US", "TP", "WTAB", "UF", "X", "A", "ZA", "RS", "RSU", "FS")
@@ -78,13 +78,32 @@ ND = 40
 SEMAPHORES = ["sV", "sS", "sP", "sG", "la", "lr", "lu", "lf"] + ["fai%d" % k for k in range(RO)] + ["reu%d" % k for k in range(RO)] + ["ask%d" % k for k in range(RO)] + ["rep%d" % k for k in range(RO)] + ["d%d" % k for k in range(ND)]
 
 NS = 5
-BYS = {0: "CT", 2: "ZP", 14: "UVP"}
+BYS = {0: "CT", 2: "ZP", 6: "UVP"}
 SUMS = {0: "DA", 4: "DB", 8: "JP", 12: "HR", 13: "CT", 14: "ZP", 15: "DA"}
-PROBE = [("gather", 0, 2), ("gather", 4, 2), ("gather", 2, 2), ("abs", 0, 2), ("gather", 6, 2), ("gather", 14, 1), ("abs", 2, 2), ("gather", 8, 2),
-         ("abs", 4, 2), ("gather", 10, 2), ("abs", 6, 2), ("four", 0, 0), ("slots", 0, 0), ("gather", 12, 1), ("abs", 8, 2), ("slots", 1, 0),
-         ("gather", 13, 1), ("abs", 10, 2), ("four", 4, 0), ("gather", 15, 1), ("abs", 14, 1), ("slots", 3, 0), ("abs", 12, 1), ("abs", 13, 1),
-         ("slots", 2, 0), ("four", 8, 0), ("abs", 15, 1), ("single", 14, 0), ("fold", 0, 0), ("single", 12, 1), ("single", 13, 2), ("single", 15, 3)]
-KEPT = ("gather", "abs", "four", "minus", "slots")
+PROBE = [("gather", 0, 2), ("gather", 4, 2), ("gather", 2, 2), ("abs", 0, 2), ("gather", 6, 2), ("gather", 8, 2), ("minus", 4, 2), ("two", 4, 0),
+         ("abs", 2, 2), ("slots", 0, 0), ("slots", 1, 0), ("slots", 2, 0), ("slots", 3, 0), ("gather", 10, 2), ("abs", 8, 2), ("four", 0, 1),
+         ("two", 8, 0), ("abs", 6, 2), ("gather", 12, 1), ("two", 6, 1), ("gather", 13, 1), ("abs", 10, 2), ("gather", 14, 1), ("abs", 12, 1),
+         ("two", 10, 1), ("gather", 15, 1), ("abs", 13, 1), ("abs", 14, 1), ("abs", 15, 1), ("single", 12, 0), ("fold", 0, 0), ("single", 13, 1),
+         ("single", 14, 2), ("single", 15, 3)]
+KEPT = ("gather", "abs", "two", "four", "minus")
+CHAINS = ("EE<WX UVS<UVP EE<WX#2 UVA<UVS", "X<ZB HV<KU#2 FI<MS HI<HV#2 NW<FI HO<HI#2 RS< X<ZB#2 RI<NW X<ZB#3",
+          "K<R SC<K POJ<NJ MI<K HT<HI OF<MS LL<MI ZA<OF HM<MWR HS<HM HM<MWR#2 HRH<HR ET<HS ET<HS#8 HS<HM#2 HRH<HR#2 FS<FAI WS<CT "
+          "ET<HS#9 LO<LA ET<HS#16 HL<HS J<KJ WS<DB lUVS<UVP LA<HD#2 lUVA<lUVS LO<LA#2 lUVW<lUVA JX<JB",
+          "lHO<lHI lHH<lHI lX<ZT lX<ZT#2 lX<ZT#3 X<LO DJ<J lRM< JL<JX lRM<#2 lKS<HR lKS<HR#2 lKS<UVP lKS<UVP#2 lMI<lKS lLL<lMI lHM<MWR lET<FL lHS<lHM lHL<lHS "
+          "lET<DMP RS<lET#4 FW<NM lWS<RS CMH<FW lWS<lHS JL<CMH lWS<DMP lLO<lWS CX<OBU PPI<MS OBU<RB",
+          "ZB<ZP#2 E<JP X<HO", "lHT<CT WX<HL WX<JL", "SJ<THR#5 EA<OF SJ<THR#6 SJ<THR#16 CX<HR UR<HR UF<LO ZT<JP UF<LO#2 ZT<JP#2 lX<lHO lA<lX lA<lX#3 lHT<CT "
+          "WD<DB MF<HL WN<MS RS<lHL TX<HL TX<JL RSU<lLO UF<lLO WX<JL CX<JL",
+          "UVP<TX ZP<TX JP<EE MS<EE#2 CT<ZB ZP<ZB MS<EE#3 MS<EE#4 CT<X", "UVP<ZL JP<ZL JP<ZL#2 UVP<PZL ZP<ZT JP<PZL CT<lHH ZP<lX DA<lA JP<lA HR<lA UVP<lA ZP<lTR HR<lTR HR<lHM ZP<lHM",
+          "<ZA <FS <RS")
+START = ("pI< IC< CG< CS< C< CG<#2 oneR< SEL<B RS<#2 SLP<B kz< SLQ<B TRG<BLKB TRL<BLKB SC< ZA< HT< CG<#3 ONEB< PK<ONEB PK<ONEB#2 FS< C<#2 RW< "
+         "CZ< ML< RL<ONEB RL<ONEB#2 <ZA RL<ONEB#3 RL<ONEB#4 K< JB< SH<B SH<B#2 lTR< lHT< <FS RS< STB< X< WN< TX< WX< WX<#2 <RS",
+         "sI<pI pF<pI sF<sI nsB<sF s2I<sI gF<sF gx<sF sge<sF slt<sF s2F<s2I pm<sge ns<s2F pm<pF g<gx IDB<pF JW<sF PH<pm g8m<slt g8p<sge BLKB<gF REP<pF "
+         "BLKH<gF hwf<hwi c8h<c hwh<hwf ksc<kmi PL<sge kh<ksc DRS<JW ws<MS PR<slt CM<CT WT<ws c8i<c WT<ws#2 CL<CM WT<ws#3 c8w<c8i WT<ws#10 KR<MS LC<IC "
+         "TX<CL LS<sF UVS<UVP", "RL<pF RL<pF#2 RL<pF#3 RL<pF#4 ZA<OF",
+         "W<P NM<rF RST<CS EA<OF B<BLKB#3 US<IC B<BLKB#2 I<IDB SJ<THR#10", "PZL<s1F lTR<pm DMP<JW DMP<JW#2 US<IC#2 ZT<JP")
+LATER = "J<JW I<pF THR<JW s1T<sF PF<IC P<one hwg<hwf k<kmi s1I<sI pm<sF KJ<IC KJ<IC#2 DJ< IC<IC RL<pF"
+AT_FIRST = ("MF<HL WN<MS RS<lHL TX<HL TX<JL RSU<lLO", "RS<lHL MF<HL WN<MS RSU<lLO TX<HL TX<JL")
+AT_LAST = ("FW<NM lWS<RS CMH<FW lWS<lHS JL<CMH lWS<DMP lLO<lWS CX<OBU", "lWS<RS lWS<lHS lWS<DMP lLO<lWS US<lLO FW<NM")
 MERGE = 3
 ZERO = 0
 SLOTS = 1
@@ -99,7 +118,7 @@ LRELU = 0
 CLATE = 2
 LB = 256
 LORD = ((0, 256), (256, 512), (768, 1024), (512, 768))
-SE = 2
+SE = 0
 SX = 3
 BEHIND, INIAT = 4, 16
 PASSES = 6
@@ -108,10 +127,10 @@ JA = 8
 
 CY = 0.00104
 GA, SCT = 1.56, 3.8
-HOP, OWN, ISSUE = 0.14, 0.08, 0.1
-FLIGHT, SEND, SFIX, PE = 2.4, 0.6, 0.03, 0.5
-GUESSES = ((CY, GA, SCT, HOP, OWN, FLIGHT, SFIX, 1.0), (0.0009, 1.15, 2.5, 0.2, 0.1, 1.2, 0.05, 1.2), (0.00125, 1.9, 5.5, 0.13, 0.07, 3.6, 0.03, 1.0),
-           (0.00092, 1.5, 3.5, 0.18, 0.1, 3.0, 0.06, 2.0))
+HOP, OWN, ISSUE = 0.2, 0.11, 0.1
+FLIGHT, SEND, SFIX, PE = 2.0, 0.5, 0.03, 0.5
+GUESSES = ((CY, GA, SCT, HOP, OWN, FLIGHT, SFIX, 0.0), (0.0009, 1.15, 2.5, 0.14, 0.08, 1.0, 0.05, 0.005), (0.00125, 1.9, 5.5, 0.2, 0.12, 2.6, 0.03, 0.0),
+           (0.00092, 1.5, 3.5, 0.18, 0.1, 3.0, 0.06, 0.04))
 TRIES, SEED, HEAT = 7000, 1, 0.03
 
 
@@ -168,7 +187,7 @@ def build(rank, core, T, topo):
     def isps(d):
         return d[0] == "a" and d[1] in _PS
 
-    def put(q, fn, reads, writes, cost, sem=None, inc=1):
+    def put(q, fn, reads, writes, cost, sem=None, inc=1, many=0):
         R, W = [], []
         for d in reads:
             R += acc(d)
@@ -178,7 +197,7 @@ def build(rank, core, T, topo):
             else:
                 W += acc(d)
         a, b, ga, sct = cost if isinstance(cost, tuple) else (cost, 0, 0, 0)
-        ops.append({"q": q, "fn": fn, "R": R, "W": W, "v": (a, b, ga, sct), "sem": sem, "inc": inc, "k": len(ops) - start[0],
+        ops.append({"q": q, "fn": fn, "R": R, "W": W, "v": (a, b, ga, sct), "many": many, "sem": sem, "inc": inc, "k": len(ops) - start[0],
                     "c": a + CY * (b + GA * ga + SCT * sct) + SFIX * (q == "S") + FLIGHT * (q == "N")})
         return len(ops) - 1
 
@@ -211,6 +230,9 @@ def build(rank, core, T, topo):
         return put("V", lambda g: g.vector.tensor_tensor_scan(res(o), res(a), res(b), first, op0, op1), [a, b], [o],
                    vcost(n_of(o), 0.5 if size(o) == size(a) == size(b) == 2 else 1, False, False))
 
+    def most(o, a):
+        return put("V", lambda g: g.vector.tensor_reduce(res(o), res(a), AxisListType.X, AluOpType.max), [a], [o], vcost(n_of(a), 1, False, False))
+
     def fill(o, v, q="V"):
         if q == "G":
             return iota(o, [[0, n_of(o)]], int(v))
@@ -234,17 +256,17 @@ def build(rank, core, T, topo):
             for o, l, rh, st, sp in lst:
                 r = g.tensor.matmul(res(o), res(l), res(rh), st, sp)
             return r
-        return put("P", fn, [x[1] for x in lst] + [x[2] for x in lst], [x[0] for x in lst], (0.0, PE * sum(max(64, n_of(x[2])) for x in lst), 0, 0))
+        return put("P", fn, [x[1] for x in lst] + [x[2] for x in lst], [x[0] for x in lst], (0.0, PE * sum(max(64, n_of(x[2])) for x in lst), 0, 0), many=len(lst))
 
     def iota(o, pattern, base, step=0):
         if _B[o[1]][2] == I:
             return put("G", lambda g: g.iota(res(o), pattern, base, step), [], [o], (0.15, 2 * n_of(o), 0, 0))
-        return put("G", lambda g: g.iota(res(o), pattern, base, step, allow_small_or_imprecise_dtypes=True), [], [o], (0.15, 2 * n_of(o), 0, 0))
+        return put("G", lambda g: g.iota(res(o), pattern, base, step, allow_small_or_imprecise_dtypes=True), [], [o], (0.22, 2 * n_of(o), 0, 0))
 
     def later(*ks):
         ops[-1].setdefault("after", []).extend(ks)
 
-    nd = [0]
+    nd, sent = [0], []
 
     def dma(o, a, cost, behind=()):
         k = "d%d" % nd[0]; nd[0] += 1
@@ -276,7 +298,7 @@ def build(rank, core, T, topo):
     AF = ActivationFunctionType
 
     def keep(o, src, pattern, base, op=EQ, step=0):
-        return put("G", lambda g: g.affine_select(res(o), res(ap(src)), pattern, op, 0.0, base, step), [ap(src)], [o], (0.18, 256, 0, 0))
+        return put("G", lambda g: g.affine_select(res(o), res(ap(src)), pattern, op, 0.0, base, step), [ap(src)], [o], (0.28, 256, 0, 0))
 
     dma(ap("c8"), T.c0[:, :], 1.7); dma(ap("hwi"), T.hw[:, :], 1.7); later(0)
     dma(ap("kmi"), T.km[:, :], 1.7); later(1); dma(ap("th8"), T.th[:, :], 1.7); later(2)
@@ -317,33 +339,34 @@ def build(rank, core, T, topo):
     ts(ap("k1"), ap("kmi"), -2048.0, ADD)
     for k in range(2):
         keep(ap("PK", 128 * k, 128 * k + 128), "ONEB", [[16, 8], [0, 2], [2, 8]], k, EQ, -1)
-    mm([(ap("MS", 4 + k, 5 + k), ap("PK", 128 * k, 128 * k + 128), ap("k1"), True, True) for k in range(2)])
-    ts(ap("kc"), ap("MS", 4, 6), 2048.0, ADD)
-    for r in range(8):
-        keep(ap("RL", 128 * r, 128 * r + 128), "ONEB", [[16, 8], [0, 8], [8, 2]], r, EQ, -1)
+    iota(ap("RW"), [[16, 8], [0, 8], [8, 2]], 0)
+    for r in range(4):
+        ts(ap("RL", 128 * r, 128 * r + 128), ap("RW"), float(r), ADD, ap("pF"), EQ)
+        keep(ap("RL", 128 * r + 512, 128 * r + 640), "ONEB", [[16, 8], [0, 8], [8, 2]], r + 4, EQ, -1)
     ts(ap("s1I"), ap("sI"), 1, SHR); cp(ap("s1F"), ap("s1I"))
     act(ap("PZL"), ap("CZ"), AF.Abs, bias=ap("ns2"), scale=8 * BIG); act(ap("PZL"), ap("PZL"), AF.Identity, bias=ap("s1F"))
-    for o, v in (("IDB", 1.0), ("IDH", 1.0), ("IDN", -1.0), ("IDHN", -1.0)):
+    for o, v in (("IDB", 1.0), ("IDH", 1.0), ("IDN", -1.0), ("I512", 512.0)):
         ts(ap(o), ap("IC", 0, 128), ap("pF"), EQ, v, MUL)
     act(ap("I255"), ap("IDB"), AF.Copy, scale=-255.0)
     act(ap("NM"), ap("CS"), AF.Abs, bias=ap("nsB"), scale=BIG)
     act(ap("PZ4"), ap("C3"), AF.Abs, bias=ap("ns2"), scale=8 * BIG); act(ap("RS4"), ap("C3"), AF.Relu, bias=8 * BIG, scale=-8 * BIG)
     act(ap("MWR"), ap("NM"), AF.Relu, bias=1.0, scale=-1.0); act(ap("RST"), ap("CS"), AF.Sign)
-    act(ap("TRH"), ap("CS", 0, 64), AF.Relu, bias=ap("s1T"), scale=-16384.0); act(ap("lTR", 0, 64), ap("IC", 0, 64), AF.Relu, bias=ap("s1T"), scale=-16384.0)
-    for o, v in (("B512", 1024.0), ("B256", 256.0), ("BLK8", 8192.0), ("BLKN", -1.0)):
+    act(ap("TRH"), ap("CS", 0, 64), AF.Relu, bias=ap("s1T"), scale=-16384.0); ts(ap("pm1"), ap("sF"), 47.0, ADD, -16384.0, MUL)
+    act(ap("lTR", 0, 64), ap("IC", 0, 64), AF.Relu, bias=ap("pm1"), scale=16384.0); fill(ap("lTR", 64, 80), UNF, "G"); fill(ap("RS", 64, 72), 0.0, "G")
+    for o, v in (("B512", 1024.0), ("B256", 256.0)):
         act(ap(o), ap("BLKB"), AF.Copy, scale=v)
     ts(ap("ksc"), ap("kmi"), -2048.0, ADD); ts(ap("kh"), ap("CS", 0, 16), ap("sF"), EQ, ap("ksc"), MUL)
     mm([(ap("MS", 16, 32), ap("BLKH"), ap("kh"), True, True)])
     ts(ap("KR"), ap("MS", 16, 32), 2048.0, ADD)
     ts(ap("LS"), ap("IC", 0, 16), 0.0, MUL, ap("sF"), ADD); cp(ap("LC"), ap("IC", 0, 16))
     act(ap("KRX"), ind(ap("KR"), ap("LC")), AF.Copy)
-    fill(ap("RS5"), 0.0, "G"); fill(ap("RS5", 0, 128, 8), 8 * BIG, "S"); fill(ap("R5", 1, 128, 2), 8 * BIG, "S")
+    fill(ap("RS5"), 0.0, "G"); fill(ap("RS5", 0, 128, 8), 8 * BIG, "S"); fill(ap("R5", 1, 128, 2), 8 * BIG, "S"); fill(ap("R5", 7, 128, 8), 0.0, "S")
     ts(ap("th8h"), ap("th8"), -2048.0, ADD)
     mm([(ap("MS", 8, 9), ap("REP8"), ap("th8h"), True, True)])
     ts(ap("th16"), ap("MS", 8, 9), 2047.5, ADD, 1024.0, MUL)
     ts(ap("JW0"), ap("IC", 0, 256, 16), ap("sF"), ADD)
     act(ap("DRS"), ap("CS"), AF.Copy, bias=-BIG, scale=0.0); ts(ap("DRS", 0, 256, 16), ap("JW0"), S - 2047.0, ADD)
-    fill(ap("DR1"), -BIG, "G"); ts(ap("DR1", 0, 64, 16), ap("JW0", 0, 4), 2.0, MUL, 258.0, ADD)
+    act(ap("DMP", 0, 4), ap("JW0", 0, 4), AF.Copy, bias=258.0, scale=2.0); act(ap("DMP", 8, 12), ap("JW0", 0, 4), AF.Copy, bias=258.0 + 2048, scale=2.0)
     ts(ap("c8h"), ap("c8"), -2048.0, ADD)
     mm([(ap("CT", 0, 256), ap("IDB"), ap("NM"), True, False), (ap("CT", 0, 256), ap("REP8"), ap("c8h"), False, True)])
     scan(ap("CM2"), ap("DRS"), ap("CT", 0, 256), MAX, MIN); ts(ap("CL0"), ap("CM2", 15, 256, 16), 2048.0, ADD)
@@ -355,31 +378,38 @@ def build(rank, core, T, topo):
 
     keep(ap("SEL", 0, 128), "B512", [[0, 8], [1, 16]], -15); fill(ap("SEL", 128, 144), 0.0, "S")
     keep(ap("SLQ", 0, 128), "B512", [[0, 32], [1, 4]], -3); fill(ap("SLQ", 128, 144), 0.0, "S")
+    keep(ap("SLP", 0, 128), "B512", [[0, 16], [1, 8]], -7); fill(ap("SLP", 128, 144), 0.0, "S")
+    ts(ap("pen2"), ap("IC", 0, 2), ap("sge8"), NE, 2 * BIG, MUL)
+    for h in range(2):
+        ts(ap("MP", h, 384, 2), ap("IC", 0, 192), ap("pen2", h, h + 1), ADD)
+
+    def slp(r):
+        return ap("SLP", 7 - r, 135 - r)
 
     def sel(s):
         return ap("SEL", 15 - s, 143 - s)
 
     def slq(r):
         return ap("SLQ", 3 - r, 131 - r)
-    keep(ap("TRIMB"), "BLKN", [[-1, 128]], 0, GE, 1)
+    keep(ap("TRG"), "BLKB", [[-1, 128]], 0, GE, 1); keep(ap("TRL"), "BLKB", [[1, 128]], 0, GT, -1); fill(ap("SC", 0, 1), 0.0, "G")
     for k in range(4):
         act(ap("WTAB", 128 * k, 128 * k + 128), ap("C3"), AF.Copy, bias=4.0)
     for k in range(1, 8):
-        wtab = dma(ap("WTAB", 512 * k, 512 * k + 512), ap("WTAB", 0, 512), 7.0); later(ldu, len(ops) - 2)
+        wtab = dma(ap("WTAB", 512 * k, 512 * k + 512), ap("WTAB", 0, 512), 4.0, [ap("US", 0, S)]); later(ldu, len(ops) - 2)
     ts(ap("c8i"), ap("c8"), 3, AND); ts(ap("c8w"), ap("c8i"), 4.0, ADD)
     mm([(ap("DB", 0, 256), ap("REP8"), ap("c8w"), True, True)])
     act(ap("WX0", OLD, OLD + L), ap("DB", 0, 256), AF.Copy)
-    iota(ap("MS1"), [[1, 64], [0, 4]], 192)
-    ts(ap("J256"), ap("JW0"), 256.0, ADD)
-    ts(ap("EE", 510, 512), ap("IC", 0, 2), 0.0, MUL, 1282.0, ADD)
+    iota(ap("kz1"), [[1, 64], [0, 4]], 192)
+    mm([(ap("DA", 0, 256), ap("IDB"), ap("kz1"), True, False)] + [(ap("DA", k, k + 128), ap("IDB"), ap("PZ4"), False, k > 0) for k in (0, 128)])
+    act(ap("MS1"), ap("DA", 0, 256), AF.Copy)
+    ts(ap("J256"), ap("JW0"), 256.0, ADD); act(ap("NJ"), ap("JW0"), AF.Copy, bias=-0.5, scale=-1.0 / 512)
+    ts(ap("EE", 255, 511), ap("CS"), 0.0, MUL, 1282.0, ADD); ts(ap("EE", 511, 512), ap("pF"), 0.0, MUL, 1282.0, ADD)
     fill(ap("one16"), 1.0, "S"); fill(ap("P2", 0, 16), 0.5, "S"); scan(ap("P2", 16, 32), ap("P2", 0, 16), ap("one16"), MUL, MAX, 2.0 ** 29)
     tt(ap("P2", 32, 48), ap("P2", 16, 32), ap("MWR", 0, 16), MUL); scan(ap("P2", 0, 16), ap("one16"), ap("P2", 32, 48)); ts(ap("rF"), ap("P2", 15, 16), -2.0, MUL)
     act(ap("W2"), ap("BLKB"), AF.Identity, scale=ap("P2", 15, 16)); act(ap("B30"), ap("BLKB"), AF.Copy, scale=2.0 ** 30)
     act(ap("NM2"), ap("NM", 0, 128), AF.Identity, bias=ap("rF"), scale=2.0 ** 23)
     ts(ap("EE", 0, 1), ap("pF"), 0.0, MUL)
     fill(ap("oneR"), 1.0, "G"); fill(ap("C255"), 255.0, "G")
-    ts(ap("lNM"), ap("NM", 0, 64), -2048.0, ADD)
-    LR = (0, 64, 112, 144)
     rng = [(11 * c, min(254, 20 * c + 19)) for c in range(16)]
     ts(ap("THR"), ap("JW0"), 5.0, MUL, 66.5, ADD)
     ts(ap("KJ", 16, 32), ap("IC", 0, 16), 31.0, MUL, 19.0, ADD); ts(ap("KJ", 32, 48), ap("IC", 0, 16), 11.0, MUL, 254.0, ADD)
@@ -393,7 +423,7 @@ def build(rank, core, T, topo):
     iota(ap("X", S, ZD), [[0, ZD - S]], 0); iota(ap("STB"), [[0, 128]], 1024)
     cp(ap("IC64"), ap("IC", 0, 64)); ts(ap("PF64"), ap("IC", 0, 64), 5.0, MUL, 1344.0, ADD)
     act(ap("HT", 256, 512), ap("IC"), AF.Copy); fill(ap("HT", 512, 528), UNF, "G"); fill(ap("lHT", 512, 528), UNF, "G")
-    fill(ap("RI", 0, 64), 8 * BIG, "S"); fill(ap("US", S, 4480), 0.0, "G")
+    fill(ap("RI", 0, 64), 8 * BIG, "S"); fill(ap("US", S, ZD), 0.0, "S"); fill(ap("US", ZD, 4480), 0.0, "S")
 
     for t in range(RO):
         start[0] = len(ops)
@@ -432,13 +462,16 @@ def build(rank, core, T, topo):
             tt(ap("HV", 16 * a, 16 * b), ind(ap("UVQ"), ap("LS", a, b)), ap("KU", 16 * a, 16 * b), ADD)
             ts(ap("HI", 16 * a, 16 * b), ap("HV", 16 * a, 16 * b), 4095, AND)
             cp(ap("HO", 16 * a, 16 * b), ap("HI", 16 * a, 16 * b))
-        scan(ap("EE", 256, 510), ap("oneR", 0, 254), ap(wx, OLD, OLD + 254)); cp(ap("EE", 1, 256), ap("EE", 256, 511))
+        for k in (1, 256):
+            scan(ap("EE", k, k + 254), ap("oneR", 0, 254), ap(wx, OLD, OLD + 254))
+        mm([(ap("JP", 256, 512), ap("IDH"), ap("EE", 0, 256), True, True)])
+        act(ap("E32"), ap("JP", 256, 512), AF.Copy, bias=64.0)
         for k in range(0, 16, 4):
             mm([(ap("MS", 32, 64), sel(s), ap("EE", s, s + 497, 16), s == 0, s == 15) for s in range(k, k + 4)])
         slots = [lambda: ts(ap("FI"), ap("MS", 32, 64), 0.2 / 16384, MUL, 256.0, MIN),
                  lambda: tt(ap("NW"), ap("FI", 16, 32), ap("FI", 0, 16), SUB),
-                 lambda: act(ap("RI", 1, 64, 4), ap("NW"), AF.Copy, bias=512.0 - 2 * BIG, scale=4 * BIG),
-                 lambda: ts(ap("RS5", 7, 128, 8), ap("NW"), b16, SUB)]
+                 lambda: ts(ap("RI", 1, 64, 4), ap("NW"), 4 * BIG, MUL, 512.0 - 2 * BIG, ADD),
+                 lambda: ts(ap("RS5", 7, 128, 8), ap("NW"), -1.0, MUL, b16, ADD)]
         prev, where, fours = {}, {}, 0
         minus = [m + i for step, m, k in PROBE if step == "minus" for i in range(k)]
         for step, m, k in PROBE:
@@ -454,22 +487,26 @@ def build(rank, core, T, topo):
             elif step == "minus":
                 j = ts(ap("A", 256 * m, 256 * (m + k)), x, 0.0, MIN, -2.0, MUL)
             elif step == "fold":
-                for h in range(2):
-                    j = tt(ap("RI", 2 + h, 64, 4), ap("RM", 128 + 32 * h, 144 + 32 * h), ap("RM", 144 + 32 * h, 160 + 32 * h), MIN)
-            elif step == "four":
-                d = SUMS[m]
-                mm([(ap(d, 0, 64), ap("IDB"), ap("IC", 16 * m, 16 * m + 64), True, False)])
-                own = [i for i in range(m, m + 4) if i in minus]
-                if own:
-                    lo, hi = own[0], own[-1] + 1
-                    mm([(ap(d, 16 * (lo - m), 16 * (hi - m)), sel(r), ap("X", 256 * lo + r, 256 * hi, 16), False, False) for r in range(16)])
-                mm([(ap(d, 0, 64), sel(r), ap("A", 256 * m + r, 256 * m + 1024, 16), False, r == 15) for r in range(16)])
-                y = ap("RM", fours, fours + 64)
-                j = tt(y, ap(d, 0, 64), ap("RM", fours - 64, fours), MIN) if fours else ts(y, ap(d, 0, 64), b16, MIN)
-                fours += 64
+                tt(ap("RM", 384, 448), ap("RM", 256, 320), ap("RM", 320, 384), MIN)
+                for lo in (384, 416):
+                    j = tt(ap("RI", lo // 32 - 10, 64, 4), ap("RM", lo, lo + 31, 2), ap("RM", lo + 1, lo + 32, 2), MIN)
+            elif step in ("two", "four"):
+                d, lo, w = SUMS[m - m % 4], 32 * (m % 4), 2 if step == "two" else 4
+                if not k or w == 4:
+                    mm([(ap(d, 0, 128), ap("IDB"), ap("MP", 32 * m - lo, 32 * m - lo + 128), True, False)])
+                if m in minus:
+                    mm([(ap(d, lo, lo + 32 * w), slp(r), ap("X", 256 * m + r, 256 * (m + w), 8), False, False) for r in range(8)])
+                j = mm([(ap(d, lo, lo + 32 * w), slp(r), ap("A", 256 * m + r, 256 * (m + w), 8), False, k == 1 and r == 7) for r in range(8)])
+                if k:
+                    y = ap("RM", fours, fours + 128)
+                    if fours:
+                        tt(y, ap(d, 0, 128), ap("RM", fours - 128, fours), MIN)
+                    else:
+                        ts(y, ap(d, 0, 128), b16, MIN)
+                    fours += 128
             elif step == "single":
                 d = ap(SUMS[m], 0, 64)
-                mm([(d, ap("IDB"), ap("MS1", 64 * (m - 12), 64 * (m - 11)), True, False), (d, ap("IDB"), ap("PZ4", 0, 64), False, False)])
+                mm([(d, ap("IDB"), ap("MS1", 64 * (m - 12), 64 * (m - 11)), True, False)])
                 if m in minus:
                     mm([(d, slq(r), ap("X", 256 * m + r, 256 * m + 256, 4), False, False) for r in range(4)])
                 mm([(d, slq(r), ap("A", 256 * m + r, 256 * m + 256, 4), False, r == 3) for r in range(4)])
@@ -488,28 +525,31 @@ def build(rank, core, T, topo):
                 if ops[j]["q"] in prev:
                     ops[j].setdefault("after", []).append(prev[ops[j]["q"]])
                 prev[ops[j]["q"]] = j
-        scan(ap("K5"), ap("RS5"), ap("R5"), ADD, MIN)
+        scan(ap("K5"), ap("RS5"), ap("R5"), SUB, MIN)
         key = ap("K5", 6, 128, 8)
-        iota(ap("ZA", 0, 64), [[0, 64]], 768)
+        iota(ap("ZA", 0, 64), [[0, 64]], 768); later(*sent[-1:])
         mm([(ap("MS", 64, 80), ap("IDH"), ap("J256"), True, False)])
-        ts(ap("PN"), ap("K5", 7, 128, 8), 0.0, MAX); ts(ap("PO"), key, b16, GE); tt(ap("POJ"), ap("PO"), ap("J256"), MUL)
-        scn = scan(ap("SC"), ap("one16"), ap("PN"))
+        poor = ap("K5", 7, 128, 8)
+        scn = scan(ap("SC", 1, 17), ap("one16"), poor, MUL, SUB); tt(ap("POJ"), poor, ap("NJ"), MAX)
         ts(ap("HT", 0, 256), ap("HI"), -2047.0, ADD); later(scn)
-        mm([(ap("MS", 64, 80), ap("TRIMB"), ap("PN"), False, False), (ap("MS", 64, 80), ap("IDHN"), ap("POJ"), False, False)])
-        ofm = mm([(ap("MS", 64, 80), ap("BLKB"), ap("SC"), False, True)])
+        mm([(ap("MS", 64, 80), ap("TRL"), ap("SC", 1, 17), False, False), (ap("MS", 64, 80), ap("TRG"), ap("SC", 0, 16), False, False)])
+        mm([(ap("MS", 64, 80), ap("I512"), ap("POJ"), False, True)])
         ts(ap("MI"), key, 1023, AND)
         cp(ap("OF"), ap("MS", 64, 80))
         cp(ap("LL"), ap("MI")); later(len(ops) - 2)
         cp(ind(ap("ZA"), ap("OF")), ap("ZB", 0, 256)); later(len(ops) - 2)
         send("ZL%d" % t, ap("ZA", 0, 64), "ask%d" % t, "la", lender)
-        tt(ap("HM"), ind(ap("HT"), ap("LL")), ap("MWR"), MUL)
-        scan(ap("HS"), ap("RST"), ap("HM"))
-        mm([(ap("HR", 0, 256), ap("BLKH"), ap("HM"), True, True)])
-        cp(ap("HRH"), ap("HR", 0, 256))
-        hsx = act(ap(cx, 0, L), ap("HR", 0, 256), AF.Copy, bias=2047.0)
+        if not t:
+            mm([(ap("UVP", 4 + k, 5 + k), ap("PK", 128 * k, 128 * k + 128), ap("k1"), True, True) for k in range(2)])
+            ts(ap("kc"), ap("UVP", 4, 6), 2048.0, ADD)
+        for lo in (128, 0):
+            tt(ap("HM", lo, lo + 128), ind(ap("HT"), ap("LL", lo // 16, lo // 16 + 8)), ap("MWR", 0, 128), MUL)
+            scan(ap("HS", lo, lo + 128), ap("RST", 0, 128), ap("HM", lo, lo + 128))
+            mm([(ap("HR", lo, lo + 128), ap("BLKH"), ap("HM", lo, lo + 128), True, True)])
+            cp(ap("HRH", lo, lo + 128), ap("HR", lo, lo + 128))
+            tt(ap("HD", lo // 16, lo // 16 + 8), ap("HS", lo + 15, lo + 128, 16), ap("DRS", lo, lo + 128, 16), MIN)
+        act(ap(cx, 0, L), ap("HR", 0, 256), AF.Copy, bias=2047.0)
         act(ap("UR"), ap("HR", 0, 256), AF.Relu, bias=-3000.0)
-        tt(ap("HD"), ap("HS", 15, 256, 16), ap("DRS", 0, 256, 16), MIN)
-
         made = []
 
         def equal(k, lo, hi, c, scalar):
@@ -538,8 +578,6 @@ def build(rank, core, T, topo):
                 cp(ind(ap("US", 0, ZD), ap("LO", 8 * h, 8 * h + 8)), ap("C255", 0, 128))
             act(ap("WD", 128 * h, 128 * h + 128), ap(d, 256, 384), AF.Sign)
         ts(ap("HL"), ap("HS", 15, 256, 16), 2047.0, ADD, 4095.0, MIN)
-        mm([(ap("DA", 256, 512), ap("IDH"), ap("EE", 0, 256), True, True)])
-        act(ap("E32"), ap("DA", 256, 512), AF.Copy, bias=64.0)
         act(ap("EA", 0, 64), ap("PF64"), AF.Copy)
         act(ind(ap("EA"), ap("OF")), ap("E32"), AF.Silu)
         scan(ap("EQ"), ap("TRH", 0, 64), ap("EA", 0, 64), MAX, MIN)
@@ -593,7 +631,7 @@ def build(rank, core, T, topo):
         mm([(ap("CT", 64 * r, 64 * r + 64), ap("RL", 128 * r, 128 * r + 128), ap("lHH"), True, True) for r in range(8)])
         act(ap("lHT", 0, 512), ap("CT"), AF.Copy); later(k)
         for n in range(4):
-            d = ("DA", "DB", "UVP", "HR")[n]
+            d = ("DA", "JP", "UVP", "HR")[n]
             mm([(ap(d, 64, 128), ap("IDB"), ap("ML", 64 * n, 64 * n + 64), True, False), (ap(d, 64, 128), ap("IDB"), ap("PZL"), False, False)])
             if n == 2 and LRELU:
                 mm([(ap(d, 64, 128), slq(r), ap3("lY", 0, 8, 8 * r, 8 * r + 8), False, False) for r in range(4)])
@@ -607,36 +645,23 @@ def build(rank, core, T, topo):
         ts(ap("lMI"), ap("lKS", 31, 128, 32), 1023, AND); cp(ap("lLL"), ap("lMI"))
         tt(ap("lHM"), ind(ap("lHT"), ap("lLL")), ap("MWR", 0, 64), MUL)
         scan(ap("lHS"), ap("RST", 0, 64), ap("lHM"))
-        reg = [ap(("HR", "ZP")[c // 2], 256 + LR[c], 320 + LR[c] - 16 * c) for c in range(4)]
+        reg = [(("HR", "ZP")[c // 2], 256 + 80 * (c % 2), 16 * c + 16) for c in range(4)]
         for c in (0, 2):
-            mm([(reg[k], ap("IDB"), ap("lTR", 0, 64 - 16 * k), k == c, False) for k in (c, c + 1)])
+            mm([(ap(d, lo, lo + w + 1), ap("IDB"), ap("lTR", 64 - w, 65), k == 0, False) for k, (d, lo, w) in enumerate(reg[c:c + 2])])
         for c in (0, 2):
-            mm([(reg[k], ap("BLKH"), ap("lHM", 16 * k, 64), False, k % 2 == 1) for k in (c, c + 1)])
+            mm([(ap(d, lo, lo + w), ap("BLKH"), ap("lHM", 0, w), False, k == 1) for k, (d, lo, w) in enumerate(reg[c:c + 2])])
         if not last:
-            lhl = ts(ap("lHL"), ap("lHS", 15, 64, 16), 2047.0, ADD, 4095.0, MIN)
+            ts(ap("lHL"), ap("lHS", 15, 64, 16), 2047.0, ADD, 4095.0, MIN)
             act(ap("RS", 0, 64), ind(ap("TP"), ap("lHL")), AF.Copy)
-        mm([(ap("CT", 256, 320), ap("IDB"), ap("lNM"), True, False)])
-        mm([(ap("CT", 256, 320), ap("IDH"), ap("lHM"), False, False)])
-        if SLOTS:
-            mm([(ap("JP", 0, 64), ap("IDB"), ap("NM", 0, 64), True, False)] + [(ap("JP", s, 64, 16), ap("IDB"), ap("FL%d" % t, 0, 4), False, False) for s in range(16)])
-            ts(ap("lUF"), ap("lHM"), 3000.0, GT, 1024.0, MUL)
-            mm([(ap("JP", 0, 64), ap("IDB"), ap("lUF"), False, False)])
-        for c in range(4):
-            e = ap("lET", LR[c], LR[c] + 64 - 16 * c)
-            ts(e, reg[c], ap("lHS", 16 * c + 15, 16 * c + 16), EQ)
-            if c == 1 and not last:
-                later(lhl)
-            if SLOTS:
-                mm([(ap("JP", 16 * c, 64), ap("BLK8"), e, False, c == 3)])
-            mm([(ap("CT", 256 + 16 * c, 320), ap("BLK8"), e, False, c == 3)])
-        scan(ap("RS", 64, 128), ap("DR1"), ap("JP", 0, 64) if SLOTS else ap("CT", 256, 320), MAX, MIN)
-        send("RB%d" % t, ap("RS", 64 * last, 128), "rep%d" % t, "lr", borrower)
-        scan(ap("lWS"), ap("DR1"), ap("CT", 256, 320), MAX, MIN)
-        ts(ap("lLO"), ap("lWS", 15, 64, 16), 4095.0, ADD)
-        if last:
-            cp(ap("RSU"), ind(ap("US"), ap("lLO")))
-        else:
-            act(ap("RSU"), ind(ap(lent), ap("lLO")), AF.Copy, bias=255.0 if t else 0.0)
+        cp(ap("lET", 0, 320, 80), ap("FL%d" % t, 0, 4))
+        for c, (d, lo, w) in enumerate(reg):
+            ts(ap("lET", 80 * c + 1, 80 * c + w + 2), ap(d, lo, lo + w + 1), ap("lHS", 16 * c + 15, 16 * c + 16), EQ, ap("DMP", c, c + 1), MUL)
+            most(ap("RS", 64 + c, 65 + c), ap("lET", 80 * c, 80 * c + w + 2))
+        sent.append(len(ops))
+        send("RB%d" % t, ap("RS", 64 * last, 72), "rep%d" % t, "lr", borrower)
+        ts(ap("lWS", 0, 4), ap("RS", 64, 68), 257.0, GT, 8192.0, MUL); tt(ap("lWS", 8, 12), ap("lWS", 0, 4), ap("lHS", 15, 64, 16), ADD)
+        tt(ap("lWS", 16, 20), ap("lWS", 8, 12), ap("DMP", 8, 12), MIN); ts(ap("lLO"), ap("lWS", 16, 20), 2047.0, ADD)
+        act(ap("RSU"), ind(ap(lent), ap("lLO")), AF.Copy, bias=255.0 if t else 0.0)
         send("RV%d" % t, ap("RSU"), "reu%d" % t, "lu", borrower)
         if last or not t:
             cp(ind(ap("US"), ap("lLO")), ap("C255", 0, 64))
@@ -649,9 +674,9 @@ def build(rank, core, T, topo):
                     ts(ap("UF", k, k + 256), ap("US", k, k + 256), -255.0, ADD)
                 else:
                     act(ap("UF", k, k + 256), ap("US", k, k + 256), AF.Copy, bias=-255.0)
-            iota(ap("UF", S, 4480), [[0, 4480 - S]], -255); iota(ap("ZERO"), [[0, 128]], 0); iota(ap("US", ZD, 4480), [[0, 4480 - ZD]], 0)
+            iota(ap("UF", S, 4480), [[0, 4480 - S]], -255); iota(ap("ZERO"), [[0, 128]], 0)
         if not last:
-            mm([(ap("MS", 96, 97), ap("ONEB"), ap("SC", 15, 16), True, True)])
+            mm([(ap("MS", 96, 97), ap("ONEB"), ap("SC", 16, 17), True, True)])
             cp(ap("PPI"), ap("MS", 96, 97)); ts(ap("PPJ"), ap("PPI"), 63, AND); ts(ap("b16b" if t % 2 else "b16a"), ap("PPJ"), 1024.0, MUL, ap("th16"), ADD)
         if t:
             ts(ind(ap(cx, OLD, END), ap("OBU")), ap("IC64"), 1.0, MUL, float(S + CAP * (t - 1)), ADD); later(scn)
@@ -665,17 +690,39 @@ def build(rank, core, T, topo):
             act(ap(wy, OLD, OLD + L), ind(ap(wx), ap("JL2")), AF.Copy)
         act(ap(cy, OLD, OLD + L), ind(ap(cx), ap("JL2")), AF.Copy)
         rb = "RB%d" % t
-        if SLOTS:
-            cp(ap("OBU"), ap(rb, 79, 128, 16))
-        else:
-            tt(ap("OB"), ap(rb, 79, 128, 16), ap("FAI"), MAX); cp(ap("OBU"), ap("OB"))
+        cp(ap("OBU"), ap(rb, 64, 68))
         if not last:
             cp(ind(ap(ty, OLD, END), ap("OBU")), ap(rb, 0, 64)); cp(ind(ap(wy, OLD, END), ap("OBU")), ap("WTAB", 0, 64))
         dma(ext("yu", S + CAP * t, S + CAP * t + CAP), ap("RV%d" % t), 2.0)
         if last:
             ts(ind(ap(cy, OLD, END), ap("OBU")), ap("IC64"), 1.0, MUL, float(S + CAP * t), ADD)
             dma(ext("yc", L * t, L * t + L), ap(cy, OLD, OLD + L, 1, slice(0, 128, 16)), 2.0)
-    dma(ext("yu", 0, S), ap("US", 0, S), 6.0)
+    dma(ext("yu", 0, S), ap("US", 0, S), 4.5)
+    seen, at, early, both = {}, {}, None, None
+    for i, o in enumerate(ops):
+        if o["k"] == 0:
+            early = early or at
+            seen, at = {}, {}
+        w = "<".join(x[-1 if k else 0][0].replace("th16", "b").rstrip("0123456789ab") if x else "" for k, x in enumerate((o["W"], o["R"])))
+        seen[o["q"], w] = seen.get((o["q"], w), 0) + 1
+        o["name"] = (o["k"] < 0, o["q"], w, seen[o["q"], w])
+        if o["q"] != "N":
+            at[w + "#%d" % seen[o["q"], w]] = i
+        if early and (i + 1 == len(ops) or ops[i + 1]["k"] == 0):
+            if not both:
+                both = dict(at, **early)
+                for chain in START + tuple("HO<HI " + y for y in LATER.split()):
+                    got = [both[y if "#" in y else y + "#1"] for y in chain.split()]
+                    for a, b in zip(got, got[1:]):
+                        ops[b].setdefault("after", []).append(a)
+            for chain in CHAINS:
+                if i + 1 == len(ops) or "X<LO#1" in at:
+                    chain = chain.replace(*AT_LAST)
+                if "X<LO#1" in at:
+                    chain = chain.replace(*AT_FIRST)
+                got = [at[x] for x in (y if "#" in y else y + "#1" for y in chain.split()) if x in at]
+                for a, b in zip(got, got[1:]):
+                    ops[b].setdefault("after", []).append(a)
     return ops
 
 
@@ -761,7 +808,8 @@ def order(ops, memo=None):
                     ready.append((key[k], k)); ready.sort()
         return beg, end
     pri = [0.0] * n
-    for i in range(n - 1, -1, -1):
+    beg, end = place(range(n), False)
+    for i in sorted(range(n), key=lambda i: (-beg[i], -i)):
         pri[i] = ops[i]["c"] + max([pri[k] + d for k, d in posts[i]], default=0.0)
     beg, end = place([-x for x in pri], False)
     best = (max(end), [max(pri) - x for x in pri])
@@ -775,7 +823,7 @@ def order(ops, memo=None):
     for o in ops:
         if o["k"] == 0:
             seen = {}
-        w = (o["k"] < 0, o["q"], o["W"][0][0].rstrip("0123456789ab") if o["W"] else "", o["R"][-1][0].rstrip("0123456789ab") if o["R"] else "")
+        w = (o["k"] < 0, o["q"], o["W"][0][0].rstrip("0123456789ab") if o["W"] else "", o["name"][2])
         seen[w] = seen.get(w, 0) + 1
         name.append(w + (seen[w],))
     first = [i for i in range(n) if ops[i]["k"] == 0] + [n]
@@ -796,7 +844,7 @@ def order(ops, memo=None):
         above.append(far)
     guess = []
     for cy, ga, sct, hop, own, flight, sfix, pe in GUESSES:
-        c = [a + cy * (b * (pe if o["q"] == "P" else 1) + ga * g + sct * s) + sfix * (o["q"] == "S") + flight * (o["q"] == "N") for o in ops for a, b, g, s in [o["v"]]]
+        c = [a + cy * (b + ga * g + sct * s) + pe * o["many"] + sfix * (o["q"] == "S") + flight * (o["q"] == "N") for o in ops for a, b, g, s in [o["v"]]]
         guess.append((c, [o.get("hold", x) for o, x in zip(ops, c)], [[(j, 0.0 if o["q"] == "N" and not o["pre"][j] else own if ops[j]["q"] == o["q"] else hop) for j in near[i]] for i, o in enumerate(ops)]))
 
     key, _ = place(base, False)
@@ -890,7 +938,7 @@ def order(ops, memo=None):
         same = {}
         for i in range(first[0], n):
             same.setdefault(name[i], []).append(i)
-        key = improve(key, first[2], first[5], goal[4], {i: same[name[i]] for i in range(first[2], first[5])}, 2 * TRIES)
+        key = improve(key, first[2], first[5], goal[4], {i: same[name[i]] for i in range(first[2], first[5])}, TRIES)
         for i in range(first[1] - 1, -1, -1):
             if name[i] not in mid:
                 key[i] = min([key[k] - d for k, d in posts[i]], default=zero) - ops[i]["c"]
@@ -898,8 +946,7 @@ def order(ops, memo=None):
         beg, _ = place(key, False, first[3])
         shift = key[first[2] + 1] - beg[first[2] + 1]
         key[:first[2]] = [x + shift for x in beg[:first[2]]]
-        key = improve(key, 0, first[1], goal[0], {i: [i] for i in range(goal[0])}, TRIES // 2)
-        key = improve(key, 0, first[2], goal[1], {i: [i] for i in range(first[1])}, TRIES // 2)
+        key = improve(key, 0, first[2], goal[1], {i: [i] for i in range(first[1])}, TRIES)
         key = improve(key, first[1] - 80, first[3], goal[2], {i: [i] for i in range(first[1] - 80, first[2])}, TRIES // 4)
         key = improve(key, first[4], n, None, {i: [i] for i in range(first[5], n)}, TRIES // 4)
         memo["key"] = key

@@ -1,5 +1,6 @@
 import numpy as np
 from concourse.mybir import dt, AluOpType, AxisListType, ActivationFunctionType
+from concourse.bass import DstId, RemoteDMATransfer
 import comms_topo
 
 RO, L, S, CAP = 6, 256, 4096, 64
@@ -7,6 +8,7 @@ UNF = 4000.0
 BIG = 4194304.0
 OLD, END = 256, 656
 TINY = 1e-7
+ROUND = 12582912.0
 ZD = 4352
 
 _B = {}
@@ -28,7 +30,7 @@ _b("g16", 16, F); _b("g8", 4, F); _b("g8m", 4, F); _b("pen2", 2, F); _b("pen4", 
 _b("MWR", 256, F); _b("RST", 256, F); _b("BLKH", 128, H); _b("BLKB", 128, BF); _b("BLKN", 128, BF); _b("ONEB", 128, BF)
 _b("IDH", 128, H); _b("IDB", 128, BF); _b("IDN", 128, BF); _b("IDHN", 128, H); _b("I255", 128, BF); _b("SH1", 128, BF); _b("SH2", 128, BF)
 _b("TRL", 128, BF); _b("TRG", 128, BF); _b("PL", 128, BF); _b("PR", 128, BF); _b("PH", 128, H); _b("SEL", 144, BF); _b("REP8", 128, H, 8)
-_b("WT", 24 * 128, H); _b("PZ4", 128, BF); _b("RS4", 128, F); _b("RS16", 64, F)
+_b("WT", 16 * 128, H); _b("PZ4", 128, BF); _b("RS4", 128, F); _b("RS16", 64, F)
 _b("C255", 128, BF); _b("THR", 16, F); _b("KJ", 48, F); _b("K256", 16, BF); _b("ZZ", 128, BF); _b("one16", 16, F); _b("oneR", 256, BF); _b("JW0", 16, F)
 _b("J256", 16, H); _b("FIX", 32, F); _b("CL", 16, U16); _b("CJ", 32, U16); _b("IC64", 64, F); _b("PF64", 64, F)
 _b("DRS", 256, F); _b("DMP", 16, F); _b("NJ", 16, F); _b("I512", 128, H); _b("lTR", 160, BF)
@@ -39,32 +41,40 @@ for _k in "01":
 _b("ZB", 512, BF); _b("UVS", 128, I); _b("UVA", 32, I); _b("UVW", 16, I); _b("UVQ", 16, I)
 _b("HV", 256, I); _b("KU", 256, F); _b("KRX", 256, F); _b("LS", 16, U16); _b("LC", 16, U16); _b("RS5", 128, F); _b("R5", 128, F); _b("K5", 128, I); _b("HI", 256, I); _b("HO", 256, U16); _b("HT", 528, F)
 _b("X", ZD, BF); _b("STB", 128, BF); _b("A", 4096, BF); _b("RM", 512, F); _b("RI", 320, F); _b("KS", 64, I)
-_b("PO", 16, F); _b("PN", 16, BF); _b("SC", 32, BF); _b("POJ", 16, H); _b("OF", 16, U16); _b("ZA", 768, BF)
+_b("PO", 16, F); _b("PN", 16, BF); _b("SC", 32, BF); _b("POJ", 16, H); _b("OF", 16, U16); _b("ZA", 768, F)
 _b("PPI", 1, I); _b("PPJ", 1, I); _b("MI", 16, I); _b("LL", 16, U16)
-_b("HM", 256, H); _b("HS", 256, F); _b("HD", 16, F); _b("LA", 16, F); _b("UR", 256, BF); _b("EX", 1024, BF); _b("W2", 128, BF); _b("B30", 128, BF); _b("NM2", 128, BF); _b("P2", 48, F); _b("HRH", 256, H); _b("HL", 16, U16)
-_b("ET", 16 * 128, BF, inner=128); _b("WD", 256, BF); _b("WN", 512, BF); _b("STP", 128, F); _b("MF", 128, BF); _b("WS", 256, F); _b("LO", 16, U16)
+_b("HM", 256, H); _b("HS", 256, F); _b("HD", 16, F); _b("LA", 16, F); _b("UR", 256, BF); _b("W2", 128, BF); _b("B30", 128, BF); _b("NM2", 128, BF); _b("P2", 48, F); _b("HRH", 256, H); _b("HL", 16, U16)
+_b("ET", 16 * 128, BF, inner=128); _b("WD", 256, BF); _b("WN", 512, BF); _b("STP", 128, F); _b("MF", 128, BF); _b("WS", 256, F); _b("LO", 32, U16)
 _b("EE", 512, H); _b("FI", 32, I); _b("FB", 32, F); _b("FC", 32, F); _b("NW", 16, F); _b("UN0", 16, F)
 _b("SG", 2048, BF); _b("SJ", 16, F); _b("J2", 16, F); _b("JB", 32, BF); _b("JL", 16, U16); _b("FW", 256, BF); _b("JX", 16, F); _b("JL2", 16, U16)
 _b("EA", 768, F); _b("E32", 256, F); _b("EM", 64, F); _b("EQ", 64, F); _b("FAI", 4, I); _b("FA", 4, F); _b("OB", 4, F); _b("OBU", 4, U16)
 for _k in range(RO):
-    _b("ZL%d" % _k, 64, BF); _b("RB%d" % _k, 72, BF); _b("RV%d" % _k, 64, BF); _b("FL%d" % _k, 8, BF)
-_b("FS", 8, BF); _b("lUF", 64, BF)
+    _b("LM%d" % _k, 32, U16); _b("LN%d" % _k, 8, U16); _b("LX%d" % _k, 8, U16)
+    if _k < RO - 1:
+        _b("UL%d" % _k, 4480, BF)
+    if _k in (0, RO - 1):
+        _b("ZN%d" % _k, 64, BF); _b("RB%d" % _k, 72, BF); _b("RV%d" % _k, 64, BF)
+for _k in range(3):
+    _b("TL%d" % _k, S, BF)
+for _k in range(4):
+    _b("LP%d" % _k, 4, F); _b("LW%d" % _k, 512, H)
+_b("ZF", 256, F); _b("ZL", 64, BF); _b("NIL", 128, BF); _b("lb", 1, F)
 _b("ZT", 512, BF); _b("lUVS", 64, I); _b("lUVA", 64, I); _b("lUVW", 32, I); _b("lUQ", 32, I); _b("lKU", 64, F)
-_b("lHV", 64, I); _b("lHI", 64, I); _b("lHO", 64, U16); _b("lHT", 528, F); _b("lX", 1024, BF); _b("lA", 1024, BF, inner=32); _b("lY", 256, BF, inner=32)
+_b("lHV", 64, I); _b("lHI", 64, I); _b("lHO", 64, U16); _b("lHT", 528, F); _b("lX", 1024, BF); _b("lA", 1024, BF, inner=32)
 _b("CG2", 128, BF); _b("CZ", 64, BF); _b("PZL", 64, BF); _b("RS32", 64, F); _b("RL", 1024, BF); _b("lHH", 64, H); _b("PK", 256, BF); _b("RW", 128, BF)
-_b("kc", 2, F); _b("k1", 1, H); _b("s1I", 1, I)
+_b("k1", 1, H); _b("s1I", 1, I)
 _b("lRM", 256, F); _b("lKS", 128, I); _b("lMI", 4, I); _b("lLL", 4, U16); _b("lHM", 64, H); _b("lHS", 64, F); _b("lHL", 4, U16)
-_b("lET", 320, BF); _b("RS", 72, BF); _b("RSU", 64, BF); _b("lWS", 64, F); _b("lLO", 4, U16)
+_b("lET", 320, F); _b("RS", 72, BF); _b("RSU", 64, BF); _b("lWS", 8, F); _b("lLO", 8, U16)
 _PS = ["UVP", "ZP", "DA", "DB", "HR", "CT", "MS", "JP"]
 _SIZE = {F: 4, BF: 2, H: 2, I: 4, U16: 2}
-_OWN = ("US", "TP", "WTAB", "UF", "X", "A", "ZA", "RS", "RSU", "FS")
+_OWN = ("US", "TP", "WTAB", "UF", "X", "A", "ZA", "RS", "RSU", "LO", "lLO", "ZL")
 SCRATCH = {}
 _AT = {}
 _fill = {}
 for _n, (_w, _sh, _d, _in) in _B.items():
     if _in:
         SCRATCH[_n] = (_w, [128, _sh[1] // _in, _in], _d); _AT[_n] = (_n, 0)
-    elif _n in _OWN or _n[:2] in ("ZL", "RB", "RV", "FL") or _sh[0] != 128:
+    elif _n in _OWN or _n[:2] in ("UL", "TL", "LM", "LN", "LX", "LP", "LW", "ZN", "RB", "RV") or _sh[0] != 128:
         SCRATCH[_n] = (_w, _sh, _d); _AT[_n] = (_n, 0)
     else:
         _q = 32 // _SIZE[_d]
@@ -74,8 +84,51 @@ for _d, _c in _fill.items():
     SCRATCH["ar_" + _d] = ("sbuf", [128, _c], _d)
 for _n in _PS:
     SCRATCH[_n] = ("psum", [128, 512], F); _AT[_n] = (_n, 0); _B[_n] = ("psum", [128, 512], F, 0)
-ND = 40
-SEMAPHORES = ["sV", "sS", "sP", "sG", "la", "lr", "lu", "lf"] + ["fai%d" % k for k in range(RO)] + ["reu%d" % k for k in range(RO)] + ["ask%d" % k for k in range(RO)] + ["rep%d" % k for k in range(RO)] + ["d%d" % k for k in range(ND)]
+ND = 42
+_AT["ksc"], _AT["th16"] = ("LP3", 2), ("LP3", 3)
+SEMAPHORES = ["sV", "sS", "sP", "sG", "lp", "hl", "hT0", "hT1", "hT2", "prm", "prw", "lq"] + ["d%d" % k for k in range(ND)] + ["x%d" % k for k in range(36)]
+SEMAPHORES += [n + str(k) for n in ("ma", "mb", "mn", "mx", "hU", "ur") for k in range(RO)] + ["tr%d" % k for k in range(3)]
+ASK = (0, RO - 1)
+NEAR = 2048
+STAGED, TNEAR = (576, 576, 896), 896
+FAR = (("T", 1, 0, 576), ("T", 1, 576, 1152), ("T", 2, 0, 1152), ("U", 1, 0, 0), ("T", 2, 1152, 2048), ("T", 0, 0, 256), ("U", 2, 0, 0),
+       ("T", 0, 256, 1408), ("U", 3, 0, 0), ("T", 0, 1408, 2048), ("U", 4, 0, 0))
+
+
+def bits(engines):
+    m = 0
+    for e in engines:
+        m |= 1 << e
+    return m
+
+
+def helpers(core, T, topo):
+    return [h for h in topo.cores_of(core) if topo.die(h) != topo.die(core) and all(topo.may_write(h, d) for d in T.cores)][:2]
+
+
+def helper_program(g, core, rank, side, T, topo):
+    n = [0]
+
+    def on(name, lo, hi, src, sem, t):
+        dst = T.cores[(rank - 1 - t % 3) % 4]
+        rid, pid, se = topo.addr(dst)
+        g.remote_dma(T[name][:, lo:hi], T[src][:, lo:hi], T.sem[sem], T.sem.hl, pid, rid, topo.mask(core, dst))
+        n[0] += len(topo.engines(core, dst))
+    own = topo.cores_of(core)
+    got = len([e for e in topo.engines(core, own[own.index(core) - 1]) if e not in topo.engines(core, T.cores[(rank + 1) % 4])]) // 2
+    landed = 0
+    for what, k, lo, hi in FAR:
+        if what == "U":
+            lo, hi = NEAR + side * (S - NEAR) // 2, NEAR + (side + 1) * (S - NEAR) // 2
+            g.wait_ge(T.sem["hU%d" % k], got)
+            on("UL%d" % k, lo, hi, "UL%d" % k, "ur%d" % k, k)
+        else:
+            while sum(STAGED[:landed]) < hi:
+                g.wait_ge(T.sem["hT%d" % landed], got); landed += 1
+            top = (side + 1) * S // 2
+            on("TL%d" % k, top - hi, top - lo, "TL0", "tr%d" % k, k)
+    g.wait_ge(T.sem.hl, n[0])
+
 
 NS = 5
 BYS = {0: "CT", 2: "ZP", 6: "UVP"}
@@ -86,28 +139,48 @@ PROBE = [("gather", 0, 2), ("gather", 4, 2), ("gather", 2, 2), ("abs", 0, 2), ("
          ("two", 10, 1), ("gather", 15, 1), ("abs", 13, 1), ("abs", 14, 1), ("abs", 15, 1), ("single", 12, 0), ("fold", 0, 0), ("single", 13, 1),
          ("single", 14, 2), ("single", 15, 3)]
 KEPT = ("gather", "abs", "two", "four", "minus")
-CHAINS = ("EE<WX UVS<UVP EE<WX#2 UVA<UVS", "X<ZB HV<KU#2 FI<MS HI<HV#2 NW<FI HO<HI#2 RS< X<ZB#2 RI<NW X<ZB#3",
-          "K<R SC<K POJ<NJ MI<K HT<HI OF<MS LL<MI ZA<OF HM<MWR HS<HM HM<MWR#2 HRH<HR ET<HS ET<HS#8 HS<HM#2 HRH<HR#2 FS<FAI WS<CT "
-          "ET<HS#9 LO<LA ET<HS#16 HL<HS J<KJ WS<DB lUVS<UVP LA<HD#2 lUVA<lUVS LO<LA#2 lUVW<lUVA JX<JB",
-          "lHO<lHI lHH<lHI lX<ZT lX<ZT#2 lX<ZT#3 X<LO DJ<J lRM< JL<JX lRM<#2 lKS<HR lKS<HR#2 lKS<UVP lKS<UVP#2 lMI<lKS lLL<lMI lHM<MWR lET<FL lHS<lHM lHL<lHS "
-          "lET<DMP RS<lET#4 FW<NM lWS<RS CMH<FW lWS<lHS JL<CMH lWS<DMP lLO<lWS CX<OBU PPI<MS OBU<RB",
-          "ZB<ZP#2 E<JP X<HO", "lHT<CT WX<HL WX<JL", "SJ<THR#5 EA<OF SJ<THR#6 SJ<THR#16 CX<HR UR<HR UF<LO ZT<JP UF<LO#2 ZT<JP#2 lX<lHO lA<lX lA<lX#3 lHT<CT "
-          "WD<DB MF<HL WN<MS RS<lHL TX<HL TX<JL RSU<lLO UF<lLO WX<JL CX<JL",
-          "UVP<TX ZP<TX JP<EE MS<EE#2 CT<ZB ZP<ZB MS<EE#3 MS<EE#4 CT<X", "UVP<ZL JP<ZL JP<ZL#2 UVP<PZL ZP<ZT JP<PZL CT<lHH ZP<lX DA<lA JP<lA HR<lA UVP<lA ZP<lTR HR<lTR HR<lHM ZP<lHM",
-          "<ZA <FS <RS")
-START = ("pI< IC< CG< CS< C< CG<#2 oneR< SEL<B RS<#2 SLP<B kz< SLQ<B TRG<BLKB TRL<BLKB SC< ZA< HT< CG<#3 ONEB< PK<ONEB PK<ONEB#2 FS< C<#2 RW< "
-         "CZ< ML< RL<ONEB RL<ONEB#2 <ZA RL<ONEB#3 RL<ONEB#4 K< JB< SH<B SH<B#2 lTR< lHT< <FS RS< STB< X< WN< TX< WX< WX<#2 <RS",
+CHAINS = ("EE<WX UVS<UVP EE<WX#2 UVA<UVS", "HO<HI KU<KRX#2 HV<KU#2 FI<MS HI<HV#2 NW<FI HO<HI#2 RS< HT<HI X<ZB RI<NW X<ZB#2 X<ZB#3",
+          "HT<HI K<R MI<K SC<K LL<MI POJ<NJ HM<MWR HM<MWR#2 OF<MS HS<HM HRH<ZP HS<HM#2 HRH<HR "
+          + " ".join("ET<HS#%d" % k for k in range(1, 17)) + " WS<CT HD<DRS ZL<ZA LA<HD HD<DRS#2 LO<LA WS<DB HL<HS LA<HD#2 J<KJ LO<LA#2 "
+          "lUVS<UVP JB<J lUVA<lUVS DJ<J lUVW<lUVA lKU<LP lUQ<lUVW lKU<LP#2 lHV<lUQ lHV<lUQ#2 lHI<lHV "
+          "UL<LX lHO<lHI UL<LM JX<JB UL<LM#2 lHH<lHI lX<ZT lX<ZT#2 lX<ZT#3 JL<JX l<LP FW<NM lRM<l CMH<FW lRM<l#2 JL<CMH lKS<DB lKS<DB#2 lKS<UVP lKS<UVP#2 "
+          "EQ<EA lMI<lKS FAI<EQ lLL<lMI FA<FAI lHM<MWR PPI<MS lHS<lHM PPJ<PPI lET<lHS lHL<lHS "
+          "lET<DMP lET<DMP#2 lET<DMP#3 lET<DMP#4 lWS<lET lWS<lET#2 lWS<lET#3 lWS<lET#4 OBU<FA lLO<lWS OBU<FA#2 OBU<FA#3 OBU<FA#4 TX<OBU WX<OBU",
+          "ZB<ZP#2 E<JP X<HO A<X#6 ZF<ZB ZA<OF", "E<JP SJ<THR#13 X<HO", "ZA<OF EA<OF UF<LO WD<CT UF<LO#2 WD<DB UR<ZP UR<HR MF<HL ZT<JP ZT<JP#2 WN<MS lX<lHO lA<lX lA<lX#3 lHT<CT TX<HL TX<JL WX<HL RS<lHL "
+          "WX<JL CX<ZP CX<HR CX<JL RSU<lLO",
+          "UVP<TX ZP<TX JP<EE MS<EE#2 MS<EE#3 MS<EE#4 CT<ZB ZP<ZB CT<X", "DB<lX DA<lA JP<lA DB<lA UVP<lA DA<lHM JP<lHM",
+          "<LO <LO#2 US<UF <US#2 <lLO <lLO#2 <US")
+ASKED = CHAINS[1:2] + (
+    "HT<HI K<R SC<K POJ<NJ MI<K LL<MI OF<MS HM<MWR HM<MWR#2 HS<HM HRH<ZP HS<HM#2 HRH<HR HD<DRS " + " ".join("ET<HS#%d" % k for k in range(1, 5)) + " ZL<ZA "
+    + " ".join("ET<HS#%d" % k for k in range(5, 17)) + " WS<CT HD<DRS#2 LA<HD LO<LA WS<DB HL<HS LA<HD#2 US<LO UL<LO LO<LA#2 J<KJ US<LO#2 UL<LO#2 "
+    "lUVS<UVP JB<J lUVA<lUVS lUVW<lUVA lKU<LP lUQ<lUVW lKU<LP#2 lHV<lUQ lHV<lUQ#2 JX<JB lHI<lHV JL<JX lHO<lHI lHH<lHI lX<ZT lX<ZT#2 lX<ZT#3 X<LO "
+    "lKS<DB lKS<DB#2 lKS<UVP lKS<UVP#2 lMI<lKS lLL<lMI lHM<MWR lHS<lHM lET<lHS lHL<lHS lET<DMP lET<DMP#2 lET<DMP#3 lET<DMP#4 lWS<lET lWS<lET#2 lWS<lET#3 lWS<lET#4 "
+    "RS<lWS lLO<lWS FW<NM US<lLO CMH<FW JL<CMH FA<FAI OBU<FA",
+    "ZB<ZP#2 E<JP X<HO A<X#6 ZF<ZB ZA<OF", "lHT<CT CX<ZP CX<HR RSU<lLO", "ZA<OF EA<OF UF<LO UF<LO#2 ZT<JP ZT<JP#2 lX<lHO lA<lX lA<lX#3 lHT<CT MF<HL TX<HL WN<MS RS<lHL RSU<lLO TX<JL WX<JL CX<JL") + CHAINS[-3:-1] + (
+    "<ZL US<UF <RS <lLO <US <US#2",)
+AFTER = tuple(c.replace("UF<LO WD<CT UF<LO#2 WD<DB UR<ZP UR<HR MF<HL ZT<JP ZT<JP#2 WN<MS lX<lHO", "UR<ZP UR<HR ZT<JP ZT<JP#2 WD<CT WD<DB UF<LO UF<LO#2 MF<HL lX<lHO WN<MS")
+              for c in CHAINS)
+FINAL = CHAINS[:1] + tuple(c.replace(" X<LO ", " FW<NM lRM< CMH<FW lRM<#2 JL<CMH ").replace("RS<lWS lLO<lWS FW<NM US<lLO CMH<FW JL<CMH", "lLO<lWS RS<lWS UL<lLO CX<OBU")
+              .replace("ZT<JP ZT<JP#2 lX<lHO lA<lX lA<lX#3 lHT<CT MF<HL TX<HL WN<MS", "MF<HL ZT<JP ZT<JP#2 lX<lHO WN<MS lA<lX lA<lX#3 lHT<CT") for c in ASKED)
+START = ("pI< IC< CG< CS< C< CG<#2 oneR< SEL<B RS< SLP<B kz< SLQ<B <TP <TP#2 <TP#3 <TP#4 HT< TRG<BLKB TRL<BLKB SC< ZA< EA< CG<#3 ONEB< PK<ONEB PK<ONEB#2 "
+         "CZ< C<#2 RL<ONEB RL<ONEB#2 RL<ONEB#3 RL<ONEB#4 US< KJ< KJ<#2 K< JB< <ZL SH<B SH<B#2 ML< STB< RL<ONEB#5 RL<ONEB#6 RL<ONEB#7 RL<ONEB#8 lHT< lTR< RS<#2 <TP#5 WN< TX< WX< WX<#2 <RS <RSU <US <US#2 "
+         "< <LW ZERO< IC<#2 NIL<",
          "sI<pI pF<pI sF<sI nsB<sF s2I<sI gF<sF gx<sF sge<sF slt<sF s2F<s2I pm<sge ns<s2F pm<pF g<gx IDB<pF JW<sF PH<pm g8m<slt g8p<sge BLKB<gF REP<pF "
          "BLKH<gF hwf<hwi c8h<c hwh<hwf ksc<kmi PL<sge kh<ksc DRS<JW ws<MS PR<slt CM<CT WT<ws c8i<c WT<ws#2 CL<CM WT<ws#3 c8w<c8i WT<ws#10 KR<MS LC<IC "
-         "TX<CL LS<sF UVS<UVP", "RL<pF RL<pF#2 RL<pF#3 RL<pF#4 ZA<OF",
-         "W<P NM<rF RST<CS EA<OF B<BLKB#3 US<IC B<BLKB#2 I<IDB SJ<THR#10", "PZL<s1F lTR<pm DMP<JW DMP<JW#2 US<IC#2 ZT<JP")
-LATER = "J<JW I<pF THR<JW s1T<sF PF<IC P<one hwg<hwf k<kmi s1I<sI pm<sF KJ<IC KJ<IC#2 DJ< IC<IC RL<pF"
-AT_FIRST = ("MF<HL WN<MS RS<lHL TX<HL TX<JL RSU<lLO", "RS<lHL MF<HL WN<MS RSU<lLO TX<HL TX<JL")
-AT_LAST = ("FW<NM lWS<RS CMH<FW lWS<lHS JL<CMH lWS<DMP lLO<lWS CX<OBU", "lWS<RS lWS<lHS lWS<DMP lLO<lWS US<lLO FW<NM")
+         "TX<CL LS<sF UVS<UVP", "EE<WX UVS<UVP EE<WX#2 UVA<UVS",
+         "HT<IC CX<IC CX<IC#2 NJ<JW B<BLKB DRS<CS NM<nsB PZ<ns RS<C MWR<NM RST<CS TX<CL WX<DB KRX<LC ZB<ZP ZB<ZP#2 E<JP MS<DA X<HO", "X<ZB#7 hwg<hwf K<R LW<hwg MI<K LW<hwg#2 LL<MI", "ET<HS#16 LW<hwg#3 LA<HD LW<hwg#4 LO<LA",
+         "lX<ZT#3 X<LO lRM< lRM<#2 lKS<DB lKS<UVP#2 DJ< lMI<lKS lLO< lLL<lMI LO< lHM<MWR",
+         "A<X#6 W<P NM<rF B<BLKB#3 ZA<OF PZL<s1F lTR<pm DMP<JW DMP<JW#2 ZT<JP",
+         "CMH<FW UF<USV JL<CMH UF<USV#2 PPI<MS UF<USV#3 PPJ<PPI UF<USV#4 FA<FAI UF<USV#5 OBU<FA OBU<FA#2 OBU<FA#3 OBU<FA#4 UF<USV#6 TX<OBU", "lKS<UVP#2 DJ<J FAI<EQ lET<DMP", "JP<lHM MS<SC#2",
+         "EA<OF UR<ZP UR<HR WD<CT WD<DB ZT<JP", "MF<HL TX<HL WN<MS RS<lHL RSU<lLO WX<HL UF<US TX<JL WX<JL CX<JL UF<US#2")
+LATER = "J<JW I<pF THR<JW s1T<sF P<one s1I<sI pm<sF"
+SECOND = ("UF<US#2 ZB<ZP ZB<ZP#2 E<JP UF<US#3 X<HO", "A<X#6 UF<US#4 UF<US#5 ZA<OF UF<US#6 EA<OF",
+          "EE<WX UF<USV#7 UVS<UVP UVA<UVS UF<USV#8 UVW<UVA UVQ<UVW UF<USV#9 HV<KU UF<USV#10 HI<HV UF<USV#11 HO<HI KU<KRX#2 UF<USV#12 HV<KU#2",
+          "RI<RI#2 UF<USV#13 RI<RI#3 UF<USV#14 R<RI UF<USV#15 K<R UF<USV#16 MI<K", "LO<LA#2 lUVA<lUVS UF<USV#17 lUVW<lUVA lUQ<lUVW UF<USV#18 lHV<lUQ#2 UF<USV#19 lHI<lHV UF<USV#20 lHO<lHI")
 MERGE = 3
 ZERO = 0
 SLOTS = 1
-CONV = 3
+CONV = 10
 PARTS = 2
 ZBF = 1
 INORDER = 0
@@ -128,10 +201,10 @@ JA = 8
 CY = 0.00104
 GA, SCT = 1.56, 3.8
 HOP, OWN, ISSUE = 0.2, 0.11, 0.1
-FLIGHT, SEND, SFIX, PE = 2.0, 0.5, 0.03, 0.5
-GUESSES = ((CY, GA, SCT, HOP, OWN, FLIGHT, SFIX, 0.0), (0.0009, 1.15, 2.5, 0.14, 0.08, 1.0, 0.05, 0.005), (0.00125, 1.9, 5.5, 0.2, 0.12, 2.6, 0.03, 0.0),
-           (0.00092, 1.5, 3.5, 0.18, 0.1, 3.0, 0.06, 0.04))
-TRIES, SEED, HEAT = 7000, 1, 0.03
+FLIGHT, SEND, SFIX, PE = 1.3, 0.35, 0.04, 0.5
+GUESSES = ((CY, GA, SCT, HOP, OWN, FLIGHT, SFIX, 0.0), (CY, GA, SCT, HOP, OWN, 2.2, 0.03, 0.0), (0.00125, 1.9, 5.5, 0.2, 0.12, 1.6, 0.03, 0.0),
+           (0.00092, 1.5, 3.5, 0.22, 0.12, 2.6, 0.06, 0.03))
+TRIES, SEED, HEAT = 9000, 1, 0.03
 
 
 def build(rank, core, T, topo):
@@ -280,17 +353,56 @@ def build(rank, core, T, topo):
         put("G", lambda g: g.dma_start(res(o), res(a), accum_op=AluOpType.add, max_dma_last_dim=4096), [a, o] + list(behind), [o], cost, sem=k, inc=16)
         ops[-1]["hold"] = 1.0
 
-    def send(o, a, sem, loc, dst):
-        rid, pid, se = topo.addr(dst)
-        m = 0
-        for e in topo.engines(core, dst)[:8]:
-            m |= 1 << e
-        k = put("G", lambda g: g.remote_dma(T[o][:, a[2]:a[3]], res(a), T.sem[sem], T.sem[loc], pid, rid, m), [a], [], SEND, sem=loc, inc=0)
-        ops[-1]["n"] = len(topo.engines(core, dst)[:8])
-        put("N", None, [], [ap(o)], 0.0, sem=sem, inc=8)
-        ops[-1]["after"] = [k]
-        put("N", None, [a], [], 0.0)
+    def dma_cast(o, a, cost):
+        k = "d%d" % nd[0]; nd[0] += 1
+        put("G", lambda g: g.dma_start(res(o), res(a)), [a], [o], cost, sem=k, inc=16)
+        ops[-1]["hold"] = 1.0
+
+    def arrives(o, sem, inc, ks, cost=0.0):
+        put("N", None, [], o, cost, sem=sem, inc=inc)
+        ops[-1]["after"] = list(ks)
+
+    def leaves(fn, reads, loc, n, cost):
+        k = put("G", fn, reads, [], SEND, sem=loc, inc=0)
+        sent.append(k)
+        ops[-1]["n"] = n
+        put("N", None, reads, [], cost)
         ops[-1]["after"] = [k]; ops[-1]["left"] = k
+        return k
+
+    def send(o, a, sem, loc, dst, cost=0.0):
+        loc = "x%d" % len(sent)
+        rid, pid, se = topo.addr(dst)
+        return leaves(lambda g: g.remote_dma(T[o][:, a[2]:a[3]], res(a), T.sem[sem], T.sem[loc], pid, rid, topo.mask(core, dst)), [a], loc,
+                      len(topo.engines(core, dst)), cost)
+
+    def swap(o, a, sem, loc, dst):
+        k = send(o, a, sem, loc, dst)
+        arrives([ap(o, a[2], a[3])], sem, ops[k]["n"], [k])
+        return k
+
+    def stage(name, src, lo, step, w, sem, loc):
+        hs, loc = helpers(core, T, topo), "x%d" % len(sent)
+        free = [e for e in topo.engines(core, hs[0]) if e not in topo.engines(core, T.cores[(rank + 1) % 4])]
+        n = len(free) // len(hs)
+
+        def fn(g):
+            tr = []
+            for i, h in enumerate(hs):
+                rid, pid, se = topo.addr(h)
+                a = lo + i * step
+                tr.append(RemoteDMATransfer(dst_ids=[DstId(rid=rid, pnc=pid)], dma_engine_mask=bits(free[n * i:n * i + n]), remote_sem=T.sem[sem],
+                                            src=T[src][:, a:a + w], dst=T[name][:, a:a + w]))
+            return g.remote_dma_fused(tr, local_sem=T.sem[loc])
+        return leaves(fn, [ap(src, lo + i * step, lo + i * step + w) for i in range(len(hs))], loc, len(free), 3.0)
+
+    def ship(t):
+        near = NEAR
+        ks = [send("UL%d" % t, ap("US", 0, near), "ur%d" % t, "lc", T.cores[(rank - 1 - t % 3) % 4], 5.0)]
+        if near < S:
+            ks.append(stage("UL%d" % t, "US", near, (S - near) // 2, (S - near) // 2, "hU%d" % t, "lb"))
+        arrives([ap("UL%d" % t, 0, S)], "ur%d" % t, ops[ks[0]]["n"] * (3 if near < S else 1), ks, 8.0)
+        return ks
 
     ADD, SUB, MUL, MIN, MAX = AluOpType.add, AluOpType.subtract, AluOpType.mult, AluOpType.min, AluOpType.max
     EQ, NE, GE, GT, LT, LE = AluOpType.is_equal, AluOpType.not_equal, AluOpType.is_ge, AluOpType.is_gt, AluOpType.is_lt, AluOpType.is_le
@@ -304,6 +416,12 @@ def build(rank, core, T, topo):
     dma(ap("kmi"), T.km[:, :], 1.7); later(1); dma(ap("th8"), T.th[:, :], 1.7); later(2)
     dma(ap("TP"), ext("tp", 0, S), 3.8); later(3)
     ldu = dma(ap("US", 0, S), ext("us", 0, S), 6.2); later(4)
+    ks = [send("TL1", ap("TP", h, h + TNEAR), "tr1", "ld", T.cores[(rank - 2) % 4], 3.0) for h in (0, S // 2)]
+    ks += [stage("TL0", "TP", S // 2 - sum(STAGED[:p + 1]), S // 2, w, "hT%d" % p, "lt") for p, w in enumerate(STAGED)]
+    for k in ks:
+        ops[k]["waits"] = [ldu]
+    for k in range(3):
+        arrives([ap("TL%d" % k)], "tr%d" % k, ops[ks[0]]["n"] * 2 * (sum(x[:2] == ("T", k) for x in FAR) + (k == 1)), ks, 8.0)
 
     iota(ap("pI"), [[0, 1]], 0, 1); iota(ap("CG"), [[1, 8], [0, 16]], 0); iota(ap("IC"), [[1, 256]], 0); iota(ap("CS"), [[0, 16], [1, 16]], 0)
     iota(ap("CG8"), [[8, 8], [0, 4], [1, 4]], 0); iota(ap("C3"), [[0, 32], [1, 4]], 0)
@@ -333,16 +451,22 @@ def build(rank, core, T, topo):
         ts(wt(1, qv, 3), ap("CG8"), ap("g8p"), EQ, ap("ws", qv, qv + 1), MUL)
     iota(ap("CG2"), [[8, 8], [1, 2], [0, 8]], 0); iota(ap("CZ"), [[0, 2], [1, 4], [0, 8]], 0); iota(ap("ML"), [[8, 8], [0, 4], [64, 8]], 0)
     fill(ap("ONEB"), 1.0, "G")
-    for qv in (0, 1):
-        for i in (0, 1):
-            ts(wt(2, qv, i), ap("CG2"), ap("g8", i, i + 1), EQ, ap("hwg", qv, qv + 1), MUL)
-    ts(ap("k1"), ap("kmi"), -2048.0, ADD)
+
+    def lw(k, qv, i):
+        return ap("LW%d" % k, 256 * qv + 128 * i, 256 * qv + 128 * i + 128)
+
+    def to_all(name, reads, sem, loc):
+        far = [T.cores[(rank - 1 - k) % 4] for k in range(3)]
+        m = topo.mask(core, far[0]) & topo.mask(core, far[1]) & topo.mask(core, far[2])
+        n = len([e for e in topo.engines(core, far[0]) if m >> e & 1])
+        to = [DstId(rid=topo.addr(c)[0], pnc=topo.addr(c)[1]) for c in far]
+        k = leaves(lambda g: g.remote_dma_fused([RemoteDMATransfer(dst_ids=to, dma_engine_mask=m, remote_sem=T.sem[sem], srcs=[T[name + "3"][:, :]],
+                                                                   dsts=[T[name + str(i)][:, :] for i in range(3)])], local_sem=T.sem[loc]), reads, loc, n, 0.0)
+        arrives([ap(name + str(i)) for i in range(3)], sem, 3 * n, [k], 2.0)
     for k in range(2):
         keep(ap("PK", 128 * k, 128 * k + 128), "ONEB", [[16, 8], [0, 2], [2, 8]], k, EQ, -1)
-    iota(ap("RW"), [[16, 8], [0, 8], [8, 2]], 0)
-    for r in range(4):
-        ts(ap("RL", 128 * r, 128 * r + 128), ap("RW"), float(r), ADD, ap("pF"), EQ)
-        keep(ap("RL", 128 * r + 512, 128 * r + 640), "ONEB", [[16, 8], [0, 8], [8, 2]], r + 4, EQ, -1)
+    for r in range(8):
+        keep(ap("RL", 128 * r, 128 * r + 128), "ONEB", [[16, 8], [0, 8], [8, 2]], r, EQ, -1)
     ts(ap("s1I"), ap("sI"), 1, SHR); cp(ap("s1F"), ap("s1I"))
     act(ap("PZL"), ap("CZ"), AF.Abs, bias=ap("ns2"), scale=8 * BIG); act(ap("PZL"), ap("PZL"), AF.Identity, bias=ap("s1F"))
     for o, v in (("IDB", 1.0), ("IDH", 1.0), ("IDN", -1.0), ("I512", 512.0)):
@@ -352,7 +476,7 @@ def build(rank, core, T, topo):
     act(ap("PZ4"), ap("C3"), AF.Abs, bias=ap("ns2"), scale=8 * BIG); act(ap("RS4"), ap("C3"), AF.Relu, bias=8 * BIG, scale=-8 * BIG)
     act(ap("MWR"), ap("NM"), AF.Relu, bias=1.0, scale=-1.0); act(ap("RST"), ap("CS"), AF.Sign)
     act(ap("TRH"), ap("CS", 0, 64), AF.Relu, bias=ap("s1T"), scale=-16384.0); ts(ap("pm1"), ap("sF"), 47.0, ADD, -16384.0, MUL)
-    act(ap("lTR", 0, 64), ap("IC", 0, 64), AF.Relu, bias=ap("pm1"), scale=16384.0); fill(ap("lTR", 64, 80), UNF, "G"); fill(ap("RS", 64, 72), 0.0, "G")
+    act(ap("lTR", 0, 64), ap("IC", 0, 64), AF.Relu, bias=ap("pm1"), scale=16384.0); fill(ap("lTR", 64, 80), UNF, "G")
     for o, v in (("B512", 1024.0), ("B256", 256.0)):
         act(ap(o), ap("BLKB"), AF.Copy, scale=v)
     ts(ap("ksc"), ap("kmi"), -2048.0, ADD); ts(ap("kh"), ap("CS", 0, 16), ap("sF"), EQ, ap("ksc"), MUL)
@@ -366,7 +490,8 @@ def build(rank, core, T, topo):
     ts(ap("th16"), ap("MS", 8, 9), 2047.5, ADD, 1024.0, MUL)
     ts(ap("JW0"), ap("IC", 0, 256, 16), ap("sF"), ADD)
     act(ap("DRS"), ap("CS"), AF.Copy, bias=-BIG, scale=0.0); ts(ap("DRS", 0, 256, 16), ap("JW0"), S - 2047.0, ADD)
-    act(ap("DMP", 0, 4), ap("JW0", 0, 4), AF.Copy, bias=258.0, scale=2.0); act(ap("DMP", 8, 12), ap("JW0", 0, 4), AF.Copy, bias=258.0 + 2048, scale=2.0)
+    for k in range(2):
+        act(ap("DMP", 8 * k, 8 * k + 4), ap("JW0", 0, 4), AF.Copy, bias=float(ZD + k), scale=2.0)
     ts(ap("c8h"), ap("c8"), -2048.0, ADD)
     mm([(ap("CT", 0, 256), ap("IDB"), ap("NM"), True, False), (ap("CT", 0, 256), ap("REP8"), ap("c8h"), False, True)])
     scan(ap("CM2"), ap("DRS"), ap("CT", 0, 256), MAX, MIN); ts(ap("CL0"), ap("CM2", 15, 256, 16), 2048.0, ADD)
@@ -412,18 +537,15 @@ def build(rank, core, T, topo):
     fill(ap("oneR"), 1.0, "G"); fill(ap("C255"), 255.0, "G")
     rng = [(11 * c, min(254, 20 * c + 19)) for c in range(16)]
     ts(ap("THR"), ap("JW0"), 5.0, MUL, 66.5, ADD)
-    ts(ap("KJ", 16, 32), ap("IC", 0, 16), 31.0, MUL, 19.0, ADD); ts(ap("KJ", 32, 48), ap("IC", 0, 16), 11.0, MUL, 254.0, ADD)
-    tt(ap("KJ", 0, 16), ap("KJ", 16, 32), ap("KJ", 32, 48), MIN)
+    iota(ap("KJ", 0, 12), [[31, 12]], 19); iota(ap("KJ", 12, 16), [[11, 4]], 11 * 12 + 254)
     keep(ap("SH1"), "B256", [[-1, 128]], 1, EQ, 1); keep(ap("SH2"), "B256", [[-1, 128]], -15, EQ, 1)
-    if ZERO:
-        fill(ap("ZZ"), 0.0)
-    if SLOTS:
-        fill(ap("FS"), 0.0, "G")
+    fill(ap("LO", 24, 32), 0); fill(ap("lLO"), 0); fill(ap("NIL"), 0.0, "G")
     fill(ap("K256"), 256.0, "G"); fill(ap("JB", 0, 16), -260.0, "G"); fill(ap("DJ"), 0.0); fill(ap("WN", 256, 512), BIG, "G")
-    iota(ap("X", S, ZD), [[0, ZD - S]], 0); iota(ap("STB"), [[0, 128]], 1024)
-    cp(ap("IC64"), ap("IC", 0, 64)); ts(ap("PF64"), ap("IC", 0, 64), 5.0, MUL, 1344.0, ADD)
+    iota(ap("ZERO"), [[0, 128]], 0); fill(ap("RS", 64, 72), 0.0, "G")
+    iota(ap("STB"), [[0, 128]], 1024); fill(ap("US", S, 4480), 0.0, "G")
+    iota(ap("IC64"), [[1, 64]], 0)
     act(ap("HT", 256, 512), ap("IC"), AF.Copy); fill(ap("HT", 512, 528), UNF, "G"); fill(ap("lHT", 512, 528), UNF, "G")
-    fill(ap("RI", 0, 64), 8 * BIG, "S"); fill(ap("US", S, ZD), 0.0, "S"); fill(ap("US", ZD, 4480), 0.0, "S")
+    fill(ap("RI", 0, 64), 8 * BIG, "S")
 
     for t in range(RO):
         start[0] = len(ops)
@@ -439,20 +561,29 @@ def build(rank, core, T, topo):
             for r in range(4):
                 lst.append((ap("UVP", 64 * qv, 64 * qv + 64), wt(0, qv, r), ap(tx, OLD + r, OLD + r + 253, 4), False, False))
             lst.append((ap("UVP", 64 * qv, 64 * qv + 64), wt(1, qv, 3), ap(tx, OLD + 4, OLD + 257, 4), False, qv == 1))
-        if ZERO:
-            lst = [(ap("UVP", 0, 128), ap("ZZ"), ap(tx, OLD, OLD + 128), False, False)] * ZERO + lst
         mm(lst)
         mm([(ap("ZP", 0, 256), ap("PL"), ap(tx, OLD, OLD + L), True, False), (ap("ZP", 0, 256), ap("PR"), ap(tx, OLD + 1, OLD + 257), False, True)])
         zb = [act(ap("ZB", 256 * k, 256 * k + 256), ap("ZP", 0, 256), AF.Copy, bias=-255.0 if t > 1 else 0.0) for k in range(2)]
+        act(ap("ZF"), ap("ZB", 0, 256), AF.Copy, bias=64.0 + 255.0 * (t > 1))
         under = ap("UF" if t > 1 else "US", 0, S)
-        lent = "UF" if t else "US"
+        less, mark = (255, "NIL") if t > 1 else (0, "C255")
+        ask, copy = t in ASK, t + 1 < RO and t + 1 not in ASK
+        who = 3 if ask else t % 3
+        lent, zl = ("UF" if t else "US", "ZN%d" % t) if ask else ("UL%d" % t, "ZL")
+        if not t:
+            for qv in (0, 1):
+                for i in (0, 1):
+                    ts(lw(3, qv, i), ap("CG2"), ap("g8", i, i + 1), EQ, ap("hwg", qv, qv + 1), MUL)
+            cp(ap("k1"), ap("ksc"))
+        if t:
+            iota(ap(lent, S, 4480), [[0, 4480 - S]], -less); later(start[0] + 1)
         if t == 2:
-            iota(ap("US", 0, 512), [[0, 512]], 255)
+            iota(ap("UL0", 0, 512), [[0, 512]], 255); later(len(ops) - 2)
             for k in range(512, S, 512):
-                dma(ap("US", k, k + 512), ap("US", 0, 512), 7.0, [ap("ZB")])
+                dma(ap("UL0", k, k + 512), ap("UL0", 0, 512), 7.0, [ap("ZB")])
         if last:
             for k in range(0, S, 2048):
-                dma_add(ap("US", k, k + 2048), ap("UF", k, k + 2048), 7.0, [ap("ZB")])
+                dma_add(ap("UL0", k, k + 2048), ap("UF", k, k + 2048), 7.0, [ap("ZB")])
         scan(ap("UVS"), ap("RS4"), ap("UVP", 0, 128), ADD, MIN); later(wtab)
         ts(ap("UVA"), ap("UVS", 3, 128, 4), 4095, AND)
         tt(ap("UVW"), ap("UVA", 0, 16), ap("UVA", 16, 32), MUL)
@@ -527,64 +658,63 @@ def build(rank, core, T, topo):
                 prev[ops[j]["q"]] = j
         scan(ap("K5"), ap("RS5"), ap("R5"), SUB, MIN)
         key = ap("K5", 6, 128, 8)
-        iota(ap("ZA", 0, 64), [[0, 64]], 768); later(*sent[-1:])
+        iota(ap("ZA", 0, 64), [[0, 64]], 768 + 64); later(start[0] + 1)
         mm([(ap("MS", 64, 80), ap("IDH"), ap("J256"), True, False)])
         poor = ap("K5", 7, 128, 8)
         scn = scan(ap("SC", 1, 17), ap("one16"), poor, MUL, SUB); tt(ap("POJ"), poor, ap("NJ"), MAX)
-        ts(ap("HT", 0, 256), ap("HI"), -2047.0, ADD); later(scn)
+        ts(ap("HT", 0, 256), ap("HI"), -2047.0, ADD)
         mm([(ap("MS", 64, 80), ap("TRL"), ap("SC", 1, 17), False, False), (ap("MS", 64, 80), ap("TRG"), ap("SC", 0, 16), False, False)])
         mm([(ap("MS", 64, 80), ap("I512"), ap("POJ"), False, True)])
         ts(ap("MI"), key, 1023, AND)
         cp(ap("OF"), ap("MS", 64, 80))
-        cp(ap("LL"), ap("MI")); later(len(ops) - 2)
-        cp(ind(ap("ZA"), ap("OF")), ap("ZB", 0, 256)); later(len(ops) - 2)
-        send("ZL%d" % t, ap("ZA", 0, 64), "ask%d" % t, "la", lender)
+        cp(ap("LL"), ap("MI"))
+        act(ind(ap("ZA"), ap("OF")), ap("ZF"), AF.Silu)
+        ts(ap("ZL"), ap("ZA", 0, 64), ROUND, ADD, -ROUND - 64.0, ADD)
+        if ask:
+            swap(zl, ap("ZL"), "ma%d" % t, "la", lender)
         if not t:
             mm([(ap("UVP", 4 + k, 5 + k), ap("PK", 128 * k, 128 * k + 128), ap("k1"), True, True) for k in range(2)])
-            ts(ap("kc"), ap("UVP", 4, 6), 2048.0, ADD)
+            ts(ap("LP3", 0, 2), ap("UVP", 4, 6), 2048.0, ADD)
+            to_all("LP", [ap("LP3", 0, 2), ap("ksc"), ap("th16")], "prm", "lp"); to_all("LW", [ap("LW3")], "prw", "lq")
         for lo in (128, 0):
             tt(ap("HM", lo, lo + 128), ind(ap("HT"), ap("LL", lo // 16, lo // 16 + 8)), ap("MWR", 0, 128), MUL)
             scan(ap("HS", lo, lo + 128), ap("RST", 0, 128), ap("HM", lo, lo + 128))
-            mm([(ap("HR", lo, lo + 128), ap("BLKH"), ap("HM", lo, lo + 128), True, True)])
-            cp(ap("HRH", lo, lo + 128), ap("HR", lo, lo + 128))
+            row = ap("ZP" if lo else "HR", 0, 128)
+            mm([(row, ap("BLKH"), ap("HM", lo, lo + 128), True, True)])
+            cp(ap("HRH", lo, lo + 128), row)
+            act(ap(cx, lo, lo + 128), row, AF.Copy, bias=2047.0)
+            act(ap("UR", lo, lo + 128), row, AF.Relu, bias=-3000.0)
             tt(ap("HD", lo // 16, lo // 16 + 8), ap("HS", lo + 15, lo + 128, 16), ap("DRS", lo, lo + 128, 16), MIN)
-        act(ap(cx, 0, L), ap("HR", 0, 256), AF.Copy, bias=2047.0)
-        act(ap("UR"), ap("HR", 0, 256), AF.Relu, bias=-3000.0)
-        made = []
 
-        def equal(k, lo, hi, c, scalar):
-            e, own = ap3("ET", k, k + 1, 0, hi - lo), ap("HS", 16 * c + 15, 16 * c + 16)
-            if scalar:
-                x = ap("EX", 128 * (k % 8), 128 * (k % 8) + hi - lo)
-                act(x, ap("HR", lo, hi), AF.Abs, bias=own, scale=-1.0)
-                made.append(act(e, x, AF.Relu, bias=1.0, scale=-1.0))
-            else:
-                ts(e, ap("HRH", lo, hi), own, EQ)
+        def equal(k, lo, hi, c):
+            ts(ap3("ET", k, k + 1, 0, hi - lo), ap("HRH", lo, hi), ap("HS", 16 * c + 15, 16 * c + 16), EQ)
         if t:
             put("G", lambda g, v=(t + 1) * TINY: g.affine_select(res(ap("STP")), res(ap("ZERO")), [[0, 128]], GT, v, 0, 0), [ap("ZERO")], [ap("STP")], (0.18, 256, 0, 0))
         for h, d in ((1, "CT"), (0, "DB")):
             mm([(ap(d, 256, 384), ap("IDB"), ap("NM2", 0, 128), True, False)])
             for c in range(8):
-                equal(8 * h + c, 128 * h + 16 * c, 128 * h + 128, 8 * h + c, 16 - 2 * c - h <= SE)
+                equal(8 * h + c, 128 * h + 16 * c, 128 * h + 128, 8 * h + c)
                 if c < 7:
                     mm([(ap(d, 272 + 16 * c, 384), ap("B30"), ap3("ET", 8 * h + c, 8 * h + c + 1, 16, 128 - 16 * c), False, False)])
             ctl = mm([(ap(d, 256, 384), ap("W2"), ap3("ET", 8 * h, 8 * h + 8, 0, 16), False, True)])
             scan(ap("WS", 128 * h, 128 * h + 128), ap("DRS", 128 * h, 128 * h + 128), ap(d, 256, 384), MAX, MIN)
             tt(ap("LA", 8 * h, 8 * h + 8), ap("WS", 128 * h + 15, 128 * h + 128, 16), ap("HD", 8 * h, 8 * h + 8), MAX)
-            ts(ap("LO", 8 * h, 8 * h + 8), ap("LA", 8 * h, 8 * h + 8), 2047.0, ADD)
+            ts(ap("LO", 16 * h, 16 * h + 8), ap("LA", 8 * h, 8 * h + 8), 2047.0, ADD)
+            if not ask:
+                swap("LM%d" % t, ap("LO", 16 * h, 24 * h + 8), ("mb%d", "ma%d")[h] % t, ("lr", "la")[h], borrower)
             if t:
-                act(ind(ap("UF", 0, ZD), ap("LO", 8 * h, 8 * h + 8)), ap("ZERO" if h else "STP"), AF.Silu)
+                act(ind(ap("UF", 0, ZD), ap("LO", 16 * h, 16 * h + 8)), ap("ZERO" if h else "STP"), AF.Silu)
             if last or not t:
-                cp(ind(ap("US", 0, ZD), ap("LO", 8 * h, 8 * h + 8)), ap("C255", 0, 128))
+                cp(ind(ap("UL0" if t else "US", 0, ZD), ap("LO", 16 * h, 16 * h + 8)), ap("C255", 0, 128))
             act(ap("WD", 128 * h, 128 * h + 128), ap(d, 256, 384), AF.Sign)
+        if copy and t:
+            dma_cast(ap("US", 0, S), ap("UF", 0, S), 4.5)
         ts(ap("HL"), ap("HS", 15, 256, 16), 2047.0, ADD, 4095.0, MIN)
-        act(ap("EA", 0, 64), ap("PF64"), AF.Copy)
+        iota(ap("EA", 0, 64), [[5, 64]], 1344); later(start[0] + 1)
         act(ind(ap("EA"), ap("OF")), ap("E32"), AF.Silu)
         scan(ap("EQ"), ap("TRH", 0, 64), ap("EA", 0, 64), MAX, MIN)
         ts(ap("FAI"), ap("EQ", 15, 64, 16), -64.0, ADD, 0.2, MUL)
-        if SLOTS:
-            cp(ap("FS", 0, 4), ap("FAI"))
-            send("FL%d" % t, ap("FS"), "fai%d" % t, "lf", lender)
+        cp(ap("FA"), ap("FAI"))
         for c, (lo, hi) in enumerate(rng):
             act(ap("SG", 128 * c, 128 * c + hi - lo), ap("E32", lo + 1, hi + 1), AF.Sign, bias=ap("THR", c, c + 1), scale=-1.0, total=ap("SJ", c, c + 1))
         tt(ap("J2"), ap("SJ"), ap("KJ", 0, 16), ADD)
@@ -596,48 +726,47 @@ def build(rank, core, T, topo):
             act(ap("MF"), ind(ap("UF", 0, S), ap("HL", 8, 16)), AF.Relu, bias=-2000.0 * t - 1000.0, scale=4000.0 / TINY)
         else:
             cp(ind(ap("X"), ap("LO", 0, 8)), ap("STB"))
-            act(ap("MF"), ind(ap("X"), ap("HL", 8, 16)), AF.Relu, bias=-256.0)
+            act(ap("MF"), ind(ap("X", 0, S), ap("HL", 8, 16)), AF.Relu, bias=-256.0)
         mm([(ap("MS", 256, 512), ap("IDB"), ap("IC"), True, False)]); mm([(ap("MS", 256, 512), ap("IDB"), ap("UR"), False, False)])
         mm([(ap("MS", 256, 512), ap("B512"), ap("WD"), False, False)])
         mm([(ap("MS", 384, 512), ap("IDB"), ap("MF"), False, True)])
         wn = act(ap("WN", 0, 256), ap("MS", 256, 512), AF.Copy, bias=-14336.0)
-        if t > 1:
-            mm([(ap("UVP", 128 + 32 * qv, 160 + 32 * qv), wt(2, qv, i), ap("C255", 0, 32), qv + i == 0, False) for qv in (0, 1) for i in (0, 1)])
-        mm([(ap("UVP", 128 + 32 * qv, 160 + 32 * qv), wt(2, qv, i), ap("ZL%d" % t, i, i + 63, 2), t < 2 and qv + i == 0, qv + i == 2) for qv in (0, 1) for i in (0, 1)])
+        mm([(ap("UVP", 128 + 32 * qv, 160 + 32 * qv), lw(who, qv, i), ap(zl, i, i + 63, 2), qv + i == 0, qv + i == 2) for qv in (0, 1) for i in (0, 1)])
         for k in range(0, 8, 4):
-            mm([(ap("JP", r, 512, 8), ap("IDB"), ap("ZL%d" % t), r == 0, r == 7) for r in range(k, k + 4)])
+            mm([(ap("JP", r, 512, 8), ap("IDB"), ap(zl), r == 0, r == 7) for r in range(k, k + 4)])
         for k in range(2):
-            act(ap("ZT", 256 * k, 256 * k + 256), ap("JP", 256 * k, 256 * k + 256), AF.Copy, bias=-255.0 if t == 1 else 0.0)
+            act(ap("ZT", 256 * k, 256 * k + 256), ap("JP", 256 * k, 256 * k + 256), AF.Copy, bias=-float(less))
         cp(ap("lUVS"), ap("UVP", 128, 192))
         ts(ap("lUVA"), ap("lUVS"), 4095, AND)
         tt(ap("lUVW"), ap("lUVA", 0, 32), ap("lUVA", 32, 64), MUL)
         for k in range(2):
-            ts(ap("lKU", 32 * k, 32 * k + 32), ap("lUVA", 0, 32), ap("kc", k, k + 1), MUL)
+            ts(ap("lKU", 32 * k, 32 * k + 32), ap("lUVA", 0, 32), ap("LP%d" % who, k, k + 1), MUL)
         ts(ap("lUQ"), ap("lUVW"), 5, SHR)
         for k in range(2):
             tt(ap("lHV", 32 * k, 32 * k + 32), ap("lKU", 32 * k, 32 * k + 32), ap("lUQ"), ADD)
         ts(ap("lHI"), ap("lHV"), 4095, AND); cp(ap("lHO"), ap("lHI")); ts(ap("lHH"), ap("lHI"), -2047.0, ADD)
+        if not ask:
+            if t > 1:
+                cp(ind(ap(lent), ap("LX%d" % (t - 1), 0, 4)), ap(mark, 0, 64))
+            for h in (1, 0):
+                cp(ind(ap(lent, 0, ZD), ap("LM%d" % t, 16 * h, 16 * h + 8)), ap(mark))
+            ts(ap("lb"), ap("LM%d" % t, 24, 25), 1024.0, MUL, ap("LP%d" % who, 3, 4), ADD)
         k = act(ap("lX", 768, 768 + LB), ind(ap(lent, 0, S), ap("lHO", 48, 48 + LB // 16)), AF.Copy)
-        mm([(ap("ZP", 256, 256 + LB), ap("IDN"), ap("ZT", 256, 256 + LB), True, False)]); mm([(ap("ZP", 256, 256 + LB), ap("IDB"), ap("lX", 768, 768 + LB), False, True)])
+        mm([(ap("DB", 256, 256 + LB), ap("IDN"), ap("ZT", 256, 256 + LB), True, False)]); mm([(ap("DB", 256, 256 + LB), ap("IDB"), ap("lX", 768, 768 + LB), False, True)])
         for lo, hi in LORD:
-            x = ap3("lY", 0, 8, 0, 32) if lo == 512 and LRELU else ap("lX", lo, hi)
+            x = ap("lX", lo, hi)
             if lo != 768:
                 tt(x, ind(ap(lent, 0, S), ap("lHO", lo // 16, hi // 16)), ap("ZT", lo % 512, (hi - 1) % 512 + 1), SUB)
-            if lo == 512 and LRELU:
-                ts(ap3("lA", lo // 32, hi // 32, 0, 32), x, 0.0, MIN, -2.0, MUL)
-                continue
-            act(ap3("lA", lo // 32, hi // 32, 0, 32), x if lo != 768 else ap("ZP", 256, 256 + LB), AF.Abs); later(k)
+            act(ap3("lA", lo // 32, hi // 32, 0, 32), x if lo != 768 else ap("DB", 256, 256 + LB), AF.Abs); later(k)
             k = len(ops) - 1
         mm([(ap("CT", 64 * r, 64 * r + 64), ap("RL", 128 * r, 128 * r + 128), ap("lHH"), True, True) for r in range(8)])
-        act(ap("lHT", 0, 512), ap("CT"), AF.Copy); later(k)
+        act(ap("lHT", 0, 512), ap("CT"), AF.Copy)
         for n in range(4):
-            d = ("DA", "JP", "UVP", "HR")[n]
+            d = ("DA", "JP", "UVP", "DB")[n]
             mm([(ap(d, 64, 128), ap("IDB"), ap("ML", 64 * n, 64 * n + 64), True, False), (ap(d, 64, 128), ap("IDB"), ap("PZL"), False, False)])
-            if n == 2 and LRELU:
-                mm([(ap(d, 64, 128), slq(r), ap3("lY", 0, 8, 8 * r, 8 * r + 8), False, False) for r in range(4)])
             mm([(ap(d, 64, 128), slq(r), ap3("lA", 8 * n, 8 * n + 8, 8 * r, 8 * r + 8), False, r == 3) for r in range(4)])
             if n < 2:
-                ts(ap("lRM", 64 * n, 64 * n + 64), ap(d, 64, 128), b16, MIN)
+                ts(ap("lRM", 64 * n, 64 * n + 64), ap(d, 64, 128), b16 if ask else ap("lb"), MIN)
             else:
                 for k in range(2):
                     lo = 64 * n - 128 + 32 * k
@@ -645,41 +774,50 @@ def build(rank, core, T, topo):
         ts(ap("lMI"), ap("lKS", 31, 128, 32), 1023, AND); cp(ap("lLL"), ap("lMI"))
         tt(ap("lHM"), ind(ap("lHT"), ap("lLL")), ap("MWR", 0, 64), MUL)
         scan(ap("lHS"), ap("RST", 0, 64), ap("lHM"))
-        reg = [(("HR", "ZP")[c // 2], 256 + 80 * (c % 2), 16 * c + 16) for c in range(4)]
+        reg = [(("DA", "JP")[c // 2], 256 + 80 * (c % 2), 16 * c + 16) for c in range(4)]
         for c in (0, 2):
             mm([(ap(d, lo, lo + w + 1), ap("IDB"), ap("lTR", 64 - w, 65), k == 0, False) for k, (d, lo, w) in enumerate(reg[c:c + 2])])
         for c in (0, 2):
             mm([(ap(d, lo, lo + w), ap("BLKH"), ap("lHM", 0, w), False, k == 1) for k, (d, lo, w) in enumerate(reg[c:c + 2])])
         if not last:
             ts(ap("lHL"), ap("lHS", 15, 64, 16), 2047.0, ADD, 4095.0, MIN)
-            act(ap("RS", 0, 64), ind(ap("TP"), ap("lHL")), AF.Copy)
-        cp(ap("lET", 0, 320, 80), ap("FL%d" % t, 0, 4))
+            act(ap("RS", 0, 64), ind(ap("TP" if ask else "TL%d" % who), ap("lHL")), AF.Copy)
+        ts(ap("lET", 0, 320, 80), ap("lHS", 15, 64, 16), 2047.0, ADD, 4095.0, MIN)
+        odd = 0 if ask else 8 * (t % 2)
         for c, (d, lo, w) in enumerate(reg):
-            ts(ap("lET", 80 * c + 1, 80 * c + w + 2), ap(d, lo, lo + w + 1), ap("lHS", 16 * c + 15, 16 * c + 16), EQ, ap("DMP", c, c + 1), MUL)
-            most(ap("RS", 64 + c, 65 + c), ap("lET", 80 * c, 80 * c + w + 2))
-        sent.append(len(ops))
-        send("RB%d" % t, ap("RS", 64 * last, 72), "rep%d" % t, "lr", borrower)
-        ts(ap("lWS", 0, 4), ap("RS", 64, 68), 257.0, GT, 8192.0, MUL); tt(ap("lWS", 8, 12), ap("lWS", 0, 4), ap("lHS", 15, 64, 16), ADD)
-        tt(ap("lWS", 16, 20), ap("lWS", 8, 12), ap("DMP", 8, 12), MIN); ts(ap("lLO"), ap("lWS", 16, 20), 2047.0, ADD)
-        act(ap("RSU"), ind(ap(lent), ap("lLO")), AF.Copy, bias=255.0 if t else 0.0)
-        send("RV%d" % t, ap("RSU"), "reu%d" % t, "lu", borrower)
-        if last or not t:
-            cp(ind(ap("US"), ap("lLO")), ap("C255", 0, 64))
+            ts(ap("lET", 80 * c + 1, 80 * c + w + 2), ap(d, lo, lo + w + 1), ap("lHS", 16 * c + 15, 16 * c + 16), EQ, ap("DMP", odd + c, odd + c + 1), MUL)
+            most(ap("lWS", c, c + 1), ap("lET", 80 * c, 80 * c + w + 2))
+        if ask:
+            ts(ap("RS", 64, 68), ap("lWS", 0, 4), -float(S), ADD, 0.0, MAX)
+            k = swap("RB%d" % t, ap("RS", 64 * last, 72), "mb%d" % t, "lr", borrower)
+        cp(ap("lLO", 0, 4), ap("lWS", 0, 4))
+        if not ask:
+            k = swap("LN%d" % t, ap("lLO"), "mn%d" % t, "lu", lender)
+        if copy and t:
+            j = swap("LX%d" % t, ap("lLO"), "mx%d" % t, "lf", T.cores[(rank + t % 3 - (t + 1) % 3) % 4]); ops[j]["after"] = [k]
+            ops[ship(t + 1)[0]]["after"] = [j]
+        act(ap("RSU"), ind(ap(lent), ap("lLO", 0, 4)), AF.Copy, bias=float(less))
+        if ask:
+            j = swap("RV%d" % t, ap("RSU"), "mn%d" % t, "lu", borrower)
+            cp(ind(ap("UL0" if t else "US"), ap("lLO", 0, 4)), ap("C255", 0, 64))
         else:
-            act(ind(ap("UF"), ap("lLO")), ap("ZERO", 0, 64), AF.Silu)
-            iota(ap("UF", ZD, 4480), [[0, 4480 - ZD]], -255)
+            act(ind(ap("UF"), ap("LN%d" % t, 0, 4)), ap("ZERO", 0, 64), AF.Silu)
         if not t:
+            for i in ship(1):
+                ops[i]["after"] = [j]
             for k in range(0, S, 256):
                 if k < 256 * CONV:
-                    ts(ap("UF", k, k + 256), ap("US", k, k + 256), -255.0, ADD)
+                    for j in (k, k + 128):
+                        ts(ap("UF", j, j + 128), ap("US", j, j + 128), -255.0, ADD); ops[-1]["tag"] = "UF<"
                 else:
                     act(ap("UF", k, k + 256), ap("US", k, k + 256), AF.Copy, bias=-255.0)
-            iota(ap("UF", S, 4480), [[0, 4480 - S]], -255); iota(ap("ZERO"), [[0, 128]], 0)
         if not last:
             mm([(ap("MS", 96, 97), ap("ONEB"), ap("SC", 16, 17), True, True)])
             cp(ap("PPI"), ap("MS", 96, 97)); ts(ap("PPJ"), ap("PPI"), 63, AND); ts(ap("b16b" if t % 2 else "b16a"), ap("PPJ"), 1024.0, MUL, ap("th16"), ADD)
+            if copy:
+                cp(ap("LO", 24, 25), ap("PPJ"))
         if t:
-            ts(ind(ap(cx, OLD, END), ap("OBU")), ap("IC64"), 1.0, MUL, float(S + CAP * (t - 1)), ADD); later(scn)
+            ts(ind(ap(cx, OLD, END), ap("OBU")), ap("IC64"), 1.0, MUL, float(S + CAP * (t - 1)), ADD)
             dma(ext("yc", L * (t - 1), L * t), ap(cx, OLD, OLD + L, 1, slice(0, 128, 16)), 2.0)
         tt(ap("FW"), ind(ap("WN"), ap("JL")), ap("NM"), ADD)
         scan(ap("CMH"), ap("DJ"), ap("FW"), MAX, MIN); cp(ap("JL2"), ap("CMH", 15, 256, 16))
@@ -689,21 +827,25 @@ def build(rank, core, T, topo):
             act(ap(ty, OLD, OLD + L), ind(ap(tx), ap("JL2")), AF.Copy)
             act(ap(wy, OLD, OLD + L), ind(ap(wx), ap("JL2")), AF.Copy)
         act(ap(cy, OLD, OLD + L), ind(ap(cx), ap("JL2")), AF.Copy)
-        rb = "RB%d" % t
-        cp(ap("OBU"), ap(rb, 64, 68))
+        for c in range(4):
+            if ask:
+                ts(ap("OBU", c, c + 1), ap("RB%d" % t, 64 + c, 65 + c), ap("FA", c, c + 1), MAX)
+            else:
+                ts(ap("OBU", c, c + 1), ap("lWS", c, c + 1), -float(S), ADD, ap("FA", c, c + 1), MAX)
         if not last:
-            cp(ind(ap(ty, OLD, END), ap("OBU")), ap(rb, 0, 64)); cp(ind(ap(wy, OLD, END), ap("OBU")), ap("WTAB", 0, 64))
-        dma(ext("yu", S + CAP * t, S + CAP * t + CAP), ap("RV%d" % t), 2.0)
+            cp(ind(ap(ty, OLD, END), ap("OBU")), ap("RB%d" % t if ask else "RS", 0, 64)); cp(ind(ap(wy, OLD, END), ap("OBU")), ap("WTAB", 0, 64))
+        dma(ext("yu", S + CAP * t, S + CAP * t + CAP), ap("RV%d" % t if ask else "RSU"), 2.0)
         if last:
             ts(ind(ap(cy, OLD, END), ap("OBU")), ap("IC64"), 1.0, MUL, float(S + CAP * t), ADD)
             dma(ext("yc", L * t, L * t + L), ap(cy, OLD, OLD + L, 1, slice(0, 128, 16)), 2.0)
-    dma(ext("yu", 0, S), ap("US", 0, S), 4.5)
+    dma(ext("yu", 0, S), ap("UL0", 0, S), 4.5)
     seen, at, early, both = {}, {}, None, None
     for i, o in enumerate(ops):
         if o["k"] == 0:
             early = early or at
             seen, at = {}, {}
         w = "<".join(x[-1 if k else 0][0].replace("th16", "b").rstrip("0123456789ab") if x else "" for k, x in enumerate((o["W"], o["R"])))
+        w = w + "V" if "tag" in o else w
         seen[o["q"], w] = seen.get((o["q"], w), 0) + 1
         o["name"] = (o["k"] < 0, o["q"], w, seen[o["q"], w])
         if o["q"] != "N":
@@ -715,11 +857,14 @@ def build(rank, core, T, topo):
                     got = [both[y if "#" in y else y + "#1"] for y in chain.split()]
                     for a, b in zip(got, got[1:]):
                         ops[b].setdefault("after", []).append(a)
-            for chain in CHAINS:
-                if i + 1 == len(ops) or "X<LO#1" in at:
-                    chain = chain.replace(*AT_LAST)
-                if "X<LO#1" in at:
-                    chain = chain.replace(*AT_FIRST)
+            elif "UF<US#1" in both:
+                both.update(at)
+                for chain in SECOND:
+                    got = [both[y if "#" in y else y + "#1"] for y in chain.split()]
+                    for a, b in zip(got, got[1:]):
+                        ops[b].setdefault("after", []).append(a)
+                del both["UF<US#1"]
+            for chain in FINAL if i + 1 == len(ops) else ASKED if "<ZL#1" in at else CHAINS if "UL<LX#1" in at else AFTER:
                 got = [at[x] for x in (y if "#" in y else y + "#1" for y in chain.split()) if x in at]
                 for a, b in zip(got, got[1:]):
                     ops[b].setdefault("after", []).append(a)
@@ -740,6 +885,8 @@ def order(ops, memo=None):
                 pre[j] = pre.get(j, False) or wait
         for j in o.get("after", ()):
             pre[j] = False
+        for j in o.get("waits", ()):
+            pre[j] = True
         for kind in ("R", "W"):
             for nm, lo, hi, st in o[kind]:
                 ps = nm in _PS
@@ -856,23 +1003,43 @@ def order(ops, memo=None):
             key[i] = zero + r * span + mid[name[i]] if name[i] in mid else key[i - 1]
     qn = ["NVSPGY".index(o["q"]) for o in ops]
     deps = [list(o["pre"]) for o in ops]
+    whole, left, nets = [i for i in range(n) if not deps[i]], [len(x) for x in deps], {}
+    for i in whole:
+        for k in succ[i]:
+            left[k] -= 1
+            if not left[k]:
+                whole.append(k)
 
     def sequence(key, lo, hi):
-        left = [0] * n
-        for i in range(lo, hi):
-            left[i] = sum(j >= lo for j in deps[i])
-        ready = sorted((key[i], i) for i in range(lo, hi) if not left[i])
+        if (lo, hi) not in nets:
+            left, nxt, up = [0] * n, [[] for _ in range(n)], {}
+            for i in whole:
+                if lo <= i < hi:
+                    mine = [j for j in deps[i] if lo <= j < hi]
+                    far = 0
+                    for j in mine:
+                        far |= up[j]
+                    for j in mine:
+                        if not far >> j & 1:
+                            left[i] += 1; nxt[j].append(i)
+                    for j in mine:
+                        far |= 1 << j
+                    up[i] = far
+            nets[lo, hi] = (left, nxt, [i for i in range(lo, hi) if not left[i]])
+        left, nxt, roots = nets[lo, hi]
+        left = list(left)
+        ready = sorted(((key[i], i) for i in roots), reverse=True)
         seq = []
         while ready:
-            i = ready.pop(0)[1]
+            i = ready.pop()[1]
             seq.append(i)
             grown = False
-            for k in succ[i]:
+            for k in nxt[i]:
                 left[k] -= 1
-                if not left[k] and k < hi:
+                if not left[k]:
                     ready.append((key[k], k)); grown = True
             if grown:
-                ready.sort()
+                ready.sort(reverse=True)
         return seq
 
     def length(seq, goal):
@@ -934,7 +1101,7 @@ def order(ops, memo=None):
         return best[1]
     if not memo:
         rnd = np.random.RandomState(SEED)
-        goal = [[i for i in range(first[r], first[r + 1]) if name[i][2] == "ZA" and name[i][1] == "V"][0] for r in range(RO)]
+        goal = [[i for i in range(first[r], first[r + 1]) if name[i][2] == "K" and name[i][1] == "V"][0] for r in range(RO)]
         same = {}
         for i in range(first[0], n):
             same.setdefault(name[i], []).append(i)
@@ -959,6 +1126,10 @@ def order(ops, memo=None):
 def rank_program(g, core, T, topo):
     rank = T.rank_of(core)
     if rank is None:
+        for r, c in enumerate(T.cores):
+            hs = helpers(c, T, topo)
+            if core in hs:
+                helper_program(g, core, r, hs.index(core), T, topo)
         return
     ops = build(rank, core, T, topo)
     seq, _ = order(ops, _MEMO)

import numpy as np
from concourse.mybir import dt, AluOpType, AxisListType, ActivationFunctionType
from concourse.bass import DstId, RemoteDMATransfer
import comms_topo

RO, L, S, CAP = 6, 256, 4096, 64
UNF = 4000.0
BIG = 4194304.0
OLD, END = 256, 656
TINY = 1e-7
ROUND = 12582912.0
ZD = 4352

_B = {}


def _b(name, cols, dtype, rows=128, inner=0):
    _B[name] = ("sbuf", [rows, cols], dtype, inner)


F, BF, H, I, U16 = "float32", "bfloat16", "float16", "int32", "uint16"
_b("US", 4480, BF); _b("TP", 4096, BF); _b("WTAB", 4096, BF); _b("UF", 4480, F); _b("ZERO", 128, F)
_b("c8", 256, I, 8); _b("hwi", 2, I); _b("kmi", 1, I); _b("th8", 1, I, 8)
_b("c8h", 256, H, 8); _b("c8i", 256, I, 8); _b("c8w", 256, H, 8); _b("th8h", 1, H, 8); _b("hwf", 2, F); _b("hwg", 2, F); _b("hwh", 2, H); _b("wl", 2, F); _b("wr", 2, F); _b("ws", 2, F)
_b("kh", 16, H); _b("KR", 16, F); _b("th16", 1, F); _b("b16a", 1, F); _b("b16b", 1, F); _b("ksc", 1, F)
_b("IC", 256, BF); _b("CS", 256, BF); _b("CG", 128, BF); _b("CG8", 128, BF); _b("C3", 128, BF); _b("pI", 1, I); _b("sI", 1, I); _b("s2I", 1, I)
for _n in ("pF", "sF", "gF", "s2F", "sge8", "slt8", "pm8", "gx8", "g8p", "nsB", "ns2", "s1T", "gx4", "pm1", "rF", "s1F"):
    _b(_n, 1, F)
_b("g16", 16, F); _b("g8", 4, F); _b("g8m", 4, F); _b("pen2", 2, F); _b("pen4", 4, F)
_b("MWR", 256, F); _b("RST", 256, F); _b("BLKH", 128, H); _b("BLKB", 128, BF); _b("BLKN", 128, BF); _b("ONEB", 128, BF)
_b("IDH", 128, H); _b("IDB", 128, BF); _b("IDN", 128, BF); _b("IDHN", 128, H); _b("I255", 128, BF); _b("SH1", 128, BF); _b("SH2", 128, BF)
_b("TRL", 128, BF); _b("TRG", 128, BF); _b("PL", 128, BF); _b("PR", 128, BF); _b("PH", 128, H); _b("SEL", 144, BF); _b("REP8", 128, H, 8)
_b("WT", 16 * 128, H); _b("PZ4", 128, BF); _b("RS4", 128, F); _b("RS16", 64, F)
_b("C255", 128, BF); _b("THR", 16, F); _b("KJ", 48, F); _b("K256", 16, BF); _b("ZZ", 128, BF); _b("one16", 16, F); _b("oneR", 256, BF); _b("JW0", 16, F)
_b("J256", 16, H); _b("FIX", 32, F); _b("CL", 16, U16); _b("CJ", 32, U16); _b("IC64", 64, F); _b("PF64", 64, F)
_b("DRS", 256, F); _b("DMP", 16, F); _b("NJ", 16, F); _b("I512", 128, H); _b("lTR", 160, BF)
_b("SLQ", 144, BF); _b("SLP", 144, BF); _b("B512", 128, BF); _b("B256", 128, BF); _b("BLK8", 128, BF); _b("NM", 256, BF); _b("TRH", 64, BF)
_b("MP", 512, BF); _b("MS1", 256, BF); _b("kz1", 256, BF); _b("ML", 256, BF); _b("CM2", 256, F); _b("CMH", 256, H); _b("DJ", 256, H); _b("CL0", 16, U16)
for _k in "01":
    _b("CX" + _k, END, F); _b("TX" + _k, END, BF); _b("WX" + _k, END, BF)
_b("ZB", 512, BF); _b("UVS", 128, I); _b("UVA", 32, I); _b("UVW", 16, I); _b("UVQ", 16, I)
_b("HV", 256, I); _b("KU", 256, F); _b("KRX", 256, F); _b("LS", 16, U16); _b("LC", 16, U16); _b("RS5", 128, F); _b("R5", 128, F); _b("K5", 128, I); _b("HI", 256, I); _b("HO", 256, U16); _b("HT", 528, F)
_b("X", ZD, BF); _b("STB", 128, BF); _b("A", 4096, BF); _b("RM", 512, F); _b("RI", 320, F); _b("KS", 64, I)
_b("PO", 16, F); _b("PN", 16, BF); _b("SC", 32, BF); _b("POJ", 16, H); _b("OF", 16, U16); _b("ZA", 768, F)
_b("PPI", 1, I); _b("PPJ", 1, I); _b("MI", 16, I); _b("LL", 16, U16)
_b("HM", 256, H); _b("HS", 256, F); _b("HD", 16, F); _b("LA", 16, F); _b("UR", 256, BF); _b("W2", 128, BF); _b("B30", 128, BF); _b("NM2", 128, BF); _b("P2", 48, F); _b("HRH", 256, H); _b("HL", 16, U16)
_b("ET", 16 * 128, BF, inner=128); _b("WD", 256, BF); _b("WN", 512, BF); _b("STP", 128, F); _b("MF", 128, BF); _b("WS", 256, F); _b("LO", 32, U16)
_b("EE", 512, H); _b("FI", 32, I); _b("FB", 32, F); _b("FC", 32, F); _b("NW", 16, F); _b("UN0", 16, F)
_b("SG", 2048, BF); _b("SJ", 16, F); _b("J2", 16, F); _b("JB", 32, BF); _b("JL", 16, U16); _b("FW", 256, BF); _b("JX", 16, F); _b("JL2", 16, U16)
_b("EA", 768, F); _b("E32", 256, F); _b("EM", 64, F); _b("EQ", 64, F); _b("FAI", 4, I); _b("FA", 4, F); _b("OB", 4, F); _b("OBU", 4, U16)
for _k in range(RO):
    _b("LM%d" % _k, 32, U16); _b("LN%d" % _k, 8, U16); _b("LX%d" % _k, 8, U16)
    if _k < RO - 1:
        _b("UL%d" % _k, 4480, BF)
    if _k in (0, RO - 1):
        _b("ZN%d" % _k, 64, BF); _b("RB%d" % _k, 72, BF); _b("RV%d" % _k, 64, BF)
for _k in range(3):
    _b("TL%d" % _k, S, BF)
for _k in range(4):
    _b("LP%d" % _k, 4, F); _b("LW%d" % _k, 512, H)
_b("ZF", 256, F); _b("ZL", 64, BF); _b("NIL", 128, BF); _b("lb", 1, F)
_b("ZT", 512, BF); _b("lUVS", 64, I); _b("lUVA", 64, I); _b("lUVW", 32, I); _b("lUQ", 32, I); _b("lKU", 64, F)
_b("lHV", 64, I); _b("lHI", 64, I); _b("lHO", 64, U16); _b("lHT", 528, F); _b("lX", 1024, BF); _b("lA", 1024, BF, inner=32)
_b("CG2", 128, BF); _b("CZ", 64, BF); _b("PZL", 64, BF); _b("RS32", 64, F); _b("RL", 1024, BF); _b("lHH", 64, H); _b("PK", 256, BF); _b("RW", 128, BF)
_b("k1", 1, H); _b("s1I", 1, I)
_b("lRM", 256, F); _b("lKS", 128, I); _b("lMI", 4, I); _b("lLL", 4, U16); _b("lHM", 64, H); _b("lHS", 64, F); _b("lHL", 4, U16)
_b("lET", 320, F); _b("RS", 72, BF); _b("RSU", 64, BF); _b("lWS", 8, F); _b("lLO", 8, U16)
_PS = ["UVP", "ZP", "DA", "DB", "HR", "CT", "MS", "JP"]
_SIZE = {F: 4, BF: 2, H: 2, I: 4, U16: 2}
_OWN = ("US", "TP", "WTAB", "UF", "X", "A", "ZA", "RS", "RSU", "LO", "lLO", "ZL")
SCRATCH = {}
_AT = {}
_fill = {}
for _n, (_w, _sh, _d, _in) in _B.items():
    if _in:
        SCRATCH[_n] = (_w, [128, _sh[1] // _in, _in], _d); _AT[_n] = (_n, 0)
    elif _n in _OWN or _n[:2] in ("UL", "TL", "LM", "LN", "LX", "LP", "LW", "ZN", "RB", "RV") or _sh[0] != 128:
        SCRATCH[_n] = (_w, _sh, _d); _AT[_n] = (_n, 0)
    else:
        _q = 32 // _SIZE[_d]
        _AT[_n] = ("ar_" + _d, _fill.get(_d, 0))
        _fill[_d] = _fill.get(_d, 0) + (_sh[1] + _q - 1) // _q * _q
for _d, _c in _fill.items():
    SCRATCH["ar_" + _d] = ("sbuf", [128, _c], _d)
for _n in _PS:
    SCRATCH[_n] = ("psum", [128, 512], F); _AT[_n] = (_n, 0); _B[_n] = ("psum", [128, 512], F, 0)
ND = 42
_AT["ksc"], _AT["th16"] = ("LP3", 2), ("LP3", 3)
SEMAPHORES = ["sV", "sS", "sP", "sG", "lp", "hl", "hT0", "hT1", "hT2", "prm", "prw", "lq"] + ["d%d" % k for k in range(ND)] + ["x%d" % k for k in range(36)]
SEMAPHORES += [n + str(k) for n in ("ma", "mb", "mn", "mx", "hU", "ur") for k in range(RO)] + ["tr%d" % k for k in range(3)]
ASK = (0, RO - 1)
NEAR = 2048
STAGED, TNEAR = (576, 576, 896), 896
FAR = (("T", 1, 0, 576), ("T", 1, 576, 1152), ("T", 2, 0, 1152), ("U", 1, 0, 0), ("T", 2, 1152, 2048), ("T", 0, 0, 256), ("U", 2, 0, 0),
       ("T", 0, 256, 1408), ("U", 3, 0, 0), ("T", 0, 1408, 2048), ("U", 4, 0, 0))


def bits(engines):
    m = 0
    for e in engines:
        m |= 1 << e
    return m


def helpers(core, T, topo):
    return [h for h in topo.cores_of(core) if topo.die(h) != topo.die(core) and all(topo.may_write(h, d) for d in T.cores)][:2]


def helper_program(g, core, rank, side, T, topo):
    n = [0]

    def on(name, lo, hi, src, sem, t):
        dst = T.cores[(rank - 1 - t % 3) % 4]
        rid, pid, se = topo.addr(dst)
        g.remote_dma(T[name][:, lo:hi], T[src][:, lo:hi], T.sem[sem], T.sem.hl, pid, rid, topo.mask(core, dst))
        n[0] += len(topo.engines(core, dst))
    own = topo.cores_of(core)
    got = len([e for e in topo.engines(core, own[own.index(core) - 1]) if e not in topo.engines(core, T.cores[(rank + 1) % 4])]) // 2
    landed = 0
    for what, k, lo, hi in FAR:
        if what == "U":
            lo, hi = NEAR + side * (S - NEAR) // 2, NEAR + (side + 1) * (S - NEAR) // 2
            g.wait_ge(T.sem["hU%d" % k], got)
            on("UL%d" % k, lo, hi, "UL%d" % k, "ur%d" % k, k)
        else:
            while sum(STAGED[:landed]) < hi:
                g.wait_ge(T.sem["hT%d" % landed], got); landed += 1
            top = (side + 1) * S // 2
            on("TL%d" % k, top - hi, top - lo, "TL0", "tr%d" % k, k)
    g.wait_ge(T.sem.hl, n[0])


NS = 5
BYS = {0: "CT", 2: "ZP", 6: "UVP"}
SUMS = {0: "DA", 4: "DB", 8: "JP", 12: "HR", 13: "CT", 14: "ZP", 15: "DA"}
PROBE = [("gather", 0, 2), ("gather", 4, 2), ("gather", 2, 2), ("abs", 0, 2), ("gather", 6, 2), ("gather", 8, 2), ("minus", 4, 2), ("two", 4, 0),
         ("abs", 2, 2), ("slots", 0, 0), ("slots", 1, 0), ("slots", 2, 0), ("slots", 3, 0), ("gather", 10, 2), ("abs", 8, 2), ("four", 0, 1),
         ("two", 8, 0), ("abs", 6, 2), ("gather", 12, 1), ("two", 6, 1), ("gather", 13, 1), ("abs", 10, 2), ("gather", 14, 1), ("abs", 12, 1),
         ("two", 10, 1), ("gather", 15, 1), ("abs", 13, 1), ("abs", 14, 1), ("abs", 15, 1), ("single", 12, 0), ("fold", 0, 0), ("single", 13, 1),
         ("single", 14, 2), ("single", 15, 3)]
KEPT = ("gather", "abs", "two", "four", "minus")
CHAINS = ("EE<WX UVS<UVP EE<WX#2 UVA<UVS", "HO<HI KU<KRX#2 HV<KU#2 FI<MS HI<HV#2 NW<FI HO<HI#2 RS< HT<HI X<ZB RI<NW X<ZB#2 X<ZB#3",
          "HT<HI K<R MI<K SC<K LL<MI POJ<NJ HM<MWR HM<MWR#2 OF<MS HS<HM HRH<ZP HS<HM#2 HRH<HR "
          + " ".join("ET<HS#%d" % k for k in range(1, 17)) + " WS<CT HD<DRS ZL<ZA LA<HD HD<DRS#2 LO<LA WS<DB HL<HS LA<HD#2 J<KJ LO<LA#2 "
          "lUVS<UVP JB<J lUVA<lUVS DJ<J lUVW<lUVA lKU<LP lUQ<lUVW lKU<LP#2 lHV<lUQ lHV<lUQ#2 lHI<lHV "
          "UL<LX lHO<lHI UL<LM JX<JB UL<LM#2 lHH<lHI lX<ZT lX<ZT#2 lX<ZT#3 JL<JX l<LP FW<NM lRM<l CMH<FW lRM<l#2 JL<CMH lKS<DB lKS<DB#2 lKS<UVP lKS<UVP#2 "
          "EQ<EA lMI<lKS FAI<EQ lLL<lMI FA<FAI lHM<MWR PPI<MS lHS<lHM PPJ<PPI lET<lHS lHL<lHS "
          "lET<DMP lET<DMP#2 lET<DMP#3 lET<DMP#4 lWS<lET lWS<lET#2 lWS<lET#3 lWS<lET#4 OBU<FA lLO<lWS OBU<FA#2 OBU<FA#3 OBU<FA#4 TX<OBU WX<OBU",
          "ZB<ZP#2 E<JP X<HO A<X#6 ZF<ZB ZA<OF", "E<JP SJ<THR#13 X<HO", "ZA<OF EA<OF UF<LO WD<CT UF<LO#2 WD<DB UR<ZP UR<HR MF<HL ZT<JP ZT<JP#2 WN<MS lX<lHO lA<lX lA<lX#3 lHT<CT TX<HL TX<JL WX<HL RS<lHL "
          "WX<JL CX<ZP CX<HR CX<JL RSU<lLO",
          "UVP<TX ZP<TX JP<EE MS<EE#2 MS<EE#3 MS<EE#4 CT<ZB ZP<ZB CT<X", "DB<lX DA<lA JP<lA DB<lA UVP<lA DA<lHM JP<lHM",
          "<LO <LO#2 US<UF <US#2 <lLO <lLO#2 <US")
ASKED = CHAINS[1:2] + (
    "HT<HI K<R SC<K POJ<NJ MI<K LL<MI OF<MS HM<MWR HM<MWR#2 HS<HM HRH<ZP HS<HM#2 HRH<HR HD<DRS " + " ".join("ET<HS#%d" % k for k in range(1, 5)) + " ZL<ZA "
    + " ".join("ET<HS#%d" % k for k in range(5, 17)) + " WS<CT HD<DRS#2 LA<HD LO<LA WS<DB HL<HS LA<HD#2 US<LO UL<LO LO<LA#2 J<KJ US<LO#2 UL<LO#2 "
    "lUVS<UVP JB<J lUVA<lUVS lUVW<lUVA lKU<LP lUQ<lUVW lKU<LP#2 lHV<lUQ lHV<lUQ#2 JX<JB lHI<lHV JL<JX lHO<lHI lHH<lHI lX<ZT lX<ZT#2 lX<ZT#3 X<LO "
    "lKS<DB lKS<DB#2 lKS<UVP lKS<UVP#2 lMI<lKS lLL<lMI lHM<MWR lHS<lHM lET<lHS lHL<lHS lET<DMP lET<DMP#2 lET<DMP#3 lET<DMP#4 lWS<lET lWS<lET#2 lWS<lET#3 lWS<lET#4 "
    "RS<lWS lLO<lWS FW<NM US<lLO CMH<FW JL<CMH FA<FAI OBU<FA",
    "ZB<ZP#2 E<JP X<HO A<X#6 ZF<ZB ZA<OF", "lHT<CT CX<ZP CX<HR RSU<lLO", "ZA<OF EA<OF UF<LO UF<LO#2 ZT<JP ZT<JP#2 lX<lHO lA<lX lA<lX#3 lHT<CT MF<HL TX<HL WN<MS RS<lHL RSU<lLO TX<JL WX<JL CX<JL") + CHAINS[-3:-1] + (
    "<ZL US<UF <RS <lLO <US <US#2",)
AFTER = tuple(c.replace("UF<LO WD<CT UF<LO#2 WD<DB UR<ZP UR<HR MF<HL ZT<JP ZT<JP#2 WN<MS lX<lHO", "UR<ZP UR<HR ZT<JP ZT<JP#2 WD<CT WD<DB UF<LO UF<LO#2 MF<HL lX<lHO WN<MS")
              for c in CHAINS)
FINAL = CHAINS[:1] + tuple(c.replace(" X<LO ", " FW<NM lRM< CMH<FW lRM<#2 JL<CMH ").replace("RS<lWS lLO<lWS FW<NM US<lLO CMH<FW JL<CMH", "lLO<lWS RS<lWS UL<lLO CX<OBU")
              .replace("ZT<JP ZT<JP#2 lX<lHO lA<lX lA<lX#3 lHT<CT MF<HL TX<HL WN<MS", "MF<HL ZT<JP ZT<JP#2 lX<lHO WN<MS lA<lX lA<lX#3 lHT<CT") for c in ASKED)
START = ("pI< IC< CG< CS< C< CG<#2 oneR< SEL<B RS< SLP<B kz< SLQ<B <TP <TP#2 <TP#3 <TP#4 HT< TRG<BLKB TRL<BLKB SC< ZA< EA< CG<#3 ONEB< PK<ONEB PK<ONEB#2 "
         "CZ< C<#2 RL<ONEB RL<ONEB#2 RL<ONEB#3 RL<ONEB#4 US< KJ< KJ<#2 K< JB< <ZL SH<B SH<B#2 ML< STB< RL<ONEB#5 RL<ONEB#6 RL<ONEB#7 RL<ONEB#8 lHT< lTR< RS<#2 <TP#5 WN< TX< WX< WX<#2 <RS <RSU <US <US#2 "
         "< <LW ZERO< IC<#2 NIL<",
         "sI<pI pF<pI sF<sI nsB<sF s2I<sI gF<sF gx<sF sge<sF slt<sF s2F<s2I pm<sge ns<s2F pm<pF g<gx IDB<pF JW<sF PH<pm g8m<slt g8p<sge BLKB<gF REP<pF "
         "BLKH<gF hwf<hwi c8h<c hwh<hwf ksc<kmi PL<sge kh<ksc DRS<JW ws<MS PR<slt CM<CT WT<ws c8i<c WT<ws#2 CL<CM WT<ws#3 c8w<c8i WT<ws#10 KR<MS LC<IC "
         "TX<CL LS<sF UVS<UVP", "EE<WX UVS<UVP EE<WX#2 UVA<UVS",
         "HT<IC CX<IC CX<IC#2 NJ<JW B<BLKB DRS<CS NM<nsB PZ<ns RS<C MWR<NM RST<CS TX<CL WX<DB KRX<LC ZB<ZP ZB<ZP#2 E<JP MS<DA X<HO", "X<ZB#7 hwg<hwf K<R LW<hwg MI<K LW<hwg#2 LL<MI", "ET<HS#16 LW<hwg#3 LA<HD LW<hwg#4 LO<LA",
         "lX<ZT#3 X<LO lRM< lRM<#2 lKS<DB lKS<UVP#2 DJ< lMI<lKS lLO< lLL<lMI LO< lHM<MWR",
         "A<X#6 W<P NM<rF B<BLKB#3 ZA<OF PZL<s1F lTR<pm DMP<JW DMP<JW#2 ZT<JP",
         "CMH<FW UF<USV JL<CMH UF<USV#2 PPI<MS UF<USV#3 PPJ<PPI UF<USV#4 FA<FAI UF<USV#5 OBU<FA OBU<FA#2 OBU<FA#3 OBU<FA#4 UF<USV#6 TX<OBU", "lKS<UVP#2 DJ<J FAI<EQ lET<DMP", "JP<lHM MS<SC#2",
         "EA<OF UR<ZP UR<HR WD<CT WD<DB ZT<JP", "MF<HL TX<HL WN<MS RS<lHL RSU<lLO WX<HL UF<US TX<JL WX<JL CX<JL UF<US#2")
LATER = "J<JW I<pF THR<JW s1T<sF P<one s1I<sI pm<sF"
SECOND = ("UF<US#2 ZB<ZP ZB<ZP#2 E<JP UF<US#3 X<HO", "A<X#6 UF<US#4 UF<US#5 ZA<OF UF<US#6 EA<OF",
          "EE<WX UF<USV#7 UVS<UVP UVA<UVS UF<USV#8 UVW<UVA UVQ<UVW UF<USV#9 HV<KU UF<USV#10 HI<HV UF<USV#11 HO<HI KU<KRX#2 UF<USV#12 HV<KU#2",
          "RI<RI#2 UF<USV#13 RI<RI#3 UF<USV#14 R<RI UF<USV#15 K<R UF<USV#16 MI<K", "LO<LA#2 lUVA<lUVS UF<USV#17 lUVW<lUVA lUQ<lUVW UF<USV#18 lHV<lUQ#2 UF<USV#19 lHI<lHV UF<USV#20 lHO<lHI")
MERGE = 3
ZERO = 0
SLOTS = 1
CONV = 10
PARTS = 2
ZBF = 1
INORDER = 0
EAS = 1
ABSW = 512
EARLY = ((0, 6), (6, 16))
LRELU = 0
CLATE = 2
LB = 256
LORD = ((0, 256), (256, 512), (768, 1024), (512, 768))
SE = 0
SX = 3
BEHIND, INIAT = 4, 16
PASSES = 6
GSEL = 10
JA = 8

CY = 0.00104
GA, SCT = 1.56, 3.8
HOP, OWN, ISSUE = 0.2, 0.11, 0.1
FLIGHT, SEND, SFIX, PE = 1.3, 0.35, 0.04, 0.5
GUESSES = ((CY, GA, SCT, HOP, OWN, FLIGHT, SFIX, 0.0), (CY, GA, SCT, HOP, OWN, 2.2, 0.03, 0.0), (0.00125, 1.9, 5.5, 0.2, 0.12, 1.6, 0.03, 0.0),
           (0.00092, 1.5, 3.5, 0.22, 0.12, 2.6, 0.06, 0.03))
TRIES, SEED, HEAT = 9000, 1, 0.03


def build(rank, core, T, topo):
    ops = []
    start = [-1000]

    def ap(name, lo=0, hi=None, st=1, rows=None):
        hi = _B[name][1][1] if hi is None else hi
        return ("a", name, lo, hi, st, rows)

    def ap3(name, a0, a1, b0, b1=None):
        return ("m", name, a0, a1, b0, b1)

    def ind(win, off):
        return ("i", win, off)

    def ext(name, lo, hi):
        return ("x", name, lo, hi)

    def res(d):
        if d[0] == "i":
            return res(d[1]).indirect(res(d[2]))
        if d[0] == "x":
            return T[d[1]][:, d[2]:d[3]]
        if d[0] == "m":
            return T[d[1]][:, d[2]:d[3], d[4]] if d[5] is None else T[d[1]][:, d[2]:d[3], d[4]:d[5]]
        _, name, lo, hi, st, rows = d
        t, off = _AT[name]
        n = _B[name][1][0]
        rs = slice(0, n) if rows is None else rows
        return T[t][rs, off + lo:off + hi] if st == 1 else T[t][rs, off + lo:off + hi:st]

    def acc(d):
        if d[0] == "x":
            return []
        if d[0] == "i":
            return acc(d[1]) + acc(d[2])
        if d[0] == "m":
            w = _B[d[1]][3]
            if d[5] is None:
                return [(d[1], w * d[2] + d[4], w * d[3], w)]
            return [(d[1], w * a + d[4], w * a + d[5], 1) for a in range(d[2], d[3])]
        return [(d[1], d[2], d[3], d[4])]

    def n_of(d):
        if d[0] == "m":
            return (d[3] - d[2]) * (1 if d[5] is None else d[5] - d[4])
        return 16 * n_of(d[2]) if d[0] == "i" else (d[3] - d[2] + d[4] - 1) // d[4]

    def size(d):
        return _SIZE[_B[d[1]][2]]

    def isps(d):
        return d[0] == "a" and d[1] in _PS

    def put(q, fn, reads, writes, cost, sem=None, inc=1, many=0):
        R, W = [], []
        for d in reads:
            R += acc(d)
        for d in writes:
            if d[0] == "i":
                W += acc(d[1]); R += acc(d[2])
            else:
                W += acc(d)
        a, b, ga, sct = cost if isinstance(cost, tuple) else (cost, 0, 0, 0)
        ops.append({"q": q, "fn": fn, "R": R, "W": W, "v": (a, b, ga, sct), "many": many, "sem": sem, "inc": inc, "k": len(ops) - start[0],
                    "c": a + CY * (b + GA * ga + SCT * sct) + SFIX * (q == "S") + FLIGHT * (q == "N")})
        return len(ops) - 1

    def vcost(n, full, inds, outs_ind):
        if outs_ind:
            return (0.06, 0, 0, n)
        if inds:
            return (0.06, 0, n, 0)
        return (0.0, max(64, n * full), 0, 0)

    def sc(x):
        return res(x) if isinstance(x, tuple) else x

    def tt(o, a, b, op):
        full = 1 if isps(a) or isps(b) else 2
        return put("V", lambda g: g.vector.tensor_tensor(res(o), res(a), res(b), op), [a, b], [o], vcost(n_of(o), full, a[0] == "i", o[0] == "i"))

    def ts(o, a, s1, op0, s2=None, op1=None):
        two = 0.5 if o[0] != "i" and a[0] != "i" and size(a) == 2 and size(o) == 2 else 1
        rd = [a] + [x for x in (s1, s2) if isinstance(x, tuple)]
        if op1 is None:
            return put("V", lambda g: g.vector.tensor_scalar(res(o), res(a), sc(s1), None, op0), rd, [o], vcost(n_of(o), two, a[0] == "i", o[0] == "i"))
        return put("V", lambda g: g.vector.tensor_scalar(res(o), res(a), sc(s1), sc(s2), op0, op1), rd, [o], vcost(n_of(o), two, a[0] == "i", o[0] == "i"))

    def cp(o, a):
        two = 0.5 if o[0] != "i" and a[0] != "i" and size(a) == 2 and size(o) == 2 else 1
        return put("V", lambda g: g.vector.tensor_copy(res(o), res(a)), [a], [o], vcost(n_of(o), two, a[0] == "i", o[0] == "i"))

    def scan(o, a, b, op0=AluOpType.mult, op1=AluOpType.add, first=0.0):
        return put("V", lambda g: g.vector.tensor_tensor_scan(res(o), res(a), res(b), first, op0, op1), [a, b], [o],
                   vcost(n_of(o), 0.5 if size(o) == size(a) == size(b) == 2 else 1, False, False))

    def most(o, a):
        return put("V", lambda g: g.vector.tensor_reduce(res(o), res(a), AxisListType.X, AluOpType.max), [a], [o], vcost(n_of(a), 1, False, False))

    def fill(o, v, q="V"):
        if q == "G":
            return iota(o, [[0, n_of(o)]], int(v))
        if q == "S":
            return act(o, ap("IC", 0, n_of(o)), AF.Copy, bias=v, scale=0.0)
        return put("V", lambda g: g.vector.memset(res(o), v), [], [o], vcost(n_of(o), size(o) / 4, False, False))

    def act(o, a, func, bias=0.0, scale=1.0, total=None):
        rd = [a] + [x for x in (bias, scale) if isinstance(x, tuple)]
        if total:
            return put("S", lambda g: g.scalar.activation(res(o), res(a), func, bias=sc(bias), scale=sc(scale), accum_out=res(total)), rd, [total, o],
                       (0.02, max(64, n_of(o)), 0, 0))
        if o[0] == "i":
            return put("S", lambda g: g.scalar.activation(res(o), res(a), func), rd, [o], (0.0, 0, 0, n_of(o)))
        return put("S", lambda g: g.scalar.activation(res(o), res(a), func, bias=sc(bias), scale=sc(scale)), rd, [o],
                   (0.05, 0, n_of(o), 0) if a[0] == "i" else (0.0, max(64, n_of(o)), 0, 0))

    def mm(lst):
        def fn(g):
            r = None
            for o, l, rh, st, sp in lst:
                r = g.tensor.matmul(res(o), res(l), res(rh), st, sp)
            return r
        return put("P", fn, [x[1] for x in lst] + [x[2] for x in lst], [x[0] for x in lst], (0.0, PE * sum(max(64, n_of(x[2])) for x in lst), 0, 0), many=len(lst))

    def iota(o, pattern, base, step=0):
        if _B[o[1]][2] == I:
            return put("G", lambda g: g.iota(res(o), pattern, base, step), [], [o], (0.15, 2 * n_of(o), 0, 0))
        return put("G", lambda g: g.iota(res(o), pattern, base, step, allow_small_or_imprecise_dtypes=True), [], [o], (0.22, 2 * n_of(o), 0, 0))

    def later(*ks):
        ops[-1].setdefault("after", []).extend(ks)

    nd, sent = [0], []

    def dma(o, a, cost, behind=()):
        k = "d%d" % nd[0]; nd[0] += 1
        put("Y", lambda g: g.sync.dma_start(res(o) if isinstance(o, tuple) else o, res(a) if isinstance(a, tuple) else a),
            ([a] if isinstance(a, tuple) else []) + list(behind), [o] if isinstance(o, tuple) else [], cost, sem=k, inc=16)
        ops[-1]["hold"] = ISSUE
        return len(ops) - 1

    def dma_add(o, a, cost, behind=()):
        k = "d%d" % nd[0]; nd[0] += 1
        put("G", lambda g: g.dma_start(res(o), res(a), accum_op=AluOpType.add, max_dma_last_dim=4096), [a, o] + list(behind), [o], cost, sem=k, inc=16)
        ops[-1]["hold"] = 1.0

    def dma_cast(o, a, cost):
        k = "d%d" % nd[0]; nd[0] += 1
        put("G", lambda g: g.dma_start(res(o), res(a)), [a], [o], cost, sem=k, inc=16)
        ops[-1]["hold"] = 1.0

    def arrives(o, sem, inc, ks, cost=0.0):
        put("N", None, [], o, cost, sem=sem, inc=inc)
        ops[-1]["after"] = list(ks)

    def leaves(fn, reads, loc, n, cost):
        k = put("G", fn, reads, [], SEND, sem=loc, inc=0)
        sent.append(k)
        ops[-1]["n"] = n
        put("N", None, reads, [], cost)
        ops[-1]["after"] = [k]; ops[-1]["left"] = k
        return k

    def send(o, a, sem, loc, dst, cost=0.0):
        loc = "x%d" % len(sent)
        rid, pid, se = topo.addr(dst)
        return leaves(lambda g: g.remote_dma(T[o][:, a[2]:a[3]], res(a), T.sem[sem], T.sem[loc], pid, rid, topo.mask(core, dst)), [a], loc,
                      len(topo.engines(core, dst)), cost)

    def swap(o, a, sem, loc, dst):
        k = send(o, a, sem, loc, dst)
        arrives([ap(o, a[2], a[3])], sem, ops[k]["n"], [k])
        return k

    def stage(name, src, lo, step, w, sem, loc):
        hs, loc = helpers(core, T, topo), "x%d" % len(sent)
        free = [e for e in topo.engines(core, hs[0]) if e not in topo.engines(core, T.cores[(rank + 1) % 4])]
        n = len(free) // len(hs)

        def fn(g):
            tr = []
            for i, h in enumerate(hs):
                rid, pid, se = topo.addr(h)
                a = lo + i * step
                tr.append(RemoteDMATransfer(dst_ids=[DstId(rid=rid, pnc=pid)], dma_engine_mask=bits(free[n * i:n * i + n]), remote_sem=T.sem[sem],
                                            src=T[src][:, a:a + w], dst=T[name][:, a:a + w]))
            return g.remote_dma_fused(tr, local_sem=T.sem[loc])
        return leaves(fn, [ap(src, lo + i * step, lo + i * step + w) for i in range(len(hs))], loc, len(free), 3.0)

    def ship(t):
        near = NEAR
        ks = [send("UL%d" % t, ap("US", 0, near), "ur%d" % t, "lc", T.cores[(rank - 1 - t % 3) % 4], 5.0)]
        if near < S:
            ks.append(stage("UL%d" % t, "US", near, (S - near) // 2, (S - near) // 2, "hU%d" % t, "lb"))
        arrives([ap("UL%d" % t, 0, S)], "ur%d" % t, ops[ks[0]]["n"] * (3 if near < S else 1), ks, 8.0)
        return ks

    ADD, SUB, MUL, MIN, MAX = AluOpType.add, AluOpType.subtract, AluOpType.mult, AluOpType.min, AluOpType.max
    EQ, NE, GE, GT, LT, LE = AluOpType.is_equal, AluOpType.not_equal, AluOpType.is_ge, AluOpType.is_gt, AluOpType.is_lt, AluOpType.is_le
    SHR, AND = AluOpType.arith_shift_right, AluOpType.bitwise_and
    AF = ActivationFunctionType

    def keep(o, src, pattern, base, op=EQ, step=0):
        return put("G", lambda g: g.affine_select(res(o), res(ap(src)), pattern, op, 0.0, base, step), [ap(src)], [o], (0.28, 256, 0, 0))

    dma(ap("c8"), T.c0[:, :], 1.7); dma(ap("hwi"), T.hw[:, :], 1.7); later(0)
    dma(ap("kmi"), T.km[:, :], 1.7); later(1); dma(ap("th8"), T.th[:, :], 1.7); later(2)
    dma(ap("TP"), ext("tp", 0, S), 3.8); later(3)
    ldu = dma(ap("US", 0, S), ext("us", 0, S), 6.2); later(4)
    ks = [send("TL1", ap("TP", h, h + TNEAR), "tr1", "ld", T.cores[(rank - 2) % 4], 3.0) for h in (0, S // 2)]
    ks += [stage("TL0", "TP", S // 2 - sum(STAGED[:p + 1]), S // 2, w, "hT%d" % p, "lt") for p, w in enumerate(STAGED)]
    for k in ks:
        ops[k]["waits"] = [ldu]
    for k in range(3):
        arrives([ap("TL%d" % k)], "tr%d" % k, ops[ks[0]]["n"] * 2 * (sum(x[:2] == ("T", k) for x in FAR) + (k == 1)), ks, 8.0)

    iota(ap("pI"), [[0, 1]], 0, 1); iota(ap("CG"), [[1, 8], [0, 16]], 0); iota(ap("IC"), [[1, 256]], 0); iota(ap("CS"), [[0, 16], [1, 16]], 0)
    iota(ap("CG8"), [[8, 8], [0, 4], [1, 4]], 0); iota(ap("C3"), [[0, 32], [1, 4]], 0)
    ts(ap("sI"), ap("pI"), 15, AND); ts(ap("s2I"), ap("sI"), 2, SHR)
    for a, b in (("pF", "pI"), ("sF", "sI"), ("s2F", "s2I")):
        cp(ap(a), ap(b))
    ts(ap("gF"), ap("pF"), ap("sF"), SUB, 1.0 / 16, MUL); ts(ap("gx8"), ap("pF"), ap("sF"), SUB, 0.5, MUL)
    ts(ap("sge8"), ap("sF"), 7.5, GT); ts(ap("slt8"), ap("sF"), 7.5, LT)
    ts(ap("pm8"), ap("sge8"), -16.0, MUL, 8.0, ADD); ts(ap("pm8"), ap("pm8"), ap("pF"), ADD)
    ts(ap("nsB"), ap("sF"), -BIG, MUL); ts(ap("ns2"), ap("s2F"), -8 * BIG, MUL); ts(ap("s1T"), ap("sF"), 1.0, ADD, 16384.0, MUL)
    ts(ap("BLKB"), ap("CG"), ap("gF"), EQ); ts(ap("BLKH"), ap("CG"), ap("gF"), EQ)
    r8 = slice(0, 8)
    ts(ap("REP8"), ap("CG", 0, 128, 1, r8), ap("pF", 0, 1, 1, r8), EQ)
    ts(ap("PH"), ap("IC", 0, 128), ap("pm8"), EQ)
    ts(ap("PL"), ap("IC", 0, 128), ap("pm8"), EQ, ap("sge8"), MUL); ts(ap("PR"), ap("IC", 0, 128), ap("pm8"), EQ, ap("slt8"), MUL)
    ts(ap("hwf"), ap("hwi"), 2047.5, GT, -4096.0, MUL); tt(ap("hwg"), ap("hwi"), ap("hwf"), ADD); tt(ap("hwh"), ap("hwi"), ap("hwf"), ADD)
    mm([(ap("MS", 0, 2), ap("PH"), ap("hwh"), True, True)])
    cp(ap("ws"), ap("MS", 0, 2))

    def wt(k, qv, r):
        i = (k * 2 + qv) * 4 + r
        return ap("WT", i * 128, i * 128 + 128)
    ts(ap("g8"), ap("IC", 0, 4), ap("gx8"), ADD); ts(ap("g8m"), ap("g8"), ap("slt8"), SUB); ts(ap("g8p"), ap("g8", 3, 4), ap("slt8"), MUL, ap("sge8"), SUB)
    for qv in (0, 1):
        for r in range(4):
            ts(wt(0, qv, r), ap("CG8"), ap("g8m", r, r + 1), EQ, ap("ws", qv, qv + 1), MUL)
        ts(wt(1, qv, 3), ap("CG8"), ap("g8p"), EQ, ap("ws", qv, qv + 1), MUL)
    iota(ap("CG2"), [[8, 8], [1, 2], [0, 8]], 0); iota(ap("CZ"), [[0, 2], [1, 4], [0, 8]], 0); iota(ap("ML"), [[8, 8], [0, 4], [64, 8]], 0)
    fill(ap("ONEB"), 1.0, "G")

    def lw(k, qv, i):
        return ap("LW%d" % k, 256 * qv + 128 * i, 256 * qv + 128 * i + 128)

    def to_all(name, reads, sem, loc):
        far = [T.cores[(rank - 1 - k) % 4] for k in range(3)]
        m = topo.mask(core, far[0]) & topo.mask(core, far[1]) & topo.mask(core, far[2])
        n = len([e for e in topo.engines(core, far[0]) if m >> e & 1])
        to = [DstId(rid=topo.addr(c)[0], pnc=topo.addr(c)[1]) for c in far]
        k = leaves(lambda g: g.remote_dma_fused([RemoteDMATransfer(dst_ids=to, dma_engine_mask=m, remote_sem=T.sem[sem], srcs=[T[name + "3"][:, :]],
                                                                   dsts=[T[name + str(i)][:, :] for i in range(3)])], local_sem=T.sem[loc]), reads, loc, n, 0.0)
        arrives([ap(name + str(i)) for i in range(3)], sem, 3 * n, [k], 2.0)
    for k in range(2):
        keep(ap("PK", 128 * k, 128 * k + 128), "ONEB", [[16, 8], [0, 2], [2, 8]], k, EQ, -1)
    for r in range(8):
        keep(ap("RL", 128 * r, 128 * r + 128), "ONEB", [[16, 8], [0, 8], [8, 2]], r, EQ, -1)
    ts(ap("s1I"), ap("sI"), 1, SHR); cp(ap("s1F"), ap("s1I"))
    act(ap("PZL"), ap("CZ"), AF.Abs, bias=ap("ns2"), scale=8 * BIG); act(ap("PZL"), ap("PZL"), AF.Identity, bias=ap("s1F"))
    for o, v in (("IDB", 1.0), ("IDH", 1.0), ("IDN", -1.0), ("I512", 512.0)):
        ts(ap(o), ap("IC", 0, 128), ap("pF"), EQ, v, MUL)
    act(ap("I255"), ap("IDB"), AF.Copy, scale=-255.0)
    act(ap("NM"), ap("CS"), AF.Abs, bias=ap("nsB"), scale=BIG)
    act(ap("PZ4"), ap("C3"), AF.Abs, bias=ap("ns2"), scale=8 * BIG); act(ap("RS4"), ap("C3"), AF.Relu, bias=8 * BIG, scale=-8 * BIG)
    act(ap("MWR"), ap("NM"), AF.Relu, bias=1.0, scale=-1.0); act(ap("RST"), ap("CS"), AF.Sign)
    act(ap("TRH"), ap("CS", 0, 64), AF.Relu, bias=ap("s1T"), scale=-16384.0); ts(ap("pm1"), ap("sF"), 47.0, ADD, -16384.0, MUL)
    act(ap("lTR", 0, 64), ap("IC", 0, 64), AF.Relu, bias=ap("pm1"), scale=16384.0); fill(ap("lTR", 64, 80), UNF, "G")
    for o, v in (("B512", 1024.0), ("B256", 256.0)):
        act(ap(o), ap("BLKB"), AF.Copy, scale=v)
    ts(ap("ksc"), ap("kmi"), -2048.0, ADD); ts(ap("kh"), ap("CS", 0, 16), ap("sF"), EQ, ap("ksc"), MUL)
    mm([(ap("MS", 16, 32), ap("BLKH"), ap("kh"), True, True)])
    ts(ap("KR"), ap("MS", 16, 32), 2048.0, ADD)
    ts(ap("LS"), ap("IC", 0, 16), 0.0, MUL, ap("sF"), ADD); cp(ap("LC"), ap("IC", 0, 16))
    act(ap("KRX"), ind(ap("KR"), ap("LC")), AF.Copy)
    fill(ap("RS5"), 0.0, "G"); fill(ap("RS5", 0, 128, 8), 8 * BIG, "S"); fill(ap("R5", 1, 128, 2), 8 * BIG, "S"); fill(ap("R5", 7, 128, 8), 0.0, "S")
    ts(ap("th8h"), ap("th8"), -2048.0, ADD)
    mm([(ap("MS", 8, 9), ap("REP8"), ap("th8h"), True, True)])
    ts(ap("th16"), ap("MS", 8, 9), 2047.5, ADD, 1024.0, MUL)
    ts(ap("JW0"), ap("IC", 0, 256, 16), ap("sF"), ADD)
    act(ap("DRS"), ap("CS"), AF.Copy, bias=-BIG, scale=0.0); ts(ap("DRS", 0, 256, 16), ap("JW0"), S - 2047.0, ADD)
    for k in range(2):
        act(ap("DMP", 8 * k, 8 * k + 4), ap("JW0", 0, 4), AF.Copy, bias=float(ZD + k), scale=2.0)
    ts(ap("c8h"), ap("c8"), -2048.0, ADD)
    mm([(ap("CT", 0, 256), ap("IDB"), ap("NM"), True, False), (ap("CT", 0, 256), ap("REP8"), ap("c8h"), False, True)])
    scan(ap("CM2"), ap("DRS"), ap("CT", 0, 256), MAX, MIN); ts(ap("CL0"), ap("CM2", 15, 256, 16), 2048.0, ADD)
    mm([(ap("HR", 0, 256), ap("REP8"), ap("c8h"), True, True)])
    act(ap("CX0", OLD, OLD + L), ap("HR", 0, 256), AF.Copy, bias=2048.0)
    for k in "01":
        fill(ap("TX" + k, OLD + L, END), 0.0, "G" if k == "1" else "S"); fill(ap("WX" + k, OLD + L, END), 0.0, "G"); act(ap("CX" + k, OLD + L, END), ap("IC", 0, END - OLD - L), AF.Copy)
    act(ap("TX0", OLD, OLD + 128), ind(ap("TP"), ap("CL0", 0, 8)), AF.Copy); cp(ap("TX0", OLD + 128, OLD + L), ind(ap("TP"), ap("CL0", 8, 16)))

    keep(ap("SEL", 0, 128), "B512", [[0, 8], [1, 16]], -15); fill(ap("SEL", 128, 144), 0.0, "S")
    keep(ap("SLQ", 0, 128), "B512", [[0, 32], [1, 4]], -3); fill(ap("SLQ", 128, 144), 0.0, "S")
    keep(ap("SLP", 0, 128), "B512", [[0, 16], [1, 8]], -7); fill(ap("SLP", 128, 144), 0.0, "S")
    ts(ap("pen2"), ap("IC", 0, 2), ap("sge8"), NE, 2 * BIG, MUL)
    for h in range(2):
        ts(ap("MP", h, 384, 2), ap("IC", 0, 192), ap("pen2", h, h + 1), ADD)

    def slp(r):
        return ap("SLP", 7 - r, 135 - r)

    def sel(s):
        return ap("SEL", 15 - s, 143 - s)

    def slq(r):
        return ap("SLQ", 3 - r, 131 - r)
    keep(ap("TRG"), "BLKB", [[-1, 128]], 0, GE, 1); keep(ap("TRL"), "BLKB", [[1, 128]], 0, GT, -1); fill(ap("SC", 0, 1), 0.0, "G")
    for k in range(4):
        act(ap("WTAB", 128 * k, 128 * k + 128), ap("C3"), AF.Copy, bias=4.0)
    for k in range(1, 8):
        wtab = dma(ap("WTAB", 512 * k, 512 * k + 512), ap("WTAB", 0, 512), 4.0, [ap("US", 0, S)]); later(ldu, len(ops) - 2)
    ts(ap("c8i"), ap("c8"), 3, AND); ts(ap("c8w"), ap("c8i"), 4.0, ADD)
    mm([(ap("DB", 0, 256), ap("REP8"), ap("c8w"), True, True)])
    act(ap("WX0", OLD, OLD + L), ap("DB", 0, 256), AF.Copy)
    iota(ap("kz1"), [[1, 64], [0, 4]], 192)
    mm([(ap("DA", 0, 256), ap("IDB"), ap("kz1"), True, False)] + [(ap("DA", k, k + 128), ap("IDB"), ap("PZ4"), False, k > 0) for k in (0, 128)])
    act(ap("MS1"), ap("DA", 0, 256), AF.Copy)
    ts(ap("J256"), ap("JW0"), 256.0, ADD); act(ap("NJ"), ap("JW0"), AF.Copy, bias=-0.5, scale=-1.0 / 512)
    ts(ap("EE", 255, 511), ap("CS"), 0.0, MUL, 1282.0, ADD); ts(ap("EE", 511, 512), ap("pF"), 0.0, MUL, 1282.0, ADD)
    fill(ap("one16"), 1.0, "S"); fill(ap("P2", 0, 16), 0.5, "S"); scan(ap("P2", 16, 32), ap("P2", 0, 16), ap("one16"), MUL, MAX, 2.0 ** 29)
    tt(ap("P2", 32, 48), ap("P2", 16, 32), ap("MWR", 0, 16), MUL); scan(ap("P2", 0, 16), ap("one16"), ap("P2", 32, 48)); ts(ap("rF"), ap("P2", 15, 16), -2.0, MUL)
    act(ap("W2"), ap("BLKB"), AF.Identity, scale=ap("P2", 15, 16)); act(ap("B30"), ap("BLKB"), AF.Copy, scale=2.0 ** 30)
    act(ap("NM2"), ap("NM", 0, 128), AF.Identity, bias=ap("rF"), scale=2.0 ** 23)
    ts(ap("EE", 0, 1), ap("pF"), 0.0, MUL)
    fill(ap("oneR"), 1.0, "G"); fill(ap("C255"), 255.0, "G")
    rng = [(11 * c, min(254, 20 * c + 19)) for c in range(16)]
    ts(ap("THR"), ap("JW0"), 5.0, MUL, 66.5, ADD)
    iota(ap("KJ", 0, 12), [[31, 12]], 19); iota(ap("KJ", 12, 16), [[11, 4]], 11 * 12 + 254)
    keep(ap("SH1"), "B256", [[-1, 128]], 1, EQ, 1); keep(ap("SH2"), "B256", [[-1, 128]], -15, EQ, 1)
    fill(ap("LO", 24, 32), 0); fill(ap("lLO"), 0); fill(ap("NIL"), 0.0, "G")
    fill(ap("K256"), 256.0, "G"); fill(ap("JB", 0, 16), -260.0, "G"); fill(ap("DJ"), 0.0); fill(ap("WN", 256, 512), BIG, "G")
    iota(ap("ZERO"), [[0, 128]], 0); fill(ap("RS", 64, 72), 0.0, "G")
    iota(ap("STB"), [[0, 128]], 1024); fill(ap("US", S, 4480), 0.0, "G")
    iota(ap("IC64"), [[1, 64]], 0)
    act(ap("HT", 256, 512), ap("IC"), AF.Copy); fill(ap("HT", 512, 528), UNF, "G"); fill(ap("lHT", 512, 528), UNF, "G")
    fill(ap("RI", 0, 64), 8 * BIG, "S")

    for t in range(RO):
        start[0] = len(ops)
        cur, nxt = str(t % 2), str(1 - t % 2)
        cx, tx, cy, ty, wx, wy = "CX" + cur, "TX" + cur, "CX" + nxt, "TX" + nxt, "WX" + cur, "WX" + nxt
        last = t == RO - 1
        b16 = ap("th16") if t == 0 else ap("b16a" if t % 2 else "b16b")
        lender = T.cores[(rank + 1 + t % 3) % 4]
        borrower = T.cores[(rank - 1 - t % 3) % 4]
        mm([(ap("UVP", 0, 128), ap("IDB"), ap("PZ4"), True, False)])
        lst = []
        for qv in (0, 1):
            for r in range(4):
                lst.append((ap("UVP", 64 * qv, 64 * qv + 64), wt(0, qv, r), ap(tx, OLD + r, OLD + r + 253, 4), False, False))
            lst.append((ap("UVP", 64 * qv, 64 * qv + 64), wt(1, qv, 3), ap(tx, OLD + 4, OLD + 257, 4), False, qv == 1))
        mm(lst)
        mm([(ap("ZP", 0, 256), ap("PL"), ap(tx, OLD, OLD + L), True, False), (ap("ZP", 0, 256), ap("PR"), ap(tx, OLD + 1, OLD + 257), False, True)])
        zb = [act(ap("ZB", 256 * k, 256 * k + 256), ap("ZP", 0, 256), AF.Copy, bias=-255.0 if t > 1 else 0.0) for k in range(2)]
        act(ap("ZF"), ap("ZB", 0, 256), AF.Copy, bias=64.0 + 255.0 * (t > 1))
        under = ap("UF" if t > 1 else "US", 0, S)
        less, mark = (255, "NIL") if t > 1 else (0, "C255")
        ask, copy = t in ASK, t + 1 < RO and t + 1 not in ASK
        who = 3 if ask else t % 3
        lent, zl = ("UF" if t else "US", "ZN%d" % t) if ask else ("UL%d" % t, "ZL")
        if not t:
            for qv in (0, 1):
                for i in (0, 1):
                    ts(lw(3, qv, i), ap("CG2"), ap("g8", i, i + 1), EQ, ap("hwg", qv, qv + 1), MUL)
            cp(ap("k1"), ap("ksc"))
        if t:
            iota(ap(lent, S, 4480), [[0, 4480 - S]], -less); later(start[0] + 1)
        if t == 2:
            iota(ap("UL0", 0, 512), [[0, 512]], 255); later(len(ops) - 2)
            for k in range(512, S, 512):
                dma(ap("UL0", k, k + 512), ap("UL0", 0, 512), 7.0, [ap("ZB")])
        if last:
            for k in range(0, S, 2048):
                dma_add(ap("UL0", k, k + 2048), ap("UF", k, k + 2048), 7.0, [ap("ZB")])
        scan(ap("UVS"), ap("RS4"), ap("UVP", 0, 128), ADD, MIN); later(wtab)
        ts(ap("UVA"), ap("UVS", 3, 128, 4), 4095, AND)
        tt(ap("UVW"), ap("UVA", 0, 16), ap("UVA", 16, 32), MUL)
        ts(ap("UVQ"), ap("UVW"), 5, SHR)
        for a, b in EARLY:
            tt(ap("KU", 16 * a, 16 * b), ind(ap("UVA", 0, 16), ap("LS", a, b)), ap("KRX", 16 * a, 16 * b), MUL)
            tt(ap("HV", 16 * a, 16 * b), ind(ap("UVQ"), ap("LS", a, b)), ap("KU", 16 * a, 16 * b), ADD)
            ts(ap("HI", 16 * a, 16 * b), ap("HV", 16 * a, 16 * b), 4095, AND)
            cp(ap("HO", 16 * a, 16 * b), ap("HI", 16 * a, 16 * b))
        for k in (1, 256):
            scan(ap("EE", k, k + 254), ap("oneR", 0, 254), ap(wx, OLD, OLD + 254))
        mm([(ap("JP", 256, 512), ap("IDH"), ap("EE", 0, 256), True, True)])
        act(ap("E32"), ap("JP", 256, 512), AF.Copy, bias=64.0)
        for k in range(0, 16, 4):
            mm([(ap("MS", 32, 64), sel(s), ap("EE", s, s + 497, 16), s == 0, s == 15) for s in range(k, k + 4)])
        slots = [lambda: ts(ap("FI"), ap("MS", 32, 64), 0.2 / 16384, MUL, 256.0, MIN),
                 lambda: tt(ap("NW"), ap("FI", 16, 32), ap("FI", 0, 16), SUB),
                 lambda: ts(ap("RI", 1, 64, 4), ap("NW"), 4 * BIG, MUL, 512.0 - 2 * BIG, ADD),
                 lambda: ts(ap("RS5", 7, 128, 8), ap("NW"), -1.0, MUL, b16, ADD)]
        prev, where, fours = {}, {}, 0
        minus = [m + i for step, m, k in PROBE if step == "minus" for i in range(k)]
        for step, m, k in PROBE:
            x = ap("X", 256 * m, 256 * (m + k))
            if step == "gather" and m in BYS:
                d = ap(BYS[m], 512 - 256 * k, 512)
                for i in range(k):
                    where[m + i] = (d[1], d[2] + 256 * i)
                j = act(x, ind(under, ap("HO", 16 * m, 16 * (m + k))), AF.Copy)
                mm([(d, ap("IDN"), ap("ZB", 0, 256 * k), True, False)]); mm([(d, ap("IDB"), x, False, True)])
            elif step == "gather":
                j = tt(x, ind(under, ap("HO", 16 * m, 16 * (m + k))), ap("ZB", 0, 256 * k), SUB)
            elif step == "minus":
                j = ts(ap("A", 256 * m, 256 * (m + k)), x, 0.0, MIN, -2.0, MUL)
            elif step == "fold":
                tt(ap("RM", 384, 448), ap("RM", 256, 320), ap("RM", 320, 384), MIN)
                for lo in (384, 416):
                    j = tt(ap("RI", lo // 32 - 10, 64, 4), ap("RM", lo, lo + 31, 2), ap("RM", lo + 1, lo + 32, 2), MIN)
            elif step in ("two", "four"):
                d, lo, w = SUMS[m - m % 4], 32 * (m % 4), 2 if step == "two" else 4
                if not k or w == 4:
                    mm([(ap(d, 0, 128), ap("IDB"), ap("MP", 32 * m - lo, 32 * m - lo + 128), True, False)])
                if m in minus:
                    mm([(ap(d, lo, lo + 32 * w), slp(r), ap("X", 256 * m + r, 256 * (m + w), 8), False, False) for r in range(8)])
                j = mm([(ap(d, lo, lo + 32 * w), slp(r), ap("A", 256 * m + r, 256 * (m + w), 8), False, k == 1 and r == 7) for r in range(8)])
                if k:
                    y = ap("RM", fours, fours + 128)
                    if fours:
                        tt(y, ap(d, 0, 128), ap("RM", fours - 128, fours), MIN)
                    else:
                        ts(y, ap(d, 0, 128), b16, MIN)
                    fours += 128
            elif step == "single":
                d = ap(SUMS[m], 0, 64)
                mm([(d, ap("IDB"), ap("MS1", 64 * (m - 12), 64 * (m - 11)), True, False)])
                if m in minus:
                    mm([(d, slq(r), ap("X", 256 * m + r, 256 * m + 256, 4), False, False) for r in range(4)])
                mm([(d, slq(r), ap("A", 256 * m + r, 256 * m + 256, 4), False, r == 3) for r in range(4)])
                if k == 0 and MERGE:
                    j = cp(ap("RI", 64, 128), d)
                else:
                    y = ap("RI", 64 * k, 64 * k + 64)
                    if k == MERGE and k:
                        tt(ap("RI", 256, 320), ap("RI", 0, 64), y, MIN); y = ap("RI", 256, 320)
                    j = tt(ap("RI", 64 * k + 64, 64 * k + 128) if k < 3 else ap("R5", 0, 128, 2), d, y, MIN)
            elif step == "abs":
                j = act(ap("A", 256 * m, 256 * (m + k)), ap(where[m][0], where[m][1], where[m][1] + 256 * k) if m in where else x, AF.Abs)
            else:
                j = slots[m]()
            if step in KEPT:
                if ops[j]["q"] in prev:
                    ops[j].setdefault("after", []).append(prev[ops[j]["q"]])
                prev[ops[j]["q"]] = j
        scan(ap("K5"), ap("RS5"), ap("R5"), SUB, MIN)
        key = ap("K5", 6, 128, 8)
        iota(ap("ZA", 0, 64), [[0, 64]], 768 + 64); later(start[0] + 1)
        mm([(ap("MS", 64, 80), ap("IDH"), ap("J256"), True, False)])
        poor = ap("K5", 7, 128, 8)
        scn = scan(ap("SC", 1, 17), ap("one16"), poor, MUL, SUB); tt(ap("POJ"), poor, ap("NJ"), MAX)
        ts(ap("HT", 0, 256), ap("HI"), -2047.0, ADD)
        mm([(ap("MS", 64, 80), ap("TRL"), ap("SC", 1, 17), False, False), (ap("MS", 64, 80), ap("TRG"), ap("SC", 0, 16), False, False)])
        mm([(ap("MS", 64, 80), ap("I512"), ap("POJ"), False, True)])
        ts(ap("MI"), key, 1023, AND)
        cp(ap("OF"), ap("MS", 64, 80))
        cp(ap("LL"), ap("MI"))
        act(ind(ap("ZA"), ap("OF")), ap("ZF"), AF.Silu)
        ts(ap("ZL"), ap("ZA", 0, 64), ROUND, ADD, -ROUND - 64.0, ADD)
        if ask:
            swap(zl, ap("ZL"), "ma%d" % t, "la", lender)
        if not t:
            mm([(ap("UVP", 4 + k, 5 + k), ap("PK", 128 * k, 128 * k + 128), ap("k1"), True, True) for k in range(2)])
            ts(ap("LP3", 0, 2), ap("UVP", 4, 6), 2048.0, ADD)
            to_all("LP", [ap("LP3", 0, 2), ap("ksc"), ap("th16")], "prm", "lp"); to_all("LW", [ap("LW3")], "prw", "lq")
        for lo in (128, 0):
            tt(ap("HM", lo, lo + 128), ind(ap("HT"), ap("LL", lo // 16, lo // 16 + 8)), ap("MWR", 0, 128), MUL)
            scan(ap("HS", lo, lo + 128), ap("RST", 0, 128), ap("HM", lo, lo + 128))
            row = ap("ZP" if lo else "HR", 0, 128)
            mm([(row, ap("BLKH"), ap("HM", lo, lo + 128), True, True)])
            cp(ap("HRH", lo, lo + 128), row)
            act(ap(cx, lo, lo + 128), row, AF.Copy, bias=2047.0)
            act(ap("UR", lo, lo + 128), row, AF.Relu, bias=-3000.0)
            tt(ap("HD", lo // 16, lo // 16 + 8), ap("HS", lo + 15, lo + 128, 16), ap("DRS", lo, lo + 128, 16), MIN)

        def equal(k, lo, hi, c):
            ts(ap3("ET", k, k + 1, 0, hi - lo), ap("HRH", lo, hi), ap("HS", 16 * c + 15, 16 * c + 16), EQ)
        if t:
            put("G", lambda g, v=(t + 1) * TINY: g.affine_select(res(ap("STP")), res(ap("ZERO")), [[0, 128]], GT, v, 0, 0), [ap("ZERO")], [ap("STP")], (0.18, 256, 0, 0))
        for h, d in ((1, "CT"), (0, "DB")):
            mm([(ap(d, 256, 384), ap("IDB"), ap("NM2", 0, 128), True, False)])
            for c in range(8):
                equal(8 * h + c, 128 * h + 16 * c, 128 * h + 128, 8 * h + c)
                if c < 7:
                    mm([(ap(d, 272 + 16 * c, 384), ap("B30"), ap3("ET", 8 * h + c, 8 * h + c + 1, 16, 128 - 16 * c), False, False)])
            ctl = mm([(ap(d, 256, 384), ap("W2"), ap3("ET", 8 * h, 8 * h + 8, 0, 16), False, True)])
            scan(ap("WS", 128 * h, 128 * h + 128), ap("DRS", 128 * h, 128 * h + 128), ap(d, 256, 384), MAX, MIN)
            tt(ap("LA", 8 * h, 8 * h + 8), ap("WS", 128 * h + 15, 128 * h + 128, 16), ap("HD", 8 * h, 8 * h + 8), MAX)
            ts(ap("LO", 16 * h, 16 * h + 8), ap("LA", 8 * h, 8 * h + 8), 2047.0, ADD)
            if not ask:
                swap("LM%d" % t, ap("LO", 16 * h, 24 * h + 8), ("mb%d", "ma%d")[h] % t, ("lr", "la")[h], borrower)
            if t:
                act(ind(ap("UF", 0, ZD), ap("LO", 16 * h, 16 * h + 8)), ap("ZERO" if h else "STP"), AF.Silu)
            if last or not t:
                cp(ind(ap("UL0" if t else "US", 0, ZD), ap("LO", 16 * h, 16 * h + 8)), ap("C255", 0, 128))
            act(ap("WD", 128 * h, 128 * h + 128), ap(d, 256, 384), AF.Sign)
        if copy and t:
            dma_cast(ap("US", 0, S), ap("UF", 0, S), 4.5)
        ts(ap("HL"), ap("HS", 15, 256, 16), 2047.0, ADD, 4095.0, MIN)
        iota(ap("EA", 0, 64), [[5, 64]], 1344); later(start[0] + 1)
        act(ind(ap("EA"), ap("OF")), ap("E32"), AF.Silu)
        scan(ap("EQ"), ap("TRH", 0, 64), ap("EA", 0, 64), MAX, MIN)
        ts(ap("FAI"), ap("EQ", 15, 64, 16), -64.0, ADD, 0.2, MUL)
        cp(ap("FA"), ap("FAI"))
        for c, (lo, hi) in enumerate(rng):
            act(ap("SG", 128 * c, 128 * c + hi - lo), ap("E32", lo + 1, hi + 1), AF.Sign, bias=ap("THR", c, c + 1), scale=-1.0, total=ap("SJ", c, c + 1))
        tt(ap("J2"), ap("SJ"), ap("KJ", 0, 16), ADD)
        ts(ap("JB", 16, 32), ap("J2"), 0.5, MUL, -256.0, ADD); ts(ap("DJ", 0, 256, 16), ap("J2"), 0.5, MUL, float(OLD), ADD)
        mm([(ap("DA", 256, 272), ap("IDB"), ap("K256"), True, False), (ap("DA", 256, 272), ap("I255"), ap("JB", 16, 32), False, False),
            (ap("DA", 256, 272), ap("SH1"), ap("JB", 16, 32), False, False), (ap("DA", 256, 272), ap("SH2"), ap("JB", 15, 31), False, True)])
        tt(ap("JX"), ap("DA", 256, 272), ap("JB", 16, 32), MAX); ts(ap("JL"), ap("JX"), 256.0, ADD)
        if t:
            act(ap("MF"), ind(ap("UF", 0, S), ap("HL", 8, 16)), AF.Relu, bias=-2000.0 * t - 1000.0, scale=4000.0 / TINY)
        else:
            cp(ind(ap("X"), ap("LO", 0, 8)), ap("STB"))
            act(ap("MF"), ind(ap("X", 0, S), ap("HL", 8, 16)), AF.Relu, bias=-256.0)
        mm([(ap("MS", 256, 512), ap("IDB"), ap("IC"), True, False)]); mm([(ap("MS", 256, 512), ap("IDB"), ap("UR"), False, False)])
        mm([(ap("MS", 256, 512), ap("B512"), ap("WD"), False, False)])
        mm([(ap("MS", 384, 512), ap("IDB"), ap("MF"), False, True)])
        wn = act(ap("WN", 0, 256), ap("MS", 256, 512), AF.Copy, bias=-14336.0)
        mm([(ap("UVP", 128 + 32 * qv, 160 + 32 * qv), lw(who, qv, i), ap(zl, i, i + 63, 2), qv + i == 0, qv + i == 2) for qv in (0, 1) for i in (0, 1)])
        for k in range(0, 8, 4):
            mm([(ap("JP", r, 512, 8), ap("IDB"), ap(zl), r == 0, r == 7) for r in range(k, k + 4)])
        for k in range(2):
            act(ap("ZT", 256 * k, 256 * k + 256), ap("JP", 256 * k, 256 * k + 256), AF.Copy, bias=-float(less))
        cp(ap("lUVS"), ap("UVP", 128, 192))
        ts(ap("lUVA"), ap("lUVS"), 4095, AND)
        tt(ap("lUVW"), ap("lUVA", 0, 32), ap("lUVA", 32, 64), MUL)
        for k in range(2):
            ts(ap("lKU", 32 * k, 32 * k + 32), ap("lUVA", 0, 32), ap("LP%d" % who, k, k + 1), MUL)
        ts(ap("lUQ"), ap("lUVW"), 5, SHR)
        for k in range(2):
            tt(ap("lHV", 32 * k, 32 * k + 32), ap("lKU", 32 * k, 32 * k + 32), ap("lUQ"), ADD)
        ts(ap("lHI"), ap("lHV"), 4095, AND); cp(ap("lHO"), ap("lHI")); ts(ap("lHH"), ap("lHI"), -2047.0, ADD)
        if not ask:
            if t > 1:
                cp(ind(ap(lent), ap("LX%d" % (t - 1), 0, 4)), ap(mark, 0, 64))
            for h in (1, 0):
                cp(ind(ap(lent, 0, ZD), ap("LM%d" % t, 16 * h, 16 * h + 8)), ap(mark))
            ts(ap("lb"), ap("LM%d" % t, 24, 25), 1024.0, MUL, ap("LP%d" % who, 3, 4), ADD)
        k = act(ap("lX", 768, 768 + LB), ind(ap(lent, 0, S), ap("lHO", 48, 48 + LB // 16)), AF.Copy)
        mm([(ap("DB", 256, 256 + LB), ap("IDN"), ap("ZT", 256, 256 + LB), True, False)]); mm([(ap("DB", 256, 256 + LB), ap("IDB"), ap("lX", 768, 768 + LB), False, True)])
        for lo, hi in LORD:
            x = ap("lX", lo, hi)
            if lo != 768:
                tt(x, ind(ap(lent, 0, S), ap("lHO", lo // 16, hi // 16)), ap("ZT", lo % 512, (hi - 1) % 512 + 1), SUB)
            act(ap3("lA", lo // 32, hi // 32, 0, 32), x if lo != 768 else ap("DB", 256, 256 + LB), AF.Abs); later(k)
            k = len(ops) - 1
        mm([(ap("CT", 64 * r, 64 * r + 64), ap("RL", 128 * r, 128 * r + 128), ap("lHH"), True, True) for r in range(8)])
        act(ap("lHT", 0, 512), ap("CT"), AF.Copy)
        for n in range(4):
            d = ("DA", "JP", "UVP", "DB")[n]
            mm([(ap(d, 64, 128), ap("IDB"), ap("ML", 64 * n, 64 * n + 64), True, False), (ap(d, 64, 128), ap("IDB"), ap("PZL"), False, False)])
            mm([(ap(d, 64, 128), slq(r), ap3("lA", 8 * n, 8 * n + 8, 8 * r, 8 * r + 8), False, r == 3) for r in range(4)])
            if n < 2:
                ts(ap("lRM", 64 * n, 64 * n + 64), ap(d, 64, 128), b16 if ask else ap("lb"), MIN)
            else:
                for k in range(2):
                    lo = 64 * n - 128 + 32 * k
                    scan(ap("lKS", lo, lo + 32), ap("lRM", lo, lo + 32), ap(d, 64 + 32 * k, 96 + 32 * k), MIN, MIN, 8 * BIG)
        ts(ap("lMI"), ap("lKS", 31, 128, 32), 1023, AND); cp(ap("lLL"), ap("lMI"))
        tt(ap("lHM"), ind(ap("lHT"), ap("lLL")), ap("MWR", 0, 64), MUL)
        scan(ap("lHS"), ap("RST", 0, 64), ap("lHM"))
        reg = [(("DA", "JP")[c // 2], 256 + 80 * (c % 2), 16 * c + 16) for c in range(4)]
        for c in (0, 2):
            mm([(ap(d, lo, lo + w + 1), ap("IDB"), ap("lTR", 64 - w, 65), k == 0, False) for k, (d, lo, w) in enumerate(reg[c:c + 2])])
        for c in (0, 2):
            mm([(ap(d, lo, lo + w), ap("BLKH"), ap("lHM", 0, w), False, k == 1) for k, (d, lo, w) in enumerate(reg[c:c + 2])])
        if not last:
            ts(ap("lHL"), ap("lHS", 15, 64, 16), 2047.0, ADD, 4095.0, MIN)
            act(ap("RS", 0, 64), ind(ap("TP" if ask else "TL%d" % who), ap("lHL")), AF.Copy)
        ts(ap("lET", 0, 320, 80), ap("lHS", 15, 64, 16), 2047.0, ADD, 4095.0, MIN)
        odd = 0 if ask else 8 * (t % 2)
        for c, (d, lo, w) in enumerate(reg):
            ts(ap("lET", 80 * c + 1, 80 * c + w + 2), ap(d, lo, lo + w + 1), ap("lHS", 16 * c + 15, 16 * c + 16), EQ, ap("DMP", odd + c, odd + c + 1), MUL)
            most(ap("lWS", c, c + 1), ap("lET", 80 * c, 80 * c + w + 2))
        if ask:
            ts(ap("RS", 64, 68), ap("lWS", 0, 4), -float(S), ADD, 0.0, MAX)
            k = swap("RB%d" % t, ap("RS", 64 * last, 72), "mb%d" % t, "lr", borrower)
        cp(ap("lLO", 0, 4), ap("lWS", 0, 4))
        if not ask:
            k = swap("LN%d" % t, ap("lLO"), "mn%d" % t, "lu", lender)
        if copy and t:
            j = swap("LX%d" % t, ap("lLO"), "mx%d" % t, "lf", T.cores[(rank + t % 3 - (t + 1) % 3) % 4]); ops[j]["after"] = [k]
            ops[ship(t + 1)[0]]["after"] = [j]
        act(ap("RSU"), ind(ap(lent), ap("lLO", 0, 4)), AF.Copy, bias=float(less))
        if ask:
            j = swap("RV%d" % t, ap("RSU"), "mn%d" % t, "lu", borrower)
            cp(ind(ap("UL0" if t else "US"), ap("lLO", 0, 4)), ap("C255", 0, 64))
        else:
            act(ind(ap("UF"), ap("LN%d" % t, 0, 4)), ap("ZERO", 0, 64), AF.Silu)
        if not t:
            for i in ship(1):
                ops[i]["after"] = [j]
            for k in range(0, S, 256):
                if k < 256 * CONV:
                    for j in (k, k + 128):
                        ts(ap("UF", j, j + 128), ap("US", j, j + 128), -255.0, ADD); ops[-1]["tag"] = "UF<"
                else:
                    act(ap("UF", k, k + 256), ap("US", k, k + 256), AF.Copy, bias=-255.0)
        if not last:
            mm([(ap("MS", 96, 97), ap("ONEB"), ap("SC", 16, 17), True, True)])
            cp(ap("PPI"), ap("MS", 96, 97)); ts(ap("PPJ"), ap("PPI"), 63, AND); ts(ap("b16b" if t % 2 else "b16a"), ap("PPJ"), 1024.0, MUL, ap("th16"), ADD)
            if copy:
                cp(ap("LO", 24, 25), ap("PPJ"))
        if t:
            ts(ind(ap(cx, OLD, END), ap("OBU")), ap("IC64"), 1.0, MUL, float(S + CAP * (t - 1)), ADD)
            dma(ext("yc", L * (t - 1), L * t), ap(cx, OLD, OLD + L, 1, slice(0, 128, 16)), 2.0)
        tt(ap("FW"), ind(ap("WN"), ap("JL")), ap("NM"), ADD)
        scan(ap("CMH"), ap("DJ"), ap("FW"), MAX, MIN); cp(ap("JL2"), ap("CMH", 15, 256, 16))
        if not last:
            act(ap(tx, 0, L), ind(ap("TP"), ap("HL")), AF.Copy)
            act(ap(wx, 0, L), ind(ap("WTAB"), ap("HL")), AF.Copy)
            act(ap(ty, OLD, OLD + L), ind(ap(tx), ap("JL2")), AF.Copy)
            act(ap(wy, OLD, OLD + L), ind(ap(wx), ap("JL2")), AF.Copy)
        act(ap(cy, OLD, OLD + L), ind(ap(cx), ap("JL2")), AF.Copy)
        for c in range(4):
            if ask:
                ts(ap("OBU", c, c + 1), ap("RB%d" % t, 64 + c, 65 + c), ap("FA", c, c + 1), MAX)
            else:
                ts(ap("OBU", c, c + 1), ap("lWS", c, c + 1), -float(S), ADD, ap("FA", c, c + 1), MAX)
        if not last:
            cp(ind(ap(ty, OLD, END), ap("OBU")), ap("RB%d" % t if ask else "RS", 0, 64)); cp(ind(ap(wy, OLD, END), ap("OBU")), ap("WTAB", 0, 64))
        dma(ext("yu", S + CAP * t, S + CAP * t + CAP), ap("RV%d" % t if ask else "RSU"), 2.0)
        if last:
            ts(ind(ap(cy, OLD, END), ap("OBU")), ap("IC64"), 1.0, MUL, float(S + CAP * t), ADD)
            dma(ext("yc", L * t, L * t + L), ap(cy, OLD, OLD + L, 1, slice(0, 128, 16)), 2.0)
    dma(ext("yu", 0, S), ap("UL0", 0, S), 4.5)
    seen, at, early, both = {}, {}, None, None
    for i, o in enumerate(ops):
        if o["k"] == 0:
            early = early or at
            seen, at = {}, {}
        w = "<".join(x[-1 if k else 0][0].replace("th16", "b").rstrip("0123456789ab") if x else "" for k, x in enumerate((o["W"], o["R"])))
        w = w + "V" if "tag" in o else w
        seen[o["q"], w] = seen.get((o["q"], w), 0) + 1
        o["name"] = (o["k"] < 0, o["q"], w, seen[o["q"], w])
        if o["q"] != "N":
            at[w + "#%d" % seen[o["q"], w]] = i
        if early and (i + 1 == len(ops) or ops[i + 1]["k"] == 0):
            if not both:
                both = dict(at, **early)
                for chain in START + tuple("HO<HI " + y for y in LATER.split()):
                    got = [both[y if "#" in y else y + "#1"] for y in chain.split()]
                    for a, b in zip(got, got[1:]):
                        ops[b].setdefault("after", []).append(a)
            elif "UF<US#1" in both:
                both.update(at)
                for chain in SECOND:
                    got = [both[y if "#" in y else y + "#1"] for y in chain.split()]
                    for a, b in zip(got, got[1:]):
                        ops[b].setdefault("after", []).append(a)
                del both["UF<US#1"]
            for chain in FINAL if i + 1 == len(ops) else ASKED if "<ZL#1" in at else CHAINS if "UL<LX#1" in at else AFTER:
                got = [at[x] for x in (y if "#" in y else y + "#1" for y in chain.split()) if x in at]
                for a, b in zip(got, got[1:]):
                    ops[b].setdefault("after", []).append(a)
    return ops


_MEMO = {}


def order(ops, memo=None):
    memo = {} if memo is None else memo
    last = {}
    for i, o in enumerate(ops):
        pre = {}

        def add(j, wait):
            if j != i:
                pre[j] = pre.get(j, False) or wait
        for j in o.get("after", ()):
            pre[j] = False
        for j in o.get("waits", ()):
            pre[j] = True
        for kind in ("R", "W"):
            for nm, lo, hi, st in o[kind]:
                ps = nm in _PS
                for j, k2, lo2, hi2, st2 in last.get(nm, []):
                    same = ops[j]["q"] == o["q"]
                    if ps:
                        if same and o["q"] == "P":
                            add(j, False)
                        elif not same:
                            add(j, True)
                        continue
                    if kind == "R" and k2 == "R":
                        continue
                    if hi <= lo2 or hi2 <= lo or (st == st2 and st > 1 and (lo - lo2) % st):
                        continue
                    add(j, not (INORDER and same and o["q"] in "VS" and kind == "W"))
        for kind in ("R", "W"):
            for nm, lo, hi, st in o[kind]:
                ps = nm in _PS
                lst = last.setdefault(nm, [])
                if ps:
                    if lst and ops[lst[-1][0]]["q"] != o["q"]:
                        lst[:] = [e for e in lst if ops[e[0]]["q"] != o["q"]][-40:]
                elif kind == "W" and st == 1:
                    lst[:] = [e for e in lst if not (lo <= e[2] and e[3] <= hi) or e[0] == i]
                lst.append((i, kind, lo, hi, st))
        o["pre"] = pre
    n = len(ops)
    succ = [[] for _ in range(n)]
    for i, o in enumerate(ops):
        for j in o["pre"]:
            succ[j].append(i)

    def lag(j, k):
        if ops[k]["pre"][j]:
            return OWN if ops[k]["q"] == ops[j]["q"] else HOP
        return ops[j]["hold"] - ops[j]["c"] if "hold" in ops[j] else 0.0
    pres = [[(j, lag(j, i)) for j in ops[i]["pre"]] for i in range(n)]
    posts = [[(k, lag(i, k)) for k in succ[i]] for i in range(n)]

    def place(key, back, n=n):
        before, after = (posts, pres) if back else (pres, posts)
        left = [len(x) for x in before]
        ready = sorted((key[i], i) for i in range(n) if not left[i])
        beg, end, busy = [0.0] * n, [0.0] * n, {}
        while ready:
            i = ready.pop(0)[1]
            q, c, t = ops[i]["q"], ops[i]["c"], 0.0
            for j, d in before[i]:
                if end[j] + d > t:
                    t = end[j] + d
            if q != "N":
                hold = ops[i].get("hold", c)
                skip = c - hold if back else 0.0
                lst = busy.setdefault(q, [])
                p = len(lst)
                while p and lst[p - 1][1] > t + skip:
                    p -= 1
                while p < len(lst) and lst[p][0] < t + skip + hold - 1e-9:
                    t = max(t, lst[p][1] - skip); p += 1
                lst.insert(p, (t + skip, t + skip + hold))
            beg[i], end[i] = t, t + c
            for k, d in after[i]:
                left[k] -= 1
                if not left[k] and k < n:
                    ready.append((key[k], k)); ready.sort()
        return beg, end
    pri = [0.0] * n
    beg, end = place(range(n), False)
    for i in sorted(range(n), key=lambda i: (-beg[i], -i)):
        pri[i] = ops[i]["c"] + max([pri[k] + d for k, d in posts[i]], default=0.0)
    beg, end = place([-x for x in pri], False)
    best = (max(end), [max(pri) - x for x in pri])
    for _ in range(PASSES):
        beg, end = place([-x for x in end], True)
        late = [max(end) - x for x in end]
        beg, end = place(late, False)
        best = min(best, (max(end), late))
    base = best[1]
    name, seen = [], {}
    for o in ops:
        if o["k"] == 0:
            seen = {}
        w = (o["k"] < 0, o["q"], o["W"][0][0].rstrip("0123456789ab") if o["W"] else "", o["name"][2])
        seen[w] = seen.get(w, 0) + 1
        name.append(w + (seen[w],))
    first = [i for i in range(n) if ops[i]["k"] == 0] + [n]
    mid = {name[i]: base[i] - base[first[2] + 1] for i in range(first[2], first[3])}
    for r in range(RO):
        zero = base[first[r] + 1]
        for i in range(first[r], first[r + 1]):
            base[i] = zero + mid[name[i]] if name[i] in mid else base[i - 1]
    above, near = [], []
    for i, o in enumerate(ops):
        waits = [j for j, w in o["pre"].items() if w or o["q"] == "N"]
        far = 0
        for j in waits:
            far |= above[j]
        near.append([j for j in waits if not far >> j & 1])
        for j in waits:
            far |= 1 << j
        above.append(far)
    guess = []
    for cy, ga, sct, hop, own, flight, sfix, pe in GUESSES:
        c = [a + cy * (b + ga * g + sct * s) + pe * o["many"] + sfix * (o["q"] == "S") + flight * (o["q"] == "N") for o in ops for a, b, g, s in [o["v"]]]
        guess.append((c, [o.get("hold", x) for o, x in zip(ops, c)], [[(j, 0.0 if o["q"] == "N" and not o["pre"][j] else own if ops[j]["q"] == o["q"] else hop) for j in near[i]] for i, o in enumerate(ops)]))

    key, _ = place(base, False)
    span = key[first[3] + 1] - key[first[2] + 1]
    mid = {name[i]: key[i] - key[first[2] + 1] for i in range(first[2], first[3])}
    zero = key[first[0] + 1]
    for r in range(RO):
        for i in range(first[r], first[r + 1]):
            key[i] = zero + r * span + mid[name[i]] if name[i] in mid else key[i - 1]
    qn = ["NVSPGY".index(o["q"]) for o in ops]
    deps = [list(o["pre"]) for o in ops]
    whole, left, nets = [i for i in range(n) if not deps[i]], [len(x) for x in deps], {}
    for i in whole:
        for k in succ[i]:
            left[k] -= 1
            if not left[k]:
                whole.append(k)

    def sequence(key, lo, hi):
        if (lo, hi) not in nets:
            left, nxt, up = [0] * n, [[] for _ in range(n)], {}
            for i in whole:
                if lo <= i < hi:
                    mine = [j for j in deps[i] if lo <= j < hi]
                    far = 0
                    for j in mine:
                        far |= up[j]
                    for j in mine:
                        if not far >> j & 1:
                            left[i] += 1; nxt[j].append(i)
                    for j in mine:
                        far |= 1 << j
                    up[i] = far
            nets[lo, hi] = (left, nxt, [i for i in range(lo, hi) if not left[i]])
        left, nxt, roots = nets[lo, hi]
        left = list(left)
        ready = sorted(((key[i], i) for i in roots), reverse=True)
        seq = []
        while ready:
            i = ready.pop()[1]
            seq.append(i)
            grown = False
            for k in nxt[i]:
                left[k] -= 1
                if not left[k]:
                    ready.append((key[k], k)); grown = True
            if grown:
                ready.sort(reverse=True)
        return seq

    def length(seq, goal):
        total, held = 0.0, set()
        if goal is not None:
            seq = seq[:seq.index(goal) + 1]
        for c, hold, pre in guess:
            free, by, end, why = [0.0] * 6, [-1] * 6, [-1.0] * n, [-1] * n
            for i in seq:
                q = qn[i]
                t, w = free[q], by[q]
                for j, d in pre[i]:
                    if end[j] + d > t:
                        t, w = end[j] + d, j
                end[i], why[i] = t + c[i], w
                if q:
                    free[q], by[q] = t + hold[i], i
            i = end.index(max(end)) if goal is None else goal
            total += end[i]
            while why[i] >= 0:
                if why[i] not in ops[i]["pre"]:
                    held.add((i, why[i]))
                i = why[i]
        return total, sorted(held)

    def filled(key, lo, hi):
        beg, _ = place(key, False, hi)
        return sorted(range(hi), key=lambda i: (beg[i], i))

    def improve(key, lo, hi, goal, alike, tries, fill=False):
        movable = sorted(alike)
        cur, held = length((filled if fill else sequence)(key, lo, hi), goal)
        best = (cur, key)
        for step in range(tries):
            new = list(key)
            pick = [p for p in held if p[0] in alike or p[1] in alike]
            kind = int(rnd.randint(5)) if pick else 4
            i, j = pick[int(rnd.randint(len(pick)))] if pick else (0, 0)
            more = abs(float(rnd.normal())) * (0.001, 0.2, 0.8)[int(rnd.randint(3))] + 1e-4
            if kind < 2 and i in alike:
                todo = [(i, key[j] - more)]
            elif kind < 4 and j in alike:
                far = min([key[k] for k in succ[j]], default=key[i] + 5.0) - 1e-4
                todo = [(j, key[i] + more if kind == 2 or far < key[i] else far - (far - key[i]) * float(rnd.random_sample()) ** 2)]
            else:
                i = movable[int(rnd.randint(len(movable)))]
                todo = [(i, key[i] + float(rnd.normal()) * (0.2, 0.8, 2.5)[int(rnd.randint(3))])]
            while todo:
                i, x = todo.pop()
                d = x - new[i]
                for k in alike[i]:
                    new[k] += d
                if d < 0:
                    todo += [(j, x - 1e-4) for j in deps[i] if j in alike and new[j] > x]
            x, h = length((filled if fill else sequence)(new, lo, hi), goal)
            if x <= cur + HEAT * (1 - step / tries) * float(rnd.exponential()):
                cur, held, key = x, h, new
                best = min(best, (cur, key))
        return best[1]
    if not memo:
        rnd = np.random.RandomState(SEED)
        goal = [[i for i in range(first[r], first[r + 1]) if name[i][2] == "K" and name[i][1] == "V"][0] for r in range(RO)]
        same = {}
        for i in range(first[0], n):
            same.setdefault(name[i], []).append(i)
        key = improve(key, first[2], first[5], goal[4], {i: same[name[i]] for i in range(first[2], first[5])}, TRIES)
        for i in range(first[1] - 1, -1, -1):
            if name[i] not in mid:
                key[i] = min([key[k] - d for k, d in posts[i]], default=zero) - ops[i]["c"]
        key = improve(key, 0, first[2], goal[1], {i: [i] for i in range(first[1])}, TRIES // 8, True)
        beg, _ = place(key, False, first[3])
        shift = key[first[2] + 1] - beg[first[2] + 1]
        key[:first[2]] = [x + shift for x in beg[:first[2]]]
        key = improve(key, 0, first[2], goal[1], {i: [i] for i in range(first[1])}, TRIES)
        key = improve(key, first[1] - 80, first[3], goal[2], {i: [i] for i in range(first[1] - 80, first[2])}, TRIES // 4)
        key = improve(key, first[4], n, None, {i: [i] for i in range(first[5], n)}, TRIES // 4)
        memo["key"] = key
    seq = sequence(memo["key"], 0, n)
    for k, i in enumerate(seq):
        ops[i]["t"] = k
    return seq, span


def rank_program(g, core, T, topo):
    rank = T.rank_of(core)
    if rank is None:
        for r, c in enumerate(T.cores):
            hs = helpers(c, T, topo)
            if core in hs:
                helper_program(g, core, r, hs.index(core), T, topo)
        return
    ops = build(rank, core, T, topo)
    seq, _ = order(ops, _MEMO)
    eng = {"V": g.vector, "S": g.scalar, "P": g.tensor, "G": g, "Y": g.sync, "Z": g.scalar}
    total = {}
    known = {q: {} for q in eng}
    for i in seq:
        o = ops[i]
        q = o["q"]
        if "left" in o:
            o["at"], o["clock"] = ops[o["left"]]["at"], ops[o["left"]]["clock"]
            continue
        if q == "N":
            o["at"] = (o["sem"], o["inc"]); o["clock"] = {}
            total[o["sem"]] = o["inc"]
            continue
        kn = known[q]
        need = [ops[j] for j, w in o["pre"].items() if w]
        need.sort(key=lambda p: -p.get("t", 0.0))
        for p in need:
            sem, val = p["at"]
            if kn.get(sem, 0) >= val:
                continue
            eng[q].wait_ge(T.sem[sem], val)
            kn[sem] = val
            for a, b in p["clock"].items():
                if kn.get(a, 0) < b:
                    kn[a] = b
        r = o["fn"](g)
        if o["sem"] is None:
            sem = "s" + q
            total[sem] = total.get(sem, 0) + 1
            r.then_inc(T.sem[sem], 1)
        elif "n" in o:
            sem = o["sem"]
            total[sem] = total.get(sem, 0) + o["n"]
        else:
            sem = o["sem"]
            total[sem] = o["inc"]
            r.then_inc(T.sem[sem], o["inc"])
        o["at"] = (sem, total[sem])
        o["clock"] = dict(kn)
    for sem, val in total.items():
        g.wait_ge(T.sem[sem], val)
